import numpy as np, ml_dtypes
CORES = [16,17,18,19,32,33,34,35]
N = 8
BF = ml_dtypes.bfloat16
P, TW, M, RO = 2048, 4096, 4, 5
def parts(rng):
    v = rng.integers(0, 128, (N, 8, 16, P)); v[:, :, 15] = rng.integers(0, 2, (N, 8, P))
    t = rng.integers(0, 128, (N, 8, 16, TW)); t[:, :, 15] = rng.integers(0, 2, (N, 8, TW))
    return v, t, rng.integers(1, 256, (N, 8, 16)), rng.integers(0, 2048, (N, 8, RO, M))
def pack(v, t, w, k):
    return {"x": v.reshape(N, 128, P).astype(np.float32).astype(BF), "tm": t.reshape(N, 128, TW).astype(np.float32).astype(BF),
            "wt": np.ascontiguousarray(w.reshape(N, 128, 1)).astype(np.int32),
            "km": np.repeat(k.reshape(N, 8, 1, RO * M), 16, axis=2).reshape(N, 128, RO * M).astype(np.int32)}
def aim(rng, q, noth):
    u = np.arange(1, 4096, 2); i = u.copy()
    for _ in range(4): i = (i * (2 - u * i)) & 4095
    kk = ((q - (u * u >> 5)) * i) & (P - 1)
    ok = np.flatnonzero((kk < 2048) & (((u * u >> 4) & (TW - 1)) != noth))
    s = int(rng.choice(ok)); return int(u[s]), int(kk[s])
def column(rng, w, u, s):
    c = rng.integers(0, 128, 16); c[15] = s; c[:2] = 0
    z = (u - int(np.sum(w * c))) & 4095; c[0] = z & 63; c[1] = z >> 6
    return c
def setup_inputs(rng):
    return pack(*parts(rng))
def setup_inputs_ends(rng):
    v, t, w, k = parts(rng); w[:, :, 0] = 1; w[:, :, 1] = 64; w[:, :, 15] = 0
    for r in range(N):
        o = (r + 1) % N
        for g in range(8):
            case = (g - r) % 9
            a = int(rng.integers(1, P // 4)); b = int(rng.integers(P // 2, 3 * P // 4))
            if case < 2: a, b = 0, P - 1
            if case in (2, 3): b = a + 1
            if case == 8: a, b = int(rng.integers(1, P // 8)), int(rng.integers(7 * P // 8, P - 8))
            p, q = a, b
            if case == 7 or (case < 6 and rng.random() < 0.5): p, q = b, a
            s = int(rng.integers(0, 2)); u, k[r, g, 0, 0] = aim(rng, q, -1); c = column(rng, w[r, g], u, s); h = (u * u >> 4) & (TW - 1)
            if case == 4: v[r, g, 15] = s
            v[r, g, :, p] = c; v[r, g, :, q] = c
            if case in (0, 3): v[r, g, 15, q] = 1 - s
            t[o, g, :15, h] = c[:15]
            if case == 6: v[r, g, :, int(rng.integers(a + 1, b))] = c
            if case == 7: v[r, g, :, b + 3] = c
            if case in (1, 4, 5, 7, 8):
                p2, q2 = {1: (P // 3, P // 2), 4: (a + 1, P - 1), 5: (b - 1, b + 1), 7: (a + 2, b - 2), 8: (P // 2, P - 3)}[case]
                if (case == 4 and r % 2 == 0) or rng.random() < 0.5: p2, q2 = q2, p2
                u2, k[r, g, 0, 1] = aim(rng, q2, h); c2 = column(rng, w[r, g], u2, s if case == 4 else int(rng.integers(0, 2))); h2 = (u2 * u2 >> 4) & (TW - 1)
                v[r, g, :, p2] = c2; v[r, g, :, q2] = c2; t[o, g, :15, h2] = c2[:15]; t[o, g, 0, h2] = c2[0] ^ (2 if case == 8 else 1)
            if case == 8:
                ks = np.arange(2048); zs = ((u * u >> 5) + ks * u) & (P - 1)
                ks = ks[(zs > a) & (zs < b) & (zs != P // 2)]
                k[r, g, 0, 2] = int(rng.choice(ks)); z = ((u * u >> 5) + int(k[r, g, 0, 2]) * u) & (P - 1)
                cz = c.copy(); cz[0] = c[0] ^ 1; uz = (u + int(cz[0]) - int(c[0])) & 4095
                v[r, g, :, z] = cz; t[o, g, :15, (u * uz >> 4) & (TW - 1)] = c[:15]
    return pack(v, t, w, k)
def setup_inputs_kinds(rng):
    v, t, w, k = parts(rng); w[:] = w[:1].copy(); w[:, :, 15] = 0
    for g in (0, 2, 4):
        w[:, g, 0] = 1; w[:, g, 1] = 64; w[:, g, (2 if g == 2 else 8):] = 0
        u = 3 if g == 4 else 2 * int(rng.integers(0, 2048)) + 1; c = column(rng, w[0, g], u, 0)
        if g != 2: v[:, g, :8] = c[:8, None]
        else:
            v[:, g, :2] = c[:2, None]; v[:, g, 2:15] = rng.integers(0, 41, (N, 13, P)); k[:, g, 0] = k[:, g, 0, :1].copy()
            for r in range(N): v[r, g, 2:15, ((u * u >> 5) + int(k[r, g, 0, 0]) * u) & (P - 1)] = rng.integers(120, 128, 13)
    for g in (1, 3, 5, 6, 7):
        n = 5 if g % 2 else int(rng.integers(2, 6)); kd = rng.integers(0, 128, (16, n))
        if g % 2:
            kd[:, 4] = rng.integers(40, 88, 16)
            kd[:, :4] = kd[:, 4:] + rng.integers(8, 41, (16, 4)) * (2 * rng.integers(0, 2, (16, 4)) - 1)
        for r in range(N):
            kind = rng.integers(0, n, P)
            if g % 2:
                c = r % 4; uc, u4 = [int(np.sum(w[r, g] * kd[:, i])) & 4095 for i in (c, 4)]
                kind[((u4 * u4 >> 5) + k[r, g, 0] * u4) & (P - 1)] = c
                t[(r + 1) % N, g, :15, (uc * u4 >> 4) & (TW - 1)] = (kd[:15, c] + kd[:15, 4]) >> 1
            v[r, g] = kd[:, kind]
    v[:, :, 15] = rng.integers(0, 2, (N, 8, P))
    return pack(v, t, w, k)
def setup_inputs_void(rng):
    v, t, w, k = parts(rng); w[:, :, 0] = 1; w[:, :, 1] = 64; k[:, ::2] = k[:, ::2, :1, :1].copy()
    for g in (0, 6):
        v[:, g, 2:15] &= 3; t[:, g, :15] = 124 + (t[:, g, :15] & 3)
    us = np.arange(4096); j = np.arange(P)
    for r in range(N):
        for g in range(8):
            pre = np.full(P, -1); pre[((us * us >> 5) + int(k[r, g, 0, 0]) * us) & (P - 1)] = us
            z = (pre - np.sum(w[r, g, 2:, None] * v[r, g, 2:], axis=0)) & 4095
            v[r, g, 0] = np.where(pre >= 0, z & 63, v[r, g, 0]); v[r, g, 1] = np.where(pre >= 0, z >> 6, v[r, g, 1])
            if g in (0, 6):
                u = np.sum(w[r, g, :, None] * v[r, g], axis=0) & 4095; q = ((u * u >> 5) + int(k[r, g, 0, 0]) * u) & (P - 1)
                h = (u * u[q] >> 4) & (TW - 1); free = np.flatnonzero((q == j) & ~np.isin(h, h[q != j]))
                if len(free):
                    p = int(rng.choice(free)); t[(r + 1) % N, g, :15, int(h[p])] = v[r, g, :15, p]
    return pack(v, t, w, k)
def setup_inputs_small(rng):
    v, t, w, k = parts(rng)
    return pack(v & 1, t & 1, w, k)
def setup_inputs_spread(rng):
    v, t, w, k = parts(rng); both = []
    for a in (v, t):
        n = a.shape[-1]; b = np.minimum((np.exp2(8 * rng.random((N, 8, 1, n))) * rng.random(a.shape)).astype(np.int64), 127)
        z = rng.integers(0, 32, (N, 8, 1, n)); b = np.where(z == 0, 0, np.where(z == 1, 127, b)); b[:, :, 15] = a[:, :, 15]; both.append(b)
    w = np.minimum(np.exp2(8.1 * rng.random((N, 8, 16))).astype(np.int64), 255); w[:, :, 3] = 0; w[:, :, 4] = 255
    w[:, 5] = rng.integers(200, 256, (N, 16)); w[:, 6] = 255
    both[0][:, 5, :15] = rng.integers(100, 128, (N, 15, P)); both[0][:, 6, :15] = rng.integers(64, 128, (N, 15, P))
    both[0][:, 6, :15, P - 1] = 127; both[0][:, 6, 15, P - 1] = 1
    k = np.minimum(np.exp2(11.1 * rng.random((N, 8, RO, M))).astype(np.int64) - 1, 2047); k[:, 1, 0, 0] = 0; k[:, 2, 0, 1] = 2047
    return pack(both[0], both[1], w, k)
def check_inputs(d):
    bad = []
    for name in ("x", "tm"):
        a = np.asarray(d[name]).astype(np.float32)
        if not np.all((a >= 0) & (a <= 127) & (np.floor(a) == a)): bad.append("whole numbers of " + name)
        if not np.all(a[:, 15::16] <= 1): bad.append("signs of " + name)
    for name, hi in (("wt", 255), ("km", 2047)):
        if np.min(d[name]) < 0 or np.max(d[name]) > hi: bad.append("range of " + name)
    a = np.asarray(d["km"]); a = a.reshape(a.shape[0], 8, 16, -1)
    if not np.all(a == a[:, :, :1]): bad.append("rows of km alike")
    return bad
def reference(x, tm, wt, km):
    v = x.astype(np.float32).astype(np.int32).reshape(N, 8, 16, P); tp = tm.astype(np.float32).astype(np.int32).reshape(N, 8, 16, TW)
    w = wt.astype(np.int32).reshape(N, 8, 16, 1); k = km.astype(np.int32).reshape(N, 8, 16, RO, M)[:, :, 0]; j = np.arange(P)
    for t in range(RO):
        u = np.add.reduce(w * v, axis=2, dtype=np.int32) & 4095
        bq = bd = None
        for m in range(M):
            q = ((u * u >> 5) + k[:, :, t, m][:, :, None] * u) & (P - 1)
            xq = np.take_along_axis(v, q[:, :, None, :], 3)
            dm = np.where(q == j, 8192, np.add.reduce(np.abs(v - xq)[:, :, :15], axis=2))
            if m == 0: bq, bd = q, dm
            else: bq, bd = np.where(dm < bd, q, bq), np.minimum(bd, dm)
        xq = np.take_along_axis(v, bq[:, :, None, :], 3)
        h = (u * np.take_along_axis(u, bq, 2) >> 4) & (TW - 1)
        got = np.stack([np.take_along_axis(tp[(r + 1 + t % (N - 1)) % N], h[r][:, None, :], 2) for r in range(N)])
        e = bd + np.add.reduce(np.abs(v + xq - 2 * got)[:, :, :15], axis=2)
        alike = v[:, :, 15] == xq[:, :, 15]; lo = np.minimum(j, bq); hi = np.maximum(j, bq)
        nv = np.empty_like(v)
        for r in range(N):
            for g in range(8):
                p = int(np.argmin(e[r, g])); a, b = int(lo[r, g, p]), int(hi[r, g, p])
                z = v[r, g].copy(); z[:15, a] = (v[r, g, :15, a] + v[r, g, :15, b]) >> 1
                tp[r, g, :, int(h[r, g, p])] = z[:, a]
                if not alike[r, g, p]:
                    z[:, a + 1:b + 1] = z[:, a + 1:b + 1][:, ::-1].copy(); z[15, a + 1:b + 1] = 1 - z[15, a + 1:b + 1]
                else:
                    c, d = b, P - 1
                    inside = alike[r, g] & (lo[r, g] > a) & (lo[r, g] < b)
                    if np.any(inside):
                        p2 = int(np.argmin(np.where(inside, e[r, g], 2 ** 20)))
                        if hi[r, g, p2] > b: c, d = int(lo[r, g, p2]), int(hi[r, g, p2])
                    z = z[:, np.concatenate([j[:a + 1], j[b + 1:d + 1], j[c + 1:b + 1], j[a + 1:c + 1], j[d + 1:]])]
                nv[r, g] = z
        v = nv
    return {"y": v.reshape(N, 128, P).astype(np.float32).astype(BF)}

@@ -1,0 +1,591 @@
+from concourse.mybir import AluOpType as A, AxisListType as AX, ActivationFunctionType as F
+
+RO, M, P, TW = 5, 4, 2048, 4096
+W0 = 16
+NX = W0 + 2 * P
+N0 = 56
+PART = ((0, N0), (N0, 128))
+VIT = {(0, 0), (0, 1), (1, 0), (1, 1), (3, 1)}
+PORD = (1, 0)
+MORD = (2, 0, 3, 1)
+BX, BP, BQ, BU, BM, BE = 3.0, 1.0, 5.0, 6.0, -8.0, -2.0
+
+SCRATCH = {}
+_PS = ["p%d" % i for i in range(8)]
+_B2 = ("bfloat16", "float16", "uint16")
+_CS = {n: i for i, n in enumerate("kg15 kg kr k odd r15 fm half dbl flw wf wu w1 mk0 padc dvc dsc bec f2 mone r1 kmin har hpf nf kmin2 "
+                                  "a b dir inv ba aI bI m1 m3 x3 K2 cdef ddef xd an1 xC xI w f valid xc xe".split())}
+_CI = {n: i for i, n in enumerate("ik ikg ikr iodd ni".split())}
+for _a in _PS:
+    SCRATCH[_a] = ("psum", [128, 512], "float32")
+for _d, _l in (("bfloat16", (("xin", P), ("tmo", TW), ("xb0", NX), ("xb1", NX), ("yo", P), ("xc", P), ("mb", 144), ("bu", 144), ("bf", 144), ("bs", 144), ("bds", 144), ("be", 144),
+                             ("ib", 128), ("nib", 128), ("d2kb", 128), ("dvoid", 128), ("dm4k", 128), ("lx", 128), ("cm", 384), ("eq", 512), ("gm", 4 * P), ("ab", 4 * P), ("vc", 128),
+                             ("dir", 128), ("sp", P), ("gq", P), ("rr", P), ("ga", P), ("ab2", P), ("t1", 128), ("t2", 128)) + tuple(("tb%d" % k, TW + 16) for k in range(RO))),
+               ("float16", (("bdv", 144), ("i16", 128), ("ni16", 128), ("p2i", 128), ("m2i", 128), ("d2k16", 128), ("dn8k", 128), ("pw16", 128), ("f1", 128), ("q16", 512),
+                            ("mx", 4 * P), ("d16", 128), ("qs16", 128), ("cc", 128), ("cmn", 128), ("gt", 896))),
+               ("float32", (("xw", P), ("cs", 64), ("kmf", RO * M), ("lxa", 128), ("lxc", 128), ("ob", 128), ("mk16", 16), ("pwf", 128), ("b0", 128), ("b1", 128), ("b2", 128),
+                            ("aa", 4), ("pd", 5), ("qd", 5), ("qe", 3), ("dg", 16), ("oh", 128), ("pr", 256), ("hpr", 128), ("k2a", 128), ("k2", 128), ("oh2", 128), ("nc", 16),
+                            ("upv", 16))),
+               ("int32", (("wti", 1), ("kmi", RO * M), ("ci", 8), ("ij", 144), ("ic", 128), ("jb", 128), ("ui", 128), ("u", 128), ("sq", 128), ("sh", 128), ("qv", 512), ("qi", 512),
+                          ("bk", 128), ("q", 128), ("di", 128), ("uq", 128), ("uq2", 128), ("uu", 128), ("h", 128))),
+               ("uint16", (("ql", 512), ("qsl", 128), ("hl", 128), ("nl", 2), ("pl", 128), ("msg", 128), ("land", 320)))):
+    for _a, _c in _l:
+        SCRATCH[_a] = ("sbuf", [128, _c], _d)
+_LK = [(t, s) for t in range(1, RO) for s in range(t)]
+SEMAPHORES = (["sv", "ss", "st", "sg", "lmsg", "lown", "lx0", "lx1", "lw", "lk", "lt0", "lt1", "lt2", "lt3", "st0", "st1"] + ["xc%d" % k for k in range(RO)]
+              + ["ta%d" % k for k in range(RO)] + ["ls%d" % k for k in range(4)] + ["m%d_%d" % ts for ts in _LK])
+
+CYC, TCY, GC, WAKE, SELF = 0.83e-3 * 1.25, 0.42e-3 * 1.25, 1.56, 0.15, 0.06
+
+
+def _ap(T, r):
+    return T[r[0]][:, r[1]:r[2]] if len(r) == 3 else T[r[0]][:, r[1]:r[2]:r[3]]
+
+
+def _n(r):
+    return r[2] - r[1]
+
+
+def _ps(r):
+    return r[0] in _PS
+
+
+def C(n):
+    return ("cs", _CS[n], _CS[n] + 1) if n in _CS else ("ci", _CI[n], _CI[n] + 1)
+
+
+def build():
+    ops, BST, AFT = [], [0.0], []
+
+    def add(q, cost, emit, reads, writes, done=None, after=()):
+        ops.append({"q": q, "cost": cost, "emit": emit, "reads": reads, "writes": writes, "done": done, "after": list(after) + AFT, "boost": BST[0]})
+        return len(ops) - 1
+
+    def isc(*xs):
+        return [x for x in xs if isinstance(x, tuple)]
+
+    def val(T, x):
+        return _ap(T, x) if isinstance(x, tuple) else x
+
+    def fast(*rs):
+        return 0.5 if all((not _ps(r)) and SCRATCH[r[0]][2] in _B2 for r in rs) else 1.0
+
+    def vt(out, a, b, op):
+        c = _n(out) * (1 if _ps(a) or _ps(b) else 2)
+        add("v", max(64, c) * CYC, lambda g, T, x: g.vector.tensor_tensor(_ap(T, out), _ap(T, a), _ap(T, b), op), [a, b], [out])
+
+    def vs(out, a, s1, op0, s2=None, op1=None):
+        def e(g, T, x):
+            if op1 is None:
+                return g.vector.tensor_scalar(_ap(T, out), _ap(T, a), val(T, s1), None, op0)
+            return g.vector.tensor_scalar(_ap(T, out), _ap(T, a), val(T, s1), val(T, s2), op0, op1)
+        return add("v", max(64, _n(out) * fast(out, a)) * CYC, e, [a] + isc(s1, s2), [out])
+
+    def vcopy(out, a):
+        add("v", max(64, _n(out) * fast(out, a)) * CYC, lambda g, T, x: g.vector.tensor_copy(_ap(T, out), _ap(T, a)), [a], [out])
+
+    def vred(out, a, op):
+        add("v", max(64, _n(a)) * CYC, lambda g, T, x: g.vector.tensor_reduce(_ap(T, out), _ap(T, a), AX.X, op), [a], [out])
+
+    def vset(out, c):
+        add("v", max(64, _n(out)) * CYC, lambda g, T, x: g.vector.memset(_ap(T, out), c), [], [out])
+
+    def vgt(out, win, off, b, op):
+        add("v", 0.05 + _n(out) * GC * CYC, lambda g, T, x: g.vector.tensor_tensor(_ap(T, out), _ap(T, win).indirect(_ap(T, off)), _ap(T, b), op), [win, off, b], [out])
+
+    def vgs(out, win, off, s):
+        add("v", 0.05 + _n(out) * GC * CYC, lambda g, T, x: g.vector.tensor_scalar(_ap(T, out), _ap(T, win).indirect(_ap(T, off)), val(T, s), None, A.mult), [win, off] + isc(s), [out])
+
+    def sa(out, a, func, bias=0.0, scale=1.0):
+        return add("s", (60 + max(64, _n(out))) * CYC, lambda g, T, x: g.scalar.activation(_ap(T, out), _ap(T, a), func, bias=val(T, bias), scale=val(T, scale)), [a] + isc(bias, scale), [out])
+
+    def lin(out, a, scale, bias):
+        sa(C(out), C(a), F.Identity, bias=bias, scale=scale)
+
+    def sg(out, win, off, bias=0.0, scale=1.0):
+        add("s", 0.065 + _n(out) * GC * CYC, lambda g, T, x: g.scalar.activation(_ap(T, out), _ap(T, win).indirect(_ap(T, off)), F.Identity, bias=bias, scale=val(T, scale)), [win, off] + isc(scale), [out])
+
+    def mm(out, parts, start=True, stop=True):
+        cost = len(parts) * max(64, _n(out)) * TCY * (4 if SCRATCH[parts[0][0][0]][2] == "float32" else 1)
+
+        def e(g, T, x):
+            for k, (l, r) in enumerate(parts):
+                i = g.tensor.matmul(_ap(T, out), _ap(T, l), _ap(T, r), start and k == 0, stop and k == len(parts) - 1)
+            return i
+        add("t", cost, e, [y for lr in parts for y in lr] + ([] if start else [out]), [out])
+
+    def wrapped(b, src, c0, n):
+        return [((b, 15 - i, 143 - i), (src, c0 + i, c0 + n, 16)) for i in range(16)]
+
+    def ld(sem, q, out, src, c0, c1):
+        add(q, 0.1, lambda g, T, x: (g.sync if q == "d" else g.scalar).dma_start(_ap(T, out), T[src][:, c0:c1]), [], [out], done=lambda x: (sem, 16))
+
+    def blocks(n):
+        return [(b, min(b + 512, n)) for b in range(0, n, 512)]
+
+    TP = [(0, 256), (256, 1536), (1536, 2816), (2816, TW)]
+    BST[0] = 50.0
+    ld("lt0", "sd", ("tmo",) + TP[0], "tm", *TP[0])
+    ld("lw", "d", ("wti", 0, 1), "wt", 0, 1)
+    ld("lx0", "d", ("xin", 0, 1024), "x", 0, 1024)
+    ld("lx1", "sd", ("xin", 1024, P), "x", 1024, P)
+    BST[0] = 0.0
+    ld("lk", "d", ("kmi", 0, RO * M), "km", 0, RO * M)
+    for k in range(1, 4):
+        ld("lt%d" % k, "d" if k % 2 else "sd", ("tmo",) + TP[k], "tm", *TP[k])
+
+    def iota(out, pat, base, cmul):
+        add("g", 0.3, lambda g, T, x: g.iota(_ap(T, out), pat, base, cmul), [], [out])
+
+    def full(n, c=128):
+        return (n, 0, c)
+    iota(C("ik"), [[1, 1]], 0, 1)
+    iota(full("ij", 144), [[1, 144]], 0, 0)
+    iota(full("ic"), [[16, 128]], 0, 0)
+    ij, J, mb, PWP = full("ij"), full("ij", 144), full("mb", 144), ("p0", 256, 384)
+    vs(C("ikg"), C("ik"), 112, A.bitwise_and)
+    vs(C("ikr"), C("ik"), 15, A.bitwise_and)
+    vcopy(C("k"), C("ik"))
+    vcopy(C("kr"), C("ikr"))
+    vs(C("kg15"), C("ikg"), 15.0, A.add)
+    vs(C("r15"), C("kr"), 15.0, A.is_equal)
+    vs(C("fm"), C("kr"), 15.0, A.is_lt)
+    vs(C("half"), C("fm"), -0.5, A.mult, 1.0, A.add)
+    for c0 in (0, 1024):
+        vs(("xb0", W0 + c0, W0 + c0 + 1024), ("xin", c0, c0 + 1024), C("half"), A.mult)
+    vs(mb, J, C("kg15"), A.is_equal)
+    vcopy(C("wf"), full("wti", 1))
+    vs(C("w1"), C("fm"), 1.0, A.add)
+    vs(C("wu"), C("wf"), C("w1"), A.mult)
+    vs(full("bu", 144), mb, C("wu"), A.mult)
+    vcopy(full("kmf", RO * M), full("kmi", RO * M))
+    vs(full("pwf"), full("ic"), C("kr"), A.add)
+    vcopy(PWP, full("pwf"))
+    vs(full("ib"), ij, C("k"), A.is_equal)
+    vs(C("f2"), C("fm"), 2.0, A.mult)
+    vs(full("lxa"), full("mb"), C("f2"), A.mult)
+    vs(full("lxc"), full("ib"), C("fm"), A.mult)
+    vt(full("lx"), full("lxa"), full("lxc"), A.add)
+    vs(C("flw"), C("fm"), 2.0, A.mult, -1.0, A.add)
+    vset(C("mone"), -1.0)
+    vs(C("dvc"), C("fm"), 40960.0, A.mult, -8192.0, A.add)
+    vs(C("dsc"), C("fm"), 16384.0, A.mult)
+    vs(C("bec"), C("fm"), 4096.0, A.mult)
+    for nm, cn in (("bf", "f2"), ("bs", "r15"), ("bdv", "dvc"), ("bds", "dsc"), ("be", "bec")):
+        vs(full(nm, 144), mb, C(cn), A.mult)
+    for nm, v in (("nib", -1.0), ("i16", 1.0), ("d2kb", 2048.0), ("dn8k", -8192.0), ("dvoid", 15728640.0), ("dm4k", -4096.0), ("d2k16", 2048.0), ("ni16", -1.0), ("p2i", 2.0), ("m2i", -2.0)):
+        vs(full(nm), full("ib"), v, A.mult)
+    vcopy(full("pw16"), full("pwf"))
+    for m in range(1, 4):
+        vset(("cm", m * 128 - 128, m * 128), float(m))
+    vs(full("jb"), ij, 112, A.bitwise_and)
+    vcopy(C("kg"), C("ikg"))
+    vs(full("ob"), full("jb"), C("kg"), A.is_equal)
+    vs(full("mk16", 16), ("ij", 0, 16), C("kr"), A.is_equal)
+    vs(C("iodd"), C("ik"), 1, A.bitwise_and)
+    vcopy(C("odd"), C("iodd"))
+    vs(C("mk0"), C("kr"), 0.0, A.is_equal)
+    vs(C("padc"), C("kr"), 0.0, A.is_gt, float(TW), A.mult)
+    vt(C("padc"), C("padc"), C("kr"), A.add)
+    vs(C("dbl"), C("fm"), 1.0, A.add)
+    vset(("xb0", 0, W0), 0.0)
+    vset(("xb1", 0, W0), 0.0)
+    vset(full("msg"), 0)
+
+    last = 0
+    for k in range(4):
+        r = TP[k]
+        last = add("g", 1.0, lambda g, T, x, r=r: x["send"](x["dn"], ("tb0",) + r, ("tmo",) + r, "ta0", "lown"), [("tmo",) + r], [], done=lambda x: ("lown", 0))
+    step = [last]
+
+    def table(k, after):
+        add("x", 12.0 if k else 8.0, None, [], [("tb%d" % k, 0, TW)], done=(lambda x, k=k: ("ta%d" % k, x["ta"][k])), after=step[:1])
+
+        def far(g, T, x):
+            if x["far"] is not None:
+                x["send"](x["far"], ("tb%d" % (RO - 1), 0, TW), full("tmo", TW), "ta%d" % (RO - 1), "lown")
+
+        def e(g, T, x):
+            if x["fwd"][k] is not None:
+                x["send"](x["fwd"][k], ("tb%d" % (k + 1), 0, TW), ("tb%d" % k, 0, TW), "ta%d" % (k + 1), "ls%d" % k)
+        if k < RO - 1:
+            step[0] = add("g", 1.0, e, [("tb%d" % k, 0, TW)], [], done=(lambda x, k=k: ("ls%d" % k, x["lf"][k])), after=after)
+        if k == 1:
+            step.append(add("g", 1.0, far, [full("tmo", TW)], [], done=lambda x: ("lown", 0), after=[step[0]]))
+
+    wk = [0]
+
+    def work(n):
+        wk[0] += 1
+        return (("p3", "p4", "p7")[wk[0] % 3], 0, n)
+    msgops = {}
+    for t in range(RO):
+        xb, xn = "xb%d" % (t % 2), "xb%d" % (1 - t % 2)
+        X, XA = (xb, W0, W0 + P), (xb, 0, NX)
+
+        def pl(h, b=xb, o=W0):
+            return (b, o + 16 * PART[h][0], o + 16 * PART[h][1])
+        table(t, [msgops[(s, t - 1)] for s in range(t, RO)] if t else [])
+        XC = ("xc", 0, 16 * N0)
+        add("d", 0.1, lambda g, T, x, s=pl(0), o=XC: g.sync.dma_start(_ap(T, o), _ap(T, s)), [pl(0)], [XC], done=(lambda x, t=t: ("xc%d" % t, 16)))
+        UP, FP = ("p0", 0, 128), ("p0", 128, 256)
+        BST[0] = BU
+        for h in range(2):
+            mm(("p0", 64 * h, 64 * h + 64), wrapped("bu", xb, W0 + 1024 * h, 1024))
+        BST[0] = 0.0
+        vcopy(full("ui"), UP)
+        vs(full("u"), full("ui"), 4095, A.bitwise_and)
+        vt(full("sq"), full("u"), full("u"), A.mult)
+        vs(full("sh"), full("sq"), 5, A.arith_shift_right)
+        for m in MORD:
+            c = (m * 128, m * 128 + 128)
+            vs(("p2",) + c, full("u"), ("kmf", t * M + m, t * M + m + 1), A.mult)
+            vt(("qv",) + c, full("sh"), ("p2",) + c, A.add)
+            vs(("qi",) + c, ("qv",) + c, 2047, A.bitwise_and)
+            vcopy(("ql",) + c, ("qi",) + c)
+        BST[0] = BX
+        for lo, hi in blocks(P):
+            w = work(512)
+            mm(w, [(full("lx"), (xb, W0 + lo, W0 + hi))])
+            sa(("xw", lo, hi), w, F.Identity, bias=C("r15"))
+        BST[0] = BQ
+        mm(FP, wrapped("bf", xb, W0, P))
+        vs(full("f1"), FP, -1.0, A.add)
+        for m in MORD:
+            c = (m * 128, m * 128 + 128)
+            vcopy(("q16",) + c, ("qi",) + c)
+            vt(("eq",) + c, ("qi",) + c, PWP, A.is_equal)
+        for h in PORD:
+            h0, h1 = PART[h]
+            BST[0] = BP if h == PORD[0] else 0.0
+            for m in MORD:
+                wc = (m * 128 + h0, m * 128 + h1)
+                o = (m * P + 16 * h0, m * P + 16 * h1)
+                if (m, h) in VIT:
+                    vgt(("mx",) + o, full("xw", P), ("ql",) + wc, pl(h), A.max)
+                    parts = [(full("dn8k"), ("f1", h0, h1))] + wrapped("bdv", "mx", o[0], o[1] - o[0])
+                else:
+                    sg(("gm",) + o, X, ("ql",) + wc)
+                    for lo, hi in blocks(o[1] - o[0]):
+                        w = work(hi - lo)
+                        mm(w, [(full("ib"), ("gm", o[0] + lo, o[0] + hi)), (full("nib"), (xb, W0 + 16 * h0 + lo, W0 + 16 * h0 + hi))])
+                        sa(("ab", o[0] + lo, o[0] + hi), w, F.Abs)
+                    parts = wrapped("bds", "ab", o[0], o[1] - o[0])
+                parts = [(full("i16"), ("q16",) + wc), (full("dvoid"), ("eq",) + wc)] + parts
+                if m:
+                    parts.insert(0, (full("d2kb"), ("cm", m * 128 - 128, m * 128 - 128 + h1 - h0)))
+                mm(("p%d" % (1 + h), m * 128, m * 128 + h1 - h0), parts)
+        BST[0] = 0.0
+        tb = "tb%d" % t
+        TB = (tb, 0, TW)
+        for s in range(t):
+            i = _LK.index((t, s)) * 32
+            add("x", 3.0, None, [], [("land", i, i + 32)], done=(lambda x, s=s, t=t: ("m%d_%d" % (t, s), x["mn"][(t, s)])), after=[msgops[(t, s)]])
+            vcopy(full("upv", 16), ("land", i + 16, i + 32))
+            add("v", 0.15, lambda g, T, x, tb=tb, i=i: g.vector.tensor_copy(T[tb][:, 0:TW + 16].indirect(T.land[:, i:i + 1]), T.upv[:, 0:16]), [full("upv", 16), ("land", i, i + 32)], [(tb, 0, TW + 16)])
+        SM, LG, E = ("p5", 256, 384), ("p5", 384, 512), ("p6", 0, 128)
+        flips = 0
+        for h in PORD:
+            BST[0] = BP if h == PORD[0] else 0.0
+            c = PART[h]
+            n = c[1] - c[0]
+            pn = 16 * n
+            Zs = [("p%d" % (1 + h), m * 128, m * 128 + n) for m in range(4)]
+            US, SG = ("p5",) + c, ("p5", 128 + c[0], 128 + c[1])
+            vcopy(("b0",) + c, Zs[0])
+            vt(("b1",) + c, ("b0",) + c, Zs[2], A.min)
+            vt(("b2",) + c, ("b1",) + c, Zs[3 if (3, h) in VIT else 1], A.min)
+            vt(("bk",) + c, ("b2",) + c, Zs[1 if (3, h) in VIT else 3], A.min)
+            vs(("q",) + c, ("bk",) + c, 2047, A.bitwise_and)
+            vcopy(("qsl",) + c, ("q",) + c)
+            if h == 0:
+                vgt(full("sp", pn), X, ("qsl",) + c, XC, A.add)
+                mm(US, wrapped("bu", "sp", 0, pn))
+                vt(("uq",) + c, US, ("ui",) + c, A.subtract)
+            else:
+                sg(full("gq", pn), X, ("qsl",) + c)
+                mm(US, wrapped("bu", "gq", 0, pn))
+                vcopy(("uq",) + c, US)
+            vs(("uq2",) + c, ("uq",) + c, 4095, A.bitwise_and)
+            vt(("uu",) + c, ("uq2",) + c, ("u",) + c, A.mult)
+            vs(("h",) + c, ("uu",) + c, 4, A.arith_shift_right, 4095, A.bitwise_and)
+            vcopy(("hl",) + c, ("h",) + c)
+            vs(("di",) + c, ("bk",) + c, 13, A.arith_shift_right)
+            vcopy(("d16",) + c, ("di",) + c)
+            vs(("vc",) + c, ("di",) + c, 1919.0, A.is_ge, 2176.0, A.mult)
+            vcopy(("qs16",) + c, ("q",) + c)
+            o = 16 * c[0]
+            b0 = BST[0]
+            if h == 0:
+                vgt(full("rr", pn), TB, ("hl",) + c, full("sp", pn), A.subtract)
+                for lo, hi in blocks(pn):
+                    flips = sa(("ab2", o + lo, o + hi), ("rr", lo, hi), F.Abs)
+                BST[0] = b0 + BE
+                mm(SG, wrapped("bs", "sp", 0, pn))
+            else:
+                sg(full("ga", pn), TB, ("hl",) + c)
+                for lo, hi in blocks(pn):
+                    w = work(hi - lo)
+                    mm(w, [(full("ib"), ("ga", lo, hi)), (full("nib"), ("gq", lo, hi)), (full("nib"), (xb, W0 + o + lo, W0 + o + hi))])
+                    flips = sa(("ab2", o + lo, o + hi), w, F.Abs)
+                BST[0] = b0 + BE
+                mm(SG, wrapped("bs", "gq", 0, pn) + wrapped("bs", xb, W0 + o, pn))
+            BST[0] = b0
+            mm(("p6",) + c, [(full("i16"), ("pw16",) + c), (full("d2k16"), ("d16",) + c), (full("d2kb"), ("vc",) + c)] + wrapped("be", "ab2", o, pn))
+        BST[0] = 0.0
+        sa(full("dir"), ("p5", 128, 256), F.Square, bias=C("mone"))
+        vt(full("cmn"), full("q"), PWP, A.min)
+        mm(LG, [(full("i16"), full("pw16")), (full("i16"), full("qs16")), (full("ni16"), full("cmn"))])
+        mm(SM, [(full("i16"), full("cmn")), (full("d2kb"), ("cm", 128, 256)), (full("dm4k"), full("dir"))])
+        vcopy(full("cc"), SM)
+        AFT.append(flips)
+        for lo, hi in blocks(P):
+            sa((xb, W0 + P + lo, W0 + P + hi), (xb, W0 + lo, W0 + hi), F.Identity, scale=C("flw"), bias=C("r15"))
+        AFT.clear()
+
+        def lowest(src, dst, kp):
+            vred(C("r1"), src, A.min)
+            vs(full("dg", 16), full("mk16", 16), C("r1"), A.mult)
+            mm(("p6", kp, kp + 16), [(full("ob"), full("dg", 16))])
+            vred(dst, ("p6", kp, kp + 16), A.min)
+
+        def fetch(oh, src, kmin, out):
+            vs(full(oh), src, kmin, A.is_equal)
+            for k, tile in ((0, SM), (1, LG)):
+                vt(("pr", 128 * k, 128 * k + 128), full(oh), tile, A.mult)
+                vred(("aa", k, k + 1), ("pr", 128 * k, 128 * k + 128), A.add)
+            mm(out, [(full("ob"), ("aa", 0, 2))])
+        A1, A2 = ("p6", 160, 162), ("p6", 224, 226)
+        aX, bX, cX, dX = ("p6", 160, 161), ("p6", 161, 162), ("p6", 224, 225), ("p6", 225, 226)
+        lowest(E, C("kmin"), 128)
+        fetch("oh", E, C("kmin"), A1)
+        BIG = float(2 ** 25)
+        vs(full("t1"), full("cc"), aX, A.is_le, BIG, A.mult)
+        vs(full("t2"), full("cc"), bX, A.is_ge, BIG, A.mult)
+        vt(full("k2a"), full("t1"), E, A.max)
+        vt(full("k2"), full("k2a"), full("t2"), A.max)
+        vs(C("inv"), aX, 4096.0, A.is_ge)
+        vs(C("xC"), aX, 4096.0, A.is_ge, -4096.0, A.mult)
+        vs(C("a"), aX, C("xC"), A.add)
+        vcopy(C("b"), bX)
+        vs(C("ba"), C("b"), C("a"), A.subtract)
+        vs(("nl", 0, 1), C("odd"), C("ba"), A.mult, C("a"), A.add)
+        sg(full("nc", 16), X, ("nl", 0, 1), bias=-0.125)
+        vs(C("nf"), ("nc", 1, 2), C("fm"), A.mult, ("nc", 0, 1), A.add)
+        vcopy(C("ni"), C("nf"))
+        vs((xb, 15, 16), C("ni"), C("half"), A.mult)
+        lin("dir", "inv", -1.0, 1.0)
+        lin("xI", "inv", -4096.0, 4096.0)
+        lin("x3", "inv", 2048.0, 0.0)
+        lin("an1", "a", -1.0, -1.0)
+        lin("xd", "b", -1.0, 2047.0)
+        lin("aI", "a", 1.0, C("xI"))
+        lin("bI", "b", 1.0, C("xI"))
+        lin("m1", "ba", 1.0, C("inv"))
+        lin("m3", "ba", C("dir"), C("x3"))
+        lin("K2", "ba", C("inv"), C("x3"))
+        lin("cdef", "ba", C("dir"), C("a"))
+        lin("ddef", "xd", C("dir"), C("b"))
+        lin("w", "cdef", -1.0, C("ddef"))
+        for k, (src, scale, bias) in enumerate((("ba", -1.0, "ddef"), ("ddef", 1.0, None), ("w", 1.0, "a"), ("K2", -1.0, "w"), ("inv", -1.0, "w"))):
+            sa(("pd", k, k + 1), C(src), F.Identity, scale=scale, bias=C(bias) if bias else 0.0)
+        pw = full("pw16")
+        G = [("gt", i * 128, i * 128 + 128) for i in range(7)]
+        vs(G[0], pw, C("a"), A.is_gt, C("m1"), A.mult)
+        vs(G[1], pw, C("aI"), A.subtract, 0.0, A.max)
+        vs(G[2], pw, C("bI"), A.subtract, 0.0, A.max)
+        vs(G[3], pw, C("a"), A.is_equal, C("an1"), A.mult)
+        PL = ("p1", 0, 128)
+        i16, n16 = full("i16"), full("ni16")
+        mm(PL, [(i16, pw), (i16, G[0]), (full("m2i"), G[1]), (full("p2i"), G[2]), (i16, G[3])], stop=False)
+        KK = full("k2")
+        lowest(KK, C("kmin2"), 192)
+        fetch("oh2", KK, C("kmin2"), A2)
+        vs(C("f"), C("kmin2"), float(2 ** 24), A.is_lt)
+        vs(C("valid"), dX, C("b"), A.is_gt, C("f"), A.mult)
+        vs(C("xe"), dX, C("ddef"), A.subtract, C("valid"), A.mult)
+        vs(C("xc"), cX, C("cdef"), A.subtract, C("valid"), A.mult)
+        vs(full("qd", 5), full("pd", 5), C("xe"), A.add)
+        vs(full("qe", 3), ("qd", 2, 5), C("xc"), A.subtract)
+        vs(G[4], pw, ("qd", 0, 1), A.is_gt, ("qe", 1, 2), A.mult)
+        vs(G[5], pw, ("qe", 0, 1), A.is_gt, C("m3"), A.mult)
+        vs(G[6], pw, ("qd", 1, 2), A.is_gt, ("qe", 2, 3), A.mult)
+        mm(PL, [(n16, G[4]), (n16, G[5]), (i16, G[6])], start=False)
+        order = vs(full("pl"), PL, float(W0), A.add)
+        if t < RO - 1:
+            for k in range(4):
+                o = (xn, W0 + 512 * k, W0 + 512 * k + 512)
+                if k % 2:
+                    sg(o, XA, ("pl", 32 * k, 32 * k + 32))
+                else:
+                    vgs(o, XA, ("pl", 32 * k, 32 * k + 32), 1.0)
+            AFT.append(order)
+            BST[0] = BM
+            vt(full("hpr"), full("oh"), full("h"), A.mult)
+            vred(C("har"), full("hpr"), A.add)
+            mm(("p6", 256, 257), [(full("ob"), C("har"))])
+            vcopy(C("hpf"), ("p6", 256, 257))
+            vs(("msg", t * 32, t * 32 + 1), C("hpf"), C("mk0"), A.mult, C("padc"), A.add)
+            vcopy(("msg", t * 32 + 16, t * 32 + 17), C("ni"))
+            for t2 in range(t + 1, RO):
+                def e(g, T, x, t=t, t2=t2):
+                    i = _LK.index((t2, t)) * 32
+                    x["send"](x["user"][t2], ("land", i, i + 32), ("msg", t * 32, t * 32 + 32), "m%d_%d" % (t2, t), "lmsg")
+                msgops[(t2, t)] = add("g", 1.0, e, [("msg", t * 32, t * 32 + 32)], [], done=lambda x: ("lmsg", 0), after=step)
+            AFT.clear()
+            BST[0] = 0.0
+        else:
+            for h in range(2):
+                yo = ("yo", 1024 * h, 1024 * h + 1024)
+                if h:
+                    sg(yo, XA, ("pl", 64, 128), scale=C("dbl"))
+                else:
+                    vgs(yo, XA, ("pl", 0, 64), C("dbl"))
+                add("sd" if h else "d", 0.1, lambda g, T, x, h=h, yo=yo: (g.scalar if h else g.sync).dma_start(T.y[:, yo[1]:yo[2]], _ap(T, yo)), [yo], [], done=(lambda x, h=h: ("st%d" % h, 16)))
+    return ops
+
+
+_QS = {"v": "sv", "s": "ss", "t": "st", "g": "sg"}
+_CACHE = {}
+
+
+def plan():
+    if "o" in _CACHE:
+        return _CACHE["o"]
+    ops = build()
+    hist = {}
+    for i, o in enumerate(ops):
+        deps = set()
+        q = o["qq"] = "s" if o["q"] == "sd" else o["q"]
+        rw = [(0, r) for r in o["reads"]] + [(1, r) for r in o["writes"]]
+        for kind, r in rw:
+            for (j, k2, a, b, q2) in hist.get(r[0], ()):
+                if (kind or k2) and a < r[2] and r[1] < b or _ps(r) and q2 != q:
+                    deps.add(j)
+        for kind, r in rw:
+            hl = hist.setdefault(r[0], [])
+            if kind:
+                hl[:] = [e for e in hl if not (r[1] <= e[2] and e[3] <= r[2] and (e[4] == q or not _ps(r)))]
+            hl.append((i, kind, r[1], r[2], q))
+        o["data"] = deps
+        o["deps"] = sorted(deps | set(o["after"]))
+    n = len(ops)
+    succ = [[] for _ in ops]
+    for i, o in enumerate(ops):
+        for j in o["deps"]:
+            succ[j].append(i)
+    prio = [0.0] * n
+    for i in range(n - 1, -1, -1):
+        prio[i] = ops[i]["cost"] + ops[i]["boost"] + max([prio[j] + (SELF if ops[i]["qq"] == ops[j]["qq"] else WAKE) for j in succ[i]] + [0.0])
+    left = [len(o["deps"]) for o in ops]
+    est, fin, free, order = [0.0] * n, [0.0] * n, {}, []
+    ready = [i for i in range(n) if left[i] == 0]
+    while ready:
+        best, byq = None, {}
+        for i in ready:
+            byq.setdefault(ops[i]["qq"], []).append(i)
+        for q, lst in byq.items():
+            st = min(est[k] for k in lst)
+            if q != "x":
+                st = max(st, free.get(q, 0.0))
+            cand = sorted((k for k in lst if est[k] <= st + 1e-9), key=lambda k: (-prio[k], k))
+            pick = None
+            for i in cand:
+                if q == "x" or not any(prio[k] > prio[i] + 0.3 and st + ops[i]["cost"] - est[k] > est[k] - st for k in lst if st < est[k] < st + ops[i]["cost"]):
+                    pick = i
+                    break
+            if pick is None:
+                later = [k for k in lst if est[k] > st + 1e-9]
+                pick = min(later, key=lambda k: (est[k], -prio[k]))
+                st = est[pick]
+            if best is None or st < best[0]:
+                best = (st, pick, q)
+        st, i, q = best
+        ready.remove(i)
+        fin[i] = st + ops[i]["cost"]
+        if q != "x":
+            free[q] = fin[i] + 0.02
+        lat = 2.0 if ops[i]["q"] in ("d", "sd") else 0.0
+        order.append(i)
+        for j in succ[i]:
+            left[j] -= 1
+            est[j] = max(est[j], fin[i] + lat + (SELF if ops[j]["qq"] == q else WAKE))
+            if left[j] == 0:
+                ready.append(j)
+    cnt = {}
+    for i in order:
+        o = ops[i]
+        if o["done"] is None:
+            s = o["inc"] = _QS[o["q"]]
+            v = cnt[s] = cnt.get(s, 0) + 1
+            o["done"] = (lambda x, s=s, v=v: (s, v))
+    _CACHE["o"] = (ops, order, cnt, max(fin), fin)
+    return _CACHE["o"]
+
+
+def rank_program(g, core, T, topo):
+    rank = T.rank_of(core)
+    if rank is None:
+        return
+    ops, order, cnt, _, _ = plan()
+    N = len(T.cores)
+
+    def neng(a, b):
+        return len(topo.engines(T.cores[a % N], T.cores[b % N]))
+
+    def direct(r):
+        return topo.chip(T.cores[(r + RO) % N]) == topo.chip(T.cores[r % N])
+    tot = {}
+
+    def send(d, out, src, rsem, lsem):
+        dst = T.cores[d]
+        rid, pid, _ = topo.addr(dst)
+        g.remote_dma(_ap(T, out), _ap(T, src), T.sem[rsem], T.sem[lsem], pid, rid, topo.mask(core, dst))
+        tot[lsem] = tot.get(lsem, 0) + neng(rank, d)
+    dn, far = (rank - 1) % N, (rank - RO) % N
+    x = {"send": send, "user": {t: (rank - 1 - t) % N for t in range(RO)}}
+    x["dn"], x["far"] = dn, far if direct(far) else None
+    x["fwd"] = [None if k == RO - 2 and direct(dn) else dn for k in range(RO - 1)]
+    x["lf"] = [0 if d is None else neng(rank, d) for d in x["fwd"]]
+    x["ta"] = [4 * neng(rank + 1, rank)] + [neng(rank + 1, rank)] * (RO - 1)
+    if direct(rank):
+        x["ta"][RO - 1] = neng(rank + RO, rank)
+    x["mn"] = {(t, s): neng(rank + 1 + t, rank) for (t, s) in _LK}
+    eng = {"v": g.vector, "s": g.scalar, "sd": g.scalar, "t": g.tensor, "g": g, "d": g.sync}
+    know, opk = {}, {}
+    for i in order:
+        o = ops[i]
+        q = o["qq"]
+        kn = dict(know.get(q, {})) if q != "x" else {}
+        if q == "x":
+            s, v = o["done"](x)
+            tot[s] = v
+        else:
+            need = {}
+            for j in sorted(o["data"]):
+                s, v = ops[j]["done"](x)
+                if v > kn.get(s, 0) and v > need.get(s, (0, 0))[0]:
+                    need[s] = (v, j)
+            for s in list(need):
+                if any(s2 != s and opk[need[s2][1]].get(s, 0) >= need[s][0] for s2 in need):
+                    need.pop(s)
+            for s, (v, j) in need.items():
+                eng[o["q"]].wait_ge(T.sem[s], v)
+                for s2, v2 in list(opk[j].items()) + [(s, v)]:
+                    kn[s2] = max(kn.get(s2, 0), v2)
+            know[q] = kn
+            ins = o["emit"](g, T, x)
+            if o["q"] in ("d", "sd"):
+                s = o["done"](x)[0]
+                ins.then_inc(T.sem[s], 16)
+                tot[s] = 16
+            elif "inc" in o:
+                ins.then_inc(T.sem[o["inc"]], 1)
+        pre = dict(kn)
+        if "inc" in o:
+            s, v = o["done"](x)
+            pre[s] = max(pre.get(s, 0), v)
+        opk[i] = pre
+    for s, v in list(cnt.items()) + list(tot.items()):
+        if v > 0:
+            g.wait_ge(T.sem[s], v)

@@ -3,39 +3,47 @@ from concourse.mybir import AluOpType as A, AxisListType as AX, ActivationFuncti
 RO, M, P, TW = 5, 4, 2048, 4096
 W0 = 16
 NX = W0 + 2 * P
-N0 = 56
-PART = ((0, N0), (N0, 128))
-VIT = {(0, 0), (0, 1), (1, 0), (1, 1), (3, 1)}
-PORD = (1, 0)
-MORD = (2, 0, 3, 1)
-BX, BP, BQ, BU, BM, BE = 3.0, 1.0, 5.0, 6.0, -8.0, -2.0
+PART = ((0, 64), (64, 128))
+PAR = {
+    "items": [(0, 0, "v", 0, 1, 12.9), (2, 0, "s", 1, 1, 12.8), (1, 0, "v", 0, 1, 15.2), (3, 0, "v", 1, 1, 17.0), (2, 1, "s", 0, 1, 15.9), (0, 1, "v", 1, 1, 18.8), (1, 1, "v", 0, 1, 20.9), (3, 1, "s", 1, 1, 18.8)],
+    "s": "f1 d16 vc qs16 pos upv aa1 idr xl nb w15 nif har msg0 msg1 ds k".split(),
+    "T": 2959, "T0": -151, "Z": 31.0, "ds": (19.8, 24.5), "vh": 32, "sh": 64, "xh": 32,
+    "xq": (0, 32),
+    "tq": (64, 32),
+    "rv": 24,
+    "CYC": 0.83e-3 * 1.25, "TCY": 0.42e-3 * 1.25, "GC": 1.56, "WAKE": 0.15, "SELF": 0.06,
+}
+TAU = "qzxp00cwqt200cetpv00oyhpm000n0u20001ipz01c0oc400ougaa010q84j000hra100w9agw01rafln02fjl9k01yra3c027i4ff02o0s2m03c8qt3057t5gv08sak730as9nf504qit3204y2c4s03k6spq02wp2dp0ajewlg04hu53o048cfe6000zfoq07zz13u0dqrfso05ozzlo0daml460ev0xry06kpkf50cl6v800b13fse0901d1j072roto05wihes0gz254a0ockzry0qt4kpe0sndqdb0g3mw180ctv2q41ju10oc06t4lr20k01yz0107xv160rqenc20mkc33n1uznil507ahf2h06osvc203pxabq0cnkz9n05h5jjh04abkro08h670s09olnqx0c274h3063q0iu0bgkdp50a9ztfb07v6ch30av09ye04wfpok092q5z50d93v740g82h7q0kt43nt0v0x15101jzc750q5548d2c7m0t503t9yqi06cx6zv07bsrxg0e50hr80gb94t50lf49e10kyeaue0mu6f2y0jshdyo0m3ti2y0no6h960olgm2y0sw2zo40ui3q2y0w5aoew1a7a4aa0lurce10otw7t50r2fqkr0sfgb8a0hfjdgj19jsj4g2are9qb0tm1qsc0d2awg90mcflqu0kayq320ig93gv0x8i94s1jda7sm07qege10u1fj3k0l6uztp0v85ajs1k32n3k27okq9y2b0eitz1tt03de1w0k1sd0eet7ga0em2q8t0f8j2560j4uehz0ph3l5w0vhcrts12ypvqi16kczqi1afy1ff1fw783c1kvnv4i1qlblev0t4bvme25e1sn519rfbxz206deio1iv0iio1qukh0r2bsg09b06lhvke09ff46j0c93zfe0f38m660egtjwe0dut5g00f1n2xb0fnynay0beq2d50gt1hjb0fogx9h0gkrdk20hne4lg0io6ua80jcxg3p0ki88z00k8bbzn0koyezn0l3lizn0ljs0m804uf4m80ly28m80me948l0n9yana0qegtkj0ua9cfd0pqh6zd0ra51840tdunhf0p2juw40vp1dud0xhokyq0nxdrdg0rzv9bp0urfdxi0g122ph0n4pt8t0jv8s5r0lf2hxi0qnnlz70rtcx8t0pv3h8h0uqw2k30mtw40s0tj5z6k000gwq10ycv9xs11aazpj11m0vl011s8ami128eevu1adfbc61as3ted16scdgt10xoco71y7i95j1z7zabt15drto112vkfwh14b7jwh195l2t31dpj84s11johuc17jbluc18cnsm019obu5n11xyx5n16qsnfp17z7s7s1bluv7s1bxzl2y1ggzr8517vjlq71b81x6i1b5o07i1eb86t31j6ofao1dy4bjx1gp44i11hhr7i11jjcj0s1lxh4651bey6hx13ilahx1hweood1mr15j212po8j21goujxm1l28xdj1myv0ej1pnltth1sg1uz01jfhp8a1n8ad4t1mjxg4t1sfadjw1w41oq21pqhjzb1spnm3b1r6aq3b1vk8xth1z9d0od1g8youc1fvlsuc1lfak6m1v9l16n1dh856n1naudoo1tkp2uk1x4c6uk1xgg8az220rzqx1ma0sn71mzm2a51ohz8k01r0fw3i1tzw6do1vvbn3u1wdi55m1wpxlvr1x8p3zo1z1hqmi1s8isih1wyk7l01ysta0u1xd71701zi8uca25k8ehx1ouvhhx1rmilhx23uf0f2269bcj21zsyfj2228ljj228kpsrb29q2p0522d20p822pmk7c232t2l623b1ad92673yd2284ie4828sxuud2951b5z29oaww82a5sh3h29wijjv2ezowu72dy40a125uxpdk2ai48re2bf8wuc1yzvzuc27ri3vc2e5r6tp2fev86n231ic6n2dc5g6n2fk722z2h3d2jb20lhrsi29dsjs72b0fns72bsy22q2hll62q2j5hqb11zt02jf2lp81bm2n1x2qj2o0d46u28dyquu2edi4ej2eyumwh2i0nd4p2kphz7s2gdp52w2h64ijp2l2dk542llrjlu2lymuvi2mb817l2mnwkag2nm3vbs2o5b11m2n7rf192nzc92w2ozx2n62q1xkoy2qxfjh72ru1u5s2psa0uo2qoj6il2qgsc6i2rcm9uw2s9ph1w2sykr5s2u93tks2uuv8ql2vmcpkz2wsyx7c2yyw56v30jumwv31ywlzt33025ql2vvpose38ogk6l2rlv0xq2si0yev2uhb0nn2w2sj6n2wnv5sc2xt6h7c2y857vc2mo204i2t3y8t22v9savc2wwl9lc2yubnga2tt70892t6j1f42uqcoxb2qern7l2qsryiy2ra057v2to6nhu2s4ft5r2wa4btx2xvxgtx2sj0uvh2rpihjo2u2ooia2zp0kxl2vef0or2yh76nv2yqxi542x55phx2zbdo7m2sq0o542tlenlu2uhzys82v5nhxq2vnjoag2wqqybs2xey41m2waej192x7yls52y8vvr62z7imxg2zfx2om2zosshx30hlngz31mdh7c34td0tc33fwnri303b4io317mks932198er32u11jf33iskwz34e3csb31c8nj22pfvqj2341iuj2356fn6n314zgaa33mmkaa35m4bgs37ftegl395b0tq3afs5zr36rxw3c37uouri3brpupm389eypf39lwj2l3b3jr6y3a08v6r3bcqgjw3cuoztn2t96c6h2yguh4n30ic5st30xlbgq3043osj32lj1gk33xyh6q30ydywv339zen134652p8376uyzq361h20r37sdomz3aoov163hlimw02okjak22pqhb522pdbd8m2zatr5n2yvjyka30262la32wt5la2ymg9la38jwqd9140j3p7000nnwg16drwj91mi67p70vgarwg1xse0k91yktap70snxuwg20f14k9216gep70snkywg237o7k923z7o8l356og7o3a5suf03c2mck035fqfe33ahd0p93cb9o7c37ofwhx3ait62o3bpxyt63dlg6l637y2rs73bb0pfi3cn6xwe3eg"
+TAU = "qzxp000wqt2000etpv00cyhpm00cn0u201c1ipz0100oc400ougaa00oq84j000hra100w9agw01rafln02wjl9k02ora3c020i4ff03k0s2m0488qt305mt5gv089ak7309h9nf504wit320552c4s05e6spq035p2dp0d3ewlg0dcu53o0facfe6000zfoq072z13u0corfso06czzlo07uml460dt0xry06kpkf508i6v8009z3fse0k51d1j0niroto04hihes0j2254a0s3kzry0cf4kpe098dqdb0ggmw180msv2q41ip10oc0fi4lr20go1yz00brxv160ykenc20pzc33n1ulnil507ihf2h0gosvc20bpxabq0cakz9n0545jjh03xbkro06b670s0b3lnqx0cw74h309wq0iu05qkdp509bztfb08p6ch30ai09ye04jfpok084q5z506x3v740g32h7q0ha43nt06tx151029zc7508r548d2cjm0t503t9yqi063x6zv0c0srxg0dk0hr80fs94t50mc49e10iueaue0nq6f2y0hshdyo0n9ti2y0ol6h960qhgm2y0rm2zo40tf3q2y0ytaoew19ja4aa0f1rce10qpw7t50pbfqkr0w5gb8a01rjdgj1s7sj4g2bee9qb0gy1qsc0biawg90p2flqu01jyq320v093gv08zi94s2bna7sm0qyege10z2fj3k0wduztp1i75ajs1j62n3k2a0kq9y2adeitz1so03de2b6k1sd0jht7ga09q2q8t0k3j2560m4uehz0n03l5w0otcrts0q8pvqi0rvczqi16sy1ff0vn783c1hznv4i1pgblev24obvme29d1sn51v3fbxz2cbdeio0to0iio1tckh0r2bwg09b069hvke092f46j0bw3zfe0eq8m660dptjwe0eat5g00ewn2xb0fhynay0a3q2d50ss1hjb0emgx9h0g0rdk20i1e4lg0hd6ua80jqxg3p0lo88z00wjbbzn0gbyezn0kylizn0mhs0m80fvf4m80kj28m80mw948l0o6yana0r7gtkj0t69cfd0u5h6zd0v851840xhunhf0pjjuw40sc1dud0twokyq0srdrdg0ukv9bp0vwfdxi0gq22ph0hwpt8t0nc8s5r0oi2hxi0o5nlz70uucx8t0rz3h8h0t5w2k30oxw40s0sc5z6k000gwq10xuv9xs11sazpj11g0vl010r8ami12oeevu11lfbc61293ted1yqcdgt16joco71vui95j1zbzabt134rto115mkfwh13h7jwh1a3l2t31d3j84s11pohuc13wbluc17pnsm019ubu5n11yyx5n16wsnfp1857s7s1c3uv7s1cfzl2y1fuzr85183jlq71al1x6i1bno07i1dz86t31ikofao1dc4bjx1g244i11idr7i11ixcj0s1lbh4651bky6hx19blahx1greood1l815j218io8j21hkujxm1mx8xdj1khv0ej1ptltth1uy1uz01ithp8a1muad4t1n8xg4t1rcadjw1x41oq21pchjzb1runm3b1swaq3b1vm8xth1xyd0od1geyouc1ktlsuc1mfak6m1wfl16n1fi856n1lmudoo1u4p2uk1tcc6uk1yhg8az20orzqx1ln0sn71mdm2a51onz8k01r6fw3i1u2w6do1vzbn3u1wci55m1woxlvr1xcp3zo1xphqmi1mmisih1zxk7l024ita0u26671701y68uca24d8ehx1nnvhhx21oilhx22hf0f226lbcj21p0yfj21x6ljj2279psrb28e2p0521120p821dmk7c21vt2l621z1ad924w3yd226uie48277xuud27k1b5z283aww828gsh3h21mijjv24xowu725c40a125rxpdk28s48re2a48wuc23avzuc26gi3vc2c1r6tp2d9v86n243ic6n2ct5g6n2dm722z2eyd2jb201hrsi281sjs729pfns72ahy22q2fnl62q2h0hqb11y402jf2ik81bm2jxx2qj2kvd46u2bayquu2cni4ej2efumwh2f1nd4p2jkhz7s2kjp52w2ly4ijp2ixdk542jgrjlu2jtmuvi2k6817l2kiwkag2lh3vbs2m0b11m2l2rf192luc92w2mux2n62nvxkoy2osfjh72pg1u5s2nna0uo2ojj6il2obsc6i2p7m9uw2pvph1w2qqkr5s2ro3tks2skv8ql2tccpkz2utyx7c2wtw56v2xyumwv2yzwlzt30125ql2u0pose32sgk6l2r7v0xq2qy0yev2rvb0nn2tosj6n2uev5sc2vo6h7c2wk57vc2lc204i2rty8t22szsavc2u5l9lc350bnga2q470892suj1f42s6coxb2o9rn7l2onryiy2ph057v2rg6nhu2qbft5r2s64btx2vwxgtx2r10uvh2ufihjo2pwooia2xb0kxl2w3f0or2v076nv2txxi542wc5phx2wxdo7m2qj0o542rgenlu2rxzys82slnhxq2t9joag2ulqybs2v9y41m2u5ej192v8yls52w9vvr62x2imxg2xax2om2xjsshx2yblngz2zcdh7c33inusz30gwnri2yeb4io2yxmks92zr98er30k11jf318skwz3243csb3918nj22navqj232eiuj232xfn6n2yxzgaa33cmkaa33s4bgs34ztegl35ub0tq37ss5zr34kxw3c369ouri37jpupm35feypf374wj2l38gjr6y3808v6r394qgjw39yoztn2tl6c6h2wwuh4n2ykc5st2xqlbgq2y53osj2zmj1gk31wyh6q31ndywv30zzen133952p832kuyzq31lh20r347domz36oov163f2imw02mfjak22nlhb522n8bd8m2p2tr5n2whjyka2x962la303t5la32xg9la35rwqd913ij3p7000nnwg17qrwj91lw67p70s4arwg1tpe0k91uhtap70s4xuwg1zy14k921dgep70s4kywg242o7k92827o8l35tog7o3atsuf03cpmck0362qfe33b5d0p93cy9o7c38bfwhx3b6t62o3ccxyt63e8g6l638l2rs73bz0pfi3da6xwe3f3"
+PAR.update({"T": 2877, "T0": -78, "rv": 12})
+MAGIC = 1.5 * 2.0 ** 34
 
 SCRATCH = {}
 _PS = ["p%d" % i for i in range(8)]
 _B2 = ("bfloat16", "float16", "uint16")
-_CS = {n: i for i, n in enumerate("kg15 kg kr k odd r15 fm half dbl flw wf wu w1 mk0 padc dvc dsc bec f2 mone r1 kmin har hpf nf kmin2 "
-                                  "a b dir inv ba aI bI m1 m3 x3 K2 cdef ddef xd an1 xC xI w f valid xc xe".split())}
-_CI = {n: i for i, n in enumerate("ik ikg ikr iodd ni".split())}
+_CS = {n: i for i, n in enumerate("kg15 kg kr k odd r15 fm flw wf mk0 mid padt padx hc0 hc1 wa wb cw wq0 wq1 wq2 wq3 wq ucol c128 n128 c128r n128r c35 t0 t1 t2 t3 t4 t5 t6 mhalf "
+                                  "r1 r2 kmax kmax2 har e1 idr nif xC a b ba inv dir aI bI nbI an1 xd wdef m1 i2 sg2 m3 u1 nz k0 k1 mba plb pb pb2 ws h0 h1 ds cs ninv2".split())}
+_CI = {n: i for i, n in enumerate("ik ikg ikr iodd ni ib16".split())}
+_MB = {n: i for i, n in enumerate("ib nib d2kb dvoid d4k i2f lx0 d23 dw15 one sgn inv vc oh oh2 oha v r2 lxa hb dvc ndw15 wb1 fb1".split())}
+_MH = {n: i for i, n in enumerate("i16 ni16 m2i d2k16 dn8k nh16 lj lf l2 dhf d2hf p2i dnhf p11 m11 p12 m12 pw16 pos16 f1 d16 qs16 cmn sh16 u16 pa pc la lb "
+                                  "g0 g0b g3 gr g4 g5 g6 h0 h1 hr h4 h5 f0 f1m gf".split())}
+_MF = {n: i for i, n in enumerate("ob m1 m2 gu b0 b1 pr0 pr1 hpr hp2 cl inn k2v rt n32 rf ta jk".split())}
+_MI = {n: i for i, n in enumerate("ic jb ui u sq sh bk q di uq uq2 uu h".split())}
 for _a in _PS:
     SCRATCH[_a] = ("psum", [128, 512], "float32")
-for _d, _l in (("bfloat16", (("xin", P), ("tmo", TW), ("xb0", NX), ("xb1", NX), ("yo", P), ("xc", P), ("mb", 144), ("bu", 144), ("bf", 144), ("bs", 144), ("bds", 144), ("be", 144),
-                             ("ib", 128), ("nib", 128), ("d2kb", 128), ("dvoid", 128), ("dm4k", 128), ("lx", 128), ("cm", 384), ("eq", 512), ("gm", 4 * P), ("ab", 4 * P), ("vc", 128),
-                             ("dir", 128), ("sp", P), ("gq", P), ("rr", P), ("ga", P), ("ab2", P), ("t1", 128), ("t2", 128)) + tuple(("tb%d" % k, TW + 16) for k in range(RO))),
-               ("float16", (("bdv", 144), ("i16", 128), ("ni16", 128), ("p2i", 128), ("m2i", 128), ("d2k16", 128), ("dn8k", 128), ("pw16", 128), ("f1", 128), ("q16", 512),
-                            ("mx", 4 * P), ("d16", 128), ("qs16", 128), ("cc", 128), ("cmn", 128), ("gt", 896))),
-               ("float32", (("xw", P), ("cs", 64), ("kmf", RO * M), ("lxa", 128), ("lxc", 128), ("ob", 128), ("mk16", 16), ("pwf", 128), ("b0", 128), ("b1", 128), ("b2", 128),
-                            ("aa", 4), ("pd", 5), ("qd", 5), ("qe", 3), ("dg", 16), ("oh", 128), ("pr", 256), ("hpr", 128), ("k2a", 128), ("k2", 128), ("oh2", 128), ("nc", 16),
-                            ("upv", 16))),
-               ("int32", (("wti", 1), ("kmi", RO * M), ("ci", 8), ("ij", 144), ("ic", 128), ("jb", 128), ("ui", 128), ("u", 128), ("sq", 128), ("sh", 128), ("qv", 512), ("qi", 512),
-                          ("bk", 128), ("q", 128), ("di", 128), ("uq", 128), ("uq2", 128), ("uu", 128), ("h", 128))),
-               ("uint16", (("ql", 512), ("qsl", 128), ("hl", 128), ("nl", 2), ("pl", 128), ("msg", 128), ("land", 320)))):
+for _d, _l in (("bfloat16", (("xin", P), ("tmo", TW), ("xb", P + 16), ("yo", P), ("mb", 144), ("bu0", 144), ("ncb", 32), ("bf", 144), ("bs", 144), ("bds", 144), ("be", 144),
+                             ("cb", 128 * len(_MB)), ("eq", 512), ("ab", 4 * P), ("ga", P), ("ab2", P)) + tuple(("tb%d" % k, TW + 16) for k in range(RO))),
+               ("float16", (("bdv", 144), ("bq", 144), ("bsq", 144), ("ch", 128 * len(_MH)), ("one16", 512), ("cmq", 256), ("q16", 512), ("mx", 4 * P), ("dk", 512), ("gq", P))),
+               ("float32", (("w0", NX), ("w1", NX), ("cs", 96), ("kmf", RO * M), ("cf", 128 * len(_MF)), ("mk32", 32), ("aa", 4), ("dg", 32), ("tr", 40), ("nc", 16), ("upv", 16),
+                            ("nb", 16), ("onef", 16), ("onefm", 16), ("rr", 512))),
+               ("int32", (("wti", 1), ("kmi", RO * M), ("ci", 8), ("ij", 144), ("it", 128 * len(_MI)))),
+               ("uint16", (("ql", 512), ("qsl", 128), ("hl", 128), ("nl", 2), ("xl", 2), ("pl", 128), ("msg", 128), ("land", 320)))):
     for _a, _c in _l:
         SCRATCH[_a] = ("sbuf", [128, _c], _d)
 _LK = [(t, s) for t in range(1, RO) for s in range(t)]
-SEMAPHORES = (["sv", "ss", "st", "sg", "lmsg", "lown", "lx0", "lx1", "lw", "lk", "lt0", "lt1", "lt2", "lt3", "st0", "st1"] + ["xc%d" % k for k in range(RO)]
+SEMAPHORES = (["sv", "ss", "st", "sg", "lmsg", "lown", "lx0", "lx1", "lw", "lk", "lt0", "lt1", "lt2", "lt3"] + ["st%d" % k for k in range(4)]
+              + ["f%s%d" % (c, k) for k in range(RO) for c in "abc"]
               + ["ta%d" % k for k in range(RO)] + ["ls%d" % k for k in range(4)] + ["m%d_%d" % ts for ts in _LK])
-
-CYC, TCY, GC, WAKE, SELF = 0.83e-3 * 1.25, 0.42e-3 * 1.25, 1.56, 0.15, 0.06
 
 
 def _ap(T, r):
@@ -54,11 +62,27 @@ def C(n):
     return ("cs", _CS[n], _CS[n] + 1) if n in _CS else ("ci", _CI[n], _CI[n] + 1)
 
 
-def build():
-    ops, BST, AFT = [], [0.0], []
+def _tile(buf, names):
+    def f(n, c0=0, c1=128):
+        return (buf, names[n] * 128 + c0, names[n] * 128 + c1)
+    return f
 
-    def add(q, cost, emit, reads, writes, done=None, after=()):
-        ops.append({"q": q, "cost": cost, "emit": emit, "reads": reads, "writes": writes, "done": done, "after": list(after) + AFT, "boost": BST[0]})
+
+B, H, S, I = _tile("cb", _MB), _tile("ch", _MH), _tile("cf", _MF), _tile("it", _MI)
+
+
+def build():
+    ops, BST, AFT, bank = [], [0.0], [], {}
+    CYC, TCY, GC = PAR["CYC"], PAR["TCY"], PAR["GC"]
+    SEC, seen_tag = [-1], {}
+
+    def add(q, cost, emit, reads, writes, done=None, after=(), lat=0.0):
+        ops.append({"q": q, "cost": cost, "emit": emit, "reads": reads, "writes": writes, "done": done, "after": list(after) + AFT, "tau0": int(100 * BST[0]), "lat": lat})
+        BST[0] += 0.1
+        r = [(y[0].rstrip("0123456789") if y[0][0] in "wt" else y[0], y[1] % 32 if y[0] in ("msg", "land") else y[1]) for y in (writes + reads)[:1]]
+        k = (SEC[0], q, str(r))
+        seen_tag[k] = seen_tag.get(k, 0) + 1
+        ops[-1]["sec"], ops[-1]["tag"] = SEC[0], (SEC[0] < 0, q, str(r), seen_tag[k])
         return len(ops) - 1
 
     def isc(*xs):
@@ -72,7 +96,7 @@ def build():
 
     def vt(out, a, b, op):
         c = _n(out) * (1 if _ps(a) or _ps(b) else 2)
-        add("v", max(64, c) * CYC, lambda g, T, x: g.vector.tensor_tensor(_ap(T, out), _ap(T, a), _ap(T, b), op), [a, b], [out])
+        return add("v", max(64, c) * CYC, lambda g, T, x: g.vector.tensor_tensor(_ap(T, out), _ap(T, a), _ap(T, b), op), [a, b], [out])
 
     def vs(out, a, s1, op0, s2=None, op1=None):
         def e(g, T, x):
@@ -90,116 +114,191 @@ def build():
     def vset(out, c):
         add("v", max(64, _n(out)) * CYC, lambda g, T, x: g.vector.memset(_ap(T, out), c), [], [out])
 
+    def vtr(out, a):
+        add("v", 64 * CYC, lambda g, T, x: g.vector.transpose(_ap(T, out), _ap(T, a)), [a], [out])
+
     def vgt(out, win, off, b, op):
         add("v", 0.05 + _n(out) * GC * CYC, lambda g, T, x: g.vector.tensor_tensor(_ap(T, out), _ap(T, win).indirect(_ap(T, off)), _ap(T, b), op), [win, off, b], [out])
 
-    def vgs(out, win, off, s):
-        add("v", 0.05 + _n(out) * GC * CYC, lambda g, T, x: g.vector.tensor_scalar(_ap(T, out), _ap(T, win).indirect(_ap(T, off)), val(T, s), None, A.mult), [win, off] + isc(s), [out])
+    def vscat(win, off, a):
+        add("v", 0.15, lambda g, T, x: g.vector.tensor_copy(_ap(T, win).indirect(_ap(T, off)), _ap(T, a)), [a, off], [win])
 
     def sa(out, a, func, bias=0.0, scale=1.0):
         return add("s", (60 + max(64, _n(out))) * CYC, lambda g, T, x: g.scalar.activation(_ap(T, out), _ap(T, a), func, bias=val(T, bias), scale=val(T, scale)), [a] + isc(bias, scale), [out])
 
-    def lin(out, a, scale, bias):
-        sa(C(out), C(a), F.Identity, bias=bias, scale=scale)
+    def lin(out, a, scale, bias, func=F.Identity):
+        sa(C(out), C(a), func, bias=C(bias) if isinstance(bias, str) else bias, scale=C(scale) if isinstance(scale, str) else scale)
 
-    def sg(out, win, off, bias=0.0, scale=1.0):
-        add("s", 0.065 + _n(out) * GC * CYC, lambda g, T, x: g.scalar.activation(_ap(T, out), _ap(T, win).indirect(_ap(T, off)), F.Identity, bias=bias, scale=val(T, scale)), [win, off] + isc(scale), [out])
+    def cv(key, out, a, scale=1.0, bias=0.0):
+        if key in PAR["s"]:
+            return sa(out, a, F.Identity, bias=bias, scale=scale)
+        if scale == 1.0:
+            return vcopy(out, a) if bias == 0.0 else vs(out, a, bias, A.add)
+        return vs(out, a, scale, A.mult, bias, A.add)
+
+    def rsum(key, out, a):
+        if key in PAR["s"]:
+            add("s", (80 + _n(a)) * CYC, lambda g, T, x: g.scalar.activation(_ap(T, a), _ap(T, a), F.Identity, accum_out=_ap(T, out)), [a], [out, a])
+        else:
+            vred(out, a, A.add)
+
+    def gather(q, out, win, off, bias=0.0, scale=1.0):
+        if q == "v":
+            add("v", 0.05 + _n(out) * GC * CYC, lambda g, T, x: g.vector.tensor_scalar(_ap(T, out), _ap(T, win).indirect(_ap(T, off)), val(T, bias), None, A.add), [win, off] + isc(bias), [out])
+        else:
+            add("s", 0.065 + _n(out) * GC * CYC, lambda g, T, x: g.scalar.activation(_ap(T, out), _ap(T, win).indirect(_ap(T, off)), F.Identity, bias=val(T, bias), scale=scale), [win, off] + isc(bias), [out])
+
+    def shared(out, win, off, c0, c1, nv, bias=0.0, step=128):
+        for q, lo, hi in (("v", c0, c0 + nv), ("s", c0 + nv, c1)):
+            for a in range(lo, hi, step):
+                b = min(a + step, hi)
+                gather(q, (out[0], out[1] + 16 * a, out[1] + 16 * b), win, (off, a, b), bias)
 
     def mm(out, parts, start=True, stop=True):
-        cost = len(parts) * max(64, _n(out)) * TCY * (4 if SCRATCH[parts[0][0][0]][2] == "float32" else 1)
+        parts = [p if len(p) == 3 else p + (out,) for p in parts]
+        cost = sum(max(64, _n(o)) * TCY * (4 if SCRATCH[l[0]][2] == "float32" else 1) for l, r, o in parts)
 
         def e(g, T, x):
-            for k, (l, r) in enumerate(parts):
-                i = g.tensor.matmul(_ap(T, out), _ap(T, l), _ap(T, r), start and k == 0, stop and k == len(parts) - 1)
+            for k, (l, r, o) in enumerate(parts):
+                i = g.tensor.matmul(_ap(T, o), _ap(T, l), _ap(T, r), start and k == 0, stop and k == len(parts) - 1)
             return i
-        add("t", cost, e, [y for lr in parts for y in lr] + ([] if start else [out]), [out])
+        i = add("t", cost, e, [y for p in parts for y in p[:2]], [out], after=[bank[out[0]]] if out[0] in bank else [])
+        ops[i]["acc"] = not start
+        bank[out[0]] = i
 
     def wrapped(b, src, c0, n):
         return [((b, 15 - i, 143 - i), (src, c0 + i, c0 + n, 16)) for i in range(16)]
 
     def ld(sem, q, out, src, c0, c1):
-        add(q, 0.1, lambda g, T, x: (g.sync if q == "d" else g.scalar).dma_start(_ap(T, out), T[src][:, c0:c1]), [], [out], done=lambda x: (sem, 16))
+        add(q, 0.1, lambda g, T, x: (g.sync if q == "d" else g.scalar).dma_start(_ap(T, out), T[src][:, c0:c1]), [], [out], done=lambda x: (sem, 16), lat=2.0)
 
-    def blocks(n):
-        return [(b, min(b + 512, n)) for b in range(0, n, 512)]
+    def full(n, c=128):
+        return (n, 0, c)
 
     TP = [(0, 256), (256, 1536), (1536, 2816), (2816, TW)]
-    BST[0] = 50.0
     ld("lt0", "sd", ("tmo",) + TP[0], "tm", *TP[0])
     ld("lw", "d", ("wti", 0, 1), "wt", 0, 1)
     ld("lx0", "d", ("xin", 0, 1024), "x", 0, 1024)
     ld("lx1", "sd", ("xin", 1024, P), "x", 1024, P)
-    BST[0] = 0.0
     ld("lk", "d", ("kmi", 0, RO * M), "km", 0, RO * M)
     for k in range(1, 4):
         ld("lt%d" % k, "d" if k % 2 else "sd", ("tmo",) + TP[k], "tm", *TP[k])
 
     def iota(out, pat, base, cmul):
         add("g", 0.3, lambda g, T, x: g.iota(_ap(T, out), pat, base, cmul), [], [out])
-
-    def full(n, c=128):
-        return (n, 0, c)
     iota(C("ik"), [[1, 1]], 0, 1)
     iota(full("ij", 144), [[1, 144]], 0, 0)
-    iota(full("ic"), [[16, 128]], 0, 0)
-    ij, J, mb, PWP = full("ij"), full("ij", 144), full("mb", 144), ("p0", 256, 384)
+    iota(I("ic"), [[16, 128]], 0, 0)
+    ij, J, mb = full("ij"), full("ij", 144), full("mb", 144)
+    c15, c0m = ("mb", 0, 128), ("mb", 15, 143)
+    PH, POS, IDX = ("p7", 256, 384), ("p7", 384, 512), ("p1", 384, 512)
     vs(C("ikg"), C("ik"), 112, A.bitwise_and)
     vs(C("ikr"), C("ik"), 15, A.bitwise_and)
     vcopy(C("k"), C("ik"))
     vcopy(C("kr"), C("ikr"))
     vs(C("kg15"), C("ikg"), 15.0, A.add)
-    vs(C("r15"), C("kr"), 15.0, A.is_equal)
-    vs(C("fm"), C("kr"), 15.0, A.is_lt)
-    vs(C("half"), C("fm"), -0.5, A.mult, 1.0, A.add)
-    for c0 in (0, 1024):
-        vs(("xb0", W0 + c0, W0 + c0 + 1024), ("xin", c0, c0 + 1024), C("half"), A.mult)
     vs(mb, J, C("kg15"), A.is_equal)
     vcopy(C("wf"), full("wti", 1))
-    vs(C("w1"), C("fm"), 1.0, A.add)
-    vs(C("wu"), C("wf"), C("w1"), A.mult)
-    vs(full("bu", 144), mb, C("wu"), A.mult)
+    vs(full("bu0", 144), mb, C("wf"), A.mult)
+    vs(C("r15"), C("kr"), 15.0, A.is_equal)
+    vs(C("fm"), C("kr"), 15.0, A.is_lt)
+    vs(C("mk0"), C("kr"), 0.0, A.is_equal)
+    vs(B("ib"), ij, C("k"), A.is_equal)
     vcopy(full("kmf", RO * M), full("kmi", RO * M))
-    vs(full("pwf"), full("ic"), C("kr"), A.add)
-    vcopy(PWP, full("pwf"))
-    vs(full("ib"), ij, C("k"), A.is_equal)
-    vs(C("f2"), C("fm"), 2.0, A.mult)
-    vs(full("lxa"), full("mb"), C("f2"), A.mult)
-    vs(full("lxc"), full("ib"), C("fm"), A.mult)
-    vt(full("lx"), full("lxa"), full("lxc"), A.add)
+    vs(H("i16"), B("ib"), 1.0, A.mult)
+    vs(H("dnhf"), B("ib"), -1023.5, A.mult)
+    vset(full("one16", 512), 1.0)
+    vt(B("lxa"), B("ib"), c15, A.add)
+    vs(S("m1"), B("lxa"), C("fm"), A.mult)
+    vs(C("t0"), C("r15"), 1.0 / 16, A.mult)
+    vs(S("ta"), c0m, C("t0"), A.mult)
+    vt(B("lx0"), S("m1"), S("ta"), A.add)
+    vs(C("c128r"), C("mk0"), 128.0, A.mult)
+    vs(C("c128"), C("r15"), 128.0, A.mult, C("c128r"), A.add)
+    for c in (0, 1024):
+        vs(("xb", c, c + 1024), ("xin", c, c + 1024), C("fm"), A.mult, C("c128r"), A.add)
+    vset(("xb", P, P + 16), 0.0)
+    vs(H("pw16"), I("ic"), C("kr"), A.add)
+    vs(PH, H("pw16"), -1023.5, A.add)
+    vcopy(H("pos16"), H("pw16"))
     vs(C("flw"), C("fm"), 2.0, A.mult, -1.0, A.add)
-    vset(C("mone"), -1.0)
-    vs(C("dvc"), C("fm"), 40960.0, A.mult, -8192.0, A.add)
-    vs(C("dsc"), C("fm"), 16384.0, A.mult)
-    vs(C("bec"), C("fm"), 4096.0, A.mult)
-    for nm, cn in (("bf", "f2"), ("bs", "r15"), ("bdv", "dvc"), ("bds", "dsc"), ("be", "bec")):
+    vs(C("t1"), C("fm"), 24576.0, A.mult, -8192.0, A.add)
+    vs(C("t2"), C("fm"), 8192.0, A.mult)
+    vs(C("t3"), C("fm"), -2048.0, A.mult)
+    vs(C("t4"), C("flw"), 16.0, A.mult)
+    for nm, cn in (("bf", "fm"), ("bs", "r15"), ("bdv", "t1"), ("bds", "t2"), ("be", "t3"), ("bsq", "t4")):
         vs(full(nm, 144), mb, C(cn), A.mult)
-    for nm, v in (("nib", -1.0), ("i16", 1.0), ("d2kb", 2048.0), ("dn8k", -8192.0), ("dvoid", 15728640.0), ("dm4k", -4096.0), ("d2k16", 2048.0), ("ni16", -1.0), ("p2i", 2.0), ("m2i", -2.0)):
-        vs(full(nm), full("ib"), v, A.mult)
-    vcopy(full("pw16"), full("pwf"))
-    for m in range(1, 4):
-        vset(("cm", m * 128 - 128, m * 128), float(m))
-    vs(full("jb"), ij, 112, A.bitwise_and)
+    for nm, v in (("nib", -1.0), ("dvoid", 15728640.0), ("d4k", 4096.0), ("d23", 2.0 ** 23 + (2228224.0 if "vc" in PAR["s"] else 0.0)), ("dvc", 2228224.0), ("hb", -0.5)):
+        cv("k", B(nm), B("ib"), v)
+    for nm, v in (("dn8k", -8192.0), ("ni16", -1.0), ("m2i", -2.0), ("d2k16", 2048.0), ("nh16", -0.5), ("dhf", 1023.5), ("d2hf", 2047.0), ("p2i", 2.0), ("p11", 2.0 ** -11), ("m11", -2.0 ** -11), ("p12", 2.0 ** -12), ("m12", -2.0 ** -12)):
+        cv("k", H(nm), B("ib"), v)
+    cv("k", S("n32"), B("ib"), -1.0)
+    vs(B("i2f"), B("ib"), C("fm"), A.mult, 2.0, A.mult)
+    vset(B("one"), 1.0)
+    vset(full("onef", 16), 1.0)
+    vs(full("onefm", 16), full("onef", 16), C("fm"), A.mult)
+    vs(I("jb"), ij, 112, A.bitwise_and)
     vcopy(C("kg"), C("ikg"))
-    vs(full("ob"), full("jb"), C("kg"), A.is_equal)
-    vs(full("mk16", 16), ("ij", 0, 16), C("kr"), A.is_equal)
+    vs(S("ob"), I("jb"), C("kg"), A.is_equal)
     vs(C("iodd"), C("ik"), 1, A.bitwise_and)
     vcopy(C("odd"), C("iodd"))
-    vs(C("mk0"), C("kr"), 0.0, A.is_equal)
-    vs(C("padc"), C("kr"), 0.0, A.is_gt, float(TW), A.mult)
-    vt(C("padc"), C("padc"), C("kr"), A.add)
-    vs(C("dbl"), C("fm"), 1.0, A.add)
-    vset(("xb0", 0, W0), 0.0)
-    vset(("xb1", 0, W0), 0.0)
+    vs(I("jb"), ij, 126, A.bitwise_and)
+    vt(C("t5"), C("k"), C("odd"), A.subtract)
+    vs(H("l2"), I("jb"), C("t5"), A.is_equal)
+    for m in range(M):
+        vs(C("t6"), C("odd"), 2048.0 * m - 1023.5, A.mult, 1023.5, A.add)
+        vs(("cmq", 64 * m, 64 * m + 64), ("one16", 0, 64), C("t6"), A.mult)
+    vs(C("ib16"), C("ik"), 16, A.bitwise_and)
+    vcopy(C("t5"), C("ib16"))
+    vs(I("jb", 0, 32), ("ij", 0, 32), 16, A.bitwise_and)
+    vs(full("mk32", 32), I("jb", 0, 32), C("t5"), A.is_equal)
+    vset(("tr", 32, 40), 0.5)
+    vs(C("padt"), C("kr"), float(TW), A.add)
+    vs(C("padx"), C("kr"), float(P), A.add)
+    vs(IDX, I("ic"), -float(P), A.add)
+    vset(C("hc0"), 1.0 / 32)
+    vset(C("hc1"), -1.0 / 32)
+    vset(C("mhalf"), -0.5)
+    vs(C("n128"), C("c128"), -1.0, A.mult)
+    vs(C("n128r"), C("c128r"), -1.0, A.mult)
+    vs(C("c35"), C("mk0"), 3.5, A.mult)
+    vt(C("mid"), C("fm"), C("mk0"), A.subtract)
+    vt(C("t5"), C("mid"), C("r15"), A.subtract)
+    vs(H("la"), B("nib"), C("mid"), A.mult)
+    vs(H("lb"), c0m, C("t5"), A.mult)
+    vt(H("lj"), H("la"), H("lb"), A.add)
+    vs(H("la"), c15, C("t4"), A.mult)
+    vt(H("lf"), H("la"), H("lj"), A.subtract)
+    vs(S("m2"), c0m, C("flw"), A.mult, 2.0, A.mult)
+    vs(H("pc"), H("pw16"), -1.0, A.mult, 2047.0, A.add)
+    vs(("aa", 0, 1), C("wf"), C("mk0"), A.mult)
+    vs(("aa", 1, 2), C("wf"), C("r15"), A.mult)
+    mm(("p6", 0, 2), [(S("ob"), ("aa", 0, 2))])
+    vcopy(("cs", _CS["wa"], _CS["wa"] + 2), ("p6", 0, 2))
+    vs(C("cw"), C("wb"), 16.0, A.mult, C("wa"), A.subtract)
+    vs(C("wq0"), C("cw"), C("flw"), A.mult)
+    vs(C("wq1"), C("wf"), C("fm"), A.mult, C("wq0"), A.add)
+    vs(C("wq2"), C("wq1"), 2048.0, A.is_ge, -4096.0, A.mult)
+    vs(C("wq2"), C("wq2"), C("mid"), A.mult, C("wq1"), A.add)
+    vs(C("wq3"), C("wq1"), -2048.0, A.is_lt, 4096.0, A.mult)
+    vt(C("wq"), C("wq2"), C("wq3"), A.add)
+    vs(full("bq", 144), mb, C("wq"), A.mult)
+    vs(B("dw15"), B("ib"), C("wb"), A.mult, 0.5, A.mult)
+    vs(B("ndw15"), B("ib"), C("wb"), A.mult, -0.5, A.mult)
+    vs(B("fb1"), S("ob"), C("fm"), A.mult)
+    vs(B("wb1"), B("fb1"), C("wf"), A.mult)
+    vset(("w0", 0, W0), 0.0)
+    vset(("w1", 0, W0), 0.0)
     vset(full("msg"), 0)
 
     last = 0
     for k in range(4):
         r = TP[k]
-        last = add("g", 1.0, lambda g, T, x, r=r: x["send"](x["dn"], ("tb0",) + r, ("tmo",) + r, "ta0", "lown"), [("tmo",) + r], [], done=lambda x: ("lown", 0))
+        last = add("g", 1.0, lambda g, T, x, r=r: x["send"](x["dn"], ("tb0",) + r, ("tmo",) + r, "ta0", "lown"), [("tmo",) + r], [], done=lambda x: ("lown", 0), after=[last] if k else [])
     step = [last]
 
     def table(k, after):
-        add("x", 12.0 if k else 8.0, None, [], [("tb%d" % k, 0, TW)], done=(lambda x, k=k: ("ta%d" % k, x["ta"][k])), after=step[:1])
+        add("x", 12.0 if k else 8.0, None, [], [("tb%d" % k, 0, TW)], done=(lambda x, k=k: ("ta%d" % k, x["ta"][k])), after=step)
 
         def far(g, T, x):
             if x["far"] is not None:
@@ -213,235 +312,331 @@ def build():
         if k == 1:
             step.append(add("g", 1.0, far, [full("tmo", TW)], [], done=lambda x: ("lown", 0), after=[step[0]]))
 
-    wk = [0]
+    mord = []
+    Z = PAR["Z"]
+    for m, h, q, zb, fold, due in sorted(PAR["items"], key=lambda z: z[5]):
+        if m not in mord:
+            mord.append(m)
+    QB, WB = ("p2", "p4"), (("p3", "p4"), ("p5", "p2"))
+    UP, FP, NF, NC = ("p3", 0, 128), ("p3", 128, 256), ("p7", 0, 128), ("p6", 132, 133)
 
-    def work(n):
-        wk[0] += 1
-        return (("p3", "p4", "p7")[wk[0] % 3], 0, n)
+    def diag(t):
+        for m in mord:
+            sa(("dk", m * 128, m * 128 + 128), B("ib"), F.Identity, scale=("kmf", t * M + m, t * M + m + 1))
+
+    def lists(t):
+        BST[0] = Z + 4.0 if t else 3.0
+        if t:
+            vt(I("ui"), UP, S("gu"), A.add)
+        else:
+            vcopy(I("ui"), UP)
+        vs(I("u"), I("ui"), 4095, A.bitwise_and)
+        if "sq" in PAR["s"]:
+            sa(I("sq"), I("u"), F.Square)
+        else:
+            vt(I("sq"), I("u"), I("u"), A.mult)
+        cv("u16", H("u16"), I("u"), bias=-2048.0)
+        vs(I("sh"), I("sq"), 5, A.arith_shift_right, 2047, A.bitwise_and)
+        cv("sh16", H("sh16"), I("sh"))
+        cv("f1", H("f1"), FP)
+        for k in range(2):
+            bk = QB[k]
+            mm((bk, 0, 256), [(H("dnhf"), ("one16", 0, 256))], stop=False)
+            parts = []
+            for j in range(2):
+                m = mord[2 * k + j]
+                parts += [(("dk", m * 128, m * 128 + 128), H("u16"), (bk, j * 128, j * 128 + 128))]
+            mm((bk, 0, 256), parts, start=False, stop=False)
+            mm((bk, 0, 256), [(H("i16"), H("sh16"), (bk, j * 128, j * 128 + 128)) for j in range(2)], start=False)
+        for k, m in enumerate(mord):
+            c = (m * 128, m * 128 + 128)
+            qv = (QB[k // 2], (k % 2) * 128, (k % 2) * 128 + 128)
+            vs(("rr",) + c, qv, MAGIC, A.add, MAGIC, A.subtract)
+            vt(("q16",) + c, qv, ("rr",) + c, A.subtract)
+            cv("ql", ("ql",) + c, ("q16",) + c, bias=1023.5)
+
+    BST[0] = 2.0
+    diag(0)
+    mm(UP, wrapped("bu0", "xin", 0, P))
+    mm(FP, wrapped("bf", "xb", 0, P))
+    lists(0)
+    BST[0] = 3.0
+    for k in range(4):
+        w = (("p5", "p6")[k % 2], 0, 512)
+        o = ("w0", W0 + 512 * k, W0 + 512 * k + 512)
+        mm(w, [(B("lx0"), ("xin", 512 * k, 512 * k + 512))])
+        sa(o, w, F.Identity, bias=C("c128"))
+    mm(("p7", 0, 128), wrapped("bs", "xin", 0, P))
+    sa(B("sgn"), ("p7", 0, 128), F.Identity, scale=2.0)
+
     msgops = {}
     for t in range(RO):
-        xb, xn = "xb%d" % (t % 2), "xb%d" % (1 - t % 2)
-        X, XA = (xb, W0, W0 + P), (xb, 0, NX)
-
-        def pl(h, b=xb, o=W0):
-            return (b, o + 16 * PART[h][0], o + 16 * PART[h][1])
+        SEC[0] = t
+        w, wn = "w%d" % (t % 2), "w%d" % (1 - t % 2)
+        X, XA, XF = (w, W0, W0 + P), (w, 0, NX), (w, W0 + P, NX)
+        BST[0] = 13.0
         table(t, [msgops[(s, t - 1)] for s in range(t, RO)] if t else [])
-        XC = ("xc", 0, 16 * N0)
-        add("d", 0.1, lambda g, T, x, s=pl(0), o=XC: g.sync.dma_start(_ap(T, o), _ap(T, s)), [pl(0)], [XC], done=(lambda x, t=t: ("xc%d" % t, 16)))
-        UP, FP = ("p0", 0, 128), ("p0", 128, 256)
-        BST[0] = BU
-        for h in range(2):
-            mm(("p0", 64 * h, 64 * h + 64), wrapped("bu", xb, W0 + 1024 * h, 1024))
-        BST[0] = 0.0
-        vcopy(full("ui"), UP)
-        vs(full("u"), full("ui"), 4095, A.bitwise_and)
-        vt(full("sq"), full("u"), full("u"), A.mult)
-        vs(full("sh"), full("sq"), 5, A.arith_shift_right)
-        for m in MORD:
+        BST[0] = 13.5
+        add("d", 0.1, lambda g, T, x, w=w: g.sync.dma_start(_ap(T, S("rt")), T[w][0:128:16, W0:W0 + P]), [X], [S("rt")], done=(lambda x, t=t: ("fa%d" % t, 16)), lat=2.0)
+        add("d", 0.1, lambda g, T, x, X=X, XF=XF: g.sync.dma_start(_ap(T, XF), _ap(T, X)), [X], [XF], done=(lambda x, t=t: ("fb%d" % t, 16)), lat=5.0)
+        BST[0] = 14.6
+        for m in mord:
             c = (m * 128, m * 128 + 128)
-            vs(("p2",) + c, full("u"), ("kmf", t * M + m, t * M + m + 1), A.mult)
-            vt(("qv",) + c, full("sh"), ("p2",) + c, A.add)
-            vs(("qi",) + c, ("qv",) + c, 2047, A.bitwise_and)
-            vcopy(("ql",) + c, ("qi",) + c)
-        BST[0] = BX
-        for lo, hi in blocks(P):
-            w = work(512)
-            mm(w, [(full("lx"), (xb, W0 + lo, W0 + hi))])
-            sa(("xw", lo, hi), w, F.Identity, bias=C("r15"))
-        BST[0] = BQ
-        mm(FP, wrapped("bf", xb, W0, P))
-        vs(full("f1"), FP, -1.0, A.add)
-        for m in MORD:
-            c = (m * 128, m * 128 + 128)
-            vcopy(("q16",) + c, ("qi",) + c)
-            vt(("eq",) + c, ("qi",) + c, PWP, A.is_equal)
-        for h in PORD:
+            vt(("eq",) + c, ("q16",) + c, PH, A.is_equal)
+        if t < RO - 1:
+            BST[0] = Z - 0.5
+            diag(t + 1)
+        seen, ns, wait, slot = {0: 0, 1: 0}, 0, {0: [], 1: []}, {0: 0, 1: 0}
+        for m, h, q, zb, fold, due in PAR["items"]:
             h0, h1 = PART[h]
-            BST[0] = BP if h == PORD[0] else 0.0
-            for m in MORD:
-                wc = (m * 128 + h0, m * 128 + h1)
-                o = (m * P + 16 * h0, m * P + 16 * h1)
-                if (m, h) in VIT:
-                    vgt(("mx",) + o, full("xw", P), ("ql",) + wc, pl(h), A.max)
-                    parts = [(full("dn8k"), ("f1", h0, h1))] + wrapped("bdv", "mx", o[0], o[1] - o[0])
+            n = h1 - h0
+            BST[0] = due
+            wc = (m * 128 + h0, m * 128 + h1)
+            o = (m * P + 16 * h0, m * P + 16 * h1)
+            zz = ("p%d" % zb, slot[zb] * 64, slot[zb] * 64 + n)
+            slot[zb] += 1
+            parts = [(H("i16"), ("q16",) + wc), (H("l2"), ("cmq", 64 * m, 64 * m + n)), (B("dvoid"), ("eq",) + wc)]
+            if q == "v":
+                for k in range(0, n, PAR["vh"]):
+                    BST[0] = due + k * 0.027
+                    vgt(("mx", o[0] + 16 * k, o[0] + 16 * (k + PAR["vh"])), X, ("ql", wc[0] + k, wc[0] + k + PAR["vh"]), ("xb", 16 * (h0 + k), 16 * (h0 + k + PAR["vh"])), A.max)
+                BST[0] = due + 1.6
+                mm(zz, parts + [(H("dn8k"), H("f1", h0, h1))], stop=False)
+                mm(zz, wrapped("bdv", "mx", o[0], 16 * n), start=False)
+                BST[0] = due + 2.6
+            else:
+                for k in range(0, n, PAR["sh"]):
+                    BST[0] = due + k * 0.027
+                    gather("s", ("mx", o[0] + 16 * k, o[0] + 16 * (k + PAR["sh"])), X, ("ql", wc[0] + k, wc[0] + k + PAR["sh"]))
+                for k in range(2):
+                    wk = (WB[ns % 2][k], 0, 512)
+                    lo = 512 * k
+                    BST[0] = due + 0.5
+                    mm(wk, [(B("nib"), ("xb", 16 * h0 + lo, 16 * h0 + lo + 512))], stop=False)
+                    BST[0] = due + 1.5 + 0.5 * k
+                    mm(wk, [(H("i16"), ("mx", o[0] + lo, o[0] + lo + 512))], start=False)
+                    sa(("ab", o[0] + lo, o[0] + lo + 512), wk, F.Abs)
+                ns += 1
+                BST[0] = due + 2.8
+                mm(zz, parts, stop=False)
+                mm(zz, wrapped("bds", "ab", o[0], 16 * n), start=False)
+                BST[0] = due + 3.7
+            wait[h].append(zz)
+            bb = (S("b0", h0, h1), S("b1", h0, h1))
+            while fold and wait[h]:
+                zz = wait[h].pop(0)
+                seen[h] += 1
+                if seen[h] == 1:
+                    cv("fold", bb[1], zz)
                 else:
-                    sg(("gm",) + o, X, ("ql",) + wc)
-                    for lo, hi in blocks(o[1] - o[0]):
-                        w = work(hi - lo)
-                        mm(w, [(full("ib"), ("gm", o[0] + lo, o[0] + hi)), (full("nib"), (xb, W0 + 16 * h0 + lo, W0 + 16 * h0 + hi))])
-                        sa(("ab", o[0] + lo, o[0] + hi), w, F.Abs)
-                    parts = wrapped("bds", "ab", o[0], o[1] - o[0])
-                parts = [(full("i16"), ("q16",) + wc), (full("dvoid"), ("eq",) + wc)] + parts
-                if m:
-                    parts.insert(0, (full("d2kb"), ("cm", m * 128 - 128, m * 128 - 128 + h1 - h0)))
-                mm(("p%d" % (1 + h), m * 128, m * 128 + h1 - h0), parts)
-        BST[0] = 0.0
+                    vt(I("bk", h0, h1) if seen[h] == M else bb[seen[h] % 2], bb[1 - seen[h] % 2], zz, A.min)
+        BST[0] = 20.0
         tb = "tb%d" % t
         TB = (tb, 0, TW)
         for s in range(t):
             i = _LK.index((t, s)) * 32
             add("x", 3.0, None, [], [("land", i, i + 32)], done=(lambda x, s=s, t=t: ("m%d_%d" % (t, s), x["mn"][(t, s)])), after=[msgops[(t, s)]])
-            vcopy(full("upv", 16), ("land", i + 16, i + 32))
-            add("v", 0.15, lambda g, T, x, tb=tb, i=i: g.vector.tensor_copy(T[tb][:, 0:TW + 16].indirect(T.land[:, i:i + 1]), T.upv[:, 0:16]), [full("upv", 16), ("land", i, i + 32)], [(tb, 0, TW + 16)])
-        SM, LG, E = ("p5", 256, 384), ("p5", 384, 512), ("p6", 0, 128)
-        flips = 0
-        for h in PORD:
-            BST[0] = BP if h == PORD[0] else 0.0
+            cv("upv", full("upv", 16), ("land", i + 16, i + 32))
+            vscat((tb, 0, TW + 16), ("land", i, i + 1), full("upv", 16))
+        N, SM, LG, HL = ("p6", 0, 128), ("p0", 0, 128), ("p0", 128, 256), ("p0", 256, 384)
+        for h in range(2):
+            d0 = BST[0] = PAR["ds"][h]
             c = PART[h]
-            n = c[1] - c[0]
-            pn = 16 * n
-            Zs = [("p%d" % (1 + h), m * 128, m * 128 + n) for m in range(4)]
-            US, SG = ("p5",) + c, ("p5", 128 + c[0], 128 + c[1])
-            vcopy(("b0",) + c, Zs[0])
-            vt(("b1",) + c, ("b0",) + c, Zs[2], A.min)
-            vt(("b2",) + c, ("b1",) + c, Zs[3 if (3, h) in VIT else 1], A.min)
-            vt(("bk",) + c, ("b2",) + c, Zs[1 if (3, h) in VIT else 3], A.min)
-            vs(("q",) + c, ("bk",) + c, 2047, A.bitwise_and)
-            vcopy(("qsl",) + c, ("q",) + c)
-            if h == 0:
-                vgt(full("sp", pn), X, ("qsl",) + c, XC, A.add)
-                mm(US, wrapped("bu", "sp", 0, pn))
-                vt(("uq",) + c, US, ("ui",) + c, A.subtract)
-            else:
-                sg(full("gq", pn), X, ("qsl",) + c)
-                mm(US, wrapped("bu", "gq", 0, pn))
-                vcopy(("uq",) + c, US)
-            vs(("uq2",) + c, ("uq",) + c, 4095, A.bitwise_and)
-            vt(("uu",) + c, ("uq2",) + c, ("u",) + c, A.mult)
-            vs(("h",) + c, ("uu",) + c, 4, A.arith_shift_right, 4095, A.bitwise_and)
-            vcopy(("hl",) + c, ("h",) + c)
-            vs(("di",) + c, ("bk",) + c, 13, A.arith_shift_right)
-            vcopy(("d16",) + c, ("di",) + c)
-            vs(("vc",) + c, ("di",) + c, 1919.0, A.is_ge, 2176.0, A.mult)
-            vcopy(("qs16",) + c, ("q",) + c)
             o = 16 * c[0]
-            b0 = BST[0]
-            if h == 0:
-                vgt(full("rr", pn), TB, ("hl",) + c, full("sp", pn), A.subtract)
-                for lo, hi in blocks(pn):
-                    flips = sa(("ab2", o + lo, o + hi), ("rr", lo, hi), F.Abs)
-                BST[0] = b0 + BE
-                mm(SG, wrapped("bs", "sp", 0, pn))
+            US = ("p7",) + c
+            vs(I("q", *c), I("bk", *c), 2047, A.bitwise_and)
+            cv("qsl", ("qsl",) + c, I("q", *c))
+            shared(("gq", 0), X, "qsl", c[0], c[1], PAR["xq"][h], C("n128"), step=PAR["xh"])
+            BST[0] = d0 + 1.8
+            mm(US, wrapped("bq", "gq", o, 1024))
+            BST[0] = d0 + 2.5
+            cv("uq", I("uq", *c), US)
+            vs(I("uq2", *c), I("uq", *c), 4095, A.bitwise_and)
+            vt(I("uu", *c), I("uq2", *c), I("u", *c), A.mult)
+            vs(I("h", *c), I("uu", *c), 4, A.arith_shift_right, 4095, A.bitwise_and)
+            cv("hl", ("hl",) + c, I("h", *c))
+            BST[0] = d0 + 2.0
+            vs(I("di", *c), I("bk", *c), 13, A.arith_shift_right)
+            cv("d16", H("d16", *c), I("di", *c), -1.0, 1920.0)
+            if "vc" in PAR["s"]:
+                sa(B("vc", *c), I("di", *c), F.Sign, scale=-1.0, bias=1918.5)
             else:
-                sg(full("ga", pn), TB, ("hl",) + c)
-                for lo, hi in blocks(pn):
-                    w = work(hi - lo)
-                    mm(w, [(full("ib"), ("ga", lo, hi)), (full("nib"), ("gq", lo, hi)), (full("nib"), (xb, W0 + o + lo, W0 + o + hi))])
-                    flips = sa(("ab2", o + lo, o + hi), w, F.Abs)
-                BST[0] = b0 + BE
-                mm(SG, wrapped("bs", "gq", 0, pn) + wrapped("bs", xb, W0 + o, pn))
-            BST[0] = b0
-            mm(("p6",) + c, [(full("i16"), ("pw16",) + c), (full("d2k16"), ("d16",) + c), (full("d2kb"), ("vc",) + c)] + wrapped("be", "ab2", o, pn))
-        BST[0] = 0.0
-        sa(full("dir"), ("p5", 128, 256), F.Square, bias=C("mone"))
-        vt(full("cmn"), full("q"), PWP, A.min)
-        mm(LG, [(full("i16"), full("pw16")), (full("i16"), full("qs16")), (full("ni16"), full("cmn"))])
-        mm(SM, [(full("i16"), full("cmn")), (full("d2kb"), ("cm", 128, 256)), (full("dm4k"), full("dir"))])
-        vcopy(full("cc"), SM)
-        AFT.append(flips)
-        for lo, hi in blocks(P):
-            sa((xb, W0 + P + lo, W0 + P + hi), (xb, W0 + lo, W0 + hi), F.Identity, scale=C("flw"), bias=C("r15"))
-        AFT.clear()
+                vs(B("vc", *c), I("di", *c), 1919.0, A.is_lt, 2.0, A.mult)
+            cv("qs16", H("qs16", *c), I("q", *c), bias=-1023.5)
+            BST[0] = d0 + 3.2
+            shared(("ga", 0), TB, "hl", c[0], c[1], PAR["tq"][h], step=32)
+            for k in range(2):
+                wk = (WB[(ns + h) % 2][k], 0, 512)
+                lo = o + 512 * k
+                BST[0] = d0 + 1.5
+                mm(wk, [(B("nib"), ("xb", lo, lo + 512))], stop=False)
+                BST[0] = d0 + 2.6
+                mm(wk, [(H("lj"), ("gq", lo, lo + 512))], start=False, stop=False)
+                BST[0] = d0 + 4.2 + 0.5 * k
+                mm(wk, [(B("i2f"), ("ga", lo, lo + 512))], start=False)
+                sa(("ab2", lo, lo + 512), wk, F.Abs, bias=C("c128r"))
+        for h, c in enumerate(PART):
+            BST[0] = PAR["ds"][h] + 3.0
+            mm(("p6", 256 + c[0], 256 + c[1]), [(B("hb"), B("sgn", *c))] + wrapped("bsq", "gq", 16 * c[0], 1024))
+        for h in range(2):
+            BST[0] = PAR["ds"][h] + 5.3
+            c = PART[h]
+            mm(("p6",) + c, [(B("d23"), B("one", *c)), (H("d2k16"), H("d16", *c)), (B("dvc"), B("vc", *c)), (H("ni16"), H("pos16", *c))], stop=False)
+            mm(("p6",) + c, wrapped("be", "ab2", 16 * c[0], 1024), start=False)
+        BST[0] = Z - 1.0
+        sa(B("r2"), S("rt"), F.Identity, scale=2.0)
+        mm(("p7", 128, 256), [(B("ib"), B("r2")), (S("n32"), S("rt"))])
+        sa(S("rf"), ("p7", 128, 256), F.Identity, bias=1.0 / 16)
+        add("d", 0.1, lambda g, T, x, w=w: g.sync.dma_start(T[w][0:128:16, W0 + P:NX], _ap(T, S("rf"))), [S("rf")], [XF], done=(lambda x, t=t: ("fc%d" % t, 16)), lat=2.0)
+        BST[0] = PAR["ds"][1] + 3.6
+        SG, XE, XW, K2 = ("p6", 256, 384), ("p1", 0, 128), ("p0", 384, 512), ("p1", 128, 256)
+        one = ("one16", 0, 128)
+        vt(H("cmn"), H("qs16"), PH, A.min)
+        sa(B("inv"), SG, F.Abs)
+        mm(LG, [(H("i16"), H("pos16")), (H("i16"), H("qs16")), (H("ni16"), H("cmn"))])
+        mm(SM, [(H("i16"), H("cmn")), (H("dhf"), one), (B("d4k"), B("inv"))])
+        mm(HL, [(H("ni16"), H("pos16")), (H("ni16"), H("qs16")), (H("p2i"), H("cmn")), (H("dhf"), one), (H("d2hf"), one)])
+        mm(XE, [(H("ni16"), H("pos16")), (H("ni16"), H("qs16")), (H("i16"), H("cmn")), (H("d2hf"), one)])
 
-        def lowest(src, dst, kp):
-            vred(C("r1"), src, A.min)
-            vs(full("dg", 16), full("mk16", 16), C("r1"), A.mult)
-            mm(("p6", kp, kp + 16), [(full("ob"), full("dg", 16))])
-            vred(dst, ("p6", kp, kp + 16), A.min)
+        def highest(src, r, dst):
+            vred(C(r), src, A.max)
+            vs(full("dg", 32), full("mk32", 32), C(r), A.mult)
+            vtr(full("tr", 32), full("dg", 32))
+            vred(C(dst), full("tr", 33), A.max)
 
-        def fetch(oh, src, kmin, out):
-            vs(full(oh), src, kmin, A.is_equal)
-            for k, tile in ((0, SM), (1, LG)):
-                vt(("pr", 128 * k, 128 * k + 128), full(oh), tile, A.mult)
-                vred(("aa", k, k + 1), ("pr", 128 * k, 128 * k + 128), A.add)
-            mm(out, [(full("ob"), ("aa", 0, 2))])
-        A1, A2 = ("p6", 160, 162), ("p6", 224, 226)
-        aX, bX, cX, dX = ("p6", 160, 161), ("p6", 161, 162), ("p6", 224, 225), ("p6", 225, 226)
-        lowest(E, C("kmin"), 128)
-        fetch("oh", E, C("kmin"), A1)
-        BIG = float(2 ** 25)
-        vs(full("t1"), full("cc"), aX, A.is_le, BIG, A.mult)
-        vs(full("t2"), full("cc"), bX, A.is_ge, BIG, A.mult)
-        vt(full("k2a"), full("t1"), E, A.max)
-        vt(full("k2"), full("k2a"), full("t2"), A.max)
-        vs(C("inv"), aX, 4096.0, A.is_ge)
+        def fetch(oh, src, kmax, tiles, out, start):
+            vs(oh, src, C(kmax), A.is_equal)
+            for k in range(2):
+                vt(S("pr%d" % k), oh, tiles[k], A.mult)
+                rsum("aa%d" % k, ("aa", k, k + 1), S("pr%d" % k))
+            mm(out, [(S("ob"), ("aa", 0, 2))], start=start)
+        BST[0] = Z
+        A1, A2 = ("p5", 128, 130), ("p6", 128, 130)
+        aX, bX, eX, wX = ("p5", 128, 129), ("p5", 129, 130), ("p6", 128, 129), ("p6", 129, 130)
+        mm(A1, [(S("ob"), ("cs", _CS["hc0"], _CS["hc0"] + 2))], stop=False)
+        highest(N, "r1", "kmax")
+        fetch(B("oh"), N, "kmax", (SM, LG), A1, False)
+        BST[0] = Z + 1.7
+        vs(S("cl"), SM, aX, A.max, bX, A.min)
+        BST[0] = Z + 1.9
+        vt(S("inn"), S("cl"), SM, A.is_equal)
+        BST[0] = Z + 2.1
+        vt(K2, S("inn"), N, A.mult)
+        BST[0] = Z + 1.75
         vs(C("xC"), aX, 4096.0, A.is_ge, -4096.0, A.mult)
-        vs(C("a"), aX, C("xC"), A.add)
-        vcopy(C("b"), bX)
+        vs(C("a"), aX, C("xC"), A.add, -0.5, A.add)
+        vs(C("b"), bX, 0.5, A.add)
         vs(C("ba"), C("b"), C("a"), A.subtract)
         vs(("nl", 0, 1), C("odd"), C("ba"), A.mult, C("a"), A.add)
-        sg(full("nc", 16), X, ("nl", 0, 1), bias=-0.125)
-        vs(C("nf"), ("nc", 1, 2), C("fm"), A.mult, ("nc", 0, 1), A.add)
-        vcopy(C("ni"), C("nf"))
-        vs((xb, 15, 16), C("ni"), C("half"), A.mult)
-        lin("dir", "inv", -1.0, 1.0)
-        lin("xI", "inv", -4096.0, 4096.0)
-        lin("x3", "inv", 2048.0, 0.0)
-        lin("an1", "a", -1.0, -1.0)
-        lin("xd", "b", -1.0, 2047.0)
-        lin("aI", "a", 1.0, C("xI"))
-        lin("bI", "b", 1.0, C("xI"))
-        lin("m1", "ba", 1.0, C("inv"))
-        lin("m3", "ba", C("dir"), C("x3"))
-        lin("K2", "ba", C("inv"), C("x3"))
-        lin("cdef", "ba", C("dir"), C("a"))
-        lin("ddef", "xd", C("dir"), C("b"))
-        lin("w", "cdef", -1.0, C("ddef"))
-        for k, (src, scale, bias) in enumerate((("ba", -1.0, "ddef"), ("ddef", 1.0, None), ("w", 1.0, "a"), ("K2", -1.0, "w"), ("inv", -1.0, "w"))):
-            sa(("pd", k, k + 1), C(src), F.Identity, scale=scale, bias=C(bias) if bias else 0.0)
-        pw = full("pw16")
-        G = [("gt", i * 128, i * 128 + 128) for i in range(7)]
-        vs(G[0], pw, C("a"), A.is_gt, C("m1"), A.mult)
-        vs(G[1], pw, C("aI"), A.subtract, 0.0, A.max)
-        vs(G[2], pw, C("bI"), A.subtract, 0.0, A.max)
-        vs(G[3], pw, C("a"), A.is_equal, C("an1"), A.mult)
-        PL = ("p1", 0, 128)
-        i16, n16 = full("i16"), full("ni16")
-        mm(PL, [(i16, pw), (i16, G[0]), (full("m2i"), G[1]), (full("p2i"), G[2]), (i16, G[3])], stop=False)
-        KK = full("k2")
-        lowest(KK, C("kmin2"), 192)
-        fetch("oh2", KK, C("kmin2"), A2)
-        vs(C("f"), C("kmin2"), float(2 ** 24), A.is_lt)
-        vs(C("valid"), dX, C("b"), A.is_gt, C("f"), A.mult)
-        vs(C("xe"), dX, C("ddef"), A.subtract, C("valid"), A.mult)
-        vs(C("xc"), cX, C("cdef"), A.subtract, C("valid"), A.mult)
-        vs(full("qd", 5), full("pd", 5), C("xe"), A.add)
-        vs(full("qe", 3), ("qd", 2, 5), C("xc"), A.subtract)
-        vs(G[4], pw, ("qd", 0, 1), A.is_gt, ("qe", 1, 2), A.mult)
-        vs(G[5], pw, ("qe", 0, 1), A.is_gt, C("m3"), A.mult)
-        vs(G[6], pw, ("qd", 1, 2), A.is_gt, ("qe", 2, 3), A.mult)
-        mm(PL, [(n16, G[4]), (n16, G[5]), (i16, G[6])], start=False)
-        order = vs(full("pl"), PL, float(W0), A.add)
+        gather("s", full("nc", 16), X, ("nl", 0, 1), bias=-0.125, scale=0.5)
+        vs(C("ni"), ("nc", 0, 1), ("nc", 1, 2), A.add)
+        cv("nif", C("nif"), C("ni"))
+        mm(NC, [(S("m2"), ("nc", 0, 1)), (S("m1"), C("nif"))])
+        cv("w15", (w, 15, 16), NC, bias=C("c35"))
         if t < RO - 1:
-            for k in range(4):
-                o = (xn, W0 + 512 * k, W0 + 512 * k + 512)
-                if k % 2:
-                    sg(o, XA, ("pl", 32 * k, 32 * k + 32))
-                else:
-                    vgs(o, XA, ("pl", 32 * k, 32 * k + 32), 1.0)
-            AFT.append(order)
-            BST[0] = BM
-            vt(full("hpr"), full("oh"), full("h"), A.mult)
-            vred(C("har"), full("hpr"), A.add)
-            mm(("p6", 256, 257), [(full("ob"), C("har"))])
-            vcopy(C("hpf"), ("p6", 256, 257))
-            vs(("msg", t * 32, t * 32 + 1), C("hpf"), C("mk0"), A.mult, C("padc"), A.add)
-            vcopy(("msg", t * 32 + 16, t * 32 + 17), C("ni"))
+            BST[0] = Z + 5.6
+            vs(B("oha"), H("pos16"), C("a"), A.is_equal)
+            vt(S("hpr"), B("oha"), IDX, A.mult)
+            rsum("idr", C("idr"), S("hpr"))
+            cv("xl", ("xl", 0, 1), C("idr"), bias=C("padx"))
+            cv("nb", full("nb", 16), full("onefm", 16), scale=C("nif"))
+            vscat(full("xb", P + 16), ("xl", 0, 1), full("nb", 16))
+            BST[0] = Z + 2.5
+            vs(H("f0"), H("pos16"), C("a"), A.is_gt, C("xC"), A.mult)
+            vs(H("f1m"), H("pos16"), C("b"), A.is_gt, C("xC"), A.mult)
+            gather("s", full("ncb", 16), X, ("nl", 0, 1))
+            vs(("ncb", 16, 17), C("ni"), ("ncb", 0, 1), A.subtract)
+            mm(("p4", 0, 2), [(B("wb1"), ("ncb", 16, 17), ("p4", 0, 1)), (B("fb1"), ("ncb", 16, 17), ("p4", 1, 2))])
+            vs(S("gu"), H("pos16"), C("a"), A.is_equal, ("p4", 0, 1), A.mult)
+            vs(H("gf"), H("pos16"), C("a"), A.is_equal, ("p4", 1, 2), A.mult)
+            mm(UP, [(H("i16"), H("u16")), (H("d2k16"), one), (B("ndw15"), B("sgn"))], stop=False)
+            mm(NF, [(B("ib"), B("sgn")), (H("p11"), H("f0")), (H("m11"), H("f1m"))])
+            sa(B("sgn"), NF, F.Abs)
+            mm(UP, [(B("dw15"), B("sgn"))], start=False)
+            mm(FP, [(H("i16"), H("f1")), (H("i16"), H("gf"))])
+        BST[0] = Z + 2.4
+        vs(B("v"), LG, C("b"), A.is_gt)
+        vs(XW, HL, C("b"), A.subtract)
+        vt(S("k2v"), B("v"), K2, A.mult)
+        BST[0] = Z + 2.0
+        lin("inv", "xC", -1.0 / 4096, 0.0)
+        lin("xd", "xC", 1.0, 2047.0)
+        lin("aI", "a", "inv", 0.0)
+        lin("bI", "b", "inv", 0.0)
+        lin("u1", "ba", -1.0, "xd", F.Relu)
+        lin("nz", "u1", 1.0, "bI")
+        sa(H("pa"), H("pw16"), F.Identity, scale=-1.0, bias=C("nz"))
+        lin("m3", "xC", 2049.0 / 4096, "ba", F.Abs)
+        lin("wdef", "b", -1.0, "xd", F.Relu)
+        lin("an1", "a", -1.0, -1.0)
+        lin("pb", "aI", 2.0, 0.0)
+        BST[0] = Z + 3.6
+        pw, i16, n16 = H("pw16"), H("i16"), H("ni16")
+        vs(H("g0"), pw, C("a"), A.is_gt, C("ba"), A.mult)
+        vs(H("g0b"), pw, C("a"), A.is_gt, C("xC"), A.mult)
+        vs(H("gr"), pw, C("aI"), A.max, C("bI"), A.min)
+        vs(H("g3"), pw, C("a"), A.is_equal, C("an1"), A.mult)
+        PL = ("p5", 0, 128)
+        mm(PL, [(i16, pw), (i16, H("g0")), (H("nh16"), H("g0b")), (H("m12"), H("g0b")), (H("m2i"), H("gr")), (i16, H("g3"))], stop=False)
+        BST[0] = Z + 2.3
+        highest(K2, "r2", "kmax2")
+        BST[0] = Z + 2.9
+        fetch(B("oh2"), S("k2v"), "kmax2", (XE, XW), A2, True)
+        BST[0] = Z + 4.2
+        vs(C("ws"), wX, -1.0, A.mult, C("wdef"), A.add)
+        vs(H("g4"), H("pa"), wX, A.is_lt, C("m3"), A.mult)
+        vs(H("g5", 0, 256), H("pa", 0, 256), eX, A.is_lt, C("ws"), A.mult)
+        mm(PL, [(n16, H("g4")), (n16, H("g5")), (i16, H("g6"))], start=False)
+        vs(full("pl"), PL, C("pb"), A.add, float(W0), A.add)
+        BST[0] = Z + 5.3
+        if t < RO - 1:
+            shared((wn, W0), XA, "pl", 0, 128, PAR["rv"])
+            lists(t + 1)
+            BST[0] = Z + 3.8
+            lin("k0", "ba", "inv", 0.0)
+            lin("mba", "k0", -1.0, "ba")
+            cv("ds", C("ds"), eX, -1.0, 2047.0)
+            lin("h0", "ws", 1.0, "k0")
+            lin("h1", "ws", -1.0, "k0")
+            lin("cs", "ws", -1.0, "ds")
+            pos = H("pos16")
+            BST[0] = Z + 7.0
+            vs(H("h0"), pos, C("a"), A.is_gt, C("h0"), A.mult)
+            vs(H("h1"), pos, C("b"), A.is_gt, C("h1"), A.mult)
+            vs(H("hr"), pos, C("aI"), A.max, C("bI"), A.min)
+            vs(H("h4"), pos, C("cs"), A.is_gt, C("mba"), A.mult)
+            vs(H("h5"), pos, C("ds"), A.is_gt, C("mba"), A.mult)
+            mm(POS, [(i16, pos), (H("m2i"), H("hr")), (H("m12"), H("f0")), (H("p12"), H("f1m"))], stop=False)
+            mm(POS, [(i16, H("h0")), (i16, H("h1")), (n16, H("h4")), (i16, H("h5"))], start=False)
+            if "ph" in PAR["s"]:
+                cv("pos", pos, POS, bias=C("pb"))
+                cv("ph", PH, pos, bias=-1023.5)
+            else:
+                vs(PH, POS, C("pb"), A.add, -1023.5, A.add)
+                cv("pos", pos, POS, bias=C("pb"))
+            BST[0] = Z + 10.5
+            vt(S("hp2"), B("oh"), I("h"), A.mult)
+            rsum("har", C("har"), S("hp2"))
+            vs(C("e1"), C("r1"), C("kmax"), A.not_equal, C("padt"), A.mult)
+            cv("msg0", ("msg", t * 32, t * 32 + 1), C("har"), bias=C("e1"))
+            cv("msg1", ("msg", t * 32 + 16, t * 32 + 32), full("onef", 16), C("nif"), C("n128r"))
             for t2 in range(t + 1, RO):
                 def e(g, T, x, t=t, t2=t2):
                     i = _LK.index((t2, t)) * 32
                     x["send"](x["user"][t2], ("land", i, i + 32), ("msg", t * 32, t * 32 + 32), "m%d_%d" % (t2, t), "lmsg")
                 msgops[(t2, t)] = add("g", 1.0, e, [("msg", t * 32, t * 32 + 32)], [], done=lambda x: ("lmsg", 0), after=step)
-            AFT.clear()
-            BST[0] = 0.0
         else:
-            for h in range(2):
-                yo = ("yo", 1024 * h, 1024 * h + 1024)
-                if h:
-                    sg(yo, XA, ("pl", 64, 128), scale=C("dbl"))
+            for k in range(4):
+                c = (512 * k, 512 * k + 512)
+                wk = ("p%d" % (3 + k), 0, 512)
+                gather("vs"[k % 2], ("gq",) + c, XA, ("pl", 32 * k, 32 * k + 32), C("n128"))
+                mm(wk, [(H("lf"), ("gq",) + c)])
+                if k % 2:
+                    sa(("yo",) + c, wk, F.Identity)
                 else:
-                    vgs(yo, XA, ("pl", 0, 64), C("dbl"))
-                add("sd" if h else "d", 0.1, lambda g, T, x, h=h, yo=yo: (g.scalar if h else g.sync).dma_start(T.y[:, yo[1]:yo[2]], _ap(T, yo)), [yo], [], done=(lambda x, h=h: ("st%d" % h, 16)))
+                    vcopy(("yo",) + c, wk)
+                add("sd" if k % 2 else "d", 0.1, lambda g, T, x, k=k, c=c: (g.scalar if k % 2 else g.sync).dma_start(T.y[:, c[0]:c[1]], _ap(T, ("yo",) + c)), [("yo",) + c], [],
+                    done=(lambda x, k=k: ("st%d" % k, 16)), lat=2.0)
     return ops
 
 
@@ -452,6 +647,7 @@ _CACHE = {}
 def plan():
     if "o" in _CACHE:
         return _CACHE["o"]
+    WAKE, SELF = PAR["WAKE"], PAR["SELF"]
     ops = build()
     hist = {}
     for i, o in enumerate(ops):
@@ -460,56 +656,48 @@ def plan():
         rw = [(0, r) for r in o["reads"]] + [(1, r) for r in o["writes"]]
         for kind, r in rw:
             for (j, k2, a, b, q2) in hist.get(r[0], ()):
-                if (kind or k2) and a < r[2] and r[1] < b or _ps(r) and q2 != q:
+                if _ps(r) and q2 == q == "t" and o["acc"]:
+                    continue
+                if (kind or k2) and a < r[2] and r[1] < b:
                     deps.add(j)
         for kind, r in rw:
             hl = hist.setdefault(r[0], [])
-            if kind:
-                hl[:] = [e for e in hl if not (r[1] <= e[2] and e[3] <= r[2] and (e[4] == q or not _ps(r)))]
+            if kind and not o.get("acc"):
+                hl[:] = [e for e in hl if not (r[1] <= e[2] and e[3] <= r[2])]
             hl.append((i, kind, r[1], r[2], q))
         o["data"] = deps
         o["deps"] = sorted(deps | set(o["after"]))
+        o["banks"] = sorted({r[0] for kind, r in rw if _ps(r)})
     n = len(ops)
     succ = [[] for _ in ops]
     for i, o in enumerate(ops):
         for j in o["deps"]:
             succ[j].append(i)
-    prio = [0.0] * n
-    for i in range(n - 1, -1, -1):
-        prio[i] = ops[i]["cost"] + ops[i]["boost"] + max([prio[j] + (SELF if ops[i]["qq"] == ops[j]["qq"] else WAKE) for j in succ[i]] + [0.0])
+    tau = {TAU[k:k + 4]: int(TAU[k + 4:k + 7], 36) for k in range(0, len(TAU), 7)}
+    for i, o in enumerate(ops):
+        hv = 0
+        for ch in str(o["tag"]):
+            hv = (hv * 131 + ord(ch)) % 1679609
+        o["key"] = "".join("0123456789abcdefghijklmnopqrstuvwxyz"[hv // 36 ** k % 36] for k in range(4))
+        o["due"] = PAR["T"] * max(o["sec"], 0) + (PAR["T0"] if o["sec"] >= 0 else 0) + tau.get(o["key"], o["tau0"])
     left = [len(o["deps"]) for o in ops]
-    est, fin, free, order = [0.0] * n, [0.0] * n, {}, []
+    order, fin, free, last = [], [0.0] * n, {}, {}
     ready = [i for i in range(n) if left[i] == 0]
     while ready:
-        best, byq = None, {}
-        for i in ready:
-            byq.setdefault(ops[i]["qq"], []).append(i)
-        for q, lst in byq.items():
-            st = min(est[k] for k in lst)
-            if q != "x":
-                st = max(st, free.get(q, 0.0))
-            cand = sorted((k for k in lst if est[k] <= st + 1e-9), key=lambda k: (-prio[k], k))
-            pick = None
-            for i in cand:
-                if q == "x" or not any(prio[k] > prio[i] + 0.3 and st + ops[i]["cost"] - est[k] > est[k] - st for k in lst if st < est[k] < st + ops[i]["cost"]):
-                    pick = i
-                    break
-            if pick is None:
-                later = [k for k in lst if est[k] > st + 1e-9]
-                pick = min(later, key=lambda k: (est[k], -prio[k]))
-                st = est[pick]
-            if best is None or st < best[0]:
-                best = (st, pick, q)
-        st, i, q = best
+        i = min(ready, key=lambda k: (ops[k]["due"], k))
         ready.remove(i)
-        fin[i] = st + ops[i]["cost"]
-        if q != "x":
-            free[q] = fin[i] + 0.02
-        lat = 2.0 if ops[i]["q"] in ("d", "sd") else 0.0
         order.append(i)
+        o = ops[i]
+        q = o["qq"]
+        o["true"] = set(o["data"])
+        for b in o["banks"]:
+            o["data"] |= {j for q2, j in last.setdefault(b, {}).items() if q2 != q}
+            last[b][q] = i
+        st = max([free.get(q, 0.0) if q != "x" else 0.0] + [fin[j] for j in o["after"]] + [fin[j] + ops[j]["lat"] + (SELF if ops[j]["qq"] == q else WAKE) for j in o["data"]])
+        fin[i] = st + o["cost"]
+        free[q] = fin[i] + 0.02
         for j in succ[i]:
             left[j] -= 1
-            est[j] = max(est[j], fin[i] + lat + (SELF if ops[j]["qq"] == q else WAKE))
             if left[j] == 0:
                 ready.append(j)
     cnt = {}
@@ -523,6 +711,21 @@ def plan():
     return _CACHE["o"]
 
 
+def links(rank, N, near, neng, send):
+    def direct(r):
+        return near(r + RO, r)
+    dn, far = (rank - 1) % N, (rank - RO) % N
+    x = {"send": send, "user": {t: (rank - 1 - t) % N for t in range(RO)}}
+    x["dn"], x["far"] = dn, far if direct(far) else None
+    x["fwd"] = [None if k == RO - 2 and direct(dn) else dn for k in range(RO - 1)]
+    x["lf"] = [0 if d is None else neng(rank, d) for d in x["fwd"]]
+    x["ta"] = [4 * neng(rank + 1, rank)] + [neng(rank + 1, rank)] * (RO - 1)
+    if direct(rank):
+        x["ta"][RO - 1] = neng(rank + RO, rank)
+    x["mn"] = {(t, s): neng(rank + 1 + t, rank) for (t, s) in _LK}
+    return x
+
+
 def rank_program(g, core, T, topo):
     rank = T.rank_of(core)
     if rank is None:
@@ -533,8 +736,8 @@ def rank_program(g, core, T, topo):
     def neng(a, b):
         return len(topo.engines(T.cores[a % N], T.cores[b % N]))
 
-    def direct(r):
-        return topo.chip(T.cores[(r + RO) % N]) == topo.chip(T.cores[r % N])
+    def near(a, b):
+        return topo.chip(T.cores[a % N]) == topo.chip(T.cores[b % N])
     tot = {}
 
     def send(d, out, src, rsem, lsem):
@@ -542,15 +745,7 @@ def rank_program(g, core, T, topo):
         rid, pid, _ = topo.addr(dst)
         g.remote_dma(_ap(T, out), _ap(T, src), T.sem[rsem], T.sem[lsem], pid, rid, topo.mask(core, dst))
         tot[lsem] = tot.get(lsem, 0) + neng(rank, d)
-    dn, far = (rank - 1) % N, (rank - RO) % N
-    x = {"send": send, "user": {t: (rank - 1 - t) % N for t in range(RO)}}
-    x["dn"], x["far"] = dn, far if direct(far) else None
-    x["fwd"] = [None if k == RO - 2 and direct(dn) else dn for k in range(RO - 1)]
-    x["lf"] = [0 if d is None else neng(rank, d) for d in x["fwd"]]
-    x["ta"] = [4 * neng(rank + 1, rank)] + [neng(rank + 1, rank)] * (RO - 1)
-    if direct(rank):
-        x["ta"][RO - 1] = neng(rank + RO, rank)
-    x["mn"] = {(t, s): neng(rank + 1 + t, rank) for (t, s) in _LK}
+    x = links(rank, N, near, neng, send)
     eng = {"v": g.vector, "s": g.scalar, "sd": g.scalar, "t": g.tensor, "g": g, "d": g.sync}
     know, opk = {}, {}
     for i in order:

@@ -1,10 +1,11 @@
 from concourse.mybir import AluOpType as A, AxisListType as AX, ActivationFunctionType as F
 
 RO, M, P, TW = 5, 4, 2048, 4096
+TP = [(0, 256), (256, 1664), (1664, 2880), (2880, TW)]
 W0 = 16
 NX = W0 + 2 * P
-PART = ((0, 64), (64, 128))
 PAR = {
+    "part": ((0, 64), (64, 128)), "wb": ("p3", "p4", "p5", "p2"), "sb": ("p5", "p2", "p3", "p4"),
     "items": [(0, 0, "v", 0, 1, 12.9), (2, 0, "s", 1, 1, 12.8), (1, 0, "v", 0, 1, 15.2), (3, 0, "v", 1, 1, 17.0), (2, 1, "s", 0, 1, 15.9), (0, 1, "v", 1, 1, 18.8), (1, 1, "v", 0, 1, 20.9), (3, 1, "s", 1, 1, 18.8)],
     "s": "f1 d16 vc qs16 pos upv aa1 idr xl nb w15 nif har msg0 msg1 ds k".split(),
     "T": 2959, "T0": -151, "Z": 31.0, "ds": (19.8, 24.5), "vh": 32, "sh": 64, "xh": 32,
@@ -15,25 +16,31 @@ PAR = {
 }
 TAU = "qzxp00cwqt200cetpv00oyhpm000n0u20001ipz01c0oc400ougaa010q84j000hra100w9agw01rafln02fjl9k01yra3c027i4ff02o0s2m03c8qt3057t5gv08sak730as9nf504qit3204y2c4s03k6spq02wp2dp0ajewlg04hu53o048cfe6000zfoq07zz13u0dqrfso05ozzlo0daml460ev0xry06kpkf50cl6v800b13fse0901d1j072roto05wihes0gz254a0ockzry0qt4kpe0sndqdb0g3mw180ctv2q41ju10oc06t4lr20k01yz0107xv160rqenc20mkc33n1uznil507ahf2h06osvc203pxabq0cnkz9n05h5jjh04abkro08h670s09olnqx0c274h3063q0iu0bgkdp50a9ztfb07v6ch30av09ye04wfpok092q5z50d93v740g82h7q0kt43nt0v0x15101jzc750q5548d2c7m0t503t9yqi06cx6zv07bsrxg0e50hr80gb94t50lf49e10kyeaue0mu6f2y0jshdyo0m3ti2y0no6h960olgm2y0sw2zo40ui3q2y0w5aoew1a7a4aa0lurce10otw7t50r2fqkr0sfgb8a0hfjdgj19jsj4g2are9qb0tm1qsc0d2awg90mcflqu0kayq320ig93gv0x8i94s1jda7sm07qege10u1fj3k0l6uztp0v85ajs1k32n3k27okq9y2b0eitz1tt03de1w0k1sd0eet7ga0em2q8t0f8j2560j4uehz0ph3l5w0vhcrts12ypvqi16kczqi1afy1ff1fw783c1kvnv4i1qlblev0t4bvme25e1sn519rfbxz206deio1iv0iio1qukh0r2bsg09b06lhvke09ff46j0c93zfe0f38m660egtjwe0dut5g00f1n2xb0fnynay0beq2d50gt1hjb0fogx9h0gkrdk20hne4lg0io6ua80jcxg3p0ki88z00k8bbzn0koyezn0l3lizn0ljs0m804uf4m80ly28m80me948l0n9yana0qegtkj0ua9cfd0pqh6zd0ra51840tdunhf0p2juw40vp1dud0xhokyq0nxdrdg0rzv9bp0urfdxi0g122ph0n4pt8t0jv8s5r0lf2hxi0qnnlz70rtcx8t0pv3h8h0uqw2k30mtw40s0tj5z6k000gwq10ycv9xs11aazpj11m0vl011s8ami128eevu1adfbc61as3ted16scdgt10xoco71y7i95j1z7zabt15drto112vkfwh14b7jwh195l2t31dpj84s11johuc17jbluc18cnsm019obu5n11xyx5n16qsnfp17z7s7s1bluv7s1bxzl2y1ggzr8517vjlq71b81x6i1b5o07i1eb86t31j6ofao1dy4bjx1gp44i11hhr7i11jjcj0s1lxh4651bey6hx13ilahx1hweood1mr15j212po8j21goujxm1l28xdj1myv0ej1pnltth1sg1uz01jfhp8a1n8ad4t1mjxg4t1sfadjw1w41oq21pqhjzb1spnm3b1r6aq3b1vk8xth1z9d0od1g8youc1fvlsuc1lfak6m1v9l16n1dh856n1naudoo1tkp2uk1x4c6uk1xgg8az220rzqx1ma0sn71mzm2a51ohz8k01r0fw3i1tzw6do1vvbn3u1wdi55m1wpxlvr1x8p3zo1z1hqmi1s8isih1wyk7l01ysta0u1xd71701zi8uca25k8ehx1ouvhhx1rmilhx23uf0f2269bcj21zsyfj2228ljj228kpsrb29q2p0522d20p822pmk7c232t2l623b1ad92673yd2284ie4828sxuud2951b5z29oaww82a5sh3h29wijjv2ezowu72dy40a125uxpdk2ai48re2bf8wuc1yzvzuc27ri3vc2e5r6tp2fev86n231ic6n2dc5g6n2fk722z2h3d2jb20lhrsi29dsjs72b0fns72bsy22q2hll62q2j5hqb11zt02jf2lp81bm2n1x2qj2o0d46u28dyquu2edi4ej2eyumwh2i0nd4p2kphz7s2gdp52w2h64ijp2l2dk542llrjlu2lymuvi2mb817l2mnwkag2nm3vbs2o5b11m2n7rf192nzc92w2ozx2n62q1xkoy2qxfjh72ru1u5s2psa0uo2qoj6il2qgsc6i2rcm9uw2s9ph1w2sykr5s2u93tks2uuv8ql2vmcpkz2wsyx7c2yyw56v30jumwv31ywlzt33025ql2vvpose38ogk6l2rlv0xq2si0yev2uhb0nn2w2sj6n2wnv5sc2xt6h7c2y857vc2mo204i2t3y8t22v9savc2wwl9lc2yubnga2tt70892t6j1f42uqcoxb2qern7l2qsryiy2ra057v2to6nhu2s4ft5r2wa4btx2xvxgtx2sj0uvh2rpihjo2u2ooia2zp0kxl2vef0or2yh76nv2yqxi542x55phx2zbdo7m2sq0o542tlenlu2uhzys82v5nhxq2vnjoag2wqqybs2xey41m2waej192x7yls52y8vvr62z7imxg2zfx2om2zosshx30hlngz31mdh7c34td0tc33fwnri303b4io317mks932198er32u11jf33iskwz34e3csb31c8nj22pfvqj2341iuj2356fn6n314zgaa33mmkaa35m4bgs37ftegl395b0tq3afs5zr36rxw3c37uouri3brpupm389eypf39lwj2l3b3jr6y3a08v6r3bcqgjw3cuoztn2t96c6h2yguh4n30ic5st30xlbgq3043osj32lj1gk33xyh6q30ydywv339zen134652p8376uyzq361h20r37sdomz3aoov163hlimw02okjak22pqhb522pdbd8m2zatr5n2yvjyka30262la32wt5la2ymg9la38jwqd9140j3p7000nnwg16drwj91mi67p70vgarwg1xse0k91yktap70snxuwg20f14k9216gep70snkywg237o7k923z7o8l356og7o3a5suf03c2mck035fqfe33ahd0p93cb9o7c37ofwhx3ait62o3bpxyt63dlg6l637y2rs73bb0pfi3cn6xwe3eg"
 TAU = "qzxp000wqt2000etpv00cyhpm00cn0u201c1ipz0100oc400ougaa00oq84j000hra100w9agw01rafln02wjl9k02ora3c020i4ff03k0s2m0488qt305mt5gv089ak7309h9nf504wit320552c4s05e6spq035p2dp0d3ewlg0dcu53o0facfe6000zfoq072z13u0corfso06czzlo07uml460dt0xry06kpkf508i6v8009z3fse0k51d1j0niroto04hihes0j2254a0s3kzry0cf4kpe098dqdb0ggmw180msv2q41ip10oc0fi4lr20go1yz00brxv160ykenc20pzc33n1ulnil507ihf2h0gosvc20bpxabq0cakz9n0545jjh03xbkro06b670s0b3lnqx0cw74h309wq0iu05qkdp509bztfb08p6ch30ai09ye04jfpok084q5z506x3v740g32h7q0ha43nt06tx151029zc7508r548d2cjm0t503t9yqi063x6zv0c0srxg0dk0hr80fs94t50mc49e10iueaue0nq6f2y0hshdyo0n9ti2y0ol6h960qhgm2y0rm2zo40tf3q2y0ytaoew19ja4aa0f1rce10qpw7t50pbfqkr0w5gb8a01rjdgj1s7sj4g2bee9qb0gy1qsc0biawg90p2flqu01jyq320v093gv08zi94s2bna7sm0qyege10z2fj3k0wduztp1i75ajs1j62n3k2a0kq9y2adeitz1so03de2b6k1sd0jht7ga09q2q8t0k3j2560m4uehz0n03l5w0otcrts0q8pvqi0rvczqi16sy1ff0vn783c1hznv4i1pgblev24obvme29d1sn51v3fbxz2cbdeio0to0iio1tckh0r2bwg09b069hvke092f46j0bw3zfe0eq8m660dptjwe0eat5g00ewn2xb0fhynay0a3q2d50ss1hjb0emgx9h0g0rdk20i1e4lg0hd6ua80jqxg3p0lo88z00wjbbzn0gbyezn0kylizn0mhs0m80fvf4m80kj28m80mw948l0o6yana0r7gtkj0t69cfd0u5h6zd0v851840xhunhf0pjjuw40sc1dud0twokyq0srdrdg0ukv9bp0vwfdxi0gq22ph0hwpt8t0nc8s5r0oi2hxi0o5nlz70uucx8t0rz3h8h0t5w2k30oxw40s0sc5z6k000gwq10xuv9xs11sazpj11g0vl010r8ami12oeevu11lfbc61293ted1yqcdgt16joco71vui95j1zbzabt134rto115mkfwh13h7jwh1a3l2t31d3j84s11pohuc13wbluc17pnsm019ubu5n11yyx5n16wsnfp1857s7s1c3uv7s1cfzl2y1fuzr85183jlq71al1x6i1bno07i1dz86t31ikofao1dc4bjx1g244i11idr7i11ixcj0s1lbh4651bky6hx19blahx1greood1l815j218io8j21hkujxm1mx8xdj1khv0ej1ptltth1uy1uz01ithp8a1muad4t1n8xg4t1rcadjw1x41oq21pchjzb1runm3b1swaq3b1vm8xth1xyd0od1geyouc1ktlsuc1mfak6m1wfl16n1fi856n1lmudoo1u4p2uk1tcc6uk1yhg8az20orzqx1ln0sn71mdm2a51onz8k01r6fw3i1u2w6do1vzbn3u1wci55m1woxlvr1xcp3zo1xphqmi1mmisih1zxk7l024ita0u26671701y68uca24d8ehx1nnvhhx21oilhx22hf0f226lbcj21p0yfj21x6ljj2279psrb28e2p0521120p821dmk7c21vt2l621z1ad924w3yd226uie48277xuud27k1b5z283aww828gsh3h21mijjv24xowu725c40a125rxpdk28s48re2a48wuc23avzuc26gi3vc2c1r6tp2d9v86n243ic6n2ct5g6n2dm722z2eyd2jb201hrsi281sjs729pfns72ahy22q2fnl62q2h0hqb11y402jf2ik81bm2jxx2qj2kvd46u2bayquu2cni4ej2efumwh2f1nd4p2jkhz7s2kjp52w2ly4ijp2ixdk542jgrjlu2jtmuvi2k6817l2kiwkag2lh3vbs2m0b11m2l2rf192luc92w2mux2n62nvxkoy2osfjh72pg1u5s2nna0uo2ojj6il2obsc6i2p7m9uw2pvph1w2qqkr5s2ro3tks2skv8ql2tccpkz2utyx7c2wtw56v2xyumwv2yzwlzt30125ql2u0pose32sgk6l2r7v0xq2qy0yev2rvb0nn2tosj6n2uev5sc2vo6h7c2wk57vc2lc204i2rty8t22szsavc2u5l9lc350bnga2q470892suj1f42s6coxb2o9rn7l2onryiy2ph057v2rg6nhu2qbft5r2s64btx2vwxgtx2r10uvh2ufihjo2pwooia2xb0kxl2w3f0or2v076nv2txxi542wc5phx2wxdo7m2qj0o542rgenlu2rxzys82slnhxq2t9joag2ulqybs2v9y41m2u5ej192v8yls52w9vvr62x2imxg2xax2om2xjsshx2yblngz2zcdh7c33inusz30gwnri2yeb4io2yxmks92zr98er30k11jf318skwz3243csb3918nj22navqj232eiuj232xfn6n2yxzgaa33cmkaa33s4bgs34ztegl35ub0tq37ss5zr34kxw3c369ouri37jpupm35feypf374wj2l38gjr6y3808v6r394qgjw39yoztn2tl6c6h2wwuh4n2ykc5st2xqlbgq2y53osj2zmj1gk31wyh6q31ndywv30zzen133952p832kuyzq31lh20r347domz36oov163f2imw02mfjak22nlhb522n8bd8m2p2tr5n2whjyka2x962la303t5la32xg9la35rwqd913ij3p7000nnwg17qrwj91lw67p70s4arwg1tpe0k91uhtap70s4xuwg1zy14k921dgep70s4kywg242o7k92827o8l35tog7o3atsuf03cpmck0362qfe33b5d0p93cy9o7c38bfwhx3b6t62o3ccxyt63e8g6l638l2rs73bz0pfi3da6xwe3f3"
-PAR.update({"T": 2877, "T0": -78, "rv": 12})
+TAU = ""
+PAR.update({"T": 2700, "T0": -700, "rv": 32, "ng": 12, "ds": (19.9, 24.8), "tq": (32, 32), "Z": 30.8,
+            "s": "f1 d16 vc qs16 pos upv aa1 idr xl nb w15 nif har msg0 msg1 ds k pa r2 rf dk sq u16 sh16 ph xw k1 k2".split(),
+            "items": [(0, 0, "v", 0, 1, 13.0), (2, 0, "s", 1, 1, 13.0), (1, 0, "v", 0, 1, 15.4), (3, 0, "v", 1, 1, 17.2), (2, 1, "s", 0, 1, 14.8), (0, 1, "v", 1, 1, 19.0), (1, 1, "v", 0, 1, 21.2), (3, 1, "s", 1, 1, 18.9)]})
+PAR.update({"tq": (32, 64), "s": "f1 d16 vc qs16 pos upv aa1 idr xl nb w15 nif har msg0 msg1 ds k pa r2 rf dk sq u16 sh16 xw k2".split()})
+ST = "00000000c00c00o01000o01c00000w01s01q01z01i02g02703c06c07106t05103302o07b06403s00004105p08908q0a104t0cy0es0h52040950a01ya0cp0as13j05q07h0di1ks06j1k604404p03j1id1rd1hs1qs1je1go1yj1z621705a07j0bn06l0800df0ch0ed09s08h0al0b90cc0zf1g71hd1gf1hu21f1zf21w21o1zn0g91zw2240d61ib1jl1j01le48n48228n20s26t07s09k0ct0gi0xi13a14314k17g17x1au1dt1yy23j22123723b23s22w06c0960c00eu1k91li1o01rr1p91mr1wq1vh1qi1t01xz1u808p09a0br08407r0990hz0jh0b80c20cx0e40dy0et0m104h0f50fu04w0g90go0gq0j20ls0in0jh0kb0kj0ld0m10jw0ky0m90b80h20h60ip0d80kd0c10fe2680l010d17z0hm14c0mh0mt0re0u80un0xr23s25n24d2810oy0rt0td0uo0y60mm0o20sl0xr0na0rt0w30w711w13u0mi0v20xb0yv14b0yf10v14j14y1780rd0ov0xq0zx0mi0wj11k13e1d41fy14s18e17w1ba1h51dj1b31en1gn1jt13813q1971eg16g18f1g41ct1i81ka17p1861bc18u1f21hm1i31ik1j61k21gw1sd1ry1sr1ol1ob1ki1ml1uk1wh19z1ne1s61tu1kq1l51m51lu1p11r11rh1rw1si1sz1sr1w31tf21m1tf1vu1lb1vc1wa1y51jq1x31yq1zz1qk1sy1zj1zy21g22222m23n25226320d22h1vi24m2582d228w25t24124n25225i25x26y27k26j27e28h29t2aw2bk29l2a829c2ao2bb2ca2d12dq2en2lp2fq2i22j62na2i12px2da2bz2d02dz2ff2hn2kx2682e12fi2gj2pz2c72b32ex2eg2ao2a92bw2e42g32hg2db2bh2ej2ih2he2jd2dr2k12cm2di2e82ev2fb2gd2gz2fy2gt2hw2jm2ka2ki2ld2mf2n22no2iy2jv2kq2m42lr2mp2un1xv2op2p52mr2oa2pk2r82s22u72qe2sh2tj2qt2rn2tb2sw2ts2y42cl2is2kb2lb2le2mu2ip2m62l52lz2ni2pi3oy27z28u28e29o2jt2ko2qc2t62ni1742w02yu2v32vf2v92uf2yc2uu3yz3zk3qr3ye2yr2vo2w431z3az2v82wj31734p2un30f36d2vf38h3dn31733n33i36p3e336338j39z3bf3ei2zz2qu35x3812tc35539p3er3f33i13fl3b73gl3ih3n63kq3ia3n03nm3pk3bd3cx3h03mw3ae3k03l83ks3p43r22ng3ok3q13ex3fd3ik3g33li3ng3nw3od3oz3pt3o43py3pj3qd3uu3vi3s83t03xq4153dp40440w42t3ri3rx3se3sm3vj3xi3xx3yd3yz3ze3s63v33xz3s63zu42a3ul41p42q44h3tt43i45546e3qm3yi44a45y47g48i3rc4bl4cz4e045444p40k47v4a04am4d544p4ag4b24bh4bx4cc4dd4dz4cy4dt4ew4g04hb4hz4fs4h34gf4ie4jh4k54l04m64n14s34m34o64t34ub4ms4wp4hq4gu4kg4lg4m44nr4ri4cj4if4jh4ki4w04jy4h34ib4kl4hi4gg4kr4j24lr4p14o84hx4q04q54qd4ph4p04r24im4j84jp4kd4lo4mq4nc4mc4nl4oo4qm4qu4r34s74t94tv4uq4ol4pq4ql4si4rz4tq51p4dx4v64vl4st4tj4ur4y04yu50z4x64z950c4xl4yf5034zo50k51n4ld4pm4ra4rp4ss4t04p94sj4rq4px4ty4wb5w14ee4f94et4n64om4ph4sb4v531m4xz52552h52a51857l51v68o6eu67d6ff55552p5355905hr52a53k5885bq51f57g5de5275fi5kg5805ag5aj5dr5kv5cv5fb5h15i75lb5704xm5cy5f25045c65gq5lk5lv5ou5me5i05ne5pa5ty5ri5p25rw5ue5wh5ie5jq5nt5tr5ki5qs5s35rl5vx5xv2t44055uq4s95vn5wp5lq5m65pm5n45sj5uh5v75vm5w85x65u75x15wm5xg61l61w5z15zt64h65p61d67n68g69o5yb5yq5z55ze62c64a64q65565r66764164q6545yz66m69260l6986a06bc6596as6by6d65xf6626cq6d56eo6fa5xu6je6l96ma6bx6bi6836gt6he6i06m46iz6h96hv6ia6iq6j56k66ks6jr6km6lp6mt6ng6or6mk6o36n86p66pu6qu6rt6t96u46yz6sw6uf6vp70y6u373i6oj6nv6r56s86sx6tl6xn6kd6p76q96ra73a6qq6nw6op6re6ob6n96rv6rg6sv6v46to6pa6xl6ws6vw6x16vo6xp6pf6q26qi6r56sh6u06uu6t46uh6vp6xf6yb6xw6yz70170n71d6v96w56x06zs6yj70d78c6ky72g72v70d70t72174t76177r73z75m77474e75776v76g77c78f6sg6wk6y36yi6yy6zf6wk6zo6z76zl7187338256l76m26lm6pp6ze70873250r75w78s7947927807ed78n8lp8n98gv8mo7bx79h7a57fo7oj78x79d7ew7ie7877e37k178z7m57r87es7h87h67ke7rn7jo7m37no7oz7s37dn74f7jm7lp76w7iu7nd7sc7sn7vm7t67os7u67w280q7ya7vu7yp8168367p17qi7ul80h7o37xk7yt7yd82p84n2vy5yf81t4v382q83k73084h85s7si7sy7w97tr7z681581k82a82x84182p83s83d84w88p89485t87d8bl8ct7ra8ao8dz8f785385k8698688958b58bk8c08cm8d185b8bl88p85r8dh8fx8868er8gd8hl86l8fj8is8k18478cd8h58jl8l38m58j98p88qm8rn8j88ic8eh8li8nn8o98qs8hk8o38op8p58pk8pz8r08rm8ql8rg8sj8tn8ub8vm8u28uy8tf8w18x48xs8yn8zc90u95r90590s92l97q9269an8vd8up8y38zx90l91a9558q68w28x48y596q8xl8u38vb8y88uw8vw8ye8wp91091l8yt8wa93t93v92i93892r94k8w98wv8xc8y08yw90e91p8zi90d92k94994i94q95p96r97d98592493g94b96595m9759f48hz97698e96b98t9989bj9cd9eh9a89cr9dl9b49by9e99d69du9np8zq93f94y95c96196i92z96a95e93o97m99ta988s18sw8sg8ui96q97l78o9g89fw9fk9fk9eq9ku9f59fz9if9gx9la9v99fp9g59mt9p59ep9nl9qt9fl9sx9xy9l99ny9od9r69yd9qe9su9ug9vp9yt9kf9bk9qd9sh9dm9pl9u59z29zea2c9zw9via1ra2sa7pa50a2la53a7wa9v9vt9x8a4ba769uva0za5ia5ia9fabd2qa8c08ir4xx8ma8n475u8o18sp9ada8uaac9z89zoa31a0ja5ya7xa8da8sa9eaa3a7gaa8a9taamaf4afeacjae3ahzale9y0akdal6an2abtac8acoacxafuahtai8ainaj9ajpahjai8aimachak4amkaewalyan0aoqadbantapgaqoaaxaisaolaq8arrassab1abtapfasxascad6acuatyatdap0aktas6aubauwavvap0auravdavsaw8awnaxoayaax9ay4az7b0bb0yb1mb02b1db0qb21b34b3sb4nb5bb66b9mb3lb1eb20b48b2lb0rb43b2zb4wb6zb5qb4ib7kb76b6xb7nb7eb8bb29b2vb3cb3zb4vb5wb6ib5hb6cb7fb8ab8jb8rb9mbaobbabe6bbjbgibdqbgmbe0bgu"
+ST = "00000000c00c00o01000o01c00000w01s01i01q02e02602n03j06c07106k03a09q02v0b50bd06200004808007s08f0bm0af0aw0dr0gt21d05008y1yr0fx03z1gj04f07905n1j806a1kx03q05207w09j1rh1in1sg0ia1jf1z021u23o05n07j08u05f06t0cx0990fi07b09i08h0a60av0hm1gs1hu1i21ij21m23w2151zu2020gk22322j0a71jo1i21kc1lw4a649k2941zf22p0ao09z0c20f90ip0k714014h14x14p18319423f23723a26722b24520b06c0fo0ji0oc0r60sf0to0ux0w60xf0yo0zw11512e13n14w0cz0bt0dk0ce08w0ak0jc0ku0ci0dc0e70gg0g50h10n406r0hh0i20760ii0ix0iy0js0l90jd0kf0lx0li0m50ne0ku0q20y10cu0es0fy0lg0ee0js0dm0i425m0nx0qn0x50r41je0nk0nw0mk0mz0ya13l25123v26s2230qh0nm0pg0td0vd0np0pv0vo0ze0s50uw0xr0sy11i1480sx0vm0z60zl1560yp11514x15c17u0sf0n50xl1120md0ye17h11419k1gb15e18z16u1bv1hd1dv1bf1b31gz1j712q13117x1ge13t18p1eq1de1ii1kk18b18r19r1c91f61h41hl1is1jw1kc1ib1ju1lk1vk1p41ol1k01n61tg1vz1dp1nz1so1tw1l01lf1mo1m41pk1rk1rz1sf1t11tg1lo1r21s21zo1tw1wb1kt1u81wr1y01or1v11z720g1ll1r220020f21x22j24g25o28i29j22s20q1t424224o2c826n25924i25425j25z26e27f28127027v28y2a22ay2bs29t2ah2ap2c72cu2do2ef2fp2go2n42ho2i32ju2m42go2n62di2eo2ee2fr2gf2ii2l627f2fc2hq2ir2q72bd2c42ep2cf2aw2ai2cv2da2dz2g32fa2bb2ib2je2j52hf2ix2k22d32dq2e62ew2fc2ge2h02fz2h32i62k12kx2ln2mi2nn2o92oi2jm2ka2lj2mj2mr2nx2vh1w02nz2oy2of2pd2ps2qp2ry2ss2rj2sd2tf2u32ux2vz2to2ui2vr2jf2j12kq2l42m22mj2kp2ma2le2ld2n72r43pm28p29k28g2bq2ni2r72u12wv2od1m63bs3em2vx2w92t033y3132vc3s043r48z3rf2yn2w72wi3213992w22wx31935j2xq33j37734t39b3bx31i36t34b3b83em39h34d3at3cr3f130t2qm36r3f92t835z3dl3fu3hd3ng3g43c63g53j03nw3ik3l03kv3o53q338v37n3e93lv3f13gl3nj3kj3pn3rm2tz3p73qc3fg3fw3gx3je3mb3oa3op3p63ps3qt3oy3q73ql3r03vc3vn3la3tk3zz4233r63uc3z740f3s13sh3sw3t53w33y13yh3yw3zi3zx3xs3yv3yg3sq40d42t3v441k43944h40r42c45p46x3ry3xl44146h47z4914654c44dj4ek45o4593zn48f4aj4b54do44g4az4bl4c14cg4cw4dx4ej4di4ed4fg4gj4h74hu4gb4hm4gy4ii4j54ka4l44mt4nn4tv4m84mw4og4pa4ne4sh4i94je4jz4ll4m94ok4qp4d34k24le4mi4xa4jm4hn4ig4kp4gz4jl4j64kl4me4po4qo4l04r34p84rc4oz4oc4s14iq4k14kh4lc4lt4nb4nx4mh4nt4ow4r44rl4rt4t64u84uu4v64pg4q24sp4ta4tq4ul52544v4uw4vm4w14wg4wv4xa4y44yy4yj4z650050n51h52b50951252k4lz4q94rw4sa4sy4tf4qh4t64s84r54u34xp5wa4f64g14ey4i14rh4sc4v64y03he57052l52x4zl5aj55851w5yn6ct6f95y255n52s53658o5fu52q53l57w5c652c5a75du5be5fy5ii5835de5bq5hw5l65g25ay5hh5je5lm57g4xp5df5lw5015cm5k95mh5o05u15mp5iq5mt5pl5ui5rl5p55r45up5wo5fi5ea5kx5sj5lp5n85u75rj5wb5y92wt48l5uq4v45vv5ww5m15mh5nk5q25sz5v75vn5w25xd5xt5u95wv5x95xo62062a5xt60764w6645rv61068269a5yp5z45zk5zt62q64p65465k66666l64g65j6545zd67169h61s67a69x6b568u6ap6cc6dl5ym65o6bh6d56en6fp68d6is6k66l76cb6bw67s6f26h76ht6jq6bw6hn6i96io6j46jj6kk6l66k56l06m36n76nu6oi6mz6o96nm6ox6pk6qi6r96tb6u66za6qx6t16uy6x26tx6yh6q16pt6qt6sd6t26uv6xl6kj6qq6rx6ta73s6qa6oa6p46rq6nn6pp6q36r46si6vl6sw6ri6xh6wl6xc6vy6va6y16p56qp6rh6s56sm6tv6ug6tg6ub6ve6x46xt6y26z670970x71a6vj6w66yp6zo6zu70p7896l470p71q71472572k73c74n75h73r75276476r77l78o76d77678f6wo6w96xw6ya6zd6zm6wu6z570o6zs72z74882e6lu6mp6ll7op70971473y59s76s78p79175p7gn7ds78084q8j28lu8br7bc78w7a37et7ji78u79a7e17ib78g7gq7jz7hj7m37om7e77jq7gb7o07ra7m67h27nl7pj7rq7dl7477jj7s175x7ir7qd7sm7u58057st7ou7sx7vp80k7xp7v97x880t82s7ln7kf7r17yn7rt7xz80b7xn82f84e2zn6fu80t4xy81z83073w83x85j7s57sl7tp7w67z381a81p82683h83x81y83d82z84c88g88v8748af8bb8ck83y86c8ei8fq84t85a86085z88w8av8bb8bq8cc8cs8528bc88g85i8d78fn87w8fa8g38he8c48gv8ij8jr84q8cw8ho8jb8ku8lv8e88oy8qd8re8ii8i38ey8l98ne8nz8px8i38nu8og8ov8pb8pq8qr8rd8qc8r78sa8te8u18up8t58ug8tt8vc8vz8x58xy8z890396c8z38zi91f93j8zu94y8v48w88wu8yf8z491d93b8qp8ww8y98zc9698wg8uh8va8xj8tu8wf8w18xg8yu9229098xu93y92o93t92f91s94i8vl8wv8xb8y78yo90c90y8zx90s91v93l94a94j95n96q97e97r92192w95695r96b9769eq8rb96s98r94099699m99t9b29bw9an9bh9ck9d79e19f39cs9dm9ev93592q94d94r95u96394295m97597797z9a8a938s08sv8rs8uw96q97l79k9fu9f69fi9c59n29k89eg9hs9fc9fr9m29sd9fb9g69ki9os9ew9la9qg9o09sk9v29kn9px9nk9uh9xq9sm9nh9u29w09y59k29a19q09yi9cc9p89s49yea0ma6k9z99va9zqa25a70a45a1pa3na79a979ts9qw9yya549xia4ea6sa42a8waav2r58lfa7r50sa8oa9j76qaagabj9adacgaf49yl9z0a06a2na5ka7ja88a8oaa0aafa78aava9oab9afsag1ab7adlainam3aafahaaluanqabaac0acfacuafsai7ainaj2ajoak4aevaiiafkabzakjamzaedammanfapeal1ao7apvar3abzajgap0aqnas6at7aixajpapuasratcakqal2atsaudapfalhaslauqavbawaapfav6avsaw7awnax2ay3aypaxoayjazmb0qb1db21b0hb1sb15b2gb33b3rb4yb63b6xbadb3gb1tb2fb4jb16b43b53b4ob5ob7qb6hb30b8bb7wb8db84b7nb91b2ob3vb4ab56b5mb6nb78b68b73b86b91b99b9ibadbbebc0bewbc9bh8begbhcberbhk"
 MAGIC = 1.5 * 2.0 ** 34
 
 SCRATCH = {}
 _PS = ["p%d" % i for i in range(8)]
 _B2 = ("bfloat16", "float16", "uint16")
-_CS = {n: i for i, n in enumerate("kg15 kg kr k odd r15 fm flw wf mk0 mid padt padx hc0 hc1 wa wb cw wq0 wq1 wq2 wq3 wq ucol c128 n128 c128r n128r c35 t0 t1 t2 t3 t4 t5 t6 mhalf "
-                                  "r1 r2 kmax kmax2 har e1 idr nif xC a b ba inv dir aI bI nbI an1 xd wdef m1 i2 sg2 m3 u1 nz k0 k1 mba plb pb pb2 ws h0 h1 ds cs ninv2".split())}
+_CS = {n: i for i, n in enumerate("kg15 kg kr k odd r15 fm flw wf mk0 mid padt padx hc0 hc1 wa wb cw wq0 wq1 wq2 wq3 wq ucol c128 n128 c128r n128r c35 t0 t1 t2 t3 t4 t5 t6 c56 "
+                                  "r1 r2 kmax kmax2 har e1 idr nif xC a b ba inv aI bI k0 ds an1 xd wdef u1 m3 nz mba pb ws h0 h1 cs nb1".split())}
 _CI = {n: i for i, n in enumerate("ik ikg ikr iodd ni ib16".split())}
-_MB = {n: i for i, n in enumerate("ib nib d2kb dvoid d4k i2f lx0 d23 dw15 one sgn inv vc oh oh2 oha v r2 lxa hb dvc ndw15 wb1 fb1".split())}
+_MB = {n: i for i, n in enumerate("ib nib d2kb dvoid d4k i2f lx0 d23 dw15 one sgn inv vc oh oh2 oha v r2 lxa hb dvc ndw15 wb1 fb1 zero".split())}
 _MH = {n: i for i, n in enumerate("i16 ni16 m2i d2k16 dn8k nh16 lj lf l2 dhf d2hf p2i dnhf p11 m11 p12 m12 pw16 pos16 f1 d16 qs16 cmn sh16 u16 pa pc la lb "
                                   "g0 g0b g3 gr g4 g5 g6 h0 h1 hr h4 h5 f0 f1m gf".split())}
-_MF = {n: i for i, n in enumerate("ob m1 m2 gu b0 b1 pr0 pr1 hpr hp2 cl inn k2v rt n32 rf ta jk".split())}
+_MF = {n: i for i, n in enumerate("ob m1 m2 m4 m5 gu b0 b1 pr0 pr1 hpr hp2 cl inn k2v rt n32 rf ta jk".split())}
 _MI = {n: i for i, n in enumerate("ic jb ui u sq sh bk q di uq uq2 uu h".split())}
 for _a in _PS:
     SCRATCH[_a] = ("psum", [128, 512], "float32")
 for _d, _l in (("bfloat16", (("xin", P), ("tmo", TW), ("xb", P + 16), ("yo", P), ("mb", 144), ("bu0", 144), ("ncb", 32), ("bf", 144), ("bs", 144), ("bds", 144), ("be", 144),
                              ("cb", 128 * len(_MB)), ("eq", 512), ("ab", 4 * P), ("ga", P), ("ab2", P)) + tuple(("tb%d" % k, TW + 16) for k in range(RO))),
-               ("float16", (("bdv", 144), ("bq", 144), ("bsq", 144), ("ch", 128 * len(_MH)), ("one16", 512), ("cmq", 256), ("q16", 512), ("mx", 4 * P), ("dk", 512), ("gq", P))),
+               ("float16", (("bdv", 144), ("bq", 144), ("bsq", 144), ("ch", 128 * len(_MH)), ("one16", 512), ("cmq", 384), ("q16", 512), ("mx", 4 * P), ("dk", 512), ("gq", P))),
                ("float32", (("w0", NX), ("w1", NX), ("cs", 96), ("kmf", RO * M), ("cf", 128 * len(_MF)), ("mk32", 32), ("aa", 4), ("dg", 32), ("tr", 40), ("nc", 16), ("upv", 16),
                             ("nb", 16), ("onef", 16), ("onefm", 16), ("rr", 512))),
                ("int32", (("wti", 1), ("kmi", RO * M), ("ci", 8), ("ij", 144), ("it", 128 * len(_MI)))),
@@ -42,7 +49,7 @@ for _d, _l in (("bfloat16", (("xin", P), ("tmo", TW), ("xb", P + 16), ("yo", P),
         SCRATCH[_a] = ("sbuf", [128, _c], _d)
 _LK = [(t, s) for t in range(1, RO) for s in range(t)]
 SEMAPHORES = (["sv", "ss", "st", "sg", "lmsg", "lown", "lx0", "lx1", "lw", "lk", "lt0", "lt1", "lt2", "lt3"] + ["st%d" % k for k in range(4)]
-              + ["f%s%d" % (c, k) for k in range(RO) for c in "abc"]
+              + ["f%s%d" % (c, k) for k in range(RO) for c in "abc"] + ["fb5", "fc5", "fc6", "fc7"]
               + ["ta%d" % k for k in range(RO)] + ["ls%d" % k for k in range(4)] + ["m%d_%d" % ts for ts in _LK])
 
 
@@ -74,7 +81,7 @@ B, H, S, I = _tile("cb", _MB), _tile("ch", _MH), _tile("cf", _MF), _tile("it", _
 def build():
     ops, BST, AFT, bank = [], [0.0], [], {}
     CYC, TCY, GC = PAR["CYC"], PAR["TCY"], PAR["GC"]
-    SEC, seen_tag = [-1], {}
+    SEC, seen_tag, PART, lds = [-1], {}, PAR["part"], {}
 
     def add(q, cost, emit, reads, writes, done=None, after=(), lat=0.0):
         ops.append({"q": q, "cost": cost, "emit": emit, "reads": reads, "writes": writes, "done": done, "after": list(after) + AFT, "tau0": int(100 * BST[0]), "lat": lat})
@@ -126,8 +133,8 @@ def build():
     def sa(out, a, func, bias=0.0, scale=1.0):
         return add("s", (60 + max(64, _n(out))) * CYC, lambda g, T, x: g.scalar.activation(_ap(T, out), _ap(T, a), func, bias=val(T, bias), scale=val(T, scale)), [a] + isc(bias, scale), [out])
 
-    def lin(out, a, scale, bias, func=F.Identity):
-        sa(C(out), C(a), func, bias=C(bias) if isinstance(bias, str) else bias, scale=C(scale) if isinstance(scale, str) else scale)
+    def lin(out, a, scale, bias, func=F.Identity, n=1):
+        sa(("cs", _CS[out], _CS[out] + n), ("cs", _CS[a], _CS[a] + n), func, bias=C(bias) if isinstance(bias, str) else bias, scale=C(scale) if isinstance(scale, str) else scale)
 
     def cv(key, out, a, scale=1.0, bias=0.0):
         if key in PAR["s"]:
@@ -169,20 +176,20 @@ def build():
     def wrapped(b, src, c0, n):
         return [((b, 15 - i, 143 - i), (src, c0 + i, c0 + n, 16)) for i in range(16)]
 
-    def ld(sem, q, out, src, c0, c1):
-        add(q, 0.1, lambda g, T, x: (g.sync if q == "d" else g.scalar).dma_start(_ap(T, out), T[src][:, c0:c1]), [], [out], done=lambda x: (sem, 16), lat=2.0)
+    def ld(sem, q, out, src, c0, c1, lat=2.0):
+        lds[q] = add(q, 0.1, lambda g, T, x: (g.sync if q == "d" else g.scalar).dma_start(_ap(T, out), T[src][:, c0:c1]), [], [out], done=lambda x: (sem, 16), lat=lat,
+                     after=[lds[q]] if q in lds else [])
 
     def full(n, c=128):
         return (n, 0, c)
 
-    TP = [(0, 256), (256, 1536), (1536, 2816), (2816, TW)]
     ld("lt0", "sd", ("tmo",) + TP[0], "tm", *TP[0])
     ld("lw", "d", ("wti", 0, 1), "wt", 0, 1)
-    ld("lx0", "d", ("xin", 0, 1024), "x", 0, 1024)
-    ld("lx1", "sd", ("xin", 1024, P), "x", 1024, P)
-    ld("lk", "d", ("kmi", 0, RO * M), "km", 0, RO * M)
+    ld("lx0", "d", ("xin", 0, 1024), "x", 0, 1024, 2.8)
+    ld("lx1", "sd", ("xin", 1024, P), "x", 1024, P, 3.4)
+    ld("lk", "d", ("kmi", 0, RO * M), "km", 0, RO * M, 3.4)
     for k in range(1, 4):
-        ld("lt%d" % k, "d" if k % 2 else "sd", ("tmo",) + TP[k], "tm", *TP[k])
+        ld("lt%d" % k, "d" if k % 2 else "sd", ("tmo",) + TP[k], "tm", *TP[k], 3.5 + 1.5 * k)
 
     def iota(out, pat, base, cmul):
         add("g", 0.3, lambda g, T, x: g.iota(_ap(T, out), pat, base, cmul), [], [out])
@@ -219,20 +226,21 @@ def build():
         vs(("xb", c, c + 1024), ("xin", c, c + 1024), C("fm"), A.mult, C("c128r"), A.add)
     vset(("xb", P, P + 16), 0.0)
     vs(H("pw16"), I("ic"), C("kr"), A.add)
-    vs(PH, H("pw16"), -1023.5, A.add)
+    cv("k2", PH, H("pw16"), bias=-1023.5)
     vcopy(H("pos16"), H("pw16"))
-    vs(C("flw"), C("fm"), 2.0, A.mult, -1.0, A.add)
-    vs(C("t1"), C("fm"), 24576.0, A.mult, -8192.0, A.add)
-    vs(C("t2"), C("fm"), 8192.0, A.mult)
-    vs(C("t3"), C("fm"), -2048.0, A.mult)
-    vs(C("t4"), C("flw"), 16.0, A.mult)
-    for nm, cn in (("bf", "fm"), ("bs", "r15"), ("bdv", "t1"), ("bds", "t2"), ("be", "t3"), ("bsq", "t4")):
-        vs(full(nm, 144), mb, C(cn), A.mult)
-    for nm, v in (("nib", -1.0), ("dvoid", 15728640.0), ("d4k", 4096.0), ("d23", 2.0 ** 23 + (2228224.0 if "vc" in PAR["s"] else 0.0)), ("dvc", 2228224.0), ("hb", -0.5)):
-        cv("k", B(nm), B("ib"), v)
-    for nm, v in (("dn8k", -8192.0), ("ni16", -1.0), ("m2i", -2.0), ("d2k16", 2048.0), ("nh16", -0.5), ("dhf", 1023.5), ("d2hf", 2047.0), ("p2i", 2.0), ("p11", 2.0 ** -11), ("m11", -2.0 ** -11), ("p12", 2.0 ** -12), ("m12", -2.0 ** -12)):
-        cv("k", H(nm), B("ib"), v)
-    cv("k", S("n32"), B("ib"), -1.0)
+    cv("k1", C("flw"), C("fm"), 2.0, -1.0)
+    cv("k1", C("t1"), C("fm"), 24576.0, -8192.0)
+    cv("k1", C("t4"), C("fm"), 32.0, -16.0)
+    for nm, cn in (("bf", "fm"), ("bs", "r15"), ("bdv", "t1"), ("bsq", "t4")):
+        cv("k2", full(nm, 144), mb, C(cn))
+    cv("k2", full("bds", 144), full("bf", 144), 8192.0)
+    cv("k2", full("be", 144), full("bf", 144), -2048.0)
+    diags = [(B("nib"), -1.0), (B("dvoid"), 15728640.0), (H("dn8k"), -8192.0), (B("hb"), -0.5), (B("d23"), 2.0 ** 23 + (2228224.0 if "vc" in PAR["s"] else 0.0)), (B("dvc"), 2228224.0),
+             (H("d2k16"), 2048.0), (H("ni16"), -1.0), (H("dhf"), 1023.5), (B("d4k"), 4096.0), (H("p2i"), 2.0), (H("d2hf"), 2047.0), (S("n32"), -1.0), (H("m2i"), -2.0), (H("nh16"), -0.5),
+             (H("p11"), 2.0 ** -11), (H("m11"), -2.0 ** -11), (H("p12"), 2.0 ** -12), (H("m12"), -2.0 ** -12)]
+    for o, v in diags[:len(diags) - PAR["ng"]]:
+        cv("k", o, B("ib"), v)
+    vset(B("zero"), 0.0)
     vs(B("i2f"), B("ib"), C("fm"), A.mult, 2.0, A.mult)
     vset(B("one"), 1.0)
     vset(full("onef", 16), 1.0)
@@ -245,32 +253,32 @@ def build():
     vs(I("jb"), ij, 126, A.bitwise_and)
     vt(C("t5"), C("k"), C("odd"), A.subtract)
     vs(H("l2"), I("jb"), C("t5"), A.is_equal)
+    cv("k1", C("t2"), C("odd"), -1023.5, 1023.5)
+    cv("k1", C("t3"), C("odd"), 2048.0)
     for m in range(M):
-        vs(C("t6"), C("odd"), 2048.0 * m - 1023.5, A.mult, 1023.5, A.add)
-        vs(("cmq", 64 * m, 64 * m + 64), ("one16", 0, 64), C("t6"), A.mult)
+        cv("k2", ("cmq", 96 * m, 96 * m + 96), ("cmq", 96 * m - 96, 96 * m) if m else ("one16", 0, 96), 1.0 if m else C("t2"), C("t3") if m else 0.0)
     vs(C("ib16"), C("ik"), 16, A.bitwise_and)
     vcopy(C("t5"), C("ib16"))
     vs(I("jb", 0, 32), ("ij", 0, 32), 16, A.bitwise_and)
     vs(full("mk32", 32), I("jb", 0, 32), C("t5"), A.is_equal)
     vset(("tr", 32, 40), 0.5)
-    vs(C("padt"), C("kr"), float(TW), A.add)
-    vs(C("padx"), C("kr"), float(P), A.add)
-    vs(IDX, I("ic"), -float(P), A.add)
+    cv("k1", C("padt"), C("kr"), bias=float(TW))
+    cv("k1", C("padx"), C("kr"), bias=float(P))
     vset(C("hc0"), 1.0 / 32)
     vset(C("hc1"), -1.0 / 32)
-    vset(C("mhalf"), -0.5)
-    vs(C("n128"), C("c128"), -1.0, A.mult)
-    vs(C("n128r"), C("c128r"), -1.0, A.mult)
-    vs(C("c35"), C("mk0"), 3.5, A.mult)
+    cv("k1", C("n128"), C("c128"), -1.0)
+    cv("k1", C("n128r"), C("c128r"), -1.0)
+    cv("k1", C("c35"), C("mk0"), 3.5)
     vt(C("mid"), C("fm"), C("mk0"), A.subtract)
     vt(C("t5"), C("mid"), C("r15"), A.subtract)
-    vs(H("la"), B("nib"), C("mid"), A.mult)
-    vs(H("lb"), c0m, C("t5"), A.mult)
+    cv("k2", H("la"), B("nib"), C("mid"))
+    cv("k2", H("lb"), c0m, C("t5"))
     vt(H("lj"), H("la"), H("lb"), A.add)
-    vs(H("la"), c15, C("t4"), A.mult)
-    vt(H("lf"), H("la"), H("lj"), A.subtract)
+    cv("k2", S("m5"), ("bsq", 0, 128), 2.0)
+    cv("k2", S("m4"), B("ib"), C("fm"))
+    cv("k1", C("c56"), C("r15"), 56.0, C("n128r"))
     vs(S("m2"), c0m, C("flw"), A.mult, 2.0, A.mult)
-    vs(H("pc"), H("pw16"), -1.0, A.mult, 2047.0, A.add)
+    cv("k2", H("pc"), H("pw16"), -1.0, 2047.0)
     vs(("aa", 0, 1), C("wf"), C("mk0"), A.mult)
     vs(("aa", 1, 2), C("wf"), C("r15"), A.mult)
     mm(("p6", 0, 2), [(S("ob"), ("aa", 0, 2))])
@@ -282,11 +290,11 @@ def build():
     vs(C("wq2"), C("wq2"), C("mid"), A.mult, C("wq1"), A.add)
     vs(C("wq3"), C("wq1"), -2048.0, A.is_lt, 4096.0, A.mult)
     vt(C("wq"), C("wq2"), C("wq3"), A.add)
-    vs(full("bq", 144), mb, C("wq"), A.mult)
+    cv("k2", full("bq", 144), mb, C("wq"))
     vs(B("dw15"), B("ib"), C("wb"), A.mult, 0.5, A.mult)
     vs(B("ndw15"), B("ib"), C("wb"), A.mult, -0.5, A.mult)
-    vs(B("fb1"), S("ob"), C("fm"), A.mult)
-    vs(B("wb1"), B("fb1"), C("wf"), A.mult)
+    cv("k2", B("fb1"), S("ob"), C("fm"))
+    cv("k2", B("wb1"), B("fb1"), C("wf"))
     vset(("w0", 0, W0), 0.0)
     vset(("w1", 0, W0), 0.0)
     vset(full("msg"), 0)
@@ -294,11 +302,13 @@ def build():
     last = 0
     for k in range(4):
         r = TP[k]
-        last = add("g", 1.0, lambda g, T, x, r=r: x["send"](x["dn"], ("tb0",) + r, ("tmo",) + r, "ta0", "lown"), [("tmo",) + r], [], done=lambda x: ("lown", 0), after=[last] if k else [])
-    step = [last]
+        last = add("g", 1.0, lambda g, T, x, r=r, k=k: x["send"](x["dn"], ("tb0",) + r, ("tmo",) + r, "ta0", "lown", k == 1), [("tmo",) + r], [], done=lambda x: ("lown", 0), after=[last] if k else [])
+    step, gc = [last], last
+    for o, v in diags[len(diags) - PAR["ng"]:]:
+        gc = add("g", 0.17 + 256 * CYC, lambda g, T, x, o=o, v=v: g.affine_select(_ap(T, o), _ap(T, B("zero")), [[-1, 128]], A.not_equal, v, 0, 1), [B("zero")], [o], after=[gc])
 
     def table(k, after):
-        add("x", 12.0 if k else 8.0, None, [], [("tb%d" % k, 0, TW)], done=(lambda x, k=k: ("ta%d" % k, x["ta"][k])), after=step)
+        add("x", 22.0 if k else 10.0, None, [], [("tb%d" % k, 0, TW)], done=(lambda x, k=k: ("ta%d" % k, x["ta"][k])), after=step)
 
         def far(g, T, x):
             if x["far"] is not None:
@@ -317,12 +327,12 @@ def build():
     for m, h, q, zb, fold, due in sorted(PAR["items"], key=lambda z: z[5]):
         if m not in mord:
             mord.append(m)
-    QB, WB = ("p2", "p4"), (("p3", "p4"), ("p5", "p2"))
+    QB = ("p2", "p4")
     UP, FP, NF, NC = ("p3", 0, 128), ("p3", 128, 256), ("p7", 0, 128), ("p6", 132, 133)
 
     def diag(t):
         for m in mord:
-            sa(("dk", m * 128, m * 128 + 128), B("ib"), F.Identity, scale=("kmf", t * M + m, t * M + m + 1))
+            cv("dk", ("dk", m * 128, m * 128 + 128), B("ib"), ("kmf", t * M + m, t * M + m + 1))
 
     def lists(t):
         BST[0] = Z + 4.0 if t else 3.0
@@ -357,17 +367,26 @@ def build():
 
     BST[0] = 2.0
     diag(0)
-    mm(UP, wrapped("bu0", "xin", 0, P))
-    mm(FP, wrapped("bf", "xb", 0, P))
+    for c in (0, 64):
+        mm(("p3", c, c + 64), wrapped("bu0", "xin", 16 * c, 1024))
+    BST[0] = 6.0
+    for c in (0, 64):
+        mm(("p3", 128 + c, 192 + c), wrapped("bf", "xb", 16 * c, 1024))
     lists(0)
     BST[0] = 3.0
     for k in range(4):
-        w = (("p5", "p6")[k % 2], 0, 512)
+        w = (("p5", "p6", "p0", "p1")[k], 0, 512)
         o = ("w0", W0 + 512 * k, W0 + 512 * k + 512)
         mm(w, [(B("lx0"), ("xin", 512 * k, 512 * k + 512))])
         sa(o, w, F.Identity, bias=C("c128"))
-    mm(("p7", 0, 128), wrapped("bs", "xin", 0, P))
+    cv("k2", IDX, I("ic"), bias=-float(P))
+    BST[0] = 9.0
+    for c in (0, 64):
+        mm(("p7", c, c + 64), wrapped("bs", "xin", 16 * c, 1024))
     sa(B("sgn"), ("p7", 0, 128), F.Identity, scale=2.0)
+
+    def rows(w, r, c, src, sem):
+        add("d", 0.1, lambda g, T, x: g.sync.dma_start(T[w][r:128:16, c:c + P], _ap(T, S(src))), [S(src)], [(w, c, c + P)], done=lambda x: (sem, 16), lat=2.0)
 
     msgops = {}
     for t in range(RO):
@@ -375,10 +394,11 @@ def build():
         w, wn = "w%d" % (t % 2), "w%d" % (1 - t % 2)
         X, XA, XF = (w, W0, W0 + P), (w, 0, NX), (w, W0 + P, NX)
         BST[0] = 13.0
-        table(t, [msgops[(s, t - 1)] for s in range(t, RO)] if t else [])
+        table(t, [msgops[(s, t - 1)] for s in range(t, RO)] if t else [gc])
         BST[0] = 13.5
         add("d", 0.1, lambda g, T, x, w=w: g.sync.dma_start(_ap(T, S("rt")), T[w][0:128:16, W0:W0 + P]), [X], [S("rt")], done=(lambda x, t=t: ("fa%d" % t, 16)), lat=2.0)
-        add("d", 0.1, lambda g, T, x, X=X, XF=XF: g.sync.dma_start(_ap(T, XF), _ap(T, X)), [X], [XF], done=(lambda x, t=t: ("fb%d" % t, 16)), lat=5.0)
+        for k, o in enumerate([XF] if t < RO - 1 else [(wn, W0, W0 + P), (wn, W0 + P, NX)]):
+            add("d", 0.1, lambda g, T, x, X=X, o=o: g.sync.dma_start(_ap(T, o), _ap(T, X)), [X], [o], done=(lambda x, s="fb%d" % (t + k): (s, 16)), lat=5.0)
         BST[0] = 14.6
         for m in mord:
             c = (m * 128, m * 128 + 128)
@@ -386,41 +406,43 @@ def build():
         if t < RO - 1:
             BST[0] = Z - 0.5
             diag(t + 1)
-        seen, ns, wait, slot = {0: 0, 1: 0}, 0, {0: [], 1: []}, {0: 0, 1: 0}
+        seen, ns, wait, slot = [0] * len(PART), 0, [[] for _ in PART], {0: 0, 1: 0}
         for m, h, q, zb, fold, due in PAR["items"]:
             h0, h1 = PART[h]
             n = h1 - h0
             BST[0] = due
             wc = (m * 128 + h0, m * 128 + h1)
             o = (m * P + 16 * h0, m * P + 16 * h1)
-            zz = ("p%d" % zb, slot[zb] * 64, slot[zb] * 64 + n)
-            slot[zb] += 1
-            parts = [(H("i16"), ("q16",) + wc), (H("l2"), ("cmq", 64 * m, 64 * m + n)), (B("dvoid"), ("eq",) + wc)]
+            zz = ("p%d" % zb, slot[zb], slot[zb] + n)
+            slot[zb] += n
+            parts = [(H("i16"), ("q16",) + wc), (H("l2"), ("cmq", 96 * m, 96 * m + n)), (B("dvoid"), ("eq",) + wc)]
             if q == "v":
                 for k in range(0, n, PAR["vh"]):
+                    k2 = min(n, k + PAR["vh"])
                     BST[0] = due + k * 0.027
-                    vgt(("mx", o[0] + 16 * k, o[0] + 16 * (k + PAR["vh"])), X, ("ql", wc[0] + k, wc[0] + k + PAR["vh"]), ("xb", 16 * (h0 + k), 16 * (h0 + k + PAR["vh"])), A.max)
-                BST[0] = due + 1.6
+                    vgt(("mx", o[0] + 16 * k, o[0] + 16 * k2), X, ("ql", wc[0] + k, wc[0] + k2), ("xb", 16 * (h0 + k), 16 * (h0 + k2)), A.max)
+                BST[0] = due + 0.026 * n
                 mm(zz, parts + [(H("dn8k"), H("f1", h0, h1))], stop=False)
                 mm(zz, wrapped("bdv", "mx", o[0], 16 * n), start=False)
-                BST[0] = due + 2.6
+                BST[0] = due + 0.026 * n + 1.0
             else:
                 for k in range(0, n, PAR["sh"]):
-                    BST[0] = due + k * 0.027
-                    gather("s", ("mx", o[0] + 16 * k, o[0] + 16 * (k + PAR["sh"])), X, ("ql", wc[0] + k, wc[0] + k + PAR["sh"]))
-                for k in range(2):
-                    wk = (WB[ns % 2][k], 0, 512)
-                    lo = 512 * k
+                    k2 = min(n, k + PAR["sh"])
+                    BST[0] = due + k * 0.045
+                    gather("s", ("mx", o[0] + 16 * k, o[0] + 16 * k2), X, ("ql", wc[0] + k, wc[0] + k2))
+                for lo in range(0, 16 * n, 512):
+                    hi = min(16 * n, lo + 512)
+                    wk = (PAR["wb"][ns % 4], 0, hi - lo)
+                    ns += 1
                     BST[0] = due + 0.5
-                    mm(wk, [(B("nib"), ("xb", 16 * h0 + lo, 16 * h0 + lo + 512))], stop=False)
-                    BST[0] = due + 1.5 + 0.5 * k
-                    mm(wk, [(H("i16"), ("mx", o[0] + lo, o[0] + lo + 512))], start=False)
-                    sa(("ab", o[0] + lo, o[0] + lo + 512), wk, F.Abs)
-                ns += 1
-                BST[0] = due + 2.8
+                    mm(wk, [(B("nib"), ("xb", 16 * h0 + lo, 16 * h0 + hi))], stop=False)
+                    BST[0] = due + 0.045 * hi / 16 - 0.5
+                    mm(wk, [(H("i16"), ("mx", o[0] + lo, o[0] + hi))], start=False)
+                    sa(("ab", o[0] + lo, o[0] + hi), wk, F.Abs)
+                BST[0] = due + 0.045 * n
                 mm(zz, parts, stop=False)
                 mm(zz, wrapped("bds", "ab", o[0], 16 * n), start=False)
-                BST[0] = due + 3.7
+                BST[0] = due + 0.045 * n + 0.9
             wait[h].append(zz)
             bb = (S("b0", h0, h1), S("b1", h0, h1))
             while fold and wait[h]:
@@ -439,16 +461,16 @@ def build():
             cv("upv", full("upv", 16), ("land", i + 16, i + 32))
             vscat((tb, 0, TW + 16), ("land", i, i + 1), full("upv", 16))
         N, SM, LG, HL = ("p6", 0, 128), ("p0", 0, 128), ("p0", 128, 256), ("p0", 256, 384)
-        for h in range(2):
+        nb = 0
+        for h, c in enumerate(PART):
             d0 = BST[0] = PAR["ds"][h]
-            c = PART[h]
-            o = 16 * c[0]
+            o, pn = 16 * c[0], 16 * (c[1] - c[0])
             US = ("p7",) + c
             vs(I("q", *c), I("bk", *c), 2047, A.bitwise_and)
             cv("qsl", ("qsl",) + c, I("q", *c))
             shared(("gq", 0), X, "qsl", c[0], c[1], PAR["xq"][h], C("n128"), step=PAR["xh"])
             BST[0] = d0 + 1.8
-            mm(US, wrapped("bq", "gq", o, 1024))
+            mm(US, wrapped("bq", "gq", o, pn))
             BST[0] = d0 + 2.5
             cv("uq", I("uq", *c), US)
             vs(I("uq2", *c), I("uq", *c), 4095, A.bitwise_and)
@@ -465,32 +487,42 @@ def build():
             cv("qs16", H("qs16", *c), I("q", *c), bias=-1023.5)
             BST[0] = d0 + 3.2
             shared(("ga", 0), TB, "hl", c[0], c[1], PAR["tq"][h], step=32)
-            for k in range(2):
-                wk = (WB[(ns + h) % 2][k], 0, 512)
-                lo = o + 512 * k
+            for k, lo in enumerate(range(o, o + pn, 512)):
+                hi = min(o + pn, lo + 512)
+                wk = (PAR["sb"][nb], 0, hi - lo)
+                nb += 1
                 BST[0] = d0 + 1.5
-                mm(wk, [(B("nib"), ("xb", lo, lo + 512))], stop=False)
+                mm(wk, [(B("nib"), ("xb", lo, hi))], stop=False)
                 BST[0] = d0 + 2.6
-                mm(wk, [(H("lj"), ("gq", lo, lo + 512))], start=False, stop=False)
+                mm(wk, [(H("lj"), ("gq", lo, hi))], start=False, stop=False)
                 BST[0] = d0 + 4.2 + 0.5 * k
-                mm(wk, [(B("i2f"), ("ga", lo, lo + 512))], start=False)
-                sa(("ab2", lo, lo + 512), wk, F.Abs, bias=C("c128r"))
+                mm(wk, [(B("i2f"), ("ga", lo, hi))], start=False)
+                sa(("ab2", lo, hi), wk, F.Abs, bias=C("c128r"))
         for h, c in enumerate(PART):
             BST[0] = PAR["ds"][h] + 3.0
-            mm(("p6", 256 + c[0], 256 + c[1]), [(B("hb"), B("sgn", *c))] + wrapped("bsq", "gq", 16 * c[0], 1024))
-        for h in range(2):
+            mm(("p6", 256 + c[0], 256 + c[1]), [(B("hb"), B("sgn", *c))] + wrapped("bsq", "gq", 16 * c[0], 16 * (c[1] - c[0])))
+        for h, c in enumerate(PART):
             BST[0] = PAR["ds"][h] + 5.3
-            c = PART[h]
             mm(("p6",) + c, [(B("d23"), B("one", *c)), (H("d2k16"), H("d16", *c)), (B("dvc"), B("vc", *c)), (H("ni16"), H("pos16", *c))], stop=False)
-            mm(("p6",) + c, wrapped("be", "ab2", 16 * c[0], 1024), start=False)
+            mm(("p6",) + c, wrapped("be", "ab2", 16 * c[0], 16 * (c[1] - c[0])), start=False)
         BST[0] = Z - 1.0
-        sa(B("r2"), S("rt"), F.Identity, scale=2.0)
-        mm(("p7", 128, 256), [(B("ib"), B("r2")), (S("n32"), S("rt"))])
-        sa(S("rf"), ("p7", 128, 256), F.Identity, bias=1.0 / 16)
-        add("d", 0.1, lambda g, T, x, w=w: g.sync.dma_start(T[w][0:128:16, W0 + P:NX], _ap(T, S("rf"))), [S("rf")], [XF], done=(lambda x, t=t: ("fc%d" % t, 16)), lat=2.0)
-        BST[0] = PAR["ds"][1] + 3.6
+        cv("r2", B("r2"), S("rt"), 2.0)
+        if t < RO - 1:
+            mm(("p7", 128, 256), [(B("ib"), B("r2")), (S("n32"), S("rt"))])
+            cv("rf", S("rf"), ("p7", 128, 256), bias=1.0 / 16)
+            rows(w, 0, W0 + P, "rf", "fc%d" % t)
+        else:
+            cv("rf", S("rf"), B("r2"), 0.5, -128.0)
+            vt(S("ta"), S("rt"), S("rf"), A.subtract)
+            cv("rf", S("gu"), S("ta"), 16.0, -2048.0)
+            cv("rf", S("hpr"), S("ta"), -16.0, 2049.0)
+            for k, (r, c, src) in enumerate(((0, W0, "rf"), (0, W0 + P, "rf"), (15, W0, "gu"), (15, W0 + P, "hpr"))):
+                rows(wn, r, c, src, "fc%d" % (t + k))
+        BST[0] = PAR["ds"][-1] + 3.6
         SG, XE, XW, K2 = ("p6", 256, 384), ("p1", 0, 128), ("p0", 384, 512), ("p1", 128, 256)
-        one = ("one16", 0, 128)
+        one, HP = ("one16", 0, 128), ("p1", 256, 384)
+        if t < RO - 1:
+            cv("hp", HP, I("h"))
         vt(H("cmn"), H("qs16"), PH, A.min)
         sa(B("inv"), SG, F.Abs)
         mm(LG, [(H("i16"), H("pos16")), (H("i16"), H("qs16")), (H("ni16"), H("cmn"))])
@@ -531,8 +563,12 @@ def build():
         gather("s", full("nc", 16), X, ("nl", 0, 1), bias=-0.125, scale=0.5)
         vs(C("ni"), ("nc", 0, 1), ("nc", 1, 2), A.add)
         cv("nif", C("nif"), C("ni"))
-        mm(NC, [(S("m2"), ("nc", 0, 1)), (S("m1"), C("nif"))])
-        cv("w15", (w, 15, 16), NC, bias=C("c35"))
+        if t < RO - 1:
+            mm(NC, [(S("m2"), ("nc", 0, 1)), (S("m1"), C("nif"))])
+            cv("w15", (w, 15, 16), NC, bias=C("c35"))
+        else:
+            mm(NC, [(S("m5"), ("nc", 0, 1)), (S("m4"), C("nif"))])
+            cv("w15", (wn, 15, 16), NC, bias=C("c56"))
         if t < RO - 1:
             BST[0] = Z + 5.6
             vs(B("oha"), H("pos16"), C("a"), A.is_equal)
@@ -556,18 +592,20 @@ def build():
             mm(FP, [(H("i16"), H("f1")), (H("i16"), H("gf"))])
         BST[0] = Z + 2.4
         vs(B("v"), LG, C("b"), A.is_gt)
-        vs(XW, HL, C("b"), A.subtract)
+        if "xw" in PAR["s"]:
+            lin("nb1", "b", -1.0, 0.0)
+            cv("xw", XW, HL, bias=C("nb1"))
+        else:
+            vs(XW, HL, C("b"), A.subtract)
         vt(S("k2v"), B("v"), K2, A.mult)
         BST[0] = Z + 2.0
         lin("inv", "xC", -1.0 / 4096, 0.0)
         lin("xd", "xC", 1.0, 2047.0)
-        lin("aI", "a", "inv", 0.0)
-        lin("bI", "b", "inv", 0.0)
-        lin("u1", "ba", -1.0, "xd", F.Relu)
+        lin("aI", "a", "inv", 0.0, n=3)
+        lin("wdef", "b", -1.0, "xd", F.Relu, n=2)
         lin("nz", "u1", 1.0, "bI")
-        sa(H("pa"), H("pw16"), F.Identity, scale=-1.0, bias=C("nz"))
+        cv("pa", H("pa"), H("pw16"), -1.0, C("nz"))
         lin("m3", "xC", 2049.0 / 4096, "ba", F.Abs)
-        lin("wdef", "b", -1.0, "xd", F.Relu)
         lin("an1", "a", -1.0, -1.0)
         lin("pb", "aI", 2.0, 0.0)
         BST[0] = Z + 3.6
@@ -583,22 +621,20 @@ def build():
         BST[0] = Z + 2.9
         fetch(B("oh2"), S("k2v"), "kmax2", (XE, XW), A2, True)
         BST[0] = Z + 4.2
-        vs(C("ws"), wX, -1.0, A.mult, C("wdef"), A.add)
+        vs(C("ws"), wX, C("wdef"), A.subtract)
         vs(H("g4"), H("pa"), wX, A.is_lt, C("m3"), A.mult)
         vs(H("g5", 0, 256), H("pa", 0, 256), eX, A.is_lt, C("ws"), A.mult)
-        mm(PL, [(n16, H("g4")), (n16, H("g5")), (i16, H("g6"))], start=False)
+        mm(PL, [(n16, H("g4")), (i16, H("g5")), (n16, H("g6"))], start=False)
         vs(full("pl"), PL, C("pb"), A.add, float(W0), A.add)
         BST[0] = Z + 5.3
         if t < RO - 1:
             shared((wn, W0), XA, "pl", 0, 128, PAR["rv"])
             lists(t + 1)
             BST[0] = Z + 3.8
-            lin("k0", "ba", "inv", 0.0)
             lin("mba", "k0", -1.0, "ba")
             cv("ds", C("ds"), eX, -1.0, 2047.0)
-            lin("h0", "ws", 1.0, "k0")
-            lin("h1", "ws", -1.0, "k0")
-            lin("cs", "ws", -1.0, "ds")
+            lin("h0", "k0", -1.0, "ws")
+            lin("h1", "k0", 1.0, "ws", n=2)
             pos = H("pos16")
             BST[0] = Z + 7.0
             vs(H("h0"), pos, C("a"), A.is_gt, C("h0"), A.mult)
@@ -607,7 +643,7 @@ def build():
             vs(H("h4"), pos, C("cs"), A.is_gt, C("mba"), A.mult)
             vs(H("h5"), pos, C("ds"), A.is_gt, C("mba"), A.mult)
             mm(POS, [(i16, pos), (H("m2i"), H("hr")), (H("m12"), H("f0")), (H("p12"), H("f1m"))], stop=False)
-            mm(POS, [(i16, H("h0")), (i16, H("h1")), (n16, H("h4")), (i16, H("h5"))], start=False)
+            mm(POS, [(n16, H("h0")), (i16, H("h1")), (n16, H("h4")), (i16, H("h5"))], start=False)
             if "ph" in PAR["s"]:
                 cv("pos", pos, POS, bias=C("pb"))
                 cv("ph", PH, pos, bias=-1023.5)
@@ -615,7 +651,7 @@ def build():
                 vs(PH, POS, C("pb"), A.add, -1023.5, A.add)
                 cv("pos", pos, POS, bias=C("pb"))
             BST[0] = Z + 10.5
-            vt(S("hp2"), B("oh"), I("h"), A.mult)
+            vt(S("hp2"), B("oh"), HP, A.mult)
             rsum("har", C("har"), S("hp2"))
             vs(C("e1"), C("r1"), C("kmax"), A.not_equal, C("padt"), A.mult)
             cv("msg0", ("msg", t * 32, t * 32 + 1), C("har"), bias=C("e1"))
@@ -628,13 +664,7 @@ def build():
         else:
             for k in range(4):
                 c = (512 * k, 512 * k + 512)
-                wk = ("p%d" % (3 + k), 0, 512)
-                gather("vs"[k % 2], ("gq",) + c, XA, ("pl", 32 * k, 32 * k + 32), C("n128"))
-                mm(wk, [(H("lf"), ("gq",) + c)])
-                if k % 2:
-                    sa(("yo",) + c, wk, F.Identity)
-                else:
-                    vcopy(("yo",) + c, wk)
+                gather("vs"[k % 2], ("yo",) + c, (wn, 0, NX), ("pl", 32 * k, 32 * k + 32))
                 add("sd" if k % 2 else "d", 0.1, lambda g, T, x, k=k, c=c: (g.scalar if k % 2 else g.sync).dma_start(T.y[:, c[0]:c[1]], _ap(T, ("yo",) + c)), [("yo",) + c], [],
                     done=(lambda x, k=k: ("st%d" % k, 16)), lat=2.0)
     return ops
@@ -680,6 +710,8 @@ def plan():
             hv = (hv * 131 + ord(ch)) % 1679609
         o["key"] = "".join("0123456789abcdefghijklmnopqrstuvwxyz"[hv // 36 ** k % 36] for k in range(4))
         o["due"] = PAR["T"] * max(o["sec"], 0) + (PAR["T0"] if o["sec"] >= 0 else 0) + tau.get(o["key"], o["tau0"])
+        if len(ST) == 3 * n:
+            o["due"] = int(ST[3 * i:3 * i + 3], 36)
     left = [len(o["deps"]) for o in ops]
     order, fin, free, last = [], [0.0] * n, {}, {}
     ready = [i for i in range(n) if left[i] == 0]
@@ -728,10 +760,25 @@ def links(rank, N, near, neng, send):
 
 def rank_program(g, core, T, topo):
     rank = T.rank_of(core)
+    N = len(T.cores)
+
+    def aide(r):
+        c, d = T.cores[r], T.cores[(r - 1) % N]
+        l = [h for h in topo.cores_of(c) if T.rank_of(h) is None and topo.die(h) != topo.die(c) and topo.may_write(h, d)]
+        return l[0] if l and topo.chip(c) != topo.chip(d) else None
+
+    def spare(r):
+        return [e for e in topo.engines(T.cores[r], aide(r)) if e not in topo.engines(T.cores[r], T.cores[(r - 1) % N])]
     if rank is None:
+        for r in range(N):
+            if aide(r) == core:
+                d = T.cores[(r - 1) % N]
+                rid, pid, _ = topo.addr(d)
+                g.wait_ge(T.sem.ta0, len(spare(r)))
+                g.remote_dma(_ap(T, ("tb0",) + TP[1]), _ap(T, ("tb0",) + TP[1]), T.sem.ta0, T.sem.lown, pid, rid, topo.mask(core, d))
+                g.wait_ge(T.sem.lown, len(topo.engines(core, d)))
         return
     ops, order, cnt, _, _ = plan()
-    N = len(T.cores)
 
     def neng(a, b):
         return len(topo.engines(T.cores[a % N], T.cores[b % N]))
@@ -740,11 +787,14 @@ def rank_program(g, core, T, topo):
         return topo.chip(T.cores[a % N]) == topo.chip(T.cores[b % N])
     tot = {}
 
-    def send(d, out, src, rsem, lsem):
+    def send(d, out, src, rsem, lsem, aided=False):
         dst = T.cores[d]
+        es = topo.engines(core, dst)
+        if aided and aide(rank) is not None:
+            dst, es = aide(rank), spare(rank)
         rid, pid, _ = topo.addr(dst)
-        g.remote_dma(_ap(T, out), _ap(T, src), T.sem[rsem], T.sem[lsem], pid, rid, topo.mask(core, dst))
-        tot[lsem] = tot.get(lsem, 0) + neng(rank, d)
+        g.remote_dma(_ap(T, out), _ap(T, src), T.sem[rsem], T.sem[lsem], pid, rid, sum(1 << e for e in es))
+        tot[lsem] = tot.get(lsem, 0) + len(es)
     x = links(rank, N, near, neng, send)
     eng = {"v": g.vector, "s": g.scalar, "sd": g.scalar, "t": g.tensor, "g": g, "d": g.sync}
     know, opk = {}, {}

@@ -1,55 +1,59 @@
+import numpy as np
 from concourse.mybir import AluOpType as A, AxisListType as AX, ActivationFunctionType as F
 
 RO, M, P, TW = 5, 4, 2048, 4096
 TP = [(0, 256), (256, 1664), (1664, 2880), (2880, TW)]
+HC = 2304
 W0 = 16
 NX = W0 + 2 * P
 PAR = {
-    "part": ((0, 64), (64, 128)), "wb": ("p3", "p4", "p5", "p2"), "sb": ("p5", "p2", "p3", "p4"),
-    "items": [(0, 0, "v", 0, 1, 12.9), (2, 0, "s", 1, 1, 12.8), (1, 0, "v", 0, 1, 15.2), (3, 0, "v", 1, 1, 17.0), (2, 1, "s", 0, 1, 15.9), (0, 1, "v", 1, 1, 18.8), (1, 1, "v", 0, 1, 20.9), (3, 1, "s", 1, 1, 18.8)],
-    "s": "f1 d16 vc qs16 pos upv aa1 idr xl nb w15 nif har msg0 msg1 ds k".split(),
-    "T": 2959, "T0": -151, "Z": 31.0, "ds": (19.8, 24.5), "vh": 32, "sh": 64, "xh": 32,
+    "part": ((0, 64), (64, 128)), "wb": ("p3", "p4", "p5", "p2"), "sb": ("p3", "p5", "p2", "p4", "p5", "p2"),
+    "items": [(0, 0, "v", 0), (2, 0, "s", 1), (1, 0, "v", 0), (2, 1, "s", 0), (3, 0, "v", 1), (3, 1, "s", 1), (0, 1, "v", 1), (1, 1, "v", 0)],
+    "s": "r2 rf sq u16 sh16 k k2 w15 dk ex aw pos d16 qs16 hh lu a".split(),
+    "vh": 32, "sh": 64, "xh": 32, "ng": 12,
     "xq": (0, 32),
-    "tq": (64, 32),
-    "rv": 24,
-    "CYC": 0.83e-3 * 1.25, "TCY": 0.42e-3 * 1.25, "GC": 1.56, "WAKE": 0.15, "SELF": 0.06,
+    "tq": (32, 32),
+    "rv": 40,
+    "grp": 2, "lw": 1,
 }
-TAU = "qzxp00cwqt200cetpv00oyhpm000n0u20001ipz01c0oc400ougaa010q84j000hra100w9agw01rafln02fjl9k01yra3c027i4ff02o0s2m03c8qt3057t5gv08sak730as9nf504qit3204y2c4s03k6spq02wp2dp0ajewlg04hu53o048cfe6000zfoq07zz13u0dqrfso05ozzlo0daml460ev0xry06kpkf50cl6v800b13fse0901d1j072roto05wihes0gz254a0ockzry0qt4kpe0sndqdb0g3mw180ctv2q41ju10oc06t4lr20k01yz0107xv160rqenc20mkc33n1uznil507ahf2h06osvc203pxabq0cnkz9n05h5jjh04abkro08h670s09olnqx0c274h3063q0iu0bgkdp50a9ztfb07v6ch30av09ye04wfpok092q5z50d93v740g82h7q0kt43nt0v0x15101jzc750q5548d2c7m0t503t9yqi06cx6zv07bsrxg0e50hr80gb94t50lf49e10kyeaue0mu6f2y0jshdyo0m3ti2y0no6h960olgm2y0sw2zo40ui3q2y0w5aoew1a7a4aa0lurce10otw7t50r2fqkr0sfgb8a0hfjdgj19jsj4g2are9qb0tm1qsc0d2awg90mcflqu0kayq320ig93gv0x8i94s1jda7sm07qege10u1fj3k0l6uztp0v85ajs1k32n3k27okq9y2b0eitz1tt03de1w0k1sd0eet7ga0em2q8t0f8j2560j4uehz0ph3l5w0vhcrts12ypvqi16kczqi1afy1ff1fw783c1kvnv4i1qlblev0t4bvme25e1sn519rfbxz206deio1iv0iio1qukh0r2bsg09b06lhvke09ff46j0c93zfe0f38m660egtjwe0dut5g00f1n2xb0fnynay0beq2d50gt1hjb0fogx9h0gkrdk20hne4lg0io6ua80jcxg3p0ki88z00k8bbzn0koyezn0l3lizn0ljs0m804uf4m80ly28m80me948l0n9yana0qegtkj0ua9cfd0pqh6zd0ra51840tdunhf0p2juw40vp1dud0xhokyq0nxdrdg0rzv9bp0urfdxi0g122ph0n4pt8t0jv8s5r0lf2hxi0qnnlz70rtcx8t0pv3h8h0uqw2k30mtw40s0tj5z6k000gwq10ycv9xs11aazpj11m0vl011s8ami128eevu1adfbc61as3ted16scdgt10xoco71y7i95j1z7zabt15drto112vkfwh14b7jwh195l2t31dpj84s11johuc17jbluc18cnsm019obu5n11xyx5n16qsnfp17z7s7s1bluv7s1bxzl2y1ggzr8517vjlq71b81x6i1b5o07i1eb86t31j6ofao1dy4bjx1gp44i11hhr7i11jjcj0s1lxh4651bey6hx13ilahx1hweood1mr15j212po8j21goujxm1l28xdj1myv0ej1pnltth1sg1uz01jfhp8a1n8ad4t1mjxg4t1sfadjw1w41oq21pqhjzb1spnm3b1r6aq3b1vk8xth1z9d0od1g8youc1fvlsuc1lfak6m1v9l16n1dh856n1naudoo1tkp2uk1x4c6uk1xgg8az220rzqx1ma0sn71mzm2a51ohz8k01r0fw3i1tzw6do1vvbn3u1wdi55m1wpxlvr1x8p3zo1z1hqmi1s8isih1wyk7l01ysta0u1xd71701zi8uca25k8ehx1ouvhhx1rmilhx23uf0f2269bcj21zsyfj2228ljj228kpsrb29q2p0522d20p822pmk7c232t2l623b1ad92673yd2284ie4828sxuud2951b5z29oaww82a5sh3h29wijjv2ezowu72dy40a125uxpdk2ai48re2bf8wuc1yzvzuc27ri3vc2e5r6tp2fev86n231ic6n2dc5g6n2fk722z2h3d2jb20lhrsi29dsjs72b0fns72bsy22q2hll62q2j5hqb11zt02jf2lp81bm2n1x2qj2o0d46u28dyquu2edi4ej2eyumwh2i0nd4p2kphz7s2gdp52w2h64ijp2l2dk542llrjlu2lymuvi2mb817l2mnwkag2nm3vbs2o5b11m2n7rf192nzc92w2ozx2n62q1xkoy2qxfjh72ru1u5s2psa0uo2qoj6il2qgsc6i2rcm9uw2s9ph1w2sykr5s2u93tks2uuv8ql2vmcpkz2wsyx7c2yyw56v30jumwv31ywlzt33025ql2vvpose38ogk6l2rlv0xq2si0yev2uhb0nn2w2sj6n2wnv5sc2xt6h7c2y857vc2mo204i2t3y8t22v9savc2wwl9lc2yubnga2tt70892t6j1f42uqcoxb2qern7l2qsryiy2ra057v2to6nhu2s4ft5r2wa4btx2xvxgtx2sj0uvh2rpihjo2u2ooia2zp0kxl2vef0or2yh76nv2yqxi542x55phx2zbdo7m2sq0o542tlenlu2uhzys82v5nhxq2vnjoag2wqqybs2xey41m2waej192x7yls52y8vvr62z7imxg2zfx2om2zosshx30hlngz31mdh7c34td0tc33fwnri303b4io317mks932198er32u11jf33iskwz34e3csb31c8nj22pfvqj2341iuj2356fn6n314zgaa33mmkaa35m4bgs37ftegl395b0tq3afs5zr36rxw3c37uouri3brpupm389eypf39lwj2l3b3jr6y3a08v6r3bcqgjw3cuoztn2t96c6h2yguh4n30ic5st30xlbgq3043osj32lj1gk33xyh6q30ydywv339zen134652p8376uyzq361h20r37sdomz3aoov163hlimw02okjak22pqhb522pdbd8m2zatr5n2yvjyka30262la32wt5la2ymg9la38jwqd9140j3p7000nnwg16drwj91mi67p70vgarwg1xse0k91yktap70snxuwg20f14k9216gep70snkywg237o7k923z7o8l356og7o3a5suf03c2mck035fqfe33ahd0p93cb9o7c37ofwhx3ait62o3bpxyt63dlg6l637y2rs73bb0pfi3cn6xwe3eg"
-TAU = "qzxp000wqt2000etpv00cyhpm00cn0u201c1ipz0100oc400ougaa00oq84j000hra100w9agw01rafln02wjl9k02ora3c020i4ff03k0s2m0488qt305mt5gv089ak7309h9nf504wit320552c4s05e6spq035p2dp0d3ewlg0dcu53o0facfe6000zfoq072z13u0corfso06czzlo07uml460dt0xry06kpkf508i6v8009z3fse0k51d1j0niroto04hihes0j2254a0s3kzry0cf4kpe098dqdb0ggmw180msv2q41ip10oc0fi4lr20go1yz00brxv160ykenc20pzc33n1ulnil507ihf2h0gosvc20bpxabq0cakz9n0545jjh03xbkro06b670s0b3lnqx0cw74h309wq0iu05qkdp509bztfb08p6ch30ai09ye04jfpok084q5z506x3v740g32h7q0ha43nt06tx151029zc7508r548d2cjm0t503t9yqi063x6zv0c0srxg0dk0hr80fs94t50mc49e10iueaue0nq6f2y0hshdyo0n9ti2y0ol6h960qhgm2y0rm2zo40tf3q2y0ytaoew19ja4aa0f1rce10qpw7t50pbfqkr0w5gb8a01rjdgj1s7sj4g2bee9qb0gy1qsc0biawg90p2flqu01jyq320v093gv08zi94s2bna7sm0qyege10z2fj3k0wduztp1i75ajs1j62n3k2a0kq9y2adeitz1so03de2b6k1sd0jht7ga09q2q8t0k3j2560m4uehz0n03l5w0otcrts0q8pvqi0rvczqi16sy1ff0vn783c1hznv4i1pgblev24obvme29d1sn51v3fbxz2cbdeio0to0iio1tckh0r2bwg09b069hvke092f46j0bw3zfe0eq8m660dptjwe0eat5g00ewn2xb0fhynay0a3q2d50ss1hjb0emgx9h0g0rdk20i1e4lg0hd6ua80jqxg3p0lo88z00wjbbzn0gbyezn0kylizn0mhs0m80fvf4m80kj28m80mw948l0o6yana0r7gtkj0t69cfd0u5h6zd0v851840xhunhf0pjjuw40sc1dud0twokyq0srdrdg0ukv9bp0vwfdxi0gq22ph0hwpt8t0nc8s5r0oi2hxi0o5nlz70uucx8t0rz3h8h0t5w2k30oxw40s0sc5z6k000gwq10xuv9xs11sazpj11g0vl010r8ami12oeevu11lfbc61293ted1yqcdgt16joco71vui95j1zbzabt134rto115mkfwh13h7jwh1a3l2t31d3j84s11pohuc13wbluc17pnsm019ubu5n11yyx5n16wsnfp1857s7s1c3uv7s1cfzl2y1fuzr85183jlq71al1x6i1bno07i1dz86t31ikofao1dc4bjx1g244i11idr7i11ixcj0s1lbh4651bky6hx19blahx1greood1l815j218io8j21hkujxm1mx8xdj1khv0ej1ptltth1uy1uz01ithp8a1muad4t1n8xg4t1rcadjw1x41oq21pchjzb1runm3b1swaq3b1vm8xth1xyd0od1geyouc1ktlsuc1mfak6m1wfl16n1fi856n1lmudoo1u4p2uk1tcc6uk1yhg8az20orzqx1ln0sn71mdm2a51onz8k01r6fw3i1u2w6do1vzbn3u1wci55m1woxlvr1xcp3zo1xphqmi1mmisih1zxk7l024ita0u26671701y68uca24d8ehx1nnvhhx21oilhx22hf0f226lbcj21p0yfj21x6ljj2279psrb28e2p0521120p821dmk7c21vt2l621z1ad924w3yd226uie48277xuud27k1b5z283aww828gsh3h21mijjv24xowu725c40a125rxpdk28s48re2a48wuc23avzuc26gi3vc2c1r6tp2d9v86n243ic6n2ct5g6n2dm722z2eyd2jb201hrsi281sjs729pfns72ahy22q2fnl62q2h0hqb11y402jf2ik81bm2jxx2qj2kvd46u2bayquu2cni4ej2efumwh2f1nd4p2jkhz7s2kjp52w2ly4ijp2ixdk542jgrjlu2jtmuvi2k6817l2kiwkag2lh3vbs2m0b11m2l2rf192luc92w2mux2n62nvxkoy2osfjh72pg1u5s2nna0uo2ojj6il2obsc6i2p7m9uw2pvph1w2qqkr5s2ro3tks2skv8ql2tccpkz2utyx7c2wtw56v2xyumwv2yzwlzt30125ql2u0pose32sgk6l2r7v0xq2qy0yev2rvb0nn2tosj6n2uev5sc2vo6h7c2wk57vc2lc204i2rty8t22szsavc2u5l9lc350bnga2q470892suj1f42s6coxb2o9rn7l2onryiy2ph057v2rg6nhu2qbft5r2s64btx2vwxgtx2r10uvh2ufihjo2pwooia2xb0kxl2w3f0or2v076nv2txxi542wc5phx2wxdo7m2qj0o542rgenlu2rxzys82slnhxq2t9joag2ulqybs2v9y41m2u5ej192v8yls52w9vvr62x2imxg2xax2om2xjsshx2yblngz2zcdh7c33inusz30gwnri2yeb4io2yxmks92zr98er30k11jf318skwz3243csb3918nj22navqj232eiuj232xfn6n2yxzgaa33cmkaa33s4bgs34ztegl35ub0tq37ss5zr34kxw3c369ouri37jpupm35feypf374wj2l38gjr6y3808v6r394qgjw39yoztn2tl6c6h2wwuh4n2ykc5st2xqlbgq2y53osj2zmj1gk31wyh6q31ndywv30zzen133952p832kuyzq31lh20r347domz36oov163f2imw02mfjak22nlhb522n8bd8m2p2tr5n2whjyka2x962la303t5la32xg9la35rwqd913ij3p7000nnwg17qrwj91lw67p70s4arwg1tpe0k91uhtap70s4xuwg1zy14k921dgep70s4kywg242o7k92827o8l35tog7o3atsuf03cpmck0362qfe33b5d0p93cy9o7c38bfwhx3b6t62o3ccxyt63e8g6l638l2rs73bz0pfi3da6xwe3f3"
-TAU = ""
-PAR.update({"T": 2700, "T0": -700, "rv": 32, "ng": 12, "ds": (19.9, 24.8), "tq": (32, 32), "Z": 30.8,
-            "s": "f1 d16 vc qs16 pos upv aa1 idr xl nb w15 nif har msg0 msg1 ds k pa r2 rf dk sq u16 sh16 ph xw k1 k2".split(),
-            "items": [(0, 0, "v", 0, 1, 13.0), (2, 0, "s", 1, 1, 13.0), (1, 0, "v", 0, 1, 15.4), (3, 0, "v", 1, 1, 17.2), (2, 1, "s", 0, 1, 14.8), (0, 1, "v", 1, 1, 19.0), (1, 1, "v", 0, 1, 21.2), (3, 1, "s", 1, 1, 18.9)]})
-PAR.update({"tq": (32, 64), "s": "f1 d16 vc qs16 pos upv aa1 idr xl nb w15 nif har msg0 msg1 ds k pa r2 rf dk sq u16 sh16 xw k2".split()})
-ST = "00000000c00c00o01000o01c00000w01s01q01z01i02g02703c06c07106t05103302o07b06403s00004105p08908q0a104t0cy0es0h52040950a01ya0cp0as13j05q07h0di1ks06j1k604404p03j1id1rd1hs1qs1je1go1yj1z621705a07j0bn06l0800df0ch0ed09s08h0al0b90cc0zf1g71hd1gf1hu21f1zf21w21o1zn0g91zw2240d61ib1jl1j01le48n48228n20s26t07s09k0ct0gi0xi13a14314k17g17x1au1dt1yy23j22123723b23s22w06c0960c00eu1k91li1o01rr1p91mr1wq1vh1qi1t01xz1u808p09a0br08407r0990hz0jh0b80c20cx0e40dy0et0m104h0f50fu04w0g90go0gq0j20ls0in0jh0kb0kj0ld0m10jw0ky0m90b80h20h60ip0d80kd0c10fe2680l010d17z0hm14c0mh0mt0re0u80un0xr23s25n24d2810oy0rt0td0uo0y60mm0o20sl0xr0na0rt0w30w711w13u0mi0v20xb0yv14b0yf10v14j14y1780rd0ov0xq0zx0mi0wj11k13e1d41fy14s18e17w1ba1h51dj1b31en1gn1jt13813q1971eg16g18f1g41ct1i81ka17p1861bc18u1f21hm1i31ik1j61k21gw1sd1ry1sr1ol1ob1ki1ml1uk1wh19z1ne1s61tu1kq1l51m51lu1p11r11rh1rw1si1sz1sr1w31tf21m1tf1vu1lb1vc1wa1y51jq1x31yq1zz1qk1sy1zj1zy21g22222m23n25226320d22h1vi24m2582d228w25t24124n25225i25x26y27k26j27e28h29t2aw2bk29l2a829c2ao2bb2ca2d12dq2en2lp2fq2i22j62na2i12px2da2bz2d02dz2ff2hn2kx2682e12fi2gj2pz2c72b32ex2eg2ao2a92bw2e42g32hg2db2bh2ej2ih2he2jd2dr2k12cm2di2e82ev2fb2gd2gz2fy2gt2hw2jm2ka2ki2ld2mf2n22no2iy2jv2kq2m42lr2mp2un1xv2op2p52mr2oa2pk2r82s22u72qe2sh2tj2qt2rn2tb2sw2ts2y42cl2is2kb2lb2le2mu2ip2m62l52lz2ni2pi3oy27z28u28e29o2jt2ko2qc2t62ni1742w02yu2v32vf2v92uf2yc2uu3yz3zk3qr3ye2yr2vo2w431z3az2v82wj31734p2un30f36d2vf38h3dn31733n33i36p3e336338j39z3bf3ei2zz2qu35x3812tc35539p3er3f33i13fl3b73gl3ih3n63kq3ia3n03nm3pk3bd3cx3h03mw3ae3k03l83ks3p43r22ng3ok3q13ex3fd3ik3g33li3ng3nw3od3oz3pt3o43py3pj3qd3uu3vi3s83t03xq4153dp40440w42t3ri3rx3se3sm3vj3xi3xx3yd3yz3ze3s63v33xz3s63zu42a3ul41p42q44h3tt43i45546e3qm3yi44a45y47g48i3rc4bl4cz4e045444p40k47v4a04am4d544p4ag4b24bh4bx4cc4dd4dz4cy4dt4ew4g04hb4hz4fs4h34gf4ie4jh4k54l04m64n14s34m34o64t34ub4ms4wp4hq4gu4kg4lg4m44nr4ri4cj4if4jh4ki4w04jy4h34ib4kl4hi4gg4kr4j24lr4p14o84hx4q04q54qd4ph4p04r24im4j84jp4kd4lo4mq4nc4mc4nl4oo4qm4qu4r34s74t94tv4uq4ol4pq4ql4si4rz4tq51p4dx4v64vl4st4tj4ur4y04yu50z4x64z950c4xl4yf5034zo50k51n4ld4pm4ra4rp4ss4t04p94sj4rq4px4ty4wb5w14ee4f94et4n64om4ph4sb4v531m4xz52552h52a51857l51v68o6eu67d6ff55552p5355905hr52a53k5885bq51f57g5de5275fi5kg5805ag5aj5dr5kv5cv5fb5h15i75lb5704xm5cy5f25045c65gq5lk5lv5ou5me5i05ne5pa5ty5ri5p25rw5ue5wh5ie5jq5nt5tr5ki5qs5s35rl5vx5xv2t44055uq4s95vn5wp5lq5m65pm5n45sj5uh5v75vm5w85x65u75x15wm5xg61l61w5z15zt64h65p61d67n68g69o5yb5yq5z55ze62c64a64q65565r66764164q6545yz66m69260l6986a06bc6596as6by6d65xf6626cq6d56eo6fa5xu6je6l96ma6bx6bi6836gt6he6i06m46iz6h96hv6ia6iq6j56k66ks6jr6km6lp6mt6ng6or6mk6o36n86p66pu6qu6rt6t96u46yz6sw6uf6vp70y6u373i6oj6nv6r56s86sx6tl6xn6kd6p76q96ra73a6qq6nw6op6re6ob6n96rv6rg6sv6v46to6pa6xl6ws6vw6x16vo6xp6pf6q26qi6r56sh6u06uu6t46uh6vp6xf6yb6xw6yz70170n71d6v96w56x06zs6yj70d78c6ky72g72v70d70t72174t76177r73z75m77474e75776v76g77c78f6sg6wk6y36yi6yy6zf6wk6zo6z76zl7187338256l76m26lm6pp6ze70873250r75w78s7947927807ed78n8lp8n98gv8mo7bx79h7a57fo7oj78x79d7ew7ie7877e37k178z7m57r87es7h87h67ke7rn7jo7m37no7oz7s37dn74f7jm7lp76w7iu7nd7sc7sn7vm7t67os7u67w280q7ya7vu7yp8168367p17qi7ul80h7o37xk7yt7yd82p84n2vy5yf81t4v382q83k73084h85s7si7sy7w97tr7z681581k82a82x84182p83s83d84w88p89485t87d8bl8ct7ra8ao8dz8f785385k8698688958b58bk8c08cm8d185b8bl88p85r8dh8fx8868er8gd8hl86l8fj8is8k18478cd8h58jl8l38m58j98p88qm8rn8j88ic8eh8li8nn8o98qs8hk8o38op8p58pk8pz8r08rm8ql8rg8sj8tn8ub8vm8u28uy8tf8w18x48xs8yn8zc90u95r90590s92l97q9269an8vd8up8y38zx90l91a9558q68w28x48y596q8xl8u38vb8y88uw8vw8ye8wp91091l8yt8wa93t93v92i93892r94k8w98wv8xc8y08yw90e91p8zi90d92k94994i94q95p96r97d98592493g94b96595m9759f48hz97698e96b98t9989bj9cd9eh9a89cr9dl9b49by9e99d69du9np8zq93f94y95c96196i92z96a95e93o97m99ta988s18sw8sg8ui96q97l78o9g89fw9fk9fk9eq9ku9f59fz9if9gx9la9v99fp9g59mt9p59ep9nl9qt9fl9sx9xy9l99ny9od9r69yd9qe9su9ug9vp9yt9kf9bk9qd9sh9dm9pl9u59z29zea2c9zw9via1ra2sa7pa50a2la53a7wa9v9vt9x8a4ba769uva0za5ia5ia9fabd2qa8c08ir4xx8ma8n475u8o18sp9ada8uaac9z89zoa31a0ja5ya7xa8da8sa9eaa3a7gaa8a9taamaf4afeacjae3ahzale9y0akdal6an2abtac8acoacxafuahtai8ainaj9ajpahjai8aimachak4amkaewalyan0aoqadbantapgaqoaaxaisaolaq8arrassab1abtapfasxascad6acuatyatdap0aktas6aubauwavvap0auravdavsaw8awnaxoayaax9ay4az7b0bb0yb1mb02b1db0qb21b34b3sb4nb5bb66b9mb3lb1eb20b48b2lb0rb43b2zb4wb6zb5qb4ib7kb76b6xb7nb7eb8bb29b2vb3cb3zb4vb5wb6ib5hb6cb7fb8ab8jb8rb9mbaobbabe6bbjbgibdqbgmbe0bgu"
-ST = "00000000c00c00o01000o01c00000w01s01i01q02e02602n03j06c07106k03a09q02v0b50bd06200004808007s08f0bm0af0aw0dr0gt21d05008y1yr0fx03z1gj04f07905n1j806a1kx03q05207w09j1rh1in1sg0ia1jf1z021u23o05n07j08u05f06t0cx0990fi07b09i08h0a60av0hm1gs1hu1i21ij21m23w2151zu2020gk22322j0a71jo1i21kc1lw4a649k2941zf22p0ao09z0c20f90ip0k714014h14x14p18319423f23723a26722b24520b06c0fo0ji0oc0r60sf0to0ux0w60xf0yo0zw11512e13n14w0cz0bt0dk0ce08w0ak0jc0ku0ci0dc0e70gg0g50h10n406r0hh0i20760ii0ix0iy0js0l90jd0kf0lx0li0m50ne0ku0q20y10cu0es0fy0lg0ee0js0dm0i425m0nx0qn0x50r41je0nk0nw0mk0mz0ya13l25123v26s2230qh0nm0pg0td0vd0np0pv0vo0ze0s50uw0xr0sy11i1480sx0vm0z60zl1560yp11514x15c17u0sf0n50xl1120md0ye17h11419k1gb15e18z16u1bv1hd1dv1bf1b31gz1j712q13117x1ge13t18p1eq1de1ii1kk18b18r19r1c91f61h41hl1is1jw1kc1ib1ju1lk1vk1p41ol1k01n61tg1vz1dp1nz1so1tw1l01lf1mo1m41pk1rk1rz1sf1t11tg1lo1r21s21zo1tw1wb1kt1u81wr1y01or1v11z720g1ll1r220020f21x22j24g25o28i29j22s20q1t424224o2c826n25924i25425j25z26e27f28127027v28y2a22ay2bs29t2ah2ap2c72cu2do2ef2fp2go2n42ho2i32ju2m42go2n62di2eo2ee2fr2gf2ii2l627f2fc2hq2ir2q72bd2c42ep2cf2aw2ai2cv2da2dz2g32fa2bb2ib2je2j52hf2ix2k22d32dq2e62ew2fc2ge2h02fz2h32i62k12kx2ln2mi2nn2o92oi2jm2ka2lj2mj2mr2nx2vh1w02nz2oy2of2pd2ps2qp2ry2ss2rj2sd2tf2u32ux2vz2to2ui2vr2jf2j12kq2l42m22mj2kp2ma2le2ld2n72r43pm28p29k28g2bq2ni2r72u12wv2od1m63bs3em2vx2w92t033y3132vc3s043r48z3rf2yn2w72wi3213992w22wx31935j2xq33j37734t39b3bx31i36t34b3b83em39h34d3at3cr3f130t2qm36r3f92t835z3dl3fu3hd3ng3g43c63g53j03nw3ik3l03kv3o53q338v37n3e93lv3f13gl3nj3kj3pn3rm2tz3p73qc3fg3fw3gx3je3mb3oa3op3p63ps3qt3oy3q73ql3r03vc3vn3la3tk3zz4233r63uc3z740f3s13sh3sw3t53w33y13yh3yw3zi3zx3xs3yv3yg3sq40d42t3v441k43944h40r42c45p46x3ry3xl44146h47z4914654c44dj4ek45o4593zn48f4aj4b54do44g4az4bl4c14cg4cw4dx4ej4di4ed4fg4gj4h74hu4gb4hm4gy4ii4j54ka4l44mt4nn4tv4m84mw4og4pa4ne4sh4i94je4jz4ll4m94ok4qp4d34k24le4mi4xa4jm4hn4ig4kp4gz4jl4j64kl4me4po4qo4l04r34p84rc4oz4oc4s14iq4k14kh4lc4lt4nb4nx4mh4nt4ow4r44rl4rt4t64u84uu4v64pg4q24sp4ta4tq4ul52544v4uw4vm4w14wg4wv4xa4y44yy4yj4z650050n51h52b50951252k4lz4q94rw4sa4sy4tf4qh4t64s84r54u34xp5wa4f64g14ey4i14rh4sc4v64y03he57052l52x4zl5aj55851w5yn6ct6f95y255n52s53658o5fu52q53l57w5c652c5a75du5be5fy5ii5835de5bq5hw5l65g25ay5hh5je5lm57g4xp5df5lw5015cm5k95mh5o05u15mp5iq5mt5pl5ui5rl5p55r45up5wo5fi5ea5kx5sj5lp5n85u75rj5wb5y92wt48l5uq4v45vv5ww5m15mh5nk5q25sz5v75vn5w25xd5xt5u95wv5x95xo62062a5xt60764w6645rv61068269a5yp5z45zk5zt62q64p65465k66666l64g65j6545zd67169h61s67a69x6b568u6ap6cc6dl5ym65o6bh6d56en6fp68d6is6k66l76cb6bw67s6f26h76ht6jq6bw6hn6i96io6j46jj6kk6l66k56l06m36n76nu6oi6mz6o96nm6ox6pk6qi6r96tb6u66za6qx6t16uy6x26tx6yh6q16pt6qt6sd6t26uv6xl6kj6qq6rx6ta73s6qa6oa6p46rq6nn6pp6q36r46si6vl6sw6ri6xh6wl6xc6vy6va6y16p56qp6rh6s56sm6tv6ug6tg6ub6ve6x46xt6y26z670970x71a6vj6w66yp6zo6zu70p7896l470p71q71472572k73c74n75h73r75276476r77l78o76d77678f6wo6w96xw6ya6zd6zm6wu6z570o6zs72z74882e6lu6mp6ll7op70971473y59s76s78p79175p7gn7ds78084q8j28lu8br7bc78w7a37et7ji78u79a7e17ib78g7gq7jz7hj7m37om7e77jq7gb7o07ra7m67h27nl7pj7rq7dl7477jj7s175x7ir7qd7sm7u58057st7ou7sx7vp80k7xp7v97x880t82s7ln7kf7r17yn7rt7xz80b7xn82f84e2zn6fu80t4xy81z83073w83x85j7s57sl7tp7w67z381a81p82683h83x81y83d82z84c88g88v8748af8bb8ck83y86c8ei8fq84t85a86085z88w8av8bb8bq8cc8cs8528bc88g85i8d78fn87w8fa8g38he8c48gv8ij8jr84q8cw8ho8jb8ku8lv8e88oy8qd8re8ii8i38ey8l98ne8nz8px8i38nu8og8ov8pb8pq8qr8rd8qc8r78sa8te8u18up8t58ug8tt8vc8vz8x58xy8z890396c8z38zi91f93j8zu94y8v48w88wu8yf8z491d93b8qp8ww8y98zc9698wg8uh8va8xj8tu8wf8w18xg8yu9229098xu93y92o93t92f91s94i8vl8wv8xb8y78yo90c90y8zx90s91v93l94a94j95n96q97e97r92192w95695r96b9769eq8rb96s98r94099699m99t9b29bw9an9bh9ck9d79e19f39cs9dm9ev93592q94d94r95u96394295m97597797z9a8a938s08sv8rs8uw96q97l79k9fu9f69fi9c59n29k89eg9hs9fc9fr9m29sd9fb9g69ki9os9ew9la9qg9o09sk9v29kn9px9nk9uh9xq9sm9nh9u29w09y59k29a19q09yi9cc9p89s49yea0ma6k9z99va9zqa25a70a45a1pa3na79a979ts9qw9yya549xia4ea6sa42a8waav2r58lfa7r50sa8oa9j76qaagabj9adacgaf49yl9z0a06a2na5ka7ja88a8oaa0aafa78aava9oab9afsag1ab7adlainam3aafahaaluanqabaac0acfacuafsai7ainaj2ajoak4aevaiiafkabzakjamzaedammanfapeal1ao7apvar3abzajgap0aqnas6at7aixajpapuasratcakqal2atsaudapfalhaslauqavbawaapfav6avsaw7awnax2ay3aypaxoayjazmb0qb1db21b0hb1sb15b2gb33b3rb4yb63b6xbadb3gb1tb2fb4jb16b43b53b4ob5ob7qb6hb30b8bb7wb8db84b7nb91b2ob3vb4ab56b5mb6nb78b68b73b86b91b99b9ibadbbebc0bewbc9bh8begbhcberbhk"
+MODELS = ((1.04e-3, 1.56, 0.0, 0.15, 0.06), (0.87e-3, 1.4, 0.05, 0.2, 0.15))
+PERIOD = 2800
+WHEN = ""
+ST = "00000000c00c00o01000o01c00000f04901o01v00x01e01n02s04606n07508b03x07t03102d0az06w00004n08209p0b70aq0e20bx04v0dt0cx08s0bp0gf0nf2ak0g00h01vy0i70fc09a0p52080q10ff0km0rh03s0hm0i705i1hn0ki08603707l1gg07e1xm1sb0re1z10bg28r03908j0990150240af0b10mz0qz1091160eu12203o06f04e07208s09x0ig1jd1i61k300o28a27b00f27k04w11l10x1rt10o1rl26u29w27227s29f28i2810ah1kl1o11lp1oj2a50630d50910f30hy0j50lu0m311u1if1jm1kt1po1px1qe1re1iw1oa29029o2at1zp06b0fn0jh0ob0r50sf0tp0uz0w90xj0yt10311d12n13x15716h16x17c17s18818n19219i19y1ad1as1b71bn1c21ch1cx1dc1dr1e61el1f11fg1fv1ga1gp1h51hk1hz1ie1iu1j926l0bm0c80cu0df08v0aj0ch0de0e80eu0fk0gf0fu0hi0ga0hx0io0jj0ke0j40jy0mb0lf0mk0pd0oy0pm0qb0mq0nj0ps0e60jk0nf0cl0gp0it0de0ic0l40oc0pv0so0r51jo0rw0s817i0qj0ww0zu1h20mt0s31fv1500rw1ak1hx0ta0ta0zc15a0u30yk13l17v1in1af12i1ee1j50y50si14718p0uw13e1701ch1nt0ue0xc15z1jv1af19s1h31ia1ga1io1k01n41pg1cx1ff1l71q61lb17x1p11rc1kc1l21mb1ou1te1vp1w71x71xu1yk22z20q1z81kf1sm25i27q1hv1rt22624b1s21sj1t71t71wd1yb1yt1za20020i27423821r1jh1zi26b29f1uy1xw24q2601ss1wc1vr2b51wr25r2661yp29u2bk12z14z1f91ga2d32ex2bq2e42di2ec2e32er2f62fl2fy2fj2h82gt2gd2ht28q2ih2jb2jz2le2h72i22in2j22jh2kb2jq2l52ke2kp2l02lf2lu2oc2mg2mu2rw2lt2m22n72di2mp2nq2or2ma2lu2os2r62pu2my2oj2tm2nx2nb2ph2mj2nv2nm2oa2p02qi2p82oz2qq2pn2re2s22t62tf2tw2ve2wf2yl2x92pe2q22ri2qx2sj2td2sr2uz2t72w02y631o32y2vt2wu2xp2x932j35k32433m34h2to2um2xx2rn2ue2u52yl3373q82n92qx2tr2o32wl1pa39b3ex34934l3ib34134p3552vr2tz2uk2v63ft35t3kk3sr3492wf3ab3fo34g39j3dy3hv3t83l83db3od3tn3942x93f63jo32j3ed3hd3mh3sz38b3at3fy3u13le3js3r33sa3qa3so3u03x43zf3nq3q93v73zu3v33iq3z041c2tr33u3xl3ug3uv3vp3y942i45b45q46546q4864934ah48u3uf40x4f44hc3rv41q4bs4dx41r42542t42t45z47x48f48t49e49t4gz4cz4bd3tg48b4g64j144147i4ec4fm42e45y45c4kr4a24fh4fx4cl4jg4l63j34aq4lc4md4mp4oj4ly4nq4n44ny4np4od4os4p64pk4p54qu4qe4pz4rf4g14s34sx4tl4v04qt4ro4s94so4t34tx4tc4ur4u04ub4um4v14vg4xy4w14wg51i4vf4vn4wt4n44wb4xc4yd4vw4vg4yd50s4zg4wk4y55384xj4wx4z34w54xh4x84xw4ym5044yu4yl50c4z951051o52s53153i55056158756v4z04zo51450j52552z52d54k52s55m57s5ba5ck55f56g57b56v5c55f65bp5d85e353954857j51953z53r5875ct5zu4wv50j53d4xp3hr5675dv5e75rx5dn5eb5er55d53l54654s5pf5ff5u662c5dv5615jx5pa5e25j45nk5rh62u5uu5mx5xz6385ip56v5os5ta5c45nz5qz5w362l5hx5kf5pk63n5v05td60o61w5zw62a63l66q6915xc5zu64t69g64p5sc68m6ay2wl3qu67753d5dg69p64264g65b67v6c46ex6fc6fq6gc6hs6ip6k36if6406aj6oq6qx61h6bb6le6ni6bc6br6cf6cf6fl6hj6i06if6j06jf6ql6ml6kz6326hx6ps6sn6dn6h46nx6p86c06fk6ey6uc6jo6p36pi6m76t26ur5sp6kc6uy6vz6wb6y56vk6xc6wq6xk6xb6xz6ye6ys6z66yr70f7006zl7116pn71o72j73774l70e71a71v72a72o73i72y74d73m73x74874n75277k75n7627b375175976f6wq75x76y77z75i75277z7ad79176677r7cu77576j78o75r77376u77i78879p78g78779y78v7am7ba7ce7cn7d47em7fn7ht7gh78m79a7aq7a47br7cl7bz7e67ce7f87he7kw7m67f17g27gw7gh7lr7os7lb7mu7no7cv7du7h57av7dl7dd7ht7me89g76h77b7a55bt7cz7nh7nt81j7n97nx7oc7ez7d67ds7ee7z17p083s8by7nh7fn7tj7yv7no7sq7x68138cg84g7wj87l8cu7sb7gh7ye82w7lq7xl80l85o8c77ri7u17z68d984l82z8aa8bi89i8bv8d78gc8in86y89g8ef8j28eb81y8i88kk2qx3r98gt56760g8ja7a57n28q68do8e28ex8hg8lq8oj8oy8pc8py8qq8sb8tm8rd8dm8k58xp8zw8b38kx8uc8wh8ky8ld8m18m18p78r58rk8ry8sk8sy8zu8w48tx8co8rj8z191l8n98qq8wx8y68lm8p68ok93a8t78ym8z28w492093p82a8v593w94x95997394i96a95o96i96996x97c97q98497p99e98y98j99z8yl9an9bh9c59dj99c9a89at9b89bn9cg9bw9db9ck9cv9d69dl9e09gi9el9f09k19dz9e79fd95o9ev9fw9gx9eg9e09gx9jb9i09f49gp9ls9g39fh9hn9ep9g19fs9gg9h69in9he9h59iw9ht9jk9k89lc9ll9m29nk9ol9qr9pf9hk9i89jo9j29kp9lj9kx9n49lc9o69qc9tu9v49nz9p09pv9pf9up9xq9u99vs9wm9lt9ms9q39jt9mj9mb9qr9vdaie9ff9g97il9wr9x39wf9xfaah9w79wv9xaa7z9xyacqakw9wf9ola2ha7t9wma1oa64aa1aleadea5hagjalsa199pfa7cabu9uoa6ja9jaenal5a0ga2za84am7adjabxaj8akgaigakuam5apaarlafwaieandas0aniaawar6ati2zf3ro92m50j60v93b7cz8a29a89j39w0aq0amvanaanxaqhauoaxhaxwayaaywb0cb19b2nb0zamkat3b7ab9hak1atvb4ib62atwaubauzauzay5b03b0kb0zb1kb1zb2wb55b3jalmb0hb8cbb7aw7azob6hb7saukay4axibcwb28b7nb82b5bbbmbdbab8aj0as8atgau2amgak0akcauhav2b0jb14bevbfjbfabfabg4bfvbgjbgybhcbh7bgybigbi1bhmbj1b87bjpbkjbl7bmmbjabjvbkabkpbljbkzbmdblmblxbm9bmnbnhbofbn1bn2bp3bqqbplbnpbovbsibombo0bpwbnabo7bnybombpcbptbpnbpfbqbbq2br5brsbsxbt5btebu2bv3bvobylbyhc1cby6c13bvxc10"
+ST = "08c08c08o08o09009c09009o08c08r0cl0a009b09q0c80ah0a30au0es0fj0c10cg0bm0dy0dm0jc0ei08c0bu0de0g60ig0ez0jj0f70h10io0k70ke0kl0o00uk1wt0n20x51i80r80py0dd18p1jr1iz0ce0m20o30ff0fw0ic0ge0iu0gw0hd0hv08w1ok1cc0q51ya0e61z10cn0d00iv09j0aa0js0l90mp0p80pl0w00ne18t0b80bf0bz0cy0dx0f00wr1bl1c51f708p1pu1rl0ei1ck0wk1is1p01p81pm1yp1zl20d1zt20k2570d71i10wy1p01qe25e1gx0fr0gt0fz0i90k80l50lc0s50u50wc1b61by1be1f01fw1vp1jj1r81vw25r1os0es0o40ry0ws0zm10w12613g14q16017a18k19u1b41ce1do1ey1fe1ft1g91go1h41hj1hy1ie1iu1j91jo1k41kj1ky1ld1lt1m81mn1n21ni1nx1oc1or1p61pm1q11sr0nl0k90kr0lq0hc0j00ks0lp0mm0n30nn0ok0on0pm0o50ra0qw0rs0t90qj0rg0sp0sw0tt0vt0sc0tg0ud0m40ne0tf0kl0oz0q60l80pz0s20mr0qm0va0xn0yw1gf0zm1qg0xk0x818318g17r15d0pj0rk0wo0us1a90z911a1am1cr19x0xn0s412415h0up12r17c1c71fl1bu19513b1f11ht1jn11k0wd1611d50x016o1ej1jz1od1dg15p0x81ds1il1ll19817e1gw1iu1991g91hg1lx1pf1n61kb1fs1ni1q61l81mc1cy1p41r11jc1k31kv1mx1qd1sc1t31vc1w91x01u62141xr1rl1s923p2541hk1tj20e23r1rs1sk1tb1tb1vy1xq1yh1z920520x1yh23521o1i71xt25t27v1sw1x624d26i1s01vv1ve20d1xx1x71wg21127229t16u1iu1k71l921p2992b12bl2ci2cu2dm2ed2fa2de2dr2ek2ex2eo2fh2fr2fz25o2gq2bo2h32de2eg2hu2hn2il2fr2gb2hw2h72hj2jg2i12kc2is2j32jn2jz2kj2nm2lo2m02p12i82ig2m22iy2js2ku2m42iu2in2lv2lg2nb2lo2mm2o32kw2lm2mq2k02kw2l92mf2nj2mi2mb2nq2n22on2of2pe2qj2qx2qq2rp2sr2wo2tn2mz2o32oz2ph2q12qy2qj2s72qv2sj2tg2v72zi2t32ui2vk2u52vy3232ts2uu2vr2r52rw2s32ou2rj2rc2tj2wb33m2lc2uq2p22m82rw1w232c37y3012zp2z532b31r36q2rf2rx2sw2se30232n37239o3d632n2zp2sw3463as2wv34u3cn3ek3hy3aw3b53943i13jt3lv36u2us3bc3jb2w43bz3hx3m83qd3ft34p2zp3g53kl3nt3e03cp3jx3m23he3j93ko3o63rj3pe3mb3ff3pr3sb3nh3oc3de3r53t22xk36i3hg3lc3m33nx3q03sm3us3vj3xs3yp3zg3vt43i4073tv3ui46447j3l83x442u4653tt3ul3vr3vc3yc40440w41n42k43b40w45k4423kk4084874a93v53zk46r48w3u13xw3xf42r40c3zn3yw43h49g4c73c53dc3nf3oh4444bn4df4dz4ew4f94g04gr4ho4ft4g54gz4hb4h24hv4i64id4834j44e34jh4ft4gu4k84k14kz4i64ip4ka4jl4jy4lu4kf4mr4l74lh4m14me4my4q04o24of4rc4kn4ku4o94lc4m74n94oi4l94l14o24nv4pm4ot4p04qd4na4o04p44me4nb4nn4om4pt4ox4op4q14ph4qx4qq4rp4st4t84t14tz4v14yy4vy4p94qd4ra4rs4sc4t84st4uh4t64uu4vq4xh51t4ve4ws4xu4wg4y95204w34x54y14tf4u64ue4r54tu4tm4vu4yl5r54nq4ua4rg4om3as4x452c52052756z51g56m4tq4v74up4u753452k54l57r5fh52d5204v656h59u4z55745bp5dn5hp5905dg57c5h35jy5ky55x4x25ae5h04ye5b15id5lb5qi5ev5be59d5f85kp5mw5d35bs5iz5l45gg5ic5jr5n85r95oh5mf5hx5p15s15mj5oh5fo5r95t22rw3445k54x45rm5sj5lh5m85mz5p25si5ua5v15xd5ya5z15v16355zs5tq5ud65q67n5jm5wd62h6695tt5uk5vc5vc5xy5zr60i61a62662x60i6566465kb5zu68b6ae5q95z766t6905xq5ym5xe62d5zy5z85yh61t69k6cb5b85cf5mi5nj63f63p6at6e46f06fd6g46gv6hs6fx6g96h36hf6h66hz6ia6ih6876j86dk6jl6fx6gy6kc6k56l46ia6it6ke6jq6k26ly6kk6mv6lb6ll6m56mi6n26q46o76oj6rk6kr6ky6ol6lg6mb6nd6om6ld6l56od6nz6pu6o66p56ql6ne6o46p86mi6nf6nr6ox6q16p16ou6q86pl6r56qy6rx6t86t16tg6u76v96z66w66ph6ql6ri6rz6sj6tg6t16up6te6v26vy6xp7206vm6x06y26wn6yh7286wb6xd6y96tn6ue6um6rd6u26tu6w16yt7rp6nu6rl6or52q6uf72k72872f79871o78w6ty6uf6ve6ux73c72s76u79g7fp72k7286ve76p7ae6zd77c7c97e77hx7ao7dn79l7ho7k67li76h6xa7b17hk6ym7bo7ix7lv7qq7ff7bm74t7fs7kx7ng7dn7cc7jj7lo7h07iw7kb7ns7rh7p17mn7i57pe7s87n37oo7fw7rh7ta2p22yy7kd4ua5rz7lw6uf7657qx7lp7mg7nj7pm7sq7ui7v97xl7yh7z97v983d8007ty7ul85y87v7k77wl82p86h7u17us7vk7vk7y67zz80q81h82e83580q85e84e7kv80288j8al7qm7zf8718987xx7yu7xm82l8067zg7yp82189s8cj7bs7cz7n27o383n83x8b18eb8f88fl8gc8h38i08g58gh8hb8hn8he8i78ii8ip88f8jg8dr8jt8g58h68kk8kd8lb8ii8j18km8jx8ka8m68kr8n38lj8lt8md8mq8na8qc8oe8or8rs8kz8l68os8lo8mj8nl8ou8ll8ld8ol8o78q28oe8pc8qt8nm8oc8pg8mq8nn8nz8p58q98p98p18qg8pt8rd8r68s48tg8to8t98uf8vh8ze8wd8pp8qt8rq8s78sr8to8t98ux8tm8v98w68xx9288vt8x88ya8wv8yp92g8wj8xl8yh8tv8um8uu8rk8ua8u28w98z19pu8o28oy70193g92s93492g92n99g91w99393k93097299n9g992s92g8vm96x9aa8zl97k9c59e29ii9aw9e89a59hj9kq9li96d8xi9b99hf8yu9bw9it9lu9ry9fb9c79519fn9li9nf9di9cj9jf9lk9gw9is9k69ns9sp9p19n89ip9pt9tg9n39pw9gh9sp9uh2uq34g87f4rg51988h6rl71g89k8rs91o9ky9m99n09ns9rf9u29vv9wm9yv9zra0j9wma4ma1a9r19rpa78a8n9k29vya3ya799v99w29wt9wt9zga19a20a2ra3oa4fa20a6oa569kqa1ca9babe9vba0pa7vaa09vg9ze9ywa3va1ga0q9zza3baakadb9bn9mx9p99qg9qy99t9nz9ob9uf9ura0va17a4xabtaf4ag0agdah4ahwaisagxahaai3aifai1ajcaj4ajja97akaaekaknagxahzaleal7am6ajjal4akgaksamkalmanwamdamoan8ankaogaq6am0altap7aosaptap0apmaqkamxannapaan2anzaocapeaq6ap3aowaqdapnaraaqxas1at6atkatdaucavdawaayvaydb10aybb0xawab0g"
+ST = "08c08c08o08o09009c09009o08c08r0a00b609q09j09b0aa0ax0ci0es0ge0bj0b40ca0cw0ak0jf0c308w0e30fc0fr0j00jt0o60dw0h80j80gt0ig0h00pv1011pl0mi0no0ne0rn0k10gc0l716v1bp0dg0p00wk0j90eg0jq0bz0fd0cy0bh0dy08c1h81h00w51pe0gm1qd0bq0da0ez09x0bc0hb0ir0io0k80l50mu0n70ra0dp0d30ey0fx0gw0hv0tb0yx0yq0zu08p1sm1qk0cg0ma0eb0ot0vj0nm0ru1r31xf1y61ed1q519h0dh13p0ei1fa1oj1x20i90jm0fj0kl0li0m90pn0s20r30tv0v40vx13i13b1bx1ii1ra1hf1vm1ru1ve0m20es0o40ry0ws0zm10w12613g14q16017a18k19u1b41ce1do1ey1fe1ft1g91go1h41hj1hy1ie1iu1j91jo1k41kj1ky1ld1lt1m81mn1n21ni1nx1oc1or1p61pm1q11s20lq0kp0m80k80hc0j00ks0lp0mp0n70nt0oq0ol0rn0o80rb0sm0ti0vb0sy0ur0wh0u20zh16b0s90uf0vq0st0tg0uo0k80qn0ry0kw0pd0qk0lj0q00tb0v80y816q0zm1us0wm0wy0z519416i15y0pp0x10w20p710111a0wp14l1c417f0xj0xl12017810e12n15d1ad1ek1a117319o1cw1gt1es11g13y16k1dw13a15x1cj1iq1oc1bm13x1cc1fr1hm1ie18m1961f41h517r1e41fr1jz1p71l71es1hu1lw1py1lk1mb1k21p31qw1jv1m31pf1mv1sq1v71vy1wq1xm1ye20g2181z51ns1s223t2581hn1r421s23u1rn1se1t61t61vy1xu1yl1zc2092101z523921s1h01yh25u27z1n51xu24g26l1st1vq1v929c1wa1zp1ys1x727529w1oy1qc1ro1v62bs29u2b52bp2cl2cy2dp2eh2fd2di2dv2eo2f12er2fl2fv2g226h2gt2ca2h62di2ek2hx2hq2ip2gh2g42h12hp2hd2jj2i52kg2j72iw2k12lm2mb2o42mi2la2sg2ij2ir2n82j12jw2ly2n02iy2ic2oq2nk2lk2mb2lr2pi2kw2ke2n72k32l02lc2m42n12lw2m42mo2mv2ns2nz2oq2q22qa2pv2r12s32t02t02o62p32q02qh2r12ry2rj2t02rw2tc2ww2yc2ze2vu2x92y52vh2xl30i2wj2z22zy2qh2rl2re2oj2rt2qo2tp2w73l02kx2lu2q22ua2yi20e3f03km2yu2z63062yp2zm3aw36r2sg2ya3ju31234s32r37y3b930m2yw2ux34138m2zy33e3783at3dh39636u38v3cf3fq3gj32u2vl39j3fm2z937b3dw3hk3ke3c230q3bg3ea3hz3fj39z3dn3gv3ig3a63fv3h33ke3nr3lm3fx3i63lz3oj3jf3l63dp3nv3pn2q23fa3n73k73ky3lq3p83sc3u53uw3vn3wk3xb41d4053y33n73p342r4463is3tl40p42s3qe3r63rx3rx3uw3wr3xj3ya3z73zy3xj42740p3qk3yu44s46w3r83ws43e45j3qm3uh3u048a3v33yn3xq3w546348u3oq3ps3rb3xe4aq48s4a24am4bq4bj4ca4d24e94cn4d04dk4dw4dw4eg4f04et45f4fs4b84g44cn4dp4gv4go4hn4fc4f04fw4gl4g94ih4h34je4hu4i54ip4j14l94n34kw4kk4re4hh4hp4m64hz4iu4k34lm4hw4ha4no4kp4ki4mj4nh4og4ju4jc4lt4j14jy4kb4l24lz4kv4l24lm4lt4mq4mx4np4ot4p84p04pz4r14ry4ry4n54o14oy4pf4pz4qw4qh4ry4qu4sa4w74x34y54us4vu4wr4uf4vh4wj4v54xs57k4pf4qj4qc4l94qr4pm4sn4xg5jd4jq4kn4ov4t33ng5224xs4y44yc53457r4yp4x84re5ju5gt4zc4z251353o58358n4xs4tv52x5704yp52a55n59n5cw54x53h55i5b85f45ch51q4uj56u5ff4y05675cb5i05jt5aw58b5ac5e55hd5fe58e5905di5ha57k5cv5e25j95n45kh5fc5d35l65nv5ku5kk5hk5n55oy2ua3kb5cd4ov5do5ml5jl5kd5l45o65rg5t95u05us5vo5wg60h5z95x75mf5pj61v63a5hd5qt5zu61w5pp5qg5r85r85u05vw5wn5xe5yb5z25wn61b5zt5fq5xy63w6615ge5vw62i64n5pw5ts5tb67e5uc5xr5wu5v965767y5no5oq5q95wc69u67w69769r6av6an6bf6c66dd6br6c46d06co6d06dx6e46dk64j6ew6ac6f86br6ct6g06fs6gr6eh6e46f16fd6fp6hs6ge6io6h66hg6i06jp6iw6m46lr6jd6n66gt6h06k66jo6i46kq6ls6g76gm6ky6kq6jz6li6js6ny6k66h46lz6ho6ik6ix6kj6la6kw6jh6lp6l86mm6mb6nd6op6ow6oi6po6qp6rm6rm6mt6nq6om6p46po6qk6q56t76qi6rm6v66wk6xh6ut6vv6wx6uh6w86z36vi6x46yd6p46q86q06jk6qf6pb6rz6u47e46j06jx6o557o6sd6xt6xh6y175e6xo77s6xe6r27fz6wx6yx6za71c73x7a66za6xw6qv7307746y472d75q79o7cf76y75r7857ax7d67c671t6tk77a7em6xh76a78h7gj7k37d67ad73d7dj7ff7g679v7917er7hz77x7fe7gm7jw7na7l57dd7fm7li7o17hs7ka7hu7mw7ot2yi3ko6yl4t35io7cm6o57ds7mc7hn7jw7kn7o67rh7t97u07us7vo7wg7yi7z97x77pj7sp81v83r7i47qt7zu82e7pk7qb7r37r37u07vw7wn7xe7yb7z27x781b7zt7ci7wj83w8557is7vw82i86i7pr7tn7t581w7u87xr7wu7v985p88g7np7oq7q97vp83587w89o8a88bc8b58bw8d38dz8c98cl8dn8da8di8ej8er8e784j8fi8728fv8c98da8gm8gf8hd8f38er8fn8gc8fz8i88gt8j58hl8hv8if8is8js8l68jt8jh8rb8h88hf8m68hq8ja8kc8m48hn8h18nf8ly8kg8l28k88o78il8k58le8is8jw8jp8kn8le8ks8l08lm8lr8mi8mv8nm8oy8p58or8px8qy8rv8rv8n28nz8ow8pd8py8qv8qf8s98qr8rx8wh8xd8ya8uq8vr8wt8ud8w48xq8vf8x18xx8pd8qi8qb8ku8pr8pk8sm8v28x68ku8lq6xz8yq8ye8y28xq92w97c8yh99q93t93990v96r9a28ze8xq8tu92u96y8xx92795k9aj9co98895a97o9c49ew9dc91n8ui98l9ck8yl9649dy9gs9kc9br8yu9aa9dp9fo9gf98b9989ex9g599v9fl9hi9jg9nh9ko9cv9fv9lo9o89ip9kk9i49nk9pc32q3nt8cl4xb5j08ey6sd7jc8hu8py9c89f49hw9k59kw9p49se9u69v19vs9wp9xg9z0a0a9y79i29osa2va4a9mx9rqa0ua2x9q49qv9rm9ro9ux9ww9xn9ye9zba029xoa2ba0u9pf9u7a4za669l19w6a3ia7j9qb9tr9u8a5n9va9yr9w59x1a6fa9h9om9r69ud9w29vl9of9wa9vy9x49wm9xs9xga7na67ab9acdac6acxadpaewadaadnaejae7aeeafgafnaf3a4uagea85agradaaecahiahbaiaafnah8agwagjaimai0ajjaj2aisajxak9aleamdai8ahtamialeakuallaknaoeajpakfaizaj6ak3akgal7alyal7al0am5alran2amuantap5apdaoyaq4ar6as3auoas3aw8au4awpau5aws"
 MAGIC = 1.5 * 2.0 ** 34
+MAG1 = 1.5 * 2.0 ** 23
+EXP = (("a", 1, 0, 0, 0), ("a1", 1, 0, 0, 1), ("aI", 1, 0, 1, -4096), ("m3", 1, -1, 1, -2047), ("pb", 2, 0, 2, -8192), ("ba", -1, 1, 0, 0), ("k0", -1, 1, 1, -4096),
+       ("mba", -1, 1, -1, 0), ("b", 0, 1, 0, 0), ("bI", 0, 1, 1, -4096), ("x", 0, 0, 1, 0))
+NE = len(EXP)
 
 SCRATCH = {}
 _PS = ["p%d" % i for i in range(8)]
 _B2 = ("bfloat16", "float16", "uint16")
-_CS = {n: i for i, n in enumerate("kg15 kg kr k odd r15 fm flw wf mk0 mid padt padx hc0 hc1 wa wb cw wq0 wq1 wq2 wq3 wq ucol c128 n128 c128r n128r c35 t0 t1 t2 t3 t4 t5 t6 c56 "
-                                  "r1 r2 kmax kmax2 har e1 idr nif xC a b ba inv aI bI k0 ds an1 xd wdef u1 m3 nz mba pb ws h0 h1 cs nb1".split())}
-_CI = {n: i for i, n in enumerate("ik ikg ikr iodd ni ib16".split())}
-_MB = {n: i for i, n in enumerate("ib nib d2kb dvoid d4k i2f lx0 d23 dw15 one sgn inv vc oh oh2 oha v r2 lxa hb dvc ndw15 wb1 fb1 zero".split())}
-_MH = {n: i for i, n in enumerate("i16 ni16 m2i d2k16 dn8k nh16 lj lf l2 dhf d2hf p2i dnhf p11 m11 p12 m12 pw16 pos16 f1 d16 qs16 cmn sh16 u16 pa pc la lb "
-                                  "g0 g0b g3 gr g4 g5 g6 h0 h1 hr h4 h5 f0 f1m gf".split())}
-_MF = {n: i for i, n in enumerate("ob m1 m2 m4 m5 gu b0 b1 pr0 pr1 hpr hp2 cl inn k2v rt n32 rf ta jk".split())}
+_CS = {n: i for i, n in enumerate([e[0] for e in EXP] + "h0 h1 kg15 kg kr k odd evn r15 fm flw wf mk0 mk1 mid padx wa wb cw wq0 wq1 wq2 wq3 wq ucor off noff n128 c2 c128r t0 t1 t2 t3 t4 t5 t6 "
+                                  "sc5 bi5 nfm sc1 bi1 q25 q4 id0 id1 id2 id3 diff r1 r2 kmax kmax2 pm0 pm1 wm2 c2r d2r".split())}
+_CI = {n: i for i, n in enumerate("ik ikg ikr iodd ib16".split())}
+_MB = {n: i for i, n in enumerate("ib nxb dvoid d24 i2f lx0 d23 dw15 ndw15 one sgn vd dvd oh oh2 v d4k inv lo hi r2 lxa hb wb1 zero m1b m4b d8k n8k".split())}
+_MH = {n: i for i, n in enumerate("i16 ni16 m2i d4k d2k16 n2k16 h16 lj l2 if16 dw dhf dnhf d2047 d2064 p2i p12 pw16 pos16 d16 qs16 inv cm lg sh16 u16 la lb ob16 nob16 obe obo idw hh nkr "
+                                  "g0 g0b g1 g3 gr g4 g5 g6 h0 h1 hr h4 h5 f0 f1m".split())}
+_MF = {n: i for i, n in enumerate("ob m5 gu b0 b1 rt rt1 n32 rf rf1 ta hpr jk nf".split())}
 _MI = {n: i for i, n in enumerate("ic jb ui u sq sh bk q di uq uq2 uu h".split())}
 for _a in _PS:
     SCRATCH[_a] = ("psum", [128, 512], "float32")
-for _d, _l in (("bfloat16", (("xin", P), ("tmo", TW), ("xb", P + 16), ("yo", P), ("mb", 144), ("bu0", 144), ("ncb", 32), ("bf", 144), ("bs", 144), ("bds", 144), ("be", 144),
-                             ("cb", 128 * len(_MB)), ("eq", 512), ("ab", 4 * P), ("ga", P), ("ab2", P)) + tuple(("tb%d" % k, TW + 16) for k in range(RO))),
-               ("float16", (("bdv", 144), ("bq", 144), ("bsq", 144), ("ch", 128 * len(_MH)), ("one16", 512), ("cmq", 384), ("q16", 512), ("mx", 4 * P), ("dk", 512), ("gq", P))),
-               ("float32", (("w0", NX), ("w1", NX), ("cs", 96), ("kmf", RO * M), ("cf", 128 * len(_MF)), ("mk32", 32), ("aa", 4), ("dg", 32), ("tr", 40), ("nc", 16), ("upv", 16),
-                            ("nb", 16), ("onef", 16), ("onefm", 16), ("rr", 512))),
-               ("int32", (("wti", 1), ("kmi", RO * M), ("ci", 8), ("ij", 144), ("it", 128 * len(_MI)))),
-               ("uint16", (("ql", 512), ("qsl", 128), ("hl", 128), ("nl", 2), ("xl", 2), ("pl", 128), ("msg", 128), ("land", 320)))):
+for _d, _l in (("bfloat16", (("xin", P), ("tmo", TW), ("xb", P + 16), ("yo", P), ("mb", 144), ("bu0", 144), ("ncb", 16), ("nib", 16), ("bs", 144),
+                             ("cb", 128 * len(_MB)), ("eq", 512), ("ga", P)) + tuple(("tb%d" % k, TW + W0) for k in range(RO))),
+               ("float16", (("bdv", 144), ("bq", 144), ("bsq", 144), ("bds", 144), ("be", 144), ("ch", 128 * len(_MH)), ("one16", 128), ("cmq", 384), ("q16", 512), ("mx", 4 * P), ("dk", 512),
+                            ("gq", P), ("ab", 4 * P), ("ab2", P), ("io16", 512), ("cf16", 4 * NE), ("ex", 3 * NE), ("aa2", 6), ("kr16", 4))),
+               ("float32", (("w0", NX), ("w1", NX), ("cs", 96), ("kmf", RO * M), ("cf", 128 * len(_MF)), ("mk32", 32), ("aa", 8), ("dg", 32), ("tr", 40), ("nc", 16),
+                            ("nb", 16), ("zf", 16), ("noff", 16), ("rr", 512), ("cf32", 4 * NE), ("msg", 100), ("land", 200))),
+               ("int32", (("wti", 1), ("kmi", RO * M), ("ci", 8), ("ij", 512), ("it", 128 * len(_MI)))),
+               ("uint16", (("ql", 512), ("qsl", 128), ("hl", 128), ("nl", 2), ("xl", 2), ("pl", 128), ("lu", 20)))):
     for _a, _c in _l:
         SCRATCH[_a] = ("sbuf", [128, _c], _d)
 _LK = [(t, s) for t in range(1, RO) for s in range(t)]
 SEMAPHORES = (["sv", "ss", "st", "sg", "lmsg", "lown", "lx0", "lx1", "lw", "lk", "lt0", "lt1", "lt2", "lt3"] + ["st%d" % k for k in range(4)]
-              + ["f%s%d" % (c, k) for k in range(RO) for c in "abc"] + ["fb5", "fc5", "fc6", "fc7"]
+              + ["f%s%d" % (c, k) for k in range(RO) for c in "abc"] + ["fa5", "fb5"] + ["fc%d" % k for k in range(5, 10)]
               + ["ta%d" % k for k in range(RO)] + ["ls%d" % k for k in range(4)] + ["m%d_%d" % ts for ts in _LK])
 
 
@@ -65,8 +69,8 @@ def _ps(r):
     return r[0] in _PS
 
 
-def C(n):
-    return ("cs", _CS[n], _CS[n] + 1) if n in _CS else ("ci", _CI[n], _CI[n] + 1)
+def C(n, k=1):
+    return ("cs", _CS[n], _CS[n] + k) if n in _CS else ("ci", _CI[n], _CI[n] + 1)
 
 
 def _tile(buf, names):
@@ -78,18 +82,29 @@ def _tile(buf, names):
 B, H, S, I = _tile("cb", _MB), _tile("ch", _MH), _tile("cf", _MF), _tile("it", _MI)
 
 
+_NM = {b: dict([(v, k) for k, v in d.items()] + [("w", w)]) for b, d, w in (("cb", _MB, 128), ("ch", _MH, 128), ("cf", _MF, 128), ("it", _MI, 128), ("cs", _CS, 1), ("ci", _CI, 1))}
+
+
+def col(r, k, n=1):
+    return (r[0], r[1] + k, r[1] + k + n)
+
+
 def build():
-    ops, BST, AFT, bank = [], [0.0], [], {}
-    CYC, TCY, GC = PAR["CYC"], PAR["TCY"], PAR["GC"]
+    ops, bank = [], {}
     SEC, seen_tag, PART, lds = [-1], {}, PAR["part"], {}
 
     def add(q, cost, emit, reads, writes, done=None, after=(), lat=0.0):
-        ops.append({"q": q, "cost": cost, "emit": emit, "reads": reads, "writes": writes, "done": done, "after": list(after) + AFT, "tau0": int(100 * BST[0]), "lat": lat})
-        BST[0] += 0.1
-        r = [(y[0].rstrip("0123456789") if y[0][0] in "wt" else y[0], y[1] % 32 if y[0] in ("msg", "land") else y[1]) for y in (writes + reads)[:1]]
-        k = (SEC[0], q, str(r))
-        seen_tag[k] = seen_tag.get(k, 0) + 1
-        ops[-1]["sec"], ops[-1]["tag"] = SEC[0], (SEC[0] < 0, q, str(r), seen_tag[k])
+        ops.append({"q": q, "cost": cost if isinstance(cost, tuple) else (cost, 0, 0), "emit": emit, "reads": reads, "writes": writes, "done": done, "after": list(after), "lat": lat})
+        b, c = (writes + reads)[0][:2]
+        if b in _NM:
+            b, c = _NM[b][c // _NM[b]["w"]], c % _NM[b]["w"]
+        elif b in ("msg", "land", "lu"):
+            c = c % 20 if b == "msg" else 0
+        elif b[:-1] in ("w", "tb"):
+            b = b[:-1]
+        name = "%s%s.%s%s" % ("0" if SEC[0] < 0 else "", q, b, "_%d" % c if c else "")
+        seen_tag[SEC[0], name] = k = seen_tag.get((SEC[0], name), 0) + 1
+        ops[-1]["sec"], ops[-1]["name"] = SEC[0], name + ("/%d" % k if k > 1 else "")
         return len(ops) - 1
 
     def isc(*xs):
@@ -103,38 +118,37 @@ def build():
 
     def vt(out, a, b, op):
         c = _n(out) * (1 if _ps(a) or _ps(b) else 2)
-        return add("v", max(64, c) * CYC, lambda g, T, x: g.vector.tensor_tensor(_ap(T, out), _ap(T, a), _ap(T, b), op), [a, b], [out])
+        return add("v", (0, c, 0), lambda g, T, x: g.vector.tensor_tensor(_ap(T, out), _ap(T, a), _ap(T, b), op), [a, b], [out])
 
     def vs(out, a, s1, op0, s2=None, op1=None):
         def e(g, T, x):
             if op1 is None:
                 return g.vector.tensor_scalar(_ap(T, out), _ap(T, a), val(T, s1), None, op0)
             return g.vector.tensor_scalar(_ap(T, out), _ap(T, a), val(T, s1), val(T, s2), op0, op1)
-        return add("v", max(64, _n(out) * fast(out, a)) * CYC, e, [a] + isc(s1, s2), [out])
+        return add("v", (0, _n(out) * fast(out, a), 0), e, [a] + isc(s1, s2), [out])
 
     def vcopy(out, a):
-        add("v", max(64, _n(out) * fast(out, a)) * CYC, lambda g, T, x: g.vector.tensor_copy(_ap(T, out), _ap(T, a)), [a], [out])
+        add("v", (0, _n(out) * fast(out, a), 0), lambda g, T, x: g.vector.tensor_copy(_ap(T, out), _ap(T, a)), [a], [out])
 
-    def vred(out, a, op):
-        add("v", max(64, _n(a)) * CYC, lambda g, T, x: g.vector.tensor_reduce(_ap(T, out), _ap(T, a), AX.X, op), [a], [out])
+    def vred(out, a, op, neg=False):
+        add("v", (0, _n(a), 0), lambda g, T, x: g.vector.tensor_reduce(_ap(T, out), _ap(T, a), AX.X, op, negate=neg), [a], [out])
 
     def vset(out, c):
-        add("v", max(64, _n(out)) * CYC, lambda g, T, x: g.vector.memset(_ap(T, out), c), [], [out])
+        add("v", (0, _n(out), 0), lambda g, T, x: g.vector.memset(_ap(T, out), c), [], [out])
 
     def vtr(out, a):
-        add("v", 64 * CYC, lambda g, T, x: g.vector.transpose(_ap(T, out), _ap(T, a)), [a], [out])
+        add("v", (0, 32, 0), lambda g, T, x: g.vector.transpose(_ap(T, out), _ap(T, a)), [a], [out])
 
     def vgt(out, win, off, b, op):
-        add("v", 0.05 + _n(out) * GC * CYC, lambda g, T, x: g.vector.tensor_tensor(_ap(T, out), _ap(T, win).indirect(_ap(T, off)), _ap(T, b), op), [win, off, b], [out])
+        add("v", (0, 0, _n(out)), lambda g, T, x: g.vector.tensor_tensor(_ap(T, out), _ap(T, win).indirect(_ap(T, off)), _ap(T, b), op), [win, off, b], [out])
 
     def vscat(win, off, a):
-        add("v", 0.15, lambda g, T, x: g.vector.tensor_copy(_ap(T, win).indirect(_ap(T, off)), _ap(T, a)), [a, off], [win])
+        add("v", (0.06, 0, 40), lambda g, T, x: g.vector.tensor_copy(_ap(T, win).indirect(_ap(T, off)), _ap(T, a)), [a, off], [win])
 
-    def sa(out, a, func, bias=0.0, scale=1.0):
-        return add("s", (60 + max(64, _n(out))) * CYC, lambda g, T, x: g.scalar.activation(_ap(T, out), _ap(T, a), func, bias=val(T, bias), scale=val(T, scale)), [a] + isc(bias, scale), [out])
-
-    def lin(out, a, scale, bias, func=F.Identity, n=1):
-        sa(("cs", _CS[out], _CS[out] + n), ("cs", _CS[a], _CS[a] + n), func, bias=C(bias) if isinstance(bias, str) else bias, scale=C(scale) if isinstance(scale, str) else scale)
+    def sa(out, a, func, bias=0.0, scale=1.0, acc=None):
+        if acc:
+            return add("s", (0.02, _n(out), 0), lambda g, T, x: g.scalar.activation(_ap(T, out), _ap(T, a), func, bias=bias, scale=scale, accum_out=_ap(T, acc)), [a], [acc, out])
+        return add("s", (0, _n(out), 0), lambda g, T, x: g.scalar.activation(_ap(T, out), _ap(T, a), func, bias=val(T, bias), scale=val(T, scale)), [a] + isc(bias, scale), [out])
 
     def cv(key, out, a, scale=1.0, bias=0.0):
         if key in PAR["s"]:
@@ -143,17 +157,12 @@ def build():
             return vcopy(out, a) if bias == 0.0 else vs(out, a, bias, A.add)
         return vs(out, a, scale, A.mult, bias, A.add)
 
-    def rsum(key, out, a):
-        if key in PAR["s"]:
-            add("s", (80 + _n(a)) * CYC, lambda g, T, x: g.scalar.activation(_ap(T, a), _ap(T, a), F.Identity, accum_out=_ap(T, out)), [a], [out, a])
-        else:
-            vred(out, a, A.add)
-
     def gather(q, out, win, off, bias=0.0, scale=1.0):
         if q == "v":
-            add("v", 0.05 + _n(out) * GC * CYC, lambda g, T, x: g.vector.tensor_scalar(_ap(T, out), _ap(T, win).indirect(_ap(T, off)), val(T, bias), None, A.add), [win, off] + isc(bias), [out])
+            add("v", (0, 0, _n(out)), lambda g, T, x: g.vector.tensor_scalar(_ap(T, out), _ap(T, win).indirect(_ap(T, off)), val(T, bias), None, A.add), [win, off] + isc(bias), [out])
         else:
-            add("s", 0.065 + _n(out) * GC * CYC, lambda g, T, x: g.scalar.activation(_ap(T, out), _ap(T, win).indirect(_ap(T, off)), F.Identity, bias=val(T, bias), scale=scale), [win, off] + isc(bias), [out])
+            add("s", (0, 0, _n(out)), lambda g, T, x: g.scalar.activation(_ap(T, out), _ap(T, win).indirect(_ap(T, off)), F.Identity, bias=val(T, bias), scale=val(T, scale)),
+                [win, off] + isc(bias, scale), [out])
 
     def shared(out, win, off, c0, c1, nv, bias=0.0, step=128):
         for q, lo, hi in (("v", c0, c0 + nv), ("s", c0 + nv, c1)):
@@ -161,17 +170,20 @@ def build():
                 b = min(a + step, hi)
                 gather(q, (out[0], out[1] + 16 * a, out[1] + 16 * b), win, (off, a, b), bias)
 
-    def mm(out, parts, start=True, stop=True):
+    def mm(out, parts, start=True, stop=True, free=False):
         parts = [p if len(p) == 3 else p + (out,) for p in parts]
-        cost = sum(max(64, _n(o)) * TCY * (4 if SCRATCH[l[0]][2] == "float32" else 1) for l, r, o in parts)
+        cost = sum(max(64, _n(o)) * (4 if SCRATCH[l[0]][2] == "float32" else 1) for l, r, o in parts)
 
         def e(g, T, x):
             for k, (l, r, o) in enumerate(parts):
-                i = g.tensor.matmul(_ap(T, o), _ap(T, l), _ap(T, r), start and k == 0, stop and k == len(parts) - 1)
+                i = g.tensor.matmul(_ap(T, o), _ap(T, l), _ap(T, r), start and k == 0, not ops[me]["open"] and k == len(parts) - 1)
             return i
-        i = add("t", cost, e, [y for p in parts for y in p[:2]], [out], after=[bank[out[0]]] if out[0] in bank else [])
-        ops[i]["acc"] = not start
-        bank[out[0]] = i
+        l, me = bank.setdefault(out[0], [[], []]), len(ops)
+        if not start:
+            ops[l[0][0]]["open"] = True
+        i = add("t", (0, cost / 2.0, 0), e, [y for p in parts for y in p[:2]], sorted({p[2] for p in parts}), after=l[0] + ([] if free else l[1]))
+        ops[i]["acc"], ops[i]["open"] = not start, not stop
+        bank[out[0]] = [l[0], l[1] + [i]] if free else [[i], []]
 
     def wrapped(b, src, c0, n):
         return [((b, 15 - i, 143 - i), (src, c0 + i, c0 + n, 16)) for i in range(16)]
@@ -191,14 +203,17 @@ def build():
     for k in range(1, 4):
         ld("lt%d" % k, "d" if k % 2 else "sd", ("tmo",) + TP[k], "tm", *TP[k], 3.5 + 1.5 * k)
 
-    def iota(out, pat, base, cmul):
-        add("g", 0.3, lambda g, T, x: g.iota(_ap(T, out), pat, base, cmul), [], [out])
+    def iota(out, pat, base, cmul, after=()):
+        flag = {} if SCRATCH[out[0]][2] == "int32" else {"allow_small_or_imprecise_dtypes": True}
+        return add("g", 0.13 + 2.1e-3 * _n(out), lambda g, T, x: g.iota(_ap(T, out), pat, base, cmul, **flag), [], [out], after=after)
     iota(C("ik"), [[1, 1]], 0, 1)
     iota(full("ij", 144), [[1, 144]], 0, 0)
     iota(I("ic"), [[16, 128]], 0, 0)
+    iota(("ij", 144, 512), [[1, 368]], 144, 0)
     ij, J, mb = full("ij"), full("ij", 144), full("mb", 144)
     c15, c0m = ("mb", 0, 128), ("mb", 15, 143)
-    PH, POS, IDX = ("p7", 256, 384), ("p7", 384, 512), ("p1", 384, 512)
+    one, i16, n16, pw, pos = full("one16"), H("i16"), H("ni16"), H("pw16"), H("pos16")
+    PH, POS = ("p6", 256, 384), ("p6", 384, 512)
     vs(C("ikg"), C("ik"), 112, A.bitwise_and)
     vs(C("ikr"), C("ik"), 15, A.bitwise_and)
     vcopy(C("k"), C("ik"))
@@ -210,46 +225,58 @@ def build():
     vs(C("r15"), C("kr"), 15.0, A.is_equal)
     vs(C("fm"), C("kr"), 15.0, A.is_lt)
     vs(C("mk0"), C("kr"), 0.0, A.is_equal)
+    vs(C("mk1"), C("kr"), 1.0, A.is_equal)
     vs(B("ib"), ij, C("k"), A.is_equal)
     vcopy(full("kmf", RO * M), full("kmi", RO * M))
-    vs(H("i16"), B("ib"), 1.0, A.mult)
-    vs(H("dnhf"), B("ib"), -1023.5, A.mult)
-    vset(full("one16", 512), 1.0)
+    vs(i16, B("ib"), 1.0, A.mult)
+    vset(one, 1.0)
+    vs(C("t6"), C("kr"), 10.0, A.is_lt, 384.0, A.mult)
+    vs(C("off"), C("t6"), -256.0, A.add, C("fm"), A.mult)
     vt(B("lxa"), B("ib"), c15, A.add)
-    vs(S("m1"), B("lxa"), C("fm"), A.mult)
-    vs(C("t0"), C("r15"), 1.0 / 16, A.mult)
-    vs(S("ta"), c0m, C("t0"), A.mult)
-    vt(B("lx0"), S("m1"), S("ta"), A.add)
-    vs(C("c128r"), C("mk0"), 128.0, A.mult)
-    vs(C("c128"), C("r15"), 128.0, A.mult, C("c128r"), A.add)
+    vs(B("m1b"), B("lxa"), C("fm"), A.mult)
+    vs(B("lo"), c0m, C("r15"), A.mult, 1.0 / 16, A.mult)
+    vt(B("lx0"), B("m1b"), B("lo"), A.add)
+    vs(H("idw"), B("ib"), C("mk1"), A.mult, 2.0 ** -11, A.mult)
+    cv("io", full("io16", 512), full("ij", 512), 1.0 / 16)
+    for k in range(4):
+        cv("k1", C("id%d" % k), C("mk1"), k / 64.0, C("off"))
     for c in (0, 1024):
-        vs(("xb", c, c + 1024), ("xin", c, c + 1024), C("fm"), A.mult, C("c128r"), A.add)
+        vs(("xb", c, c + 1024), ("xin", c, c + 1024), C("fm"), A.mult, C("off"), A.add)
     vset(("xb", P, P + 16), 0.0)
-    vs(H("pw16"), I("ic"), C("kr"), A.add)
-    cv("k2", PH, H("pw16"), bias=-1023.5)
-    vcopy(H("pos16"), H("pw16"))
+    vs(pw, I("ic"), C("kr"), A.add)
+    cv("k2", PH, pw, bias=-1023.5)
+    vcopy(pos, pw)
     cv("k1", C("flw"), C("fm"), 2.0, -1.0)
     cv("k1", C("t1"), C("fm"), 24576.0, -8192.0)
-    cv("k1", C("t4"), C("fm"), 32.0, -16.0)
-    for nm, cn in (("bf", "fm"), ("bs", "r15"), ("bdv", "t1"), ("bsq", "t4")):
+    for nm, cn in (("bs", "r15"), ("bdv", "t1")):
         cv("k2", full(nm, 144), mb, C(cn))
-    cv("k2", full("bds", 144), full("bf", 144), 8192.0)
-    cv("k2", full("be", 144), full("bf", 144), -2048.0)
-    diags = [(B("nib"), -1.0), (B("dvoid"), 15728640.0), (H("dn8k"), -8192.0), (B("hb"), -0.5), (B("d23"), 2.0 ** 23 + (2228224.0 if "vc" in PAR["s"] else 0.0)), (B("dvc"), 2228224.0),
-             (H("d2k16"), 2048.0), (H("ni16"), -1.0), (H("dhf"), 1023.5), (B("d4k"), 4096.0), (H("p2i"), 2.0), (H("d2hf"), 2047.0), (S("n32"), -1.0), (H("m2i"), -2.0), (H("nh16"), -0.5),
-             (H("p11"), 2.0 ** -11), (H("m11"), -2.0 ** -11), (H("p12"), 2.0 ** -12), (H("m12"), -2.0 ** -12)]
+    vs(full("bsq", 144), mb, C("flw"), A.mult, 16.0, A.mult)
+    vs(full("be", 144), mb, C("flw"), A.mult, -2048.0, A.mult)
+    cv("k2", full("bds", 144), mb, 8192.0)
+    vt(B("hi"), c15, B("ib"), A.subtract)
+    cv("k2", B("nxb"), B("hi"), C("fm"))
+    diags = [(B("dvoid"), 15728640.0), (B("d24"), -2.0 ** 24), (B("hb"), -0.5), (n16, -1.0), (H("h16"), 0.5), (H("n2k16"), -2048.0), (B("d23"), 3 * 2.0 ** 22),
+             (B("dvd"), -4456448.0), (B("d4k"), 4096.0), (H("d2047"), 2047.0), (H("dhf"), 1023.5), (H("dnhf"), -1023.5), (H("d2064"), 2064.0), (B("n8k"), -8192.0), (B("d8k"), 8192.0), (S("n32"), -1.0), (H("d2k16"), 2048.0),
+             (H("m2i"), -2.0), (H("p2i"), 2.0), (H("p12"), 2.0 ** -12)]
     for o, v in diags[:len(diags) - PAR["ng"]]:
         cv("k", o, B("ib"), v)
     vset(B("zero"), 0.0)
+    vs(H("nkr"), B("ib"), C("kr"), A.mult, -1.0, A.mult)
     vs(B("i2f"), B("ib"), C("fm"), A.mult, 2.0, A.mult)
     vset(B("one"), 1.0)
-    vset(full("onef", 16), 1.0)
-    vs(full("onefm", 16), full("onef", 16), C("fm"), A.mult)
+    vset(full("zf", 16), 0.0)
+    cv("k1", C("noff"), C("off"), -1.0)
+    cv("k1", full("noff", 16), full("zf", 16), bias=C("noff"))
     vs(I("jb"), ij, 112, A.bitwise_and)
     vcopy(C("kg"), C("ikg"))
     vs(S("ob"), I("jb"), C("kg"), A.is_equal)
     vs(C("iodd"), C("ik"), 1, A.bitwise_and)
     vcopy(C("odd"), C("iodd"))
+    cv("k2", H("ob16"), S("ob"))
+    cv("k2", H("nob16"), S("ob"), -1.0)
+    vs(I("jb"), ij, 113, A.bitwise_and)
+    vs(H("obe"), I("jb"), C("kg"), A.is_equal)
+    vs(H("obo"), I("jb"), -1.0, A.add, C("kg"), A.is_equal)
     vs(I("jb"), ij, 126, A.bitwise_and)
     vt(C("t5"), C("k"), C("odd"), A.subtract)
     vs(H("l2"), I("jb"), C("t5"), A.is_equal)
@@ -262,27 +289,35 @@ def build():
     vs(I("jb", 0, 32), ("ij", 0, 32), 16, A.bitwise_and)
     vs(full("mk32", 32), I("jb", 0, 32), C("t5"), A.is_equal)
     vset(("tr", 32, 40), 0.5)
-    cv("k1", C("padt"), C("kr"), bias=float(TW))
+    vset(("kr16", 1, 2), -1.0)
+    vset(("nib", 1, 2), 0.25)
+    cv("k2", H("if16"), B("ib"), C("fm"))
+    cv("k1", C("c128r"), C("mk0"), 128.0)
+    vs(C("n128"), C("r15"), C("mk0"), A.add, -128.0, A.mult)
+    vs(C("c2"), C("off"), 2.0, A.mult, C("c128r"), A.subtract)
+    cv("k1", C("sc5"), C("fm"), 0.5)
+    cv("k1", C("bi5"), C("fm"), -0.125)
+    cv("k1", C("nfm"), C("fm"), -1.0)
+    cv("k1", C("sc1"), C("mk1"), 32768.0)
     cv("k1", C("padx"), C("kr"), bias=float(P))
-    vset(C("hc0"), 1.0 / 32)
-    vset(C("hc1"), -1.0 / 32)
-    cv("k1", C("n128"), C("c128"), -1.0)
-    cv("k1", C("n128r"), C("c128r"), -1.0)
-    cv("k1", C("c35"), C("mk0"), 3.5)
+    vs(C("bi1"), C("mk1"), 8192.0 - P - 1, A.mult, C("padx"), A.add)
+    cv("k1", C("q4"), C("r15"), 4.0)
+    vset(C("pm0"), 1.0)
+    vset(C("pm1"), -1.0)
     vt(C("mid"), C("fm"), C("mk0"), A.subtract)
     vt(C("t5"), C("mid"), C("r15"), A.subtract)
-    cv("k2", H("la"), B("nib"), C("mid"))
+    vs(H("la"), B("ib"), C("mid"), A.mult, -1.0, A.mult)
     cv("k2", H("lb"), c0m, C("t5"))
     vt(H("lj"), H("la"), H("lb"), A.add)
-    cv("k2", S("m5"), ("bsq", 0, 128), 2.0)
-    cv("k2", S("m4"), B("ib"), C("fm"))
-    cv("k1", C("c56"), C("r15"), 56.0, C("n128r"))
-    vs(S("m2"), c0m, C("flw"), A.mult, 2.0, A.mult)
-    cv("k2", H("pc"), H("pw16"), -1.0, 2047.0)
+    vs(S("m5"), c15, C("mk0"), A.mult, 16.0, A.mult)
+    cv("k2", B("m4b"), B("ib"), C("fm"))
     vs(("aa", 0, 1), C("wf"), C("mk0"), A.mult)
     vs(("aa", 1, 2), C("wf"), C("r15"), A.mult)
-    mm(("p6", 0, 2), [(S("ob"), ("aa", 0, 2))])
-    vcopy(("cs", _CS["wa"], _CS["wa"] + 2), ("p6", 0, 2))
+    vs(C("t3"), C("wf"), C("mid"), A.mult)
+    vs(("aa", 2, 3), C("t3"), C("noff"), A.mult)
+    mm(("p5", 0, 3), [(S("ob"), ("aa", 0, 3))])
+    vcopy(C("wa", 2), ("p5", 0, 2))
+    vcopy(C("ucor"), ("p5", 2, 3))
     vs(C("cw"), C("wb"), 16.0, A.mult, C("wa"), A.subtract)
     vs(C("wq0"), C("cw"), C("flw"), A.mult)
     vs(C("wq1"), C("wf"), C("fm"), A.mult, C("wq0"), A.add)
@@ -293,49 +328,58 @@ def build():
     cv("k2", full("bq", 144), mb, C("wq"))
     vs(B("dw15"), B("ib"), C("wb"), A.mult, 0.5, A.mult)
     vs(B("ndw15"), B("ib"), C("wb"), A.mult, -0.5, A.mult)
-    cv("k2", B("fb1"), S("ob"), C("fm"))
-    cv("k2", B("wb1"), B("fb1"), C("wf"))
+    vs(B("wb1"), S("ob"), C("fm"), A.mult, C("wf"), A.mult)
     vset(("w0", 0, W0), 0.0)
     vset(("w1", 0, W0), 0.0)
-    vset(full("msg"), 0)
+    vset(full("msg", 80), 0.0)
 
+    def tab(k, c0=0, c1=TW):
+        return ("tb%d" % k, W0 + c0, W0 + c1)
     last = 0
     for k in range(4):
         r = TP[k]
-        last = add("g", 1.0, lambda g, T, x, r=r, k=k: x["send"](x["dn"], ("tb0",) + r, ("tmo",) + r, "ta0", "lown", k == 1), [("tmo",) + r], [], done=lambda x: ("lown", 0), after=[last] if k else [])
+        last = add("g", 1.0, lambda g, T, x, r=r, k=k: x["send"](x["dn"], tab(0, *r), ("tmo",) + r, "ta0", "lown", k == 1), [("tmo",) + r], [], done=lambda x: ("lown", 0), after=[last] if k else [])
     step, gc = [last], last
     for o, v in diags[len(diags) - PAR["ng"]:]:
-        gc = add("g", 0.17 + 256 * CYC, lambda g, T, x, o=o, v=v: g.affine_select(_ap(T, o), _ap(T, B("zero")), [[-1, 128]], A.not_equal, v, 0, 1), [B("zero")], [o], after=[gc])
+        gc = add("g", 0.44, lambda g, T, x, o=o, v=v: g.affine_select(_ap(T, o), _ap(T, B("zero")), [[-1, 128]], A.not_equal, v, 0, 1), [B("zero")], [o], after=[gc])
+    for k in range(4):
+        c = 0
+        while c < NE:
+            n = 1
+            while c + n < NE and EXP[c + n][k + 1] == EXP[c][k + 1]:
+                n += 1
+            gc = iota(("cf32", k * NE + c, k * NE + c + n), [[0, n]], EXP[c][k + 1], 0, [gc])
+            c += n
+    vcopy(full("cf16", 4 * NE), full("cf32", 4 * NE))
 
     def table(k, after):
-        add("x", 22.0 if k else 10.0, None, [], [("tb%d" % k, 0, TW)], done=(lambda x, k=k: ("ta%d" % k, x["ta"][k])), after=step)
+        add("x", 18.0 if k else 11.0, None, [], [tab(k)], done=(lambda x, k=k: ("ta%d" % k, x["ta"][k])), after=step)
 
         def far(g, T, x):
             if x["far"] is not None:
-                x["send"](x["far"], ("tb%d" % (RO - 1), 0, TW), full("tmo", TW), "ta%d" % (RO - 1), "lown")
+                x["send"](x["far"], tab(RO - 1), full("tmo", TW), "ta%d" % (RO - 1), "lown")
 
         def e(g, T, x):
             if x["fwd"][k] is not None:
-                x["send"](x["fwd"][k], ("tb%d" % (k + 1), 0, TW), ("tb%d" % k, 0, TW), "ta%d" % (k + 1), "ls%d" % k)
+                for c in ((0, HC), (HC, TW)) if x["cross"] else ((0, TW),):
+                    x["send"](x["fwd"][k], tab(k + 1, *c), tab(k, *c), "ta%d" % (k + 1), "ls%d" % k, c[0] > 0)
         if k < RO - 1:
-            step[0] = add("g", 1.0, e, [("tb%d" % k, 0, TW)], [], done=(lambda x, k=k: ("ls%d" % k, x["lf"][k])), after=after)
+            step[0] = add("g", 2.0, e, [tab(k)], [], done=(lambda x, k=k: ("ls%d" % k, x["lf"][k])), after=after)
         if k == 1:
             step.append(add("g", 1.0, far, [full("tmo", TW)], [], done=lambda x: ("lown", 0), after=[step[0]]))
 
     mord = []
-    Z = PAR["Z"]
-    for m, h, q, zb, fold, due in sorted(PAR["items"], key=lambda z: z[5]):
+    for m, h, q, zb in PAR["items"]:
         if m not in mord:
             mord.append(m)
-    QB = ("p2", "p4")
-    UP, FP, NF, NC = ("p3", 0, 128), ("p3", 128, 256), ("p7", 0, 128), ("p6", 132, 133)
+    QB, LP = ("p2", "p4"), {m: k for k, m in enumerate(mord)}
+    UP, NF = ("p1", 0, 128), ("p7", 0, 128)
 
     def diag(t):
         for m in mord:
             cv("dk", ("dk", m * 128, m * 128 + 128), B("ib"), ("kmf", t * M + m, t * M + m + 1))
 
     def lists(t):
-        BST[0] = Z + 4.0 if t else 3.0
         if t:
             vt(I("ui"), UP, S("gu"), A.add)
         else:
@@ -347,324 +391,269 @@ def build():
             vt(I("sq"), I("u"), I("u"), A.mult)
         cv("u16", H("u16"), I("u"), bias=-2048.0)
         vs(I("sh"), I("sq"), 5, A.arith_shift_right, 2047, A.bitwise_and)
-        cv("sh16", H("sh16"), I("sh"))
-        cv("f1", H("f1"), FP)
+        cv("sh16", H("sh16"), I("sh"), bias=-1023.5)
         for k in range(2):
-            bk = QB[k]
-            mm((bk, 0, 256), [(H("dnhf"), ("one16", 0, 256))], stop=False)
-            parts = []
-            for j in range(2):
-                m = mord[2 * k + j]
-                parts += [(("dk", m * 128, m * 128 + 128), H("u16"), (bk, j * 128, j * 128 + 128))]
-            mm((bk, 0, 256), parts, start=False, stop=False)
-            mm((bk, 0, 256), [(H("i16"), H("sh16"), (bk, j * 128, j * 128 + 128)) for j in range(2)], start=False)
-        for k, m in enumerate(mord):
-            c = (m * 128, m * 128 + 128)
-            qv = (QB[k // 2], (k % 2) * 128, (k % 2) * 128 + 128)
+            o = [(QB[k], j * 128, j * 128 + 128) for j in range(2)]
+            mm(o[0], [(("dk", mord[2 * k + j] * 128, mord[2 * k + j] * 128 + 128), H("u16"), o[j]) for j in range(2)], stop=False)
+            mm(o[0], [(i16, H("sh16"), o[j]) for j in range(2)], start=False)
+        lw = PAR["lw"]
+        for k in range(0, M, lw):
+            c = (LP[mord[k]] * 128, (LP[mord[k]] + lw) * 128)
+            qv = (QB[k // 2], (k % 2) * 128, (k % 2 + lw) * 128)
             vs(("rr",) + c, qv, MAGIC, A.add, MAGIC, A.subtract)
             vt(("q16",) + c, qv, ("rr",) + c, A.subtract)
             cv("ql", ("ql",) + c, ("q16",) + c, bias=1023.5)
 
-    BST[0] = 2.0
     diag(0)
     for c in (0, 64):
-        mm(("p3", c, c + 64), wrapped("bu0", "xin", 16 * c, 1024))
-    BST[0] = 6.0
-    for c in (0, 64):
-        mm(("p3", 128 + c, 192 + c), wrapped("bf", "xb", 16 * c, 1024))
+        mm(("p1", c, c + 64), wrapped("bu0", "xin", 16 * c, 1024))
     lists(0)
-    BST[0] = 3.0
     for k in range(4):
-        w = (("p5", "p6", "p0", "p1")[k], 0, 512)
-        o = ("w0", W0 + 512 * k, W0 + 512 * k + 512)
-        mm(w, [(B("lx0"), ("xin", 512 * k, 512 * k + 512))])
-        sa(o, w, F.Identity, bias=C("c128"))
-    cv("k2", IDX, I("ic"), bias=-float(P))
-    BST[0] = 9.0
+        w = (("p5", "p3", "p0", "p7")[k], 0, 512)
+        mm(w, [(H("idw"), full("io16", 512))], stop=False)
+        mm(w, [(B("lx0"), ("xin", 512 * k, 512 * k + 512))], start=False)
+        sa(("w0", W0 + 512 * k, W0 + 512 * k + 512), w, F.Identity, bias=C("id%d" % k))
     for c in (0, 64):
         mm(("p7", c, c + 64), wrapped("bs", "xin", 16 * c, 1024))
     sa(B("sgn"), ("p7", 0, 128), F.Identity, scale=2.0)
 
     def rows(w, r, c, src, sem):
-        add("d", 0.1, lambda g, T, x: g.sync.dma_start(T[w][r:128:16, c:c + P], _ap(T, S(src))), [S(src)], [(w, c, c + P)], done=lambda x: (sem, 16), lat=2.0)
+        add("d", 0.1, lambda g, T, x: g.sync.dma_start(T[w][r:128:16, c:c + P], _ap(T, S(src))), [S(src)], [(w, c, c + P)], done=lambda x: (sem, 16), lat=4.0)
+        ops[-1]["acc"] = ops[-1]["row"] = True
 
     msgops = {}
     for t in range(RO):
         SEC[0] = t
         w, wn = "w%d" % (t % 2), "w%d" % (1 - t % 2)
         X, XA, XF = (w, W0, W0 + P), (w, 0, NX), (w, W0 + P, NX)
-        BST[0] = 13.0
         table(t, [msgops[(s, t - 1)] for s in range(t, RO)] if t else [gc])
-        BST[0] = 13.5
-        add("d", 0.1, lambda g, T, x, w=w: g.sync.dma_start(_ap(T, S("rt")), T[w][0:128:16, W0:W0 + P]), [X], [S("rt")], done=(lambda x, t=t: ("fa%d" % t, 16)), lat=2.0)
+        for r in range(1 if t < RO - 1 else 2):
+            add("d", 0.1, lambda g, T, x, w=w, r=r: g.sync.dma_start(_ap(T, S(("rt", "rt1")[r])), T[w][r:128:16, W0:W0 + P]), [X], [S(("rt", "rt1")[r])],
+                done=(lambda x, s="fa%d" % (t + r): (s, 16)), lat=9.0)
         for k, o in enumerate([XF] if t < RO - 1 else [(wn, W0, W0 + P), (wn, W0 + P, NX)]):
-            add("d", 0.1, lambda g, T, x, X=X, o=o: g.sync.dma_start(_ap(T, o), _ap(T, X)), [X], [o], done=(lambda x, s="fb%d" % (t + k): (s, 16)), lat=5.0)
-        BST[0] = 14.6
+            add("d", 0.1, lambda g, T, x, X=X, o=o: g.sync.dma_start(_ap(T, o), _ap(T, X)), [X], [o], done=(lambda x, s="fb%d" % (t + k): (s, 16)), lat=12.0)
         for m in mord:
             c = (m * 128, m * 128 + 128)
             vt(("eq",) + c, ("q16",) + c, PH, A.is_equal)
         if t < RO - 1:
-            BST[0] = Z - 0.5
             diag(t + 1)
-        seen, ns, wait, slot = [0] * len(PART), 0, [[] for _ in PART], {0: 0, 1: 0}
-        for m, h, q, zb, fold, due in PAR["items"]:
+        seen, ns, slot = [0] * len(PART), 0, {0: 0, 1: 0}
+        for m, h, q, zb in PAR["items"]:
             h0, h1 = PART[h]
             n = h1 - h0
-            BST[0] = due
-            wc = (m * 128 + h0, m * 128 + h1)
+            wc = (LP[m] * 128 + h0, LP[m] * 128 + h1)
             o = (m * P + 16 * h0, m * P + 16 * h1)
             zz = ("p%d" % zb, slot[zb], slot[zb] + n)
             slot[zb] += n
-            parts = [(H("i16"), ("q16",) + wc), (H("l2"), ("cmq", 96 * m, 96 * m + n)), (B("dvoid"), ("eq",) + wc)]
+            parts = [(i16, ("q16",) + wc), (H("l2"), ("cmq", 96 * m, 96 * m + n)), (B("d24"), B("one", 0, n)), (B("dvoid"), ("eq",) + wc)]
+            grp = PAR["grp"]
+            if grp == 2:
+                mm(zz, parts)
+                parts = []
             if q == "v":
                 for k in range(0, n, PAR["vh"]):
                     k2 = min(n, k + PAR["vh"])
-                    BST[0] = due + k * 0.027
                     vgt(("mx", o[0] + 16 * k, o[0] + 16 * k2), X, ("ql", wc[0] + k, wc[0] + k2), ("xb", 16 * (h0 + k), 16 * (h0 + k2)), A.max)
-                BST[0] = due + 0.026 * n
-                mm(zz, parts + [(H("dn8k"), H("f1", h0, h1))], stop=False)
-                mm(zz, wrapped("bdv", "mx", o[0], 16 * n), start=False)
-                BST[0] = due + 0.026 * n + 1.0
+                mm(zz, parts + wrapped("bdv", "mx", o[0], 16 * n), free=not grp, start=not grp)
             else:
                 for k in range(0, n, PAR["sh"]):
                     k2 = min(n, k + PAR["sh"])
-                    BST[0] = due + k * 0.045
                     gather("s", ("mx", o[0] + 16 * k, o[0] + 16 * k2), X, ("ql", wc[0] + k, wc[0] + k2))
                 for lo in range(0, 16 * n, 512):
                     hi = min(16 * n, lo + 512)
                     wk = (PAR["wb"][ns % 4], 0, hi - lo)
                     ns += 1
-                    BST[0] = due + 0.5
-                    mm(wk, [(B("nib"), ("xb", 16 * h0 + lo, 16 * h0 + hi))], stop=False)
-                    BST[0] = due + 0.045 * hi / 16 - 0.5
-                    mm(wk, [(H("i16"), ("mx", o[0] + lo, o[0] + hi))], start=False)
+                    mm(wk, [(B("nxb"), ("xb", 16 * h0 + lo, 16 * h0 + hi))], stop=False)
+                    mm(wk, [(H("if16"), ("mx", o[0] + lo, o[0] + hi))], start=False)
                     sa(("ab", o[0] + lo, o[0] + hi), wk, F.Abs)
-                BST[0] = due + 0.045 * n
-                mm(zz, parts, stop=False)
-                mm(zz, wrapped("bds", "ab", o[0], 16 * n), start=False)
-                BST[0] = due + 0.045 * n + 0.9
-            wait[h].append(zz)
+                mm(zz, parts + wrapped("bds", "ab", o[0], 16 * n), free=not grp, start=not grp)
             bb = (S("b0", h0, h1), S("b1", h0, h1))
-            while fold and wait[h]:
-                zz = wait[h].pop(0)
-                seen[h] += 1
-                if seen[h] == 1:
-                    cv("fold", bb[1], zz)
-                else:
-                    vt(I("bk", h0, h1) if seen[h] == M else bb[seen[h] % 2], bb[1 - seen[h] % 2], zz, A.min)
-        BST[0] = 20.0
+            seen[h] += 1
+            if seen[h] == 1:
+                cv("fold", bb[1], zz)
+            else:
+                vt(I("bk", h0, h1) if seen[h] == M else bb[seen[h] % 2], bb[1 - seen[h] % 2], zz, A.min)
         tb = "tb%d" % t
-        TB = (tb, 0, TW)
+        TB = tab(t)
         for s in range(t):
-            i = _LK.index((t, s)) * 32
-            add("x", 3.0, None, [], [("land", i, i + 32)], done=(lambda x, s=s, t=t: ("m%d_%d" % (t, s), x["mn"][(t, s)])), after=[msgops[(t, s)]])
-            cv("upv", full("upv", 16), ("land", i + 16, i + 32))
-            vscat((tb, 0, TW + 16), ("land", i, i + 1), full("upv", 16))
-        N, SM, LG, HL = ("p6", 0, 128), ("p0", 0, 128), ("p0", 128, 256), ("p0", 256, 384)
+            i = _LK.index((t, s))
+            add("x", 7.0, None, [], [("land", 20 * i, 20 * i + 20)], done=(lambda x, s=s, t=t: ("m%d_%d" % (t, s), x["mn"][(t, s)])), after=[msgops[(t, s)]])
+            cv("lu", ("lu", 2 * i, 2 * i + 1), ("land", 20 * i, 20 * i + 1), ("land", 20 * i + 1, 20 * i + 2), C("kr"))
+            vscat((tb, 0, TW + W0), ("lu", 2 * i, 2 * i + 1), ("land", 20 * i + 4, 20 * i + 20))
+        N, SG, DQ = ("p6", 0, 128), ("p7", 128, 256), ("p7", 256, 384)
         nb = 0
         for h, c in enumerate(PART):
-            d0 = BST[0] = PAR["ds"][h]
             o, pn = 16 * c[0], 16 * (c[1] - c[0])
             US = ("p7",) + c
             vs(I("q", *c), I("bk", *c), 2047, A.bitwise_and)
             cv("qsl", ("qsl",) + c, I("q", *c))
             shared(("gq", 0), X, "qsl", c[0], c[1], PAR["xq"][h], C("n128"), step=PAR["xh"])
-            BST[0] = d0 + 1.8
-            mm(US, wrapped("bq", "gq", o, pn))
-            BST[0] = d0 + 2.5
-            cv("uq", I("uq", *c), US)
+            mm(US, wrapped("bq", "gq", o, pn), free=True)
+            cv("uq", I("uq", *c), US, bias=C("ucor"))
             vs(I("uq2", *c), I("uq", *c), 4095, A.bitwise_and)
             vt(I("uu", *c), I("uq2", *c), I("u", *c), A.mult)
             vs(I("h", *c), I("uu", *c), 4, A.arith_shift_right, 4095, A.bitwise_and)
             cv("hl", ("hl",) + c, I("h", *c))
-            BST[0] = d0 + 2.0
-            vs(I("di", *c), I("bk", *c), 13, A.arith_shift_right)
-            cv("d16", H("d16", *c), I("di", *c), -1.0, 1920.0)
-            if "vc" in PAR["s"]:
-                sa(B("vc", *c), I("di", *c), F.Sign, scale=-1.0, bias=1918.5)
-            else:
-                vs(B("vc", *c), I("di", *c), 1919.0, A.is_lt, 2.0, A.mult)
-            cv("qs16", H("qs16", *c), I("q", *c), bias=-1023.5)
-            BST[0] = d0 + 3.2
+            mm(col(SG, c[0], c[1] - c[0]), [(B("hb"), B("sgn", *c))] + wrapped("bsq", "gq", o, pn), free=True)
             shared(("ga", 0), TB, "hl", c[0], c[1], PAR["tq"][h], step=32)
             for k, lo in enumerate(range(o, o + pn, 512)):
                 hi = min(o + pn, lo + 512)
                 wk = (PAR["sb"][nb], 0, hi - lo)
                 nb += 1
-                BST[0] = d0 + 1.5
-                mm(wk, [(B("nib"), ("xb", lo, hi))], stop=False)
-                BST[0] = d0 + 2.6
+                mm(wk, [(B("nxb"), ("xb", lo, hi))], stop=False)
                 mm(wk, [(H("lj"), ("gq", lo, hi))], start=False, stop=False)
-                BST[0] = d0 + 4.2 + 0.5 * k
                 mm(wk, [(B("i2f"), ("ga", lo, hi))], start=False)
-                sa(("ab2", lo, hi), wk, F.Abs, bias=C("c128r"))
+                sa(("ab2", lo, hi), wk, F.Abs, bias=C("c2"))
+        vs(I("di"), I("bk"), 13, A.arith_shift_right)
+        cv("d16", H("d16"), I("di"))
+        cv("qs16", H("qs16"), full("qsl"), bias=-1023.5)
+        sa(B("inv"), SG, F.Abs)
+        vt(B("vd"), H("qs16"), PH, A.is_equal)
+        vt(H("cm"), H("qs16"), PH, A.min)
+        vt(H("lg"), H("qs16"), PH, A.max)
+        mm(N, [(B("d23"), B("one")), (H("n2k16"), H("d16")), (B("dvd"), B("vd")), (n16, pos)], stop=False)
         for h, c in enumerate(PART):
-            BST[0] = PAR["ds"][h] + 3.0
-            mm(("p6", 256 + c[0], 256 + c[1]), [(B("hb"), B("sgn", *c))] + wrapped("bsq", "gq", 16 * c[0], 16 * (c[1] - c[0])))
-        for h, c in enumerate(PART):
-            BST[0] = PAR["ds"][h] + 5.3
-            mm(("p6",) + c, [(B("d23"), B("one", *c)), (H("d2k16"), H("d16", *c)), (B("dvc"), B("vc", *c)), (H("ni16"), H("pos16", *c))], stop=False)
-            mm(("p6",) + c, wrapped("be", "ab2", 16 * c[0], 16 * (c[1] - c[0])), start=False)
-        BST[0] = Z - 1.0
+            mm(("p6",) + c, wrapped("be", "ab2", 16 * c[0], 16 * (c[1] - c[0])), start=False, stop=h == len(PART) - 1)
         cv("r2", B("r2"), S("rt"), 2.0)
         if t < RO - 1:
-            mm(("p7", 128, 256), [(B("ib"), B("r2")), (S("n32"), S("rt"))])
-            cv("rf", S("rf"), ("p7", 128, 256), bias=1.0 / 16)
+            mm(("p7", 384, 512), [(B("ib"), B("r2")), (S("n32"), S("rt"))], free=True)
+            cv("rf", S("rf"), ("p7", 384, 512), bias=1.0 / 16)
             rows(w, 0, W0 + P, "rf", "fc%d" % t)
         else:
-            cv("rf", S("rf"), B("r2"), 0.5, -128.0)
+            cv("rf", S("rf"), B("r2"), 0.5)
             vt(S("ta"), S("rt"), S("rf"), A.subtract)
-            cv("rf", S("gu"), S("ta"), 16.0, -2048.0)
-            cv("rf", S("hpr"), S("ta"), -16.0, 2049.0)
-            for k, (r, c, src) in enumerate(((0, W0, "rf"), (0, W0 + P, "rf"), (15, W0, "gu"), (15, W0 + P, "hpr"))):
+            cv("rf", S("gu"), S("ta"), 16.0)
+            cv("rf", S("hpr"), S("ta"), -16.0, 1.0)
+            vs(S("rf1"), S("rt1"), MAG1, A.add, MAG1, A.subtract)
+            for k, (r, c, src) in enumerate(((0, W0, "rf"), (0, W0 + P, "rf"), (15, W0, "gu"), (15, W0 + P, "hpr"), (1, W0, "rf1"), (1, W0 + P, "rf1"))):
                 rows(wn, r, c, src, "fc%d" % (t + k))
-        BST[0] = PAR["ds"][-1] + 3.6
-        SG, XE, XW, K2 = ("p6", 256, 384), ("p1", 0, 128), ("p0", 384, 512), ("p1", 128, 256)
-        one, HP = ("one16", 0, 128), ("p1", 256, 384)
+        SA, XI, LG, HH = ("p0", 0, 128), ("p0", 128, 256), ("p3", 0, 128), ("p3", 128, 256)
+        o1, hf = col(one, 0), H("h16")
+        ob, nob, dw, top = H("ob16"), H("nob16"), H("dw"), H("d2047")
+        SA2, LG2 = ("p0", 256, 384), ("p3", 256, 384)
+        mm(SA, [(i16, H("cm")), (H("dhf"), one), (B("d4k"), B("inv"), XI)])
+        parts = [(i16, H("lg"))]
         if t < RO - 1:
-            cv("hp", HP, I("h"))
-        vt(H("cmn"), H("qs16"), PH, A.min)
-        sa(B("inv"), SG, F.Abs)
-        mm(LG, [(H("i16"), H("pos16")), (H("i16"), H("qs16")), (H("ni16"), H("cmn"))])
-        mm(SM, [(H("i16"), H("cmn")), (H("dhf"), one), (B("d4k"), B("inv"))])
-        mm(HL, [(H("ni16"), H("pos16")), (H("ni16"), H("qs16")), (H("p2i"), H("cmn")), (H("dhf"), one), (H("d2hf"), one)])
-        mm(XE, [(H("ni16"), H("pos16")), (H("ni16"), H("qs16")), (H("i16"), H("cmn")), (H("d2hf"), one)])
+            cv("hh", H("hh"), full("hl"), bias=-2048.0)
+            parts += [(i16, H("hh"), HH), (H("d2064"), one, HH), (H("nkr"), one, HH)]
+        mm(LG, parts)
 
-        def highest(src, r, dst):
+        def highest(src, r, dst, oh, wm):
             vred(C(r), src, A.max)
+            vs(oh, src, C(r), A.not_equal)
             vs(full("dg", 32), full("mk32", 32), C(r), A.mult)
             vtr(full("tr", 32), full("dg", 32))
             vred(C(dst), full("tr", 33), A.max)
-
-        def fetch(oh, src, kmax, tiles, out, start):
-            vs(oh, src, C(kmax), A.is_equal)
-            for k in range(2):
-                vt(S("pr%d" % k), oh, tiles[k], A.mult)
-                rsum("aa%d" % k, ("aa", k, k + 1), S("pr%d" % k))
-            mm(out, [(S("ob"), ("aa", 0, 2))], start=start)
-        BST[0] = Z
-        A1, A2 = ("p5", 128, 130), ("p6", 128, 130)
-        aX, bX, eX, wX = ("p5", 128, 129), ("p5", 129, 130), ("p6", 128, 129), ("p6", 129, 130)
-        mm(A1, [(S("ob"), ("cs", _CS["hc0"], _CS["hc0"] + 2))], stop=False)
-        highest(N, "r1", "kmax")
-        fetch(B("oh"), N, "kmax", (SM, LG), A1, False)
-        BST[0] = Z + 1.7
-        vs(S("cl"), SM, aX, A.max, bX, A.min)
-        BST[0] = Z + 1.9
-        vt(S("inn"), S("cl"), SM, A.is_equal)
-        BST[0] = Z + 2.1
-        vt(K2, S("inn"), N, A.mult)
-        BST[0] = Z + 1.75
-        vs(C("xC"), aX, 4096.0, A.is_ge, -4096.0, A.mult)
-        vs(C("a"), aX, C("xC"), A.add, -0.5, A.add)
-        vs(C("b"), bX, 0.5, A.add)
-        vs(C("ba"), C("b"), C("a"), A.subtract)
-        vs(("nl", 0, 1), C("odd"), C("ba"), A.mult, C("a"), A.add)
-        gather("s", full("nc", 16), X, ("nl", 0, 1), bias=-0.125, scale=0.5)
-        vs(C("ni"), ("nc", 0, 1), ("nc", 1, 2), A.add)
-        cv("nif", C("nif"), C("ni"))
+            if wm:
+                vs(wm, C(r), C(dst), A.is_equal)
+        A1, EP, A2, NC, DU = ("p5", 128, 131), ("p2", 384, 384 + NE), ("p7", 132, 137), ("p4", 256, 257), ("p4", 257, 258)
+        wm = ("msg", t * 20 + 1, t * 20 + 2)
+        highest(N, "r1", "kmax", B("oh"), wm)
+        mm(SA, [(B("n8k"), B("oh")), (B("n8k"), B("oh"), XI)], start=False)
+        mm(LG, [(B("n8k"), B("oh"))] + ([(B("n8k"), B("oh"), HH)] if t < RO - 1 else []), start=False)
+        vred(("aa", 0, 1), SA, A.max)
+        vred(("aa", 2, 3), XI, A.max)
+        sa(S("jk"), LG, F.Relu, bias=1023.5, acc=("aa", 1, 2))
+        ea, eb, ei = [("aa2", k, k + 1) for k in (2, 3, 4)]
+        for k in range(3):
+            vs(("aa2", 2 + k, 3 + k), C("r1"), C("kmax"), A.is_equal, ("aa", k, k + 1), A.mult)
+        mm(A1, [(H("dnhf"), col(one, 0, 2), col(A1, 0, 2))])
+        mm(A1, [(ob, ("aa2", 2, 4), col(A1, 0, 2)), (ob, ei, col(A1, 0)), (H("obe"), ea, col(A1, 2)), (H("obo"), eb, col(A1, 2))], start=False)
+        A3 = ("p2", 400, 404)
+        mm(A3, [(B("d4k"), B("one", 0, 2), col(A3, 0, 2)), (top, o1, col(A3, 3))])
+        mm(A3, [(ob, ("aa2", 2, 4), col(A3, 0, 2)), (nob, ei, col(A3, 0)), (nob, ei, col(A3, 1)), (ob, ea, col(A3, 2)), (nob, eb, col(A3, 3)), (nob, ei, col(A3, 3))], start=False)
+        N2 = ("p1", 128, 256)
+        sa(S("nf"), N, F.Identity, scale=-1.0)
+        mm(N2, [(B("d24"), B("inv")), (S("n32"), S("nf"))])
+        vs(B("lo"), H("cm"), col(A1, 0), A.is_le)
+        vs(B("hi"), H("cm"), col(A1, 1), A.is_ge)
+        mm(N2, [(B("d24"), B("lo")), (B("d24"), B("hi"))], start=False)
         if t < RO - 1:
-            mm(NC, [(S("m2"), ("nc", 0, 1)), (S("m1"), C("nif"))])
-            cv("w15", (w, 15, 16), NC, bias=C("c35"))
+            sa(S("jk"), HH, F.Relu, acc=("msg", t * 20, t * 20 + 1))
+        ex = [("ex", k * NE, k * NE + NE) for k in range(3)]
+        if "ex" in PAR["s"]:
+            cv("aw", ("aa", 4, 7), ("aa", 0, 3), wm)
+        for k in range(3):
+            if "ex" in PAR["s"]:
+                cv("ex", ex[k], ("cf16", k * NE, k * NE + NE), ("aa", 4 + k, 5 + k))
+            else:
+                vs(ex[k], ("cf16", k * NE, k * NE + NE), ("aa", k, k + 1), A.mult, wm, A.mult)
+        mm(EP, [(ob, e) for e in ex] + [(i16, ("cf16", 3 * NE, 4 * NE))])
+        cv("nl", ("nl", 0, 1), col(A1, 2))
+        if "a" in PAR["s"]:
+            sa(C("a", NE), EP, F.Relu)
         else:
-            mm(NC, [(S("m5"), ("nc", 0, 1)), (S("m4"), C("nif"))])
-            cv("w15", (wn, 15, 16), NC, bias=C("c56"))
+            vs(C("a", NE), EP, 0.0, A.max)
+        nib = ("nib", 0, 1)
+        gather("s", full("nc", 16), X, ("nl", 0, 1), bias=C("bi5"), scale=C("sc5"))
+        gather("s", full("ncb", 16), X, ("nl", 0, 1), scale=C("nfm"))
+        sa(nib, ("nc", 0, 1), F.Identity, bias=("nc", 1, 2))
+        sa(C("diff"), ("nc", 0, 1), F.Identity, scale=2.0, bias=("ncb", 0, 1))
         if t < RO - 1:
-            BST[0] = Z + 5.6
-            vs(B("oha"), H("pos16"), C("a"), A.is_equal)
-            vt(S("hpr"), B("oha"), IDX, A.mult)
-            rsum("idr", C("idr"), S("hpr"))
-            cv("xl", ("xl", 0, 1), C("idr"), bias=C("padx"))
-            cv("nb", full("nb", 16), full("onefm", 16), scale=C("nif"))
+            mm(NC, [(B("wb1"), nib, DU), (B("wb1"), ("ncb", 0, 1), DU), (B("m1b"), nib), (B("m4b"), ("nib", 1, 2))])
+            cv("w15", (w, 15, 16), NC, bias=C("diff"))
+            sa(("xl", 0, 1), C("diff"), F.Identity, scale=C("sc1"), bias=C("bi1"))
+            sa(full("nb", 16), full("zf", 16), F.Identity, bias=nib)
             vscat(full("xb", P + 16), ("xl", 0, 1), full("nb", 16))
-            BST[0] = Z + 2.5
-            vs(H("f0"), H("pos16"), C("a"), A.is_gt, C("xC"), A.mult)
-            vs(H("f1m"), H("pos16"), C("b"), A.is_gt, C("xC"), A.mult)
-            gather("s", full("ncb", 16), X, ("nl", 0, 1))
-            vs(("ncb", 16, 17), C("ni"), ("ncb", 0, 1), A.subtract)
-            mm(("p4", 0, 2), [(B("wb1"), ("ncb", 16, 17), ("p4", 0, 1)), (B("fb1"), ("ncb", 16, 17), ("p4", 1, 2))])
-            vs(S("gu"), H("pos16"), C("a"), A.is_equal, ("p4", 0, 1), A.mult)
-            vs(H("gf"), H("pos16"), C("a"), A.is_equal, ("p4", 1, 2), A.mult)
-            mm(UP, [(H("i16"), H("u16")), (H("d2k16"), one), (B("ndw15"), B("sgn"))], stop=False)
-            mm(NF, [(B("ib"), B("sgn")), (H("p11"), H("f0")), (H("m11"), H("f1m"))])
+            vs(H("f0"), pos, col(A3, 0), A.is_gt)
+            vs(H("f1m"), pos, col(A3, 1), A.is_gt)
+            vs(S("gu"), pos, col(A3, 2), A.is_equal, DU, A.mult)
+            mm(UP, [(i16, H("u16")), (H("d2k16"), one), (B("ndw15"), B("sgn"))], stop=False)
+            mm(NF, [(B("ib"), B("sgn")), (H("m2i"), H("f0")), (H("p2i"), H("f1m"))])
             sa(B("sgn"), NF, F.Abs)
             mm(UP, [(B("dw15"), B("sgn"))], start=False)
-            mm(FP, [(H("i16"), H("f1")), (H("i16"), H("gf"))])
-        BST[0] = Z + 2.4
-        vs(B("v"), LG, C("b"), A.is_gt)
-        if "xw" in PAR["s"]:
-            lin("nb1", "b", -1.0, 0.0)
-            cv("xw", XW, HL, bias=C("nb1"))
         else:
-            vs(XW, HL, C("b"), A.subtract)
-        vt(S("k2v"), B("v"), K2, A.mult)
-        BST[0] = Z + 2.0
-        lin("inv", "xC", -1.0 / 4096, 0.0)
-        lin("xd", "xC", 1.0, 2047.0)
-        lin("aI", "a", "inv", 0.0, n=3)
-        lin("wdef", "b", -1.0, "xd", F.Relu, n=2)
-        lin("nz", "u1", 1.0, "bI")
-        cv("pa", H("pa"), H("pw16"), -1.0, C("nz"))
-        lin("m3", "xC", 2049.0 / 4096, "ba", F.Abs)
-        lin("an1", "a", -1.0, -1.0)
-        lin("pb", "aI", 2.0, 0.0)
-        BST[0] = Z + 3.6
-        pw, i16, n16 = H("pw16"), H("i16"), H("ni16")
+            mm(NC, [(B("m4b"), nib), (S("m5"), C("diff"))])
+            cv("w15", (wn, 15, 16), NC, bias=C("q4"))
+        vs(B("v"), H("lg"), col(A1, 1), A.is_le)
+        vs(H("dw"), B("ib"), col(A3, 3), A.mult, 0.0, A.max)
         vs(H("g0"), pw, C("a"), A.is_gt, C("ba"), A.mult)
-        vs(H("g0b"), pw, C("a"), A.is_gt, C("xC"), A.mult)
+        vs(H("g0b"), pw, C("a"), A.is_gt, C("x"), A.mult)
+        vs(H("g1"), pw, C("b"), A.is_gt, C("m3"), A.mult)
         vs(H("gr"), pw, C("aI"), A.max, C("bI"), A.min)
-        vs(H("g3"), pw, C("a"), A.is_equal, C("an1"), A.mult)
+        vs(H("g3"), pw, C("a"), A.is_equal, C("a1"), A.mult)
         PL = ("p5", 0, 128)
-        mm(PL, [(i16, pw), (i16, H("g0")), (H("nh16"), H("g0b")), (H("m12"), H("g0b")), (H("m2i"), H("gr")), (i16, H("g3"))], stop=False)
-        BST[0] = Z + 2.3
-        highest(K2, "r2", "kmax2")
-        BST[0] = Z + 2.9
-        fetch(B("oh2"), S("k2v"), "kmax2", (XE, XW), A2, True)
-        BST[0] = Z + 4.2
-        vs(C("ws"), wX, C("wdef"), A.subtract)
-        vs(H("g4"), H("pa"), wX, A.is_lt, C("m3"), A.mult)
-        vs(H("g5", 0, 256), H("pa", 0, 256), eX, A.is_lt, C("ws"), A.mult)
-        mm(PL, [(n16, H("g4")), (i16, H("g5")), (n16, H("g6"))], start=False)
+        mm(PL, [(i16, pw), (i16, H("g0")), (hf, H("g0b")), (H("p12"), H("g0b")), (H("m2i"), H("gr")), (n16, H("g3")), (n16, H("g1"))], stop=False)
+        mm(SA2, [(i16, H("cm")), (H("dnhf"), one), (B("d8k"), B("v")), (dw, one), (B("zero"), B("one", 0, 1), ("p0", 384, 385))])
+        mm(LG2, [(i16, H("lg")), (H("dnhf"), one), (B("d8k"), B("v"))])
+        d_, dl, t3, t2, c_ = [col(A2, k) for k in range(5)]
+        mm(A2, [(top, o1, d_), (dw, o1, dl), (dw, o1, t3), (ob, ea, t3), (top, o1, t2), (ob, ea, t2), (nob, eb, t2), (top, o1, c_), (dw, ("kr16", 1, 2), c_)], stop=False)
+        highest(N2, "r2", "kmax2", B("oh2"), None)
+        mm(SA2, [(B("d8k"), B("oh2"))], start=False)
+        mm(LG2, [(B("d8k"), B("oh2"))], start=False)
+        cc, dd = ("aa2", 0, 1), ("aa2", 1, 2)
+        vred(C("c2r"), ("p0", 256, 385), A.min, True)
+        sa(S("jk"), LG2, F.Relu, scale=-1.0, acc=C("d2r"))
+        vs(cc, C("r2"), C("kmax2"), A.is_equal, C("c2r"), A.mult)
+        vs(dd, C("r2"), C("kmax2"), A.is_equal, C("d2r"), A.mult)
+        mm(A2, [(ob, cc, dl), (ob, cc, t3), (nob, cc, c_)] + [(nob, dd, o) for o in (d_, dl, t3, t2)], start=False)
+        vs(H("g4"), pw, t3, A.is_gt, C("mba"), A.mult)
+        vs(H("g5"), pw, t2, A.is_gt, dl, A.mult)
+        vs(H("g6"), pw, d_, A.is_gt, dl, A.mult)
+        mm(PL, [(n16, H("g4")), (n16, H("g5")), (i16, H("g6"))], start=False)
         vs(full("pl"), PL, C("pb"), A.add, float(W0), A.add)
-        BST[0] = Z + 5.3
         if t < RO - 1:
             shared((wn, W0), XA, "pl", 0, 128, PAR["rv"])
             lists(t + 1)
-            BST[0] = Z + 3.8
-            lin("mba", "k0", -1.0, "ba")
-            cv("ds", C("ds"), eX, -1.0, 2047.0)
-            lin("h0", "k0", -1.0, "ws")
-            lin("h1", "k0", 1.0, "ws", n=2)
-            pos = H("pos16")
-            BST[0] = Z + 7.0
+            vs(C("h0", 2), C("pm0", 2), dl, A.mult, C("k0"), A.add)
             vs(H("h0"), pos, C("a"), A.is_gt, C("h0"), A.mult)
             vs(H("h1"), pos, C("b"), A.is_gt, C("h1"), A.mult)
             vs(H("hr"), pos, C("aI"), A.max, C("bI"), A.min)
-            vs(H("h4"), pos, C("cs"), A.is_gt, C("mba"), A.mult)
-            vs(H("h5"), pos, C("ds"), A.is_gt, C("mba"), A.mult)
-            mm(POS, [(i16, pos), (H("m2i"), H("hr")), (H("m12"), H("f0")), (H("p12"), H("f1m"))], stop=False)
-            mm(POS, [(n16, H("h0")), (i16, H("h1")), (n16, H("h4")), (i16, H("h5"))], start=False)
-            if "ph" in PAR["s"]:
-                cv("pos", pos, POS, bias=C("pb"))
-                cv("ph", PH, pos, bias=-1023.5)
-            else:
-                vs(PH, POS, C("pb"), A.add, -1023.5, A.add)
-                cv("pos", pos, POS, bias=C("pb"))
-            BST[0] = Z + 10.5
-            vt(S("hp2"), B("oh"), HP, A.mult)
-            rsum("har", C("har"), S("hp2"))
-            vs(C("e1"), C("r1"), C("kmax"), A.not_equal, C("padt"), A.mult)
-            cv("msg0", ("msg", t * 32, t * 32 + 1), C("har"), bias=C("e1"))
-            cv("msg1", ("msg", t * 32 + 16, t * 32 + 32), full("onef", 16), C("nif"), C("n128r"))
+            vs(H("h4"), pos, c_, A.is_gt, C("mba"), A.mult)
+            vs(H("h5"), pos, d_, A.is_gt, C("mba"), A.mult)
+            mm(POS, [(i16, pos), (H("m2i"), H("hr")), (i16, H("f0")), (n16, H("f1m")), (i16, H("h0")), (i16, H("h1")), (n16, H("h4")), (i16, H("h5"))])
+            vs(PH, POS, C("pb"), A.add, -1023.5, A.add)
+            cv("pos", pos, POS, bias=C("pb"))
+            sa(("msg", t * 20 + 4, t * 20 + 20), full("noff", 16), F.Identity, bias=nib)
             for t2 in range(t + 1, RO):
                 def e(g, T, x, t=t, t2=t2):
-                    i = _LK.index((t2, t)) * 32
-                    x["send"](x["user"][t2], ("land", i, i + 32), ("msg", t * 32, t * 32 + 32), "m%d_%d" % (t2, t), "lmsg")
-                msgops[(t2, t)] = add("g", 1.0, e, [("msg", t * 32, t * 32 + 32)], [], done=lambda x: ("lmsg", 0), after=step)
+                    i = _LK.index((t2, t)) * 20
+                    x["send"](x["user"][t2], ("land", i, i + 20), ("msg", t * 20, t * 20 + 20), "m%d_%d" % (t2, t), "lmsg")
+                msgops[(t2, t)] = add("g", 1.5, e, [("msg", t * 20, t * 20 + 20)], [], done=lambda x: ("lmsg", 0), after=step if t2 == t + 1 else [msgops[(t2 - 1, t)]])
         else:
             for k in range(4):
                 c = (512 * k, 512 * k + 512)
-                gather("vs"[k % 2], ("yo",) + c, (wn, 0, NX), ("pl", 32 * k, 32 * k + 32))
+                gather("vs"[k % 2], ("yo",) + c, (wn, 0, NX), ("pl", 32 * k, 32 * k + 32), C("noff"))
                 add("sd" if k % 2 else "d", 0.1, lambda g, T, x, k=k, c=c: (g.scalar if k % 2 else g.sync).dma_start(T.y[:, c[0]:c[1]], _ap(T, ("yo",) + c)), [("yo",) + c], [],
                     done=(lambda x, k=k: ("st%d" % k, 16)), lat=2.0)
     return ops
@@ -674,10 +663,105 @@ _QS = {"v": "sv", "s": "ss", "t": "st", "g": "sg"}
 _CACHE = {}
 
 
-def plan():
-    if "o" in _CACHE:
-        return _CACHE["o"]
-    WAKE, SELF = PAR["WAKE"], PAR["SELF"]
+def costs(ops, model):
+    cyc, gc, fix = model[:3]
+    out = []
+    for o in ops:
+        f, c, n = o["cost"]
+        if o["q"] in "vs" and n:
+            f += (0.05 if o["q"] == "v" else 0.065) + n * gc * cyc
+        elif o["q"] == "v":
+            f += fix + c * cyc if fix else max(64, c) * cyc
+        elif o["q"] == "s":
+            f += fix + 0.015 + c * cyc if fix else (60 + max(64, c)) * cyc
+        else:
+            f += c * cyc
+        out.append(f + 0.02)
+    return out
+
+
+def timing(ops, order, cost, wake, own):
+    fin, why, free, last = [0.0] * len(ops), [-1] * len(ops), {}, {}
+    for i in order:
+        q, after, data, banks = ops[i]["t"]
+        st, w = 0.0, -1
+        if q in free:
+            w = free[q]
+            st = fin[w]
+        for j in after:
+            if fin[j] > st:
+                st, w = fin[j], j
+        for j, lat, same in data:
+            s = fin[j] + lat + (own if same else wake)
+            if s > st:
+                st, w = s, j
+        for b in banks:
+            j = last.get(b)
+            if j is not None:
+                if j[0] != q:
+                    j[1], j[0] = j[2], q
+                if j[1] >= 0 and fin[j[1]] + wake > st:
+                    st, w = fin[j[1]] + wake, j[1]
+                j[2] = i
+            else:
+                last[b] = [q, -1, i]
+        fin[i], why[i] = st + cost[i], w
+        if q != "x":
+            free[q] = i
+    return fin, why
+
+
+def first_order(ops, succ, cost, wake, own):
+    n = len(ops)
+    way = [0.0] * n
+    for i in range(n - 1, -1, -1):
+        way[i] = cost[i] + ops[i]["lat"] + max([0.0] + [way[j] + (own if ops[j]["qq"] == ops[i]["qq"] else wake) for j in succ[i]])
+    left, est, ready = [len(o["deps"]) for o in ops], [0.0] * n, {}
+    for i in range(n):
+        if not left[i]:
+            ready.setdefault(ops[i]["qq"], []).append(i)
+    free, last, order = {}, {}, []
+    while len(order) < n:
+        best = None
+        for q, l in ready.items():
+            if l:
+                ss = [max([est[i], free.get(q, 0.0) if q != "x" else 0.0] + [t + wake for b in ops[i]["banks"] for q2, t in last.get(b, {}).items() if q2 != q]) for i in l]
+                if best is None or min(ss) < best[0]:
+                    best = (min(ss), q, l, ss)
+        m, q, l, ss = best
+        k = max((k for k in range(len(l)) if ss[k] <= m + 0.1), key=lambda k: way[l[k]])
+        i = l.pop(k)
+        order.append(i)
+        free[q] = f = ss[k] + cost[i]
+        for b in ops[i]["banks"]:
+            last.setdefault(b, {})[q] = f
+        for j in succ[i]:
+            est[j] = max(est[j], f + (ops[i]["lat"] + (own if ops[j]["qq"] == q else wake) if i in ops[j]["data"] else 0.0))
+            left[j] -= 1
+            if not left[j]:
+                ready.setdefault(ops[j]["qq"], []).append(j)
+    return order
+
+
+def moved(ops, order, pairs):
+    for i, j in pairs:
+        a, b = order.index(j), order.index(i)
+        if a >= b:
+            continue
+        need, up, stay = set(ops[i]["deps"]), [i], []
+        for k in order[b - 1:a:-1]:
+            if k in need:
+                need.update(ops[k]["deps"])
+                up.append(k)
+            else:
+                stay.append(k)
+        if j in need:
+            continue
+        order = order[:a] + up[::-1] + [j] + stay[::-1] + order[b + 1:]
+    return order
+
+
+def graph():
     ops = build()
     hist = {}
     for i, o in enumerate(ops):
@@ -686,7 +770,9 @@ def plan():
         rw = [(0, r) for r in o["reads"]] + [(1, r) for r in o["writes"]]
         for kind, r in rw:
             for (j, k2, a, b, q2) in hist.get(r[0], ()):
-                if _ps(r) and q2 == q == "t" and o["acc"]:
+                if _ps(r) and q2 == q == "t" and o["acc"] and ops[j]["open"]:
+                    continue
+                if "row" in o and "row" in ops[j] and kind and o["sec"] == ops[j]["sec"]:
                     continue
                 if (kind or k2) and a < r[2] and r[1] < b:
                     deps.add(j)
@@ -698,40 +784,35 @@ def plan():
         o["data"] = deps
         o["deps"] = sorted(deps | set(o["after"]))
         o["banks"] = sorted({r[0] for kind, r in rw if _ps(r)})
-    n = len(ops)
-    succ = [[] for _ in ops]
+        o["t"] = (q, o["after"], [(j, ops[j]["lat"], ops[j]["qq"] == q) for j in sorted(deps)], o["banks"])
+    return ops
+
+
+def plan():
+    if "o" in _CACHE:
+        return _CACHE["o"]
+    ops = graph()
+    when = {a: int(b) for a, b in (x.rsplit(":", 1) for x in WHEN.split())}
+    succ, left = [[] for _ in ops], [len(o["deps"]) for o in ops]
     for i, o in enumerate(ops):
+        o["due"] = int(ST[3 * i:3 * i + 3], 36) if len(ST) == 3 * len(ops) else when.get(o["name"], 0) + PERIOD * max(o["sec"], 0)
         for j in o["deps"]:
             succ[j].append(i)
-    tau = {TAU[k:k + 4]: int(TAU[k + 4:k + 7], 36) for k in range(0, len(TAU), 7)}
-    for i, o in enumerate(ops):
-        hv = 0
-        for ch in str(o["tag"]):
-            hv = (hv * 131 + ord(ch)) % 1679609
-        o["key"] = "".join("0123456789abcdefghijklmnopqrstuvwxyz"[hv // 36 ** k % 36] for k in range(4))
-        o["due"] = PAR["T"] * max(o["sec"], 0) + (PAR["T0"] if o["sec"] >= 0 else 0) + tau.get(o["key"], o["tau0"])
-        if len(ST) == 3 * n:
-            o["due"] = int(ST[3 * i:3 * i + 3], 36)
-    left = [len(o["deps"]) for o in ops]
-    order, fin, free, last = [], [0.0] * n, {}, {}
-    ready = [i for i in range(n) if left[i] == 0]
+    order, ready = [], [i for i in range(len(ops)) if not left[i]]
     while ready:
         i = min(ready, key=lambda k: (ops[k]["due"], k))
         ready.remove(i)
         order.append(i)
-        o = ops[i]
-        q = o["qq"]
-        o["true"] = set(o["data"])
-        for b in o["banks"]:
-            o["data"] |= {j for q2, j in last.setdefault(b, {}).items() if q2 != q}
-            last[b][q] = i
-        st = max([free.get(q, 0.0) if q != "x" else 0.0] + [fin[j] for j in o["after"]] + [fin[j] + ops[j]["lat"] + (SELF if ops[j]["qq"] == q else WAKE) for j in o["data"]])
-        fin[i] = st + o["cost"]
-        free[q] = fin[i] + 0.02
         for j in succ[i]:
             left[j] -= 1
-            if left[j] == 0:
+            if not left[j]:
                 ready.append(j)
+    last = {}
+    for i in order:
+        o = ops[i]
+        for b in o["banks"]:
+            o["data"] |= {j for q2, j in last.setdefault(b, {}).items() if q2 != o["qq"]}
+            last[b][o["qq"]] = i
     cnt = {}
     for i in order:
         o = ops[i]
@@ -739,19 +820,22 @@ def plan():
             s = o["inc"] = _QS[o["q"]]
             v = cnt[s] = cnt.get(s, 0) + 1
             o["done"] = (lambda x, s=s, v=v: (s, v))
-    _CACHE["o"] = (ops, order, cnt, max(fin), fin)
+    _CACHE["o"] = (ops, order, cnt, None)
     return _CACHE["o"]
 
 
 def links(rank, N, near, neng, send):
     def direct(r):
         return near(r + RO, r)
+
+    def count(r):
+        return neng(r, r - 1) * (1 if near(r, r - 1) else 2)
     dn, far = (rank - 1) % N, (rank - RO) % N
     x = {"send": send, "user": {t: (rank - 1 - t) % N for t in range(RO)}}
-    x["dn"], x["far"] = dn, far if direct(far) else None
+    x["dn"], x["far"], x["cross"] = dn, far if direct(far) else None, not near(rank, dn)
     x["fwd"] = [None if k == RO - 2 and direct(dn) else dn for k in range(RO - 1)]
-    x["lf"] = [0 if d is None else neng(rank, d) for d in x["fwd"]]
-    x["ta"] = [4 * neng(rank + 1, rank)] + [neng(rank + 1, rank)] * (RO - 1)
+    x["lf"] = [0 if d is None else count(rank) for d in x["fwd"]]
+    x["ta"] = [4 * neng(rank + 1, rank)] + [count(rank + 1)] * (RO - 1)
     if direct(rank):
         x["ta"][RO - 1] = neng(rank + RO, rank)
     x["mn"] = {(t, s): neng(rank + 1 + t, rank) for (t, s) in _LK}
@@ -761,6 +845,12 @@ def links(rank, N, near, neng, send):
 def rank_program(g, core, T, topo):
     rank = T.rank_of(core)
     N = len(T.cores)
+
+    def neng(a, b):
+        return len(topo.engines(T.cores[a % N], T.cores[b % N]))
+
+    def near(a, b):
+        return topo.chip(T.cores[a % N]) == topo.chip(T.cores[b % N])
 
     def aide(r):
         c, d = T.cores[r], T.cores[(r - 1) % N]
@@ -774,17 +864,15 @@ def rank_program(g, core, T, topo):
             if aide(r) == core:
                 d = T.cores[(r - 1) % N]
                 rid, pid, _ = topo.addr(d)
-                g.wait_ge(T.sem.ta0, len(spare(r)))
-                g.remote_dma(_ap(T, ("tb0",) + TP[1]), _ap(T, ("tb0",) + TP[1]), T.sem.ta0, T.sem.lown, pid, rid, topo.mask(core, d))
-                g.wait_ge(T.sem.lown, len(topo.engines(core, d)))
+                fwd = links(r, N, near, neng, None)["fwd"]
+                pieces = [(0, TP[1])] + [(k + 1, (HC, TW)) for k in range(RO - 1) if fwd[k] is not None]
+                for k, c in pieces:
+                    a = _ap(T, ("tb%d" % k, W0 + c[0], W0 + c[1]))
+                    g.wait_ge(T.sem["ta%d" % k], len(spare(r)))
+                    g.remote_dma(a, a, T.sem["ta%d" % k], T.sem.lown, pid, rid, topo.mask(core, d))
+                g.wait_ge(T.sem.lown, len(pieces) * len(topo.engines(core, d)))
         return
-    ops, order, cnt, _, _ = plan()
-
-    def neng(a, b):
-        return len(topo.engines(T.cores[a % N], T.cores[b % N]))
-
-    def near(a, b):
-        return topo.chip(T.cores[a % N]) == topo.chip(T.cores[b % N])
+    ops, order, cnt, _ = plan()
     tot = {}
 
     def send(d, out, src, rsem, lsem, aided=False):

import numpy as np
from concourse.mybir import AluOpType as A, AxisListType as AX, ActivationFunctionType as F

RO, M, P, TW = 5, 4, 2048, 4096
TP = [(0, 256), (256, 1664), (1664, 2880), (2880, TW)]
HC = 2304
W0 = 16
NX = W0 + 2 * P
PAR = {
    "part": ((0, 64), (64, 128)), "wb": ("p3", "p4", "p5", "p2"), "sb": ("p3", "p5", "p2", "p4", "p5", "p2"),
    "items": [(0, 0, "v", 0), (2, 0, "s", 1), (1, 0, "v", 0), (2, 1, "s", 0), (3, 0, "v", 1), (3, 1, "s", 1), (0, 1, "v", 1), (1, 1, "v", 0)],
    "s": "r2 rf sq u16 sh16 k k2 w15 dk ex aw pos d16 qs16 hh lu a".split(),
    "vh": 32, "sh": 64, "xh": 32, "ng": 12,
    "xq": (0, 32),
    "tq": (32, 32),
    "rv": 40,
    "grp": 2, "lw": 1,
}
MODELS = ((1.04e-3, 1.56, 0.0, 0.15, 0.06), (0.87e-3, 1.4, 0.05, 0.2, 0.15))
PERIOD = 2800
WHEN = ""
ST = "00000000c00c00o01000o01c00000f04901o01v00x01e01n02s04606n07508b03x07t03102d0az06w00004n08209p0b70aq0e20bx04v0dt0cx08s0bp0gf0nf2ak0g00h01vy0i70fc09a0p52080q10ff0km0rh03s0hm0i705i1hn0ki08603707l1gg07e1xm1sb0re1z10bg28r03908j0990150240af0b10mz0qz1091160eu12203o06f04e07208s09x0ig1jd1i61k300o28a27b00f27k04w11l10x1rt10o1rl26u29w27227s29f28i2810ah1kl1o11lp1oj2a50630d50910f30hy0j50lu0m311u1if1jm1kt1po1px1qe1re1iw1oa29029o2at1zp06b0fn0jh0ob0r50sf0tp0uz0w90xj0yt10311d12n13x15716h16x17c17s18818n19219i19y1ad1as1b71bn1c21ch1cx1dc1dr1e61el1f11fg1fv1ga1gp1h51hk1hz1ie1iu1j926l0bm0c80cu0df08v0aj0ch0de0e80eu0fk0gf0fu0hi0ga0hx0io0jj0ke0j40jy0mb0lf0mk0pd0oy0pm0qb0mq0nj0ps0e60jk0nf0cl0gp0it0de0ic0l40oc0pv0so0r51jo0rw0s817i0qj0ww0zu1h20mt0s31fv1500rw1ak1hx0ta0ta0zc15a0u30yk13l17v1in1af12i1ee1j50y50si14718p0uw13e1701ch1nt0ue0xc15z1jv1af19s1h31ia1ga1io1k01n41pg1cx1ff1l71q61lb17x1p11rc1kc1l21mb1ou1te1vp1w71x71xu1yk22z20q1z81kf1sm25i27q1hv1rt22624b1s21sj1t71t71wd1yb1yt1za20020i27423821r1jh1zi26b29f1uy1xw24q2601ss1wc1vr2b51wr25r2661yp29u2bk12z14z1f91ga2d32ex2bq2e42di2ec2e32er2f62fl2fy2fj2h82gt2gd2ht28q2ih2jb2jz2le2h72i22in2j22jh2kb2jq2l52ke2kp2l02lf2lu2oc2mg2mu2rw2lt2m22n72di2mp2nq2or2ma2lu2os2r62pu2my2oj2tm2nx2nb2ph2mj2nv2nm2oa2p02qi2p82oz2qq2pn2re2s22t62tf2tw2ve2wf2yl2x92pe2q22ri2qx2sj2td2sr2uz2t72w02y631o32y2vt2wu2xp2x932j35k32433m34h2to2um2xx2rn2ue2u52yl3373q82n92qx2tr2o32wl1pa39b3ex34934l3ib34134p3552vr2tz2uk2v63ft35t3kk3sr3492wf3ab3fo34g39j3dy3hv3t83l83db3od3tn3942x93f63jo32j3ed3hd3mh3sz38b3at3fy3u13le3js3r33sa3qa3so3u03x43zf3nq3q93v73zu3v33iq3z041c2tr33u3xl3ug3uv3vp3y942i45b45q46546q4864934ah48u3uf40x4f44hc3rv41q4bs4dx41r42542t42t45z47x48f48t49e49t4gz4cz4bd3tg48b4g64j144147i4ec4fm42e45y45c4kr4a24fh4fx4cl4jg4l63j34aq4lc4md4mp4oj4ly4nq4n44ny4np4od4os4p64pk4p54qu4qe4pz4rf4g14s34sx4tl4v04qt4ro4s94so4t34tx4tc4ur4u04ub4um4v14vg4xy4w14wg51i4vf4vn4wt4n44wb4xc4yd4vw4vg4yd50s4zg4wk4y55384xj4wx4z34w54xh4x84xw4ym5044yu4yl50c4z951051o52s53153i55056158756v4z04zo51450j52552z52d54k52s55m57s5ba5ck55f56g57b56v5c55f65bp5d85e353954857j51953z53r5875ct5zu4wv50j53d4xp3hr5675dv5e75rx5dn5eb5er55d53l54654s5pf5ff5u662c5dv5615jx5pa5e25j45nk5rh62u5uu5mx5xz6385ip56v5os5ta5c45nz5qz5w362l5hx5kf5pk63n5v05td60o61w5zw62a63l66q6915xc5zu64t69g64p5sc68m6ay2wl3qu67753d5dg69p64264g65b67v6c46ex6fc6fq6gc6hs6ip6k36if6406aj6oq6qx61h6bb6le6ni6bc6br6cf6cf6fl6hj6i06if6j06jf6ql6ml6kz6326hx6ps6sn6dn6h46nx6p86c06fk6ey6uc6jo6p36pi6m76t26ur5sp6kc6uy6vz6wb6y56vk6xc6wq6xk6xb6xz6ye6ys6z66yr70f7006zl7116pn71o72j73774l70e71a71v72a72o73i72y74d73m73x74874n75277k75n7627b375175976f6wq75x76y77z75i75277z7ad79176677r7cu77576j78o75r77376u77i78879p78g78779y78v7am7ba7ce7cn7d47em7fn7ht7gh78m79a7aq7a47br7cl7bz7e67ce7f87he7kw7m67f17g27gw7gh7lr7os7lb7mu7no7cv7du7h57av7dl7dd7ht7me89g76h77b7a55bt7cz7nh7nt81j7n97nx7oc7ez7d67ds7ee7z17p083s8by7nh7fn7tj7yv7no7sq7x68138cg84g7wj87l8cu7sb7gh7ye82w7lq7xl80l85o8c77ri7u17z68d984l82z8aa8bi89i8bv8d78gc8in86y89g8ef8j28eb81y8i88kk2qx3r98gt56760g8ja7a57n28q68do8e28ex8hg8lq8oj8oy8pc8py8qq8sb8tm8rd8dm8k58xp8zw8b38kx8uc8wh8ky8ld8m18m18p78r58rk8ry8sk8sy8zu8w48tx8co8rj8z191l8n98qq8wx8y68lm8p68ok93a8t78ym8z28w492093p82a8v593w94x95997394i96a95o96i96996x97c97q98497p99e98y98j99z8yl9an9bh9c59dj99c9a89at9b89bn9cg9bw9db9ck9cv9d69dl9e09gi9el9f09k19dz9e79fd95o9ev9fw9gx9eg9e09gx9jb9i09f49gp9ls9g39fh9hn9ep9g19fs9gg9h69in9he9h59iw9ht9jk9k89lc9ll9m29nk9ol9qr9pf9hk9i89jo9j29kp9lj9kx9n49lc9o69qc9tu9v49nz9p09pv9pf9up9xq9u99vs9wm9lt9ms9q39jt9mj9mb9qr9vdaie9ff9g97il9wr9x39wf9xfaah9w79wv9xaa7z9xyacqakw9wf9ola2ha7t9wma1oa64aa1aleadea5hagjalsa199pfa7cabu9uoa6ja9jaenal5a0ga2za84am7adjabxaj8akgaigakuam5apaarlafwaieandas0aniaawar6ati2zf3ro92m50j60v93b7cz8a29a89j39w0aq0amvanaanxaqhauoaxhaxwayaaywb0cb19b2nb0zamkat3b7ab9hak1atvb4ib62atwaubauzauzay5b03b0kb0zb1kb1zb2wb55b3jalmb0hb8cbb7aw7azob6hb7saukay4axibcwb28b7nb82b5bbbmbdbab8aj0as8atgau2amgak0akcauhav2b0jb14bevbfjbfabfabg4bfvbgjbgybhcbh7bgybigbi1bhmbj1b87bjpbkjbl7bmmbjabjvbkabkpbljbkzbmdblmblxbm9bmnbnhbofbn1bn2bp3bqqbplbnpbovbsibombo0bpwbnabo7bnybombpcbptbpnbpfbqbbq2br5brsbsxbt5btebu2bv3bvobylbyhc1cby6c13bvxc10"
ST = "08c08c08o08o09009c09009o08c08r0cl0a009b09q0c80ah0a30au0es0fj0c10cg0bm0dy0dm0jc0ei08c0bu0de0g60ig0ez0jj0f70h10io0k70ke0kl0o00uk1wt0n20x51i80r80py0dd18p1jr1iz0ce0m20o30ff0fw0ic0ge0iu0gw0hd0hv08w1ok1cc0q51ya0e61z10cn0d00iv09j0aa0js0l90mp0p80pl0w00ne18t0b80bf0bz0cy0dx0f00wr1bl1c51f708p1pu1rl0ei1ck0wk1is1p01p81pm1yp1zl20d1zt20k2570d71i10wy1p01qe25e1gx0fr0gt0fz0i90k80l50lc0s50u50wc1b61by1be1f01fw1vp1jj1r81vw25r1os0es0o40ry0ws0zm10w12613g14q16017a18k19u1b41ce1do1ey1fe1ft1g91go1h41hj1hy1ie1iu1j91jo1k41kj1ky1ld1lt1m81mn1n21ni1nx1oc1or1p61pm1q11sr0nl0k90kr0lq0hc0j00ks0lp0mm0n30nn0ok0on0pm0o50ra0qw0rs0t90qj0rg0sp0sw0tt0vt0sc0tg0ud0m40ne0tf0kl0oz0q60l80pz0s20mr0qm0va0xn0yw1gf0zm1qg0xk0x818318g17r15d0pj0rk0wo0us1a90z911a1am1cr19x0xn0s412415h0up12r17c1c71fl1bu19513b1f11ht1jn11k0wd1611d50x016o1ej1jz1od1dg15p0x81ds1il1ll19817e1gw1iu1991g91hg1lx1pf1n61kb1fs1ni1q61l81mc1cy1p41r11jc1k31kv1mx1qd1sc1t31vc1w91x01u62141xr1rl1s923p2541hk1tj20e23r1rs1sk1tb1tb1vy1xq1yh1z920520x1yh23521o1i71xt25t27v1sw1x624d26i1s01vv1ve20d1xx1x71wg21127229t16u1iu1k71l921p2992b12bl2ci2cu2dm2ed2fa2de2dr2ek2ex2eo2fh2fr2fz25o2gq2bo2h32de2eg2hu2hn2il2fr2gb2hw2h72hj2jg2i12kc2is2j32jn2jz2kj2nm2lo2m02p12i82ig2m22iy2js2ku2m42iu2in2lv2lg2nb2lo2mm2o32kw2lm2mq2k02kw2l92mf2nj2mi2mb2nq2n22on2of2pe2qj2qx2qq2rp2sr2wo2tn2mz2o32oz2ph2q12qy2qj2s72qv2sj2tg2v72zi2t32ui2vk2u52vy3232ts2uu2vr2r52rw2s32ou2rj2rc2tj2wb33m2lc2uq2p22m82rw1w232c37y3012zp2z532b31r36q2rf2rx2sw2se30232n37239o3d632n2zp2sw3463as2wv34u3cn3ek3hy3aw3b53943i13jt3lv36u2us3bc3jb2w43bz3hx3m83qd3ft34p2zp3g53kl3nt3e03cp3jx3m23he3j93ko3o63rj3pe3mb3ff3pr3sb3nh3oc3de3r53t22xk36i3hg3lc3m33nx3q03sm3us3vj3xs3yp3zg3vt43i4073tv3ui46447j3l83x442u4653tt3ul3vr3vc3yc40440w41n42k43b40w45k4423kk4084874a93v53zk46r48w3u13xw3xf42r40c3zn3yw43h49g4c73c53dc3nf3oh4444bn4df4dz4ew4f94g04gr4ho4ft4g54gz4hb4h24hv4i64id4834j44e34jh4ft4gu4k84k14kz4i64ip4ka4jl4jy4lu4kf4mr4l74lh4m14me4my4q04o24of4rc4kn4ku4o94lc4m74n94oi4l94l14o24nv4pm4ot4p04qd4na4o04p44me4nb4nn4om4pt4ox4op4q14ph4qx4qq4rp4st4t84t14tz4v14yy4vy4p94qd4ra4rs4sc4t84st4uh4t64uu4vq4xh51t4ve4ws4xu4wg4y95204w34x54y14tf4u64ue4r54tu4tm4vu4yl5r54nq4ua4rg4om3as4x452c52052756z51g56m4tq4v74up4u753452k54l57r5fh52d5204v656h59u4z55745bp5dn5hp5905dg57c5h35jy5ky55x4x25ae5h04ye5b15id5lb5qi5ev5be59d5f85kp5mw5d35bs5iz5l45gg5ic5jr5n85r95oh5mf5hx5p15s15mj5oh5fo5r95t22rw3445k54x45rm5sj5lh5m85mz5p25si5ua5v15xd5ya5z15v16355zs5tq5ud65q67n5jm5wd62h6695tt5uk5vc5vc5xy5zr60i61a62662x60i6566465kb5zu68b6ae5q95z766t6905xq5ym5xe62d5zy5z85yh61t69k6cb5b85cf5mi5nj63f63p6at6e46f06fd6g46gv6hs6fx6g96h36hf6h66hz6ia6ih6876j86dk6jl6fx6gy6kc6k56l46ia6it6ke6jq6k26ly6kk6mv6lb6ll6m56mi6n26q46o76oj6rk6kr6ky6ol6lg6mb6nd6om6ld6l56od6nz6pu6o66p56ql6ne6o46p86mi6nf6nr6ox6q16p16ou6q86pl6r56qy6rx6t86t16tg6u76v96z66w66ph6ql6ri6rz6sj6tg6t16up6te6v26vy6xp7206vm6x06y26wn6yh7286wb6xd6y96tn6ue6um6rd6u26tu6w16yt7rp6nu6rl6or52q6uf72k72872f79871o78w6ty6uf6ve6ux73c72s76u79g7fp72k7286ve76p7ae6zd77c7c97e77hx7ao7dn79l7ho7k67li76h6xa7b17hk6ym7bo7ix7lv7qq7ff7bm74t7fs7kx7ng7dn7cc7jj7lo7h07iw7kb7ns7rh7p17mn7i57pe7s87n37oo7fw7rh7ta2p22yy7kd4ua5rz7lw6uf7657qx7lp7mg7nj7pm7sq7ui7v97xl7yh7z97v983d8007ty7ul85y87v7k77wl82p86h7u17us7vk7vk7y67zz80q81h82e83580q85e84e7kv80288j8al7qm7zf8718987xx7yu7xm82l8067zg7yp82189s8cj7bs7cz7n27o383n83x8b18eb8f88fl8gc8h38i08g58gh8hb8hn8he8i78ii8ip88f8jg8dr8jt8g58h68kk8kd8lb8ii8j18km8jx8ka8m68kr8n38lj8lt8md8mq8na8qc8oe8or8rs8kz8l68os8lo8mj8nl8ou8ll8ld8ol8o78q28oe8pc8qt8nm8oc8pg8mq8nn8nz8p58q98p98p18qg8pt8rd8r68s48tg8to8t98uf8vh8ze8wd8pp8qt8rq8s78sr8to8t98ux8tm8v98w68xx9288vt8x88ya8wv8yp92g8wj8xl8yh8tv8um8uu8rk8ua8u28w98z19pu8o28oy70193g92s93492g92n99g91w99393k93097299n9g992s92g8vm96x9aa8zl97k9c59e29ii9aw9e89a59hj9kq9li96d8xi9b99hf8yu9bw9it9lu9ry9fb9c79519fn9li9nf9di9cj9jf9lk9gw9is9k69ns9sp9p19n89ip9pt9tg9n39pw9gh9sp9uh2uq34g87f4rg51988h6rl71g89k8rs91o9ky9m99n09ns9rf9u29vv9wm9yv9zra0j9wma4ma1a9r19rpa78a8n9k29vya3ya799v99w29wt9wt9zga19a20a2ra3oa4fa20a6oa569kqa1ca9babe9vba0pa7vaa09vg9ze9ywa3va1ga0q9zza3baakadb9bn9mx9p99qg9qy99t9nz9ob9uf9ura0va17a4xabtaf4ag0agdah4ahwaisagxahaai3aifai1ajcaj4ajja97akaaekaknagxahzaleal7am6ajjal4akgaksamkalmanwamdamoan8ankaogaq6am0altap7aosaptap0apmaqkamxannapaan2anzaocapeaq6ap3aowaqdapnaraaqxas1at6atkatdaucavdawaayvaydb10aybb0xawab0g"
ST = "08c08c08o08o09009c09009o08c08r0a00b609q09j09b0aa0ax0ci0es0ge0bj0b40ca0cw0ak0jf0c308w0e30fc0fr0j00jt0o60dw0h80j80gt0ig0h00pv1011pl0mi0no0ne0rn0k10gc0l716v1bp0dg0p00wk0j90eg0jq0bz0fd0cy0bh0dy08c1h81h00w51pe0gm1qd0bq0da0ez09x0bc0hb0ir0io0k80l50mu0n70ra0dp0d30ey0fx0gw0hv0tb0yx0yq0zu08p1sm1qk0cg0ma0eb0ot0vj0nm0ru1r31xf1y61ed1q519h0dh13p0ei1fa1oj1x20i90jm0fj0kl0li0m90pn0s20r30tv0v40vx13i13b1bx1ii1ra1hf1vm1ru1ve0m20es0o40ry0ws0zm10w12613g14q16017a18k19u1b41ce1do1ey1fe1ft1g91go1h41hj1hy1ie1iu1j91jo1k41kj1ky1ld1lt1m81mn1n21ni1nx1oc1or1p61pm1q11s20lq0kp0m80k80hc0j00ks0lp0mp0n70nt0oq0ol0rn0o80rb0sm0ti0vb0sy0ur0wh0u20zh16b0s90uf0vq0st0tg0uo0k80qn0ry0kw0pd0qk0lj0q00tb0v80y816q0zm1us0wm0wy0z519416i15y0pp0x10w20p710111a0wp14l1c417f0xj0xl12017810e12n15d1ad1ek1a117319o1cw1gt1es11g13y16k1dw13a15x1cj1iq1oc1bm13x1cc1fr1hm1ie18m1961f41h517r1e41fr1jz1p71l71es1hu1lw1py1lk1mb1k21p31qw1jv1m31pf1mv1sq1v71vy1wq1xm1ye20g2181z51ns1s223t2581hn1r421s23u1rn1se1t61t61vy1xu1yl1zc2092101z523921s1h01yh25u27z1n51xu24g26l1st1vq1v929c1wa1zp1ys1x727529w1oy1qc1ro1v62bs29u2b52bp2cl2cy2dp2eh2fd2di2dv2eo2f12er2fl2fv2g226h2gt2ca2h62di2ek2hx2hq2ip2gh2g42h12hp2hd2jj2i52kg2j72iw2k12lm2mb2o42mi2la2sg2ij2ir2n82j12jw2ly2n02iy2ic2oq2nk2lk2mb2lr2pi2kw2ke2n72k32l02lc2m42n12lw2m42mo2mv2ns2nz2oq2q22qa2pv2r12s32t02t02o62p32q02qh2r12ry2rj2t02rw2tc2ww2yc2ze2vu2x92y52vh2xl30i2wj2z22zy2qh2rl2re2oj2rt2qo2tp2w73l02kx2lu2q22ua2yi20e3f03km2yu2z63062yp2zm3aw36r2sg2ya3ju31234s32r37y3b930m2yw2ux34138m2zy33e3783at3dh39636u38v3cf3fq3gj32u2vl39j3fm2z937b3dw3hk3ke3c230q3bg3ea3hz3fj39z3dn3gv3ig3a63fv3h33ke3nr3lm3fx3i63lz3oj3jf3l63dp3nv3pn2q23fa3n73k73ky3lq3p83sc3u53uw3vn3wk3xb41d4053y33n73p342r4463is3tl40p42s3qe3r63rx3rx3uw3wr3xj3ya3z73zy3xj42740p3qk3yu44s46w3r83ws43e45j3qm3uh3u048a3v33yn3xq3w546348u3oq3ps3rb3xe4aq48s4a24am4bq4bj4ca4d24e94cn4d04dk4dw4dw4eg4f04et45f4fs4b84g44cn4dp4gv4go4hn4fc4f04fw4gl4g94ih4h34je4hu4i54ip4j14l94n34kw4kk4re4hh4hp4m64hz4iu4k34lm4hw4ha4no4kp4ki4mj4nh4og4ju4jc4lt4j14jy4kb4l24lz4kv4l24lm4lt4mq4mx4np4ot4p84p04pz4r14ry4ry4n54o14oy4pf4pz4qw4qh4ry4qu4sa4w74x34y54us4vu4wr4uf4vh4wj4v54xs57k4pf4qj4qc4l94qr4pm4sn4xg5jd4jq4kn4ov4t33ng5224xs4y44yc53457r4yp4x84re5ju5gt4zc4z251353o58358n4xs4tv52x5704yp52a55n59n5cw54x53h55i5b85f45ch51q4uj56u5ff4y05675cb5i05jt5aw58b5ac5e55hd5fe58e5905di5ha57k5cv5e25j95n45kh5fc5d35l65nv5ku5kk5hk5n55oy2ua3kb5cd4ov5do5ml5jl5kd5l45o65rg5t95u05us5vo5wg60h5z95x75mf5pj61v63a5hd5qt5zu61w5pp5qg5r85r85u05vw5wn5xe5yb5z25wn61b5zt5fq5xy63w6615ge5vw62i64n5pw5ts5tb67e5uc5xr5wu5v965767y5no5oq5q95wc69u67w69769r6av6an6bf6c66dd6br6c46d06co6d06dx6e46dk64j6ew6ac6f86br6ct6g06fs6gr6eh6e46f16fd6fp6hs6ge6io6h66hg6i06jp6iw6m46lr6jd6n66gt6h06k66jo6i46kq6ls6g76gm6ky6kq6jz6li6js6ny6k66h46lz6ho6ik6ix6kj6la6kw6jh6lp6l86mm6mb6nd6op6ow6oi6po6qp6rm6rm6mt6nq6om6p46po6qk6q56t76qi6rm6v66wk6xh6ut6vv6wx6uh6w86z36vi6x46yd6p46q86q06jk6qf6pb6rz6u47e46j06jx6o557o6sd6xt6xh6y175e6xo77s6xe6r27fz6wx6yx6za71c73x7a66za6xw6qv7307746y472d75q79o7cf76y75r7857ax7d67c671t6tk77a7em6xh76a78h7gj7k37d67ad73d7dj7ff7g679v7917er7hz77x7fe7gm7jw7na7l57dd7fm7li7o17hs7ka7hu7mw7ot2yi3ko6yl4t35io7cm6o57ds7mc7hn7jw7kn7o67rh7t97u07us7vo7wg7yi7z97x77pj7sp81v83r7i47qt7zu82e7pk7qb7r37r37u07vw7wn7xe7yb7z27x781b7zt7ci7wj83w8557is7vw82i86i7pr7tn7t581w7u87xr7wu7v985p88g7np7oq7q97vp83587w89o8a88bc8b58bw8d38dz8c98cl8dn8da8di8ej8er8e784j8fi8728fv8c98da8gm8gf8hd8f38er8fn8gc8fz8i88gt8j58hl8hv8if8is8js8l68jt8jh8rb8h88hf8m68hq8ja8kc8m48hn8h18nf8ly8kg8l28k88o78il8k58le8is8jw8jp8kn8le8ks8l08lm8lr8mi8mv8nm8oy8p58or8px8qy8rv8rv8n28nz8ow8pd8py8qv8qf8s98qr8rx8wh8xd8ya8uq8vr8wt8ud8w48xq8vf8x18xx8pd8qi8qb8ku8pr8pk8sm8v28x68ku8lq6xz8yq8ye8y28xq92w97c8yh99q93t93990v96r9a28ze8xq8tu92u96y8xx92795k9aj9co98895a97o9c49ew9dc91n8ui98l9ck8yl9649dy9gs9kc9br8yu9aa9dp9fo9gf98b9989ex9g599v9fl9hi9jg9nh9ko9cv9fv9lo9o89ip9kk9i49nk9pc32q3nt8cl4xb5j08ey6sd7jc8hu8py9c89f49hw9k59kw9p49se9u69v19vs9wp9xg9z0a0a9y79i29osa2va4a9mx9rqa0ua2x9q49qv9rm9ro9ux9ww9xn9ye9zba029xoa2ba0u9pf9u7a4za669l19w6a3ia7j9qb9tr9u8a5n9va9yr9w59x1a6fa9h9om9r69ud9w29vl9of9wa9vy9x49wm9xs9xga7na67ab9acdac6acxadpaewadaadnaejae7aeeafgafnaf3a4uagea85agradaaecahiahbaiaafnah8agwagjaimai0ajjaj2aisajxak9aleamdai8ahtamialeakuallaknaoeajpakfaizaj6ak3akgal7alyal7al0am5alran2amuantap5apdaoyaq4ar6as3auoas3aw8au4awpau5aws"
MAGIC = 1.5 * 2.0 ** 34
MAG1 = 1.5 * 2.0 ** 23
EXP = (("a", 1, 0, 0, 0), ("a1", 1, 0, 0, 1), ("aI", 1, 0, 1, -4096), ("m3", 1, -1, 1, -2047), ("pb", 2, 0, 2, -8192), ("ba", -1, 1, 0, 0), ("k0", -1, 1, 1, -4096),
       ("mba", -1, 1, -1, 0), ("b", 0, 1, 0, 0), ("bI", 0, 1, 1, -4096), ("x", 0, 0, 1, 0))
NE = len(EXP)

SCRATCH = {}
_PS = ["p%d" % i for i in range(8)]
_B2 = ("bfloat16", "float16", "uint16")
_CS = {n: i for i, n in enumerate([e[0] for e in EXP] + "h0 h1 kg15 kg kr k odd evn r15 fm flw wf mk0 mk1 mid padx wa wb cw wq0 wq1 wq2 wq3 wq ucor off noff n128 c2 c128r t0 t1 t2 t3 t4 t5 t6 "
                                  "sc5 bi5 nfm sc1 bi1 q25 q4 id0 id1 id2 id3 diff r1 r2 kmax kmax2 pm0 pm1 wm2 c2r d2r".split())}
_CI = {n: i for i, n in enumerate("ik ikg ikr iodd ib16".split())}
_MB = {n: i for i, n in enumerate("ib nxb dvoid d24 i2f lx0 d23 dw15 ndw15 one sgn vd dvd oh oh2 v d4k inv lo hi r2 lxa hb wb1 zero m1b m4b d8k n8k".split())}
_MH = {n: i for i, n in enumerate("i16 ni16 m2i d4k d2k16 n2k16 h16 lj l2 if16 dw dhf dnhf d2047 d2064 p2i p12 pw16 pos16 d16 qs16 inv cm lg sh16 u16 la lb ob16 nob16 obe obo idw hh nkr "
                                  "g0 g0b g1 g3 gr g4 g5 g6 h0 h1 hr h4 h5 f0 f1m".split())}
_MF = {n: i for i, n in enumerate("ob m5 gu b0 b1 rt rt1 n32 rf rf1 ta hpr jk nf".split())}
_MI = {n: i for i, n in enumerate("ic jb ui u sq sh bk q di uq uq2 uu h".split())}
for _a in _PS:
    SCRATCH[_a] = ("psum", [128, 512], "float32")
for _d, _l in (("bfloat16", (("xin", P), ("tmo", TW), ("xb", P + 16), ("yo", P), ("mb", 144), ("bu0", 144), ("ncb", 16), ("nib", 16), ("bs", 144),
                             ("cb", 128 * len(_MB)), ("eq", 512), ("ga", P)) + tuple(("tb%d" % k, TW + W0) for k in range(RO))),
               ("float16", (("bdv", 144), ("bq", 144), ("bsq", 144), ("bds", 144), ("be", 144), ("ch", 128 * len(_MH)), ("one16", 128), ("cmq", 384), ("q16", 512), ("mx", 4 * P), ("dk", 512),
                            ("gq", P), ("ab", 4 * P), ("ab2", P), ("io16", 512), ("cf16", 4 * NE), ("ex", 3 * NE), ("aa2", 6), ("kr16", 4))),
               ("float32", (("w0", NX), ("w1", NX), ("cs", 96), ("kmf", RO * M), ("cf", 128 * len(_MF)), ("mk32", 32), ("aa", 8), ("dg", 32), ("tr", 40), ("nc", 16),
                            ("nb", 16), ("zf", 16), ("noff", 16), ("rr", 512), ("cf32", 4 * NE), ("msg", 100), ("land", 200))),
               ("int32", (("wti", 1), ("kmi", RO * M), ("ci", 8), ("ij", 512), ("it", 128 * len(_MI)))),
               ("uint16", (("ql", 512), ("qsl", 128), ("hl", 128), ("nl", 2), ("xl", 2), ("pl", 128), ("lu", 20)))):
    for _a, _c in _l:
        SCRATCH[_a] = ("sbuf", [128, _c], _d)
_LK = [(t, s) for t in range(1, RO) for s in range(t)]
SEMAPHORES = (["sv", "ss", "st", "sg", "lmsg", "lown", "lx0", "lx1", "lw", "lk", "lt0", "lt1", "lt2", "lt3"] + ["st%d" % k for k in range(4)]
              + ["f%s%d" % (c, k) for k in range(RO) for c in "abc"] + ["fa5", "fb5"] + ["fc%d" % k for k in range(5, 10)]
              + ["ta%d" % k for k in range(RO)] + ["ls%d" % k for k in range(4)] + ["m%d_%d" % ts for ts in _LK])


def _ap(T, r):
    return T[r[0]][:, r[1]:r[2]] if len(r) == 3 else T[r[0]][:, r[1]:r[2]:r[3]]


def _n(r):
    return r[2] - r[1]


def _ps(r):
    return r[0] in _PS


def C(n, k=1):
    return ("cs", _CS[n], _CS[n] + k) if n in _CS else ("ci", _CI[n], _CI[n] + 1)


def _tile(buf, names):
    def f(n, c0=0, c1=128):
        return (buf, names[n] * 128 + c0, names[n] * 128 + c1)
    return f


B, H, S, I = _tile("cb", _MB), _tile("ch", _MH), _tile("cf", _MF), _tile("it", _MI)


_NM = {b: dict([(v, k) for k, v in d.items()] + [("w", w)]) for b, d, w in (("cb", _MB, 128), ("ch", _MH, 128), ("cf", _MF, 128), ("it", _MI, 128), ("cs", _CS, 1), ("ci", _CI, 1))}


def col(r, k, n=1):
    return (r[0], r[1] + k, r[1] + k + n)


def build():
    ops, bank = [], {}
    SEC, seen_tag, PART, lds = [-1], {}, PAR["part"], {}

    def add(q, cost, emit, reads, writes, done=None, after=(), lat=0.0):
        ops.append({"q": q, "cost": cost if isinstance(cost, tuple) else (cost, 0, 0), "emit": emit, "reads": reads, "writes": writes, "done": done, "after": list(after), "lat": lat})
        b, c = (writes + reads)[0][:2]
        if b in _NM:
            b, c = _NM[b][c // _NM[b]["w"]], c % _NM[b]["w"]
        elif b in ("msg", "land", "lu"):
            c = c % 20 if b == "msg" else 0
        elif b[:-1] in ("w", "tb"):
            b = b[:-1]
        name = "%s%s.%s%s" % ("0" if SEC[0] < 0 else "", q, b, "_%d" % c if c else "")
        seen_tag[SEC[0], name] = k = seen_tag.get((SEC[0], name), 0) + 1
        ops[-1]["sec"], ops[-1]["name"] = SEC[0], name + ("/%d" % k if k > 1 else "")
        return len(ops) - 1

    def isc(*xs):
        return [x for x in xs if isinstance(x, tuple)]

    def val(T, x):
        return _ap(T, x) if isinstance(x, tuple) else x

    def fast(*rs):
        return 0.5 if all((not _ps(r)) and SCRATCH[r[0]][2] in _B2 for r in rs) else 1.0

    def vt(out, a, b, op):
        c = _n(out) * (1 if _ps(a) or _ps(b) else 2)
        return add("v", (0, c, 0), lambda g, T, x: g.vector.tensor_tensor(_ap(T, out), _ap(T, a), _ap(T, b), op), [a, b], [out])

    def vs(out, a, s1, op0, s2=None, op1=None):
        def e(g, T, x):
            if op1 is None:
                return g.vector.tensor_scalar(_ap(T, out), _ap(T, a), val(T, s1), None, op0)
            return g.vector.tensor_scalar(_ap(T, out), _ap(T, a), val(T, s1), val(T, s2), op0, op1)
        return add("v", (0, _n(out) * fast(out, a), 0), e, [a] + isc(s1, s2), [out])

    def vcopy(out, a):
        add("v", (0, _n(out) * fast(out, a), 0), lambda g, T, x: g.vector.tensor_copy(_ap(T, out), _ap(T, a)), [a], [out])

    def vred(out, a, op, neg=False):
        add("v", (0, _n(a), 0), lambda g, T, x: g.vector.tensor_reduce(_ap(T, out), _ap(T, a), AX.X, op, negate=neg), [a], [out])

    def vset(out, c):
        add("v", (0, _n(out), 0), lambda g, T, x: g.vector.memset(_ap(T, out), c), [], [out])

    def vtr(out, a):
        add("v", (0, 32, 0), lambda g, T, x: g.vector.transpose(_ap(T, out), _ap(T, a)), [a], [out])

    def vgt(out, win, off, b, op):
        add("v", (0, 0, _n(out)), lambda g, T, x: g.vector.tensor_tensor(_ap(T, out), _ap(T, win).indirect(_ap(T, off)), _ap(T, b), op), [win, off, b], [out])

    def vscat(win, off, a):
        add("v", (0.06, 0, 40), lambda g, T, x: g.vector.tensor_copy(_ap(T, win).indirect(_ap(T, off)), _ap(T, a)), [a, off], [win])

    def sa(out, a, func, bias=0.0, scale=1.0, acc=None):
        if acc:
            return add("s", (0.02, _n(out), 0), lambda g, T, x: g.scalar.activation(_ap(T, out), _ap(T, a), func, bias=bias, scale=scale, accum_out=_ap(T, acc)), [a], [acc, out])
        return add("s", (0, _n(out), 0), lambda g, T, x: g.scalar.activation(_ap(T, out), _ap(T, a), func, bias=val(T, bias), scale=val(T, scale)), [a] + isc(bias, scale), [out])

    def cv(key, out, a, scale=1.0, bias=0.0):
        if key in PAR["s"]:
            return sa(out, a, F.Identity, bias=bias, scale=scale)
        if scale == 1.0:
            return vcopy(out, a) if bias == 0.0 else vs(out, a, bias, A.add)
        return vs(out, a, scale, A.mult, bias, A.add)

    def gather(q, out, win, off, bias=0.0, scale=1.0):
        if q == "v":
            add("v", (0, 0, _n(out)), lambda g, T, x: g.vector.tensor_scalar(_ap(T, out), _ap(T, win).indirect(_ap(T, off)), val(T, bias), None, A.add), [win, off] + isc(bias), [out])
        else:
            add("s", (0, 0, _n(out)), lambda g, T, x: g.scalar.activation(_ap(T, out), _ap(T, win).indirect(_ap(T, off)), F.Identity, bias=val(T, bias), scale=val(T, scale)),
                [win, off] + isc(bias, scale), [out])

    def shared(out, win, off, c0, c1, nv, bias=0.0, step=128):
        for q, lo, hi in (("v", c0, c0 + nv), ("s", c0 + nv, c1)):
            for a in range(lo, hi, step):
                b = min(a + step, hi)
                gather(q, (out[0], out[1] + 16 * a, out[1] + 16 * b), win, (off, a, b), bias)

    def mm(out, parts, start=True, stop=True, free=False):
        parts = [p if len(p) == 3 else p + (out,) for p in parts]
        cost = sum(max(64, _n(o)) * (4 if SCRATCH[l[0]][2] == "float32" else 1) for l, r, o in parts)

        def e(g, T, x):
            for k, (l, r, o) in enumerate(parts):
                i = g.tensor.matmul(_ap(T, o), _ap(T, l), _ap(T, r), start and k == 0, not ops[me]["open"] and k == len(parts) - 1)
            return i
        l, me = bank.setdefault(out[0], [[], []]), len(ops)
        if not start:
            ops[l[0][0]]["open"] = True
        i = add("t", (0, cost / 2.0, 0), e, [y for p in parts for y in p[:2]], sorted({p[2] for p in parts}), after=l[0] + ([] if free else l[1]))
        ops[i]["acc"], ops[i]["open"] = not start, not stop
        bank[out[0]] = [l[0], l[1] + [i]] if free else [[i], []]

    def wrapped(b, src, c0, n):
        return [((b, 15 - i, 143 - i), (src, c0 + i, c0 + n, 16)) for i in range(16)]

    def ld(sem, q, out, src, c0, c1, lat=2.0):
        lds[q] = add(q, 0.1, lambda g, T, x: (g.sync if q == "d" else g.scalar).dma_start(_ap(T, out), T[src][:, c0:c1]), [], [out], done=lambda x: (sem, 16), lat=lat,
                     after=[lds[q]] if q in lds else [])

    def full(n, c=128):
        return (n, 0, c)

    ld("lt0", "sd", ("tmo",) + TP[0], "tm", *TP[0])
    ld("lw", "d", ("wti", 0, 1), "wt", 0, 1)
    ld("lx0", "d", ("xin", 0, 1024), "x", 0, 1024, 2.8)
    ld("lx1", "sd", ("xin", 1024, P), "x", 1024, P, 3.4)
    ld("lk", "d", ("kmi", 0, RO * M), "km", 0, RO * M, 3.4)
    for k in range(1, 4):
        ld("lt%d" % k, "d" if k % 2 else "sd", ("tmo",) + TP[k], "tm", *TP[k], 3.5 + 1.5 * k)

    def iota(out, pat, base, cmul, after=()):
        flag = {} if SCRATCH[out[0]][2] == "int32" else {"allow_small_or_imprecise_dtypes": True}
        return add("g", 0.13 + 2.1e-3 * _n(out), lambda g, T, x: g.iota(_ap(T, out), pat, base, cmul, **flag), [], [out], after=after)
    iota(C("ik"), [[1, 1]], 0, 1)
    iota(full("ij", 144), [[1, 144]], 0, 0)
    iota(I("ic"), [[16, 128]], 0, 0)
    iota(("ij", 144, 512), [[1, 368]], 144, 0)
    ij, J, mb = full("ij"), full("ij", 144), full("mb", 144)
    c15, c0m = ("mb", 0, 128), ("mb", 15, 143)
    one, i16, n16, pw, pos = full("one16"), H("i16"), H("ni16"), H("pw16"), H("pos16")
    PH, POS = ("p6", 256, 384), ("p6", 384, 512)
    vs(C("ikg"), C("ik"), 112, A.bitwise_and)
    vs(C("ikr"), C("ik"), 15, A.bitwise_and)
    vcopy(C("k"), C("ik"))
    vcopy(C("kr"), C("ikr"))
    vs(C("kg15"), C("ikg"), 15.0, A.add)
    vs(mb, J, C("kg15"), A.is_equal)
    vcopy(C("wf"), full("wti", 1))
    vs(full("bu0", 144), mb, C("wf"), A.mult)
    vs(C("r15"), C("kr"), 15.0, A.is_equal)
    vs(C("fm"), C("kr"), 15.0, A.is_lt)
    vs(C("mk0"), C("kr"), 0.0, A.is_equal)
    vs(C("mk1"), C("kr"), 1.0, A.is_equal)
    vs(B("ib"), ij, C("k"), A.is_equal)
    vcopy(full("kmf", RO * M), full("kmi", RO * M))
    vs(i16, B("ib"), 1.0, A.mult)
    vset(one, 1.0)
    vs(C("t6"), C("kr"), 10.0, A.is_lt, 384.0, A.mult)
    vs(C("off"), C("t6"), -256.0, A.add, C("fm"), A.mult)
    vt(B("lxa"), B("ib"), c15, A.add)
    vs(B("m1b"), B("lxa"), C("fm"), A.mult)
    vs(B("lo"), c0m, C("r15"), A.mult, 1.0 / 16, A.mult)
    vt(B("lx0"), B("m1b"), B("lo"), A.add)
    vs(H("idw"), B("ib"), C("mk1"), A.mult, 2.0 ** -11, A.mult)
    cv("io", full("io16", 512), full("ij", 512), 1.0 / 16)
    for k in range(4):
        cv("k1", C("id%d" % k), C("mk1"), k / 64.0, C("off"))
    for c in (0, 1024):
        vs(("xb", c, c + 1024), ("xin", c, c + 1024), C("fm"), A.mult, C("off"), A.add)
    vset(("xb", P, P + 16), 0.0)
    vs(pw, I("ic"), C("kr"), A.add)
    cv("k2", PH, pw, bias=-1023.5)
    vcopy(pos, pw)
    cv("k1", C("flw"), C("fm"), 2.0, -1.0)
    cv("k1", C("t1"), C("fm"), 24576.0, -8192.0)
    for nm, cn in (("bs", "r15"), ("bdv", "t1")):
        cv("k2", full(nm, 144), mb, C(cn))
    vs(full("bsq", 144), mb, C("flw"), A.mult, 16.0, A.mult)
    vs(full("be", 144), mb, C("flw"), A.mult, -2048.0, A.mult)
    cv("k2", full("bds", 144), mb, 8192.0)
    vt(B("hi"), c15, B("ib"), A.subtract)
    cv("k2", B("nxb"), B("hi"), C("fm"))
    diags = [(B("dvoid"), 15728640.0), (B("d24"), -2.0 ** 24), (B("hb"), -0.5), (n16, -1.0), (H("h16"), 0.5), (H("n2k16"), -2048.0), (B("d23"), 3 * 2.0 ** 22),
             (B("dvd"), -4456448.0), (B("d4k"), 4096.0), (H("d2047"), 2047.0), (H("dhf"), 1023.5), (H("dnhf"), -1023.5), (H("d2064"), 2064.0), (B("n8k"), -8192.0), (B("d8k"), 8192.0), (S("n32"), -1.0), (H("d2k16"), 2048.0),
             (H("m2i"), -2.0), (H("p2i"), 2.0), (H("p12"), 2.0 ** -12)]
    for o, v in diags[:len(diags) - PAR["ng"]]:
        cv("k", o, B("ib"), v)
    vset(B("zero"), 0.0)
    vs(H("nkr"), B("ib"), C("kr"), A.mult, -1.0, A.mult)
    vs(B("i2f"), B("ib"), C("fm"), A.mult, 2.0, A.mult)
    vset(B("one"), 1.0)
    vset(full("zf", 16), 0.0)
    cv("k1", C("noff"), C("off"), -1.0)
    cv("k1", full("noff", 16), full("zf", 16), bias=C("noff"))
    vs(I("jb"), ij, 112, A.bitwise_and)
    vcopy(C("kg"), C("ikg"))
    vs(S("ob"), I("jb"), C("kg"), A.is_equal)
    vs(C("iodd"), C("ik"), 1, A.bitwise_and)
    vcopy(C("odd"), C("iodd"))
    cv("k2", H("ob16"), S("ob"))
    cv("k2", H("nob16"), S("ob"), -1.0)
    vs(I("jb"), ij, 113, A.bitwise_and)
    vs(H("obe"), I("jb"), C("kg"), A.is_equal)
    vs(H("obo"), I("jb"), -1.0, A.add, C("kg"), A.is_equal)
    vs(I("jb"), ij, 126, A.bitwise_and)
    vt(C("t5"), C("k"), C("odd"), A.subtract)
    vs(H("l2"), I("jb"), C("t5"), A.is_equal)
    cv("k1", C("t2"), C("odd"), -1023.5, 1023.5)
    cv("k1", C("t3"), C("odd"), 2048.0)
    for m in range(M):
        cv("k2", ("cmq", 96 * m, 96 * m + 96), ("cmq", 96 * m - 96, 96 * m) if m else ("one16", 0, 96), 1.0 if m else C("t2"), C("t3") if m else 0.0)
    vs(C("ib16"), C("ik"), 16, A.bitwise_and)
    vcopy(C("t5"), C("ib16"))
    vs(I("jb", 0, 32), ("ij", 0, 32), 16, A.bitwise_and)
    vs(full("mk32", 32), I("jb", 0, 32), C("t5"), A.is_equal)
    vset(("tr", 32, 40), 0.5)
    vset(("kr16", 1, 2), -1.0)
    vset(("nib", 1, 2), 0.25)
    cv("k2", H("if16"), B("ib"), C("fm"))
    cv("k1", C("c128r"), C("mk0"), 128.0)
    vs(C("n128"), C("r15"), C("mk0"), A.add, -128.0, A.mult)
    vs(C("c2"), C("off"), 2.0, A.mult, C("c128r"), A.subtract)
    cv("k1", C("sc5"), C("fm"), 0.5)
    cv("k1", C("bi5"), C("fm"), -0.125)
    cv("k1", C("nfm"), C("fm"), -1.0)
    cv("k1", C("sc1"), C("mk1"), 32768.0)
    cv("k1", C("padx"), C("kr"), bias=float(P))
    vs(C("bi1"), C("mk1"), 8192.0 - P - 1, A.mult, C("padx"), A.add)
    cv("k1", C("q4"), C("r15"), 4.0)
    vset(C("pm0"), 1.0)
    vset(C("pm1"), -1.0)
    vt(C("mid"), C("fm"), C("mk0"), A.subtract)
    vt(C("t5"), C("mid"), C("r15"), A.subtract)
    vs(H("la"), B("ib"), C("mid"), A.mult, -1.0, A.mult)
    cv("k2", H("lb"), c0m, C("t5"))
    vt(H("lj"), H("la"), H("lb"), A.add)
    vs(S("m5"), c15, C("mk0"), A.mult, 16.0, A.mult)
    cv("k2", B("m4b"), B("ib"), C("fm"))
    vs(("aa", 0, 1), C("wf"), C("mk0"), A.mult)
    vs(("aa", 1, 2), C("wf"), C("r15"), A.mult)
    vs(C("t3"), C("wf"), C("mid"), A.mult)
    vs(("aa", 2, 3), C("t3"), C("noff"), A.mult)
    mm(("p5", 0, 3), [(S("ob"), ("aa", 0, 3))])
    vcopy(C("wa", 2), ("p5", 0, 2))
    vcopy(C("ucor"), ("p5", 2, 3))
    vs(C("cw"), C("wb"), 16.0, A.mult, C("wa"), A.subtract)
    vs(C("wq0"), C("cw"), C("flw"), A.mult)
    vs(C("wq1"), C("wf"), C("fm"), A.mult, C("wq0"), A.add)
    vs(C("wq2"), C("wq1"), 2048.0, A.is_ge, -4096.0, A.mult)
    vs(C("wq2"), C("wq2"), C("mid"), A.mult, C("wq1"), A.add)
    vs(C("wq3"), C("wq1"), -2048.0, A.is_lt, 4096.0, A.mult)
    vt(C("wq"), C("wq2"), C("wq3"), A.add)
    cv("k2", full("bq", 144), mb, C("wq"))
    vs(B("dw15"), B("ib"), C("wb"), A.mult, 0.5, A.mult)
    vs(B("ndw15"), B("ib"), C("wb"), A.mult, -0.5, A.mult)
    vs(B("wb1"), S("ob"), C("fm"), A.mult, C("wf"), A.mult)
    vset(("w0", 0, W0), 0.0)
    vset(("w1", 0, W0), 0.0)
    vset(full("msg", 80), 0.0)

    def tab(k, c0=0, c1=TW):
        return ("tb%d" % k, W0 + c0, W0 + c1)
    last = 0
    for k in range(4):
        r = TP[k]
        last = add("g", 1.0, lambda g, T, x, r=r, k=k: x["send"](x["dn"], tab(0, *r), ("tmo",) + r, "ta0", "lown", k == 1), [("tmo",) + r], [], done=lambda x: ("lown", 0), after=[last] if k else [])
    step, gc = [last], last
    for o, v in diags[len(diags) - PAR["ng"]:]:
        gc = add("g", 0.44, lambda g, T, x, o=o, v=v: g.affine_select(_ap(T, o), _ap(T, B("zero")), [[-1, 128]], A.not_equal, v, 0, 1), [B("zero")], [o], after=[gc])
    for k in range(4):
        c = 0
        while c < NE:
            n = 1
            while c + n < NE and EXP[c + n][k + 1] == EXP[c][k + 1]:
                n += 1
            gc = iota(("cf32", k * NE + c, k * NE + c + n), [[0, n]], EXP[c][k + 1], 0, [gc])
            c += n
    vcopy(full("cf16", 4 * NE), full("cf32", 4 * NE))

    def table(k, after):
        add("x", 18.0 if k else 11.0, None, [], [tab(k)], done=(lambda x, k=k: ("ta%d" % k, x["ta"][k])), after=step)

        def far(g, T, x):
            if x["far"] is not None:
                x["send"](x["far"], tab(RO - 1), full("tmo", TW), "ta%d" % (RO - 1), "lown")

        def e(g, T, x):
            if x["fwd"][k] is not None:
                for c in ((0, HC), (HC, TW)) if x["cross"] else ((0, TW),):
                    x["send"](x["fwd"][k], tab(k + 1, *c), tab(k, *c), "ta%d" % (k + 1), "ls%d" % k, c[0] > 0)
        if k < RO - 1:
            step[0] = add("g", 2.0, e, [tab(k)], [], done=(lambda x, k=k: ("ls%d" % k, x["lf"][k])), after=after)
        if k == 1:
            step.append(add("g", 1.0, far, [full("tmo", TW)], [], done=lambda x: ("lown", 0), after=[step[0]]))

    mord = []
    for m, h, q, zb in PAR["items"]:
        if m not in mord:
            mord.append(m)
    QB, LP = ("p2", "p4"), {m: k for k, m in enumerate(mord)}
    UP, NF = ("p1", 0, 128), ("p7", 0, 128)

    def diag(t):
        for m in mord:
            cv("dk", ("dk", m * 128, m * 128 + 128), B("ib"), ("kmf", t * M + m, t * M + m + 1))

    def lists(t):
        if t:
            vt(I("ui"), UP, S("gu"), A.add)
        else:
            vcopy(I("ui"), UP)
        vs(I("u"), I("ui"), 4095, A.bitwise_and)
        if "sq" in PAR["s"]:
            sa(I("sq"), I("u"), F.Square)
        else:
            vt(I("sq"), I("u"), I("u"), A.mult)
        cv("u16", H("u16"), I("u"), bias=-2048.0)
        vs(I("sh"), I("sq"), 5, A.arith_shift_right, 2047, A.bitwise_and)
        cv("sh16", H("sh16"), I("sh"), bias=-1023.5)
        for k in range(2):
            o = [(QB[k], j * 128, j * 128 + 128) for j in range(2)]
            mm(o[0], [(("dk", mord[2 * k + j] * 128, mord[2 * k + j] * 128 + 128), H("u16"), o[j]) for j in range(2)], stop=False)
            mm(o[0], [(i16, H("sh16"), o[j]) for j in range(2)], start=False)
        lw = PAR["lw"]
        for k in range(0, M, lw):
            c = (LP[mord[k]] * 128, (LP[mord[k]] + lw) * 128)
            qv = (QB[k // 2], (k % 2) * 128, (k % 2 + lw) * 128)
            vs(("rr",) + c, qv, MAGIC, A.add, MAGIC, A.subtract)
            vt(("q16",) + c, qv, ("rr",) + c, A.subtract)
            cv("ql", ("ql",) + c, ("q16",) + c, bias=1023.5)

    diag(0)
    for c in (0, 64):
        mm(("p1", c, c + 64), wrapped("bu0", "xin", 16 * c, 1024))
    lists(0)
    for k in range(4):
        w = (("p5", "p3", "p0", "p7")[k], 0, 512)
        mm(w, [(H("idw"), full("io16", 512))], stop=False)
        mm(w, [(B("lx0"), ("xin", 512 * k, 512 * k + 512))], start=False)
        sa(("w0", W0 + 512 * k, W0 + 512 * k + 512), w, F.Identity, bias=C("id%d" % k))
    for c in (0, 64):
        mm(("p7", c, c + 64), wrapped("bs", "xin", 16 * c, 1024))
    sa(B("sgn"), ("p7", 0, 128), F.Identity, scale=2.0)

    def rows(w, r, c, src, sem):
        add("d", 0.1, lambda g, T, x: g.sync.dma_start(T[w][r:128:16, c:c + P], _ap(T, S(src))), [S(src)], [(w, c, c + P)], done=lambda x: (sem, 16), lat=4.0)
        ops[-1]["acc"] = ops[-1]["row"] = True

    msgops = {}
    for t in range(RO):
        SEC[0] = t
        w, wn = "w%d" % (t % 2), "w%d" % (1 - t % 2)
        X, XA, XF = (w, W0, W0 + P), (w, 0, NX), (w, W0 + P, NX)
        table(t, [msgops[(s, t - 1)] for s in range(t, RO)] if t else [gc])
        for r in range(1 if t < RO - 1 else 2):
            add("d", 0.1, lambda g, T, x, w=w, r=r: g.sync.dma_start(_ap(T, S(("rt", "rt1")[r])), T[w][r:128:16, W0:W0 + P]), [X], [S(("rt", "rt1")[r])],
                done=(lambda x, s="fa%d" % (t + r): (s, 16)), lat=9.0)
        for k, o in enumerate([XF] if t < RO - 1 else [(wn, W0, W0 + P), (wn, W0 + P, NX)]):
            add("d", 0.1, lambda g, T, x, X=X, o=o: g.sync.dma_start(_ap(T, o), _ap(T, X)), [X], [o], done=(lambda x, s="fb%d" % (t + k): (s, 16)), lat=12.0)
        for m in mord:
            c = (m * 128, m * 128 + 128)
            vt(("eq",) + c, ("q16",) + c, PH, A.is_equal)
        if t < RO - 1:
            diag(t + 1)
        seen, ns, slot = [0] * len(PART), 0, {0: 0, 1: 0}
        for m, h, q, zb in PAR["items"]:
            h0, h1 = PART[h]
            n = h1 - h0
            wc = (LP[m] * 128 + h0, LP[m] * 128 + h1)
            o = (m * P + 16 * h0, m * P + 16 * h1)
            zz = ("p%d" % zb, slot[zb], slot[zb] + n)
            slot[zb] += n
            parts = [(i16, ("q16",) + wc), (H("l2"), ("cmq", 96 * m, 96 * m + n)), (B("d24"), B("one", 0, n)), (B("dvoid"), ("eq",) + wc)]
            grp = PAR["grp"]
            if grp == 2:
                mm(zz, parts)
                parts = []
            if q == "v":
                for k in range(0, n, PAR["vh"]):
                    k2 = min(n, k + PAR["vh"])
                    vgt(("mx", o[0] + 16 * k, o[0] + 16 * k2), X, ("ql", wc[0] + k, wc[0] + k2), ("xb", 16 * (h0 + k), 16 * (h0 + k2)), A.max)
                mm(zz, parts + wrapped("bdv", "mx", o[0], 16 * n), free=not grp, start=not grp)
            else:
                for k in range(0, n, PAR["sh"]):
                    k2 = min(n, k + PAR["sh"])
                    gather("s", ("mx", o[0] + 16 * k, o[0] + 16 * k2), X, ("ql", wc[0] + k, wc[0] + k2))
                for lo in range(0, 16 * n, 512):
                    hi = min(16 * n, lo + 512)
                    wk = (PAR["wb"][ns % 4], 0, hi - lo)
                    ns += 1
                    mm(wk, [(B("nxb"), ("xb", 16 * h0 + lo, 16 * h0 + hi))], stop=False)
                    mm(wk, [(H("if16"), ("mx", o[0] + lo, o[0] + hi))], start=False)
                    sa(("ab", o[0] + lo, o[0] + hi), wk, F.Abs)
                mm(zz, parts + wrapped("bds", "ab", o[0], 16 * n), free=not grp, start=not grp)
            bb = (S("b0", h0, h1), S("b1", h0, h1))
            seen[h] += 1
            if seen[h] == 1:
                cv("fold", bb[1], zz)
            else:
                vt(I("bk", h0, h1) if seen[h] == M else bb[seen[h] % 2], bb[1 - seen[h] % 2], zz, A.min)
        tb = "tb%d" % t
        TB = tab(t)
        for s in range(t):
            i = _LK.index((t, s))
            add("x", 7.0, None, [], [("land", 20 * i, 20 * i + 20)], done=(lambda x, s=s, t=t: ("m%d_%d" % (t, s), x["mn"][(t, s)])), after=[msgops[(t, s)]])
            cv("lu", ("lu", 2 * i, 2 * i + 1), ("land", 20 * i, 20 * i + 1), ("land", 20 * i + 1, 20 * i + 2), C("kr"))
            vscat((tb, 0, TW + W0), ("lu", 2 * i, 2 * i + 1), ("land", 20 * i + 4, 20 * i + 20))
        N, SG, DQ = ("p6", 0, 128), ("p7", 128, 256), ("p7", 256, 384)
        nb = 0
        for h, c in enumerate(PART):
            o, pn = 16 * c[0], 16 * (c[1] - c[0])
            US = ("p7",) + c
            vs(I("q", *c), I("bk", *c), 2047, A.bitwise_and)
            cv("qsl", ("qsl",) + c, I("q", *c))
            shared(("gq", 0), X, "qsl", c[0], c[1], PAR["xq"][h], C("n128"), step=PAR["xh"])
            mm(US, wrapped("bq", "gq", o, pn), free=True)
            cv("uq", I("uq", *c), US, bias=C("ucor"))
            vs(I("uq2", *c), I("uq", *c), 4095, A.bitwise_and)
            vt(I("uu", *c), I("uq2", *c), I("u", *c), A.mult)
            vs(I("h", *c), I("uu", *c), 4, A.arith_shift_right, 4095, A.bitwise_and)
            cv("hl", ("hl",) + c, I("h", *c))
            mm(col(SG, c[0], c[1] - c[0]), [(B("hb"), B("sgn", *c))] + wrapped("bsq", "gq", o, pn), free=True)
            shared(("ga", 0), TB, "hl", c[0], c[1], PAR["tq"][h], step=32)
            for k, lo in enumerate(range(o, o + pn, 512)):
                hi = min(o + pn, lo + 512)
                wk = (PAR["sb"][nb], 0, hi - lo)
                nb += 1
                mm(wk, [(B("nxb"), ("xb", lo, hi))], stop=False)
                mm(wk, [(H("lj"), ("gq", lo, hi))], start=False, stop=False)
                mm(wk, [(B("i2f"), ("ga", lo, hi))], start=False)
                sa(("ab2", lo, hi), wk, F.Abs, bias=C("c2"))
        vs(I("di"), I("bk"), 13, A.arith_shift_right)
        cv("d16", H("d16"), I("di"))
        cv("qs16", H("qs16"), full("qsl"), bias=-1023.5)
        sa(B("inv"), SG, F.Abs)
        vt(B("vd"), H("qs16"), PH, A.is_equal)
        vt(H("cm"), H("qs16"), PH, A.min)
        vt(H("lg"), H("qs16"), PH, A.max)
        mm(N, [(B("d23"), B("one")), (H("n2k16"), H("d16")), (B("dvd"), B("vd")), (n16, pos)], stop=False)
        for h, c in enumerate(PART):
            mm(("p6",) + c, wrapped("be", "ab2", 16 * c[0], 16 * (c[1] - c[0])), start=False, stop=h == len(PART) - 1)
        cv("r2", B("r2"), S("rt"), 2.0)
        if t < RO - 1:
            mm(("p7", 384, 512), [(B("ib"), B("r2")), (S("n32"), S("rt"))], free=True)
            cv("rf", S("rf"), ("p7", 384, 512), bias=1.0 / 16)
            rows(w, 0, W0 + P, "rf", "fc%d" % t)
        else:
            cv("rf", S("rf"), B("r2"), 0.5)
            vt(S("ta"), S("rt"), S("rf"), A.subtract)
            cv("rf", S("gu"), S("ta"), 16.0)
            cv("rf", S("hpr"), S("ta"), -16.0, 1.0)
            vs(S("rf1"), S("rt1"), MAG1, A.add, MAG1, A.subtract)
            for k, (r, c, src) in enumerate(((0, W0, "rf"), (0, W0 + P, "rf"), (15, W0, "gu"), (15, W0 + P, "hpr"), (1, W0, "rf1"), (1, W0 + P, "rf1"))):
                rows(wn, r, c, src, "fc%d" % (t + k))
        SA, XI, LG, HH = ("p0", 0, 128), ("p0", 128, 256), ("p3", 0, 128), ("p3", 128, 256)
        o1, hf = col(one, 0), H("h16")
        ob, nob, dw, top = H("ob16"), H("nob16"), H("dw"), H("d2047")
        SA2, LG2 = ("p0", 256, 384), ("p3", 256, 384)
        mm(SA, [(i16, H("cm")), (H("dhf"), one), (B("d4k"), B("inv"), XI)])
        parts = [(i16, H("lg"))]
        if t < RO - 1:
            cv("hh", H("hh"), full("hl"), bias=-2048.0)
            parts += [(i16, H("hh"), HH), (H("d2064"), one, HH), (H("nkr"), one, HH)]
        mm(LG, parts)

        def highest(src, r, dst, oh, wm):
            vred(C(r), src, A.max)
            vs(oh, src, C(r), A.not_equal)
            vs(full("dg", 32), full("mk32", 32), C(r), A.mult)
            vtr(full("tr", 32), full("dg", 32))
            vred(C(dst), full("tr", 33), A.max)
            if wm:
                vs(wm, C(r), C(dst), A.is_equal)
        A1, EP, A2, NC, DU = ("p5", 128, 131), ("p2", 384, 384 + NE), ("p7", 132, 137), ("p4", 256, 257), ("p4", 257, 258)
        wm = ("msg", t * 20 + 1, t * 20 + 2)
        highest(N, "r1", "kmax", B("oh"), wm)
        mm(SA, [(B("n8k"), B("oh")), (B("n8k"), B("oh"), XI)], start=False)
        mm(LG, [(B("n8k"), B("oh"))] + ([(B("n8k"), B("oh"), HH)] if t < RO - 1 else []), start=False)
        vred(("aa", 0, 1), SA, A.max)
        vred(("aa", 2, 3), XI, A.max)
        sa(S("jk"), LG, F.Relu, bias=1023.5, acc=("aa", 1, 2))
        ea, eb, ei = [("aa2", k, k + 1) for k in (2, 3, 4)]
        for k in range(3):
            vs(("aa2", 2 + k, 3 + k), C("r1"), C("kmax"), A.is_equal, ("aa", k, k + 1), A.mult)
        mm(A1, [(H("dnhf"), col(one, 0, 2), col(A1, 0, 2))])
        mm(A1, [(ob, ("aa2", 2, 4), col(A1, 0, 2)), (ob, ei, col(A1, 0)), (H("obe"), ea, col(A1, 2)), (H("obo"), eb, col(A1, 2))], start=False)
        A3 = ("p2", 400, 404)
        mm(A3, [(B("d4k"), B("one", 0, 2), col(A3, 0, 2)), (top, o1, col(A3, 3))])
        mm(A3, [(ob, ("aa2", 2, 4), col(A3, 0, 2)), (nob, ei, col(A3, 0)), (nob, ei, col(A3, 1)), (ob, ea, col(A3, 2)), (nob, eb, col(A3, 3)), (nob, ei, col(A3, 3))], start=False)
        N2 = ("p1", 128, 256)
        sa(S("nf"), N, F.Identity, scale=-1.0)
        mm(N2, [(B("d24"), B("inv")), (S("n32"), S("nf"))])
        vs(B("lo"), H("cm"), col(A1, 0), A.is_le)
        vs(B("hi"), H("cm"), col(A1, 1), A.is_ge)
        mm(N2, [(B("d24"), B("lo")), (B("d24"), B("hi"))], start=False)
        if t < RO - 1:
            sa(S("jk"), HH, F.Relu, acc=("msg", t * 20, t * 20 + 1))
        ex = [("ex", k * NE, k * NE + NE) for k in range(3)]
        if "ex" in PAR["s"]:
            cv("aw", ("aa", 4, 7), ("aa", 0, 3), wm)
        for k in range(3):
            if "ex" in PAR["s"]:
                cv("ex", ex[k], ("cf16", k * NE, k * NE + NE), ("aa", 4 + k, 5 + k))
            else:
                vs(ex[k], ("cf16", k * NE, k * NE + NE), ("aa", k, k + 1), A.mult, wm, A.mult)
        mm(EP, [(ob, e) for e in ex] + [(i16, ("cf16", 3 * NE, 4 * NE))])
        cv("nl", ("nl", 0, 1), col(A1, 2))
        if "a" in PAR["s"]:
            sa(C("a", NE), EP, F.Relu)
        else:
            vs(C("a", NE), EP, 0.0, A.max)
        nib = ("nib", 0, 1)
        gather("s", full("nc", 16), X, ("nl", 0, 1), bias=C("bi5"), scale=C("sc5"))
        gather("s", full("ncb", 16), X, ("nl", 0, 1), scale=C("nfm"))
        sa(nib, ("nc", 0, 1), F.Identity, bias=("nc", 1, 2))
        sa(C("diff"), ("nc", 0, 1), F.Identity, scale=2.0, bias=("ncb", 0, 1))
        if t < RO - 1:
            mm(NC, [(B("wb1"), nib, DU), (B("wb1"), ("ncb", 0, 1), DU), (B("m1b"), nib), (B("m4b"), ("nib", 1, 2))])
            cv("w15", (w, 15, 16), NC, bias=C("diff"))
            sa(("xl", 0, 1), C("diff"), F.Identity, scale=C("sc1"), bias=C("bi1"))
            sa(full("nb", 16), full("zf", 16), F.Identity, bias=nib)
            vscat(full("xb", P + 16), ("xl", 0, 1), full("nb", 16))
            vs(H("f0"), pos, col(A3, 0), A.is_gt)
            vs(H("f1m"), pos, col(A3, 1), A.is_gt)
            vs(S("gu"), pos, col(A3, 2), A.is_equal, DU, A.mult)
            mm(UP, [(i16, H("u16")), (H("d2k16"), one), (B("ndw15"), B("sgn"))], stop=False)
            mm(NF, [(B("ib"), B("sgn")), (H("m2i"), H("f0")), (H("p2i"), H("f1m"))])
            sa(B("sgn"), NF, F.Abs)
            mm(UP, [(B("dw15"), B("sgn"))], start=False)
        else:
            mm(NC, [(B("m4b"), nib), (S("m5"), C("diff"))])
            cv("w15", (wn, 15, 16), NC, bias=C("q4"))
        vs(B("v"), H("lg"), col(A1, 1), A.is_le)
        vs(H("dw"), B("ib"), col(A3, 3), A.mult, 0.0, A.max)
        vs(H("g0"), pw, C("a"), A.is_gt, C("ba"), A.mult)
        vs(H("g0b"), pw, C("a"), A.is_gt, C("x"), A.mult)
        vs(H("g1"), pw, C("b"), A.is_gt, C("m3"), A.mult)
        vs(H("gr"), pw, C("aI"), A.max, C("bI"), A.min)
        vs(H("g3"), pw, C("a"), A.is_equal, C("a1"), A.mult)
        PL = ("p5", 0, 128)
        mm(PL, [(i16, pw), (i16, H("g0")), (hf, H("g0b")), (H("p12"), H("g0b")), (H("m2i"), H("gr")), (n16, H("g3")), (n16, H("g1"))], stop=False)
        mm(SA2, [(i16, H("cm")), (H("dnhf"), one), (B("d8k"), B("v")), (dw, one), (B("zero"), B("one", 0, 1), ("p0", 384, 385))])
        mm(LG2, [(i16, H("lg")), (H("dnhf"), one), (B("d8k"), B("v"))])
        d_, dl, t3, t2, c_ = [col(A2, k) for k in range(5)]
        mm(A2, [(top, o1, d_), (dw, o1, dl), (dw, o1, t3), (ob, ea, t3), (top, o1, t2), (ob, ea, t2), (nob, eb, t2), (top, o1, c_), (dw, ("kr16", 1, 2), c_)], stop=False)
        highest(N2, "r2", "kmax2", B("oh2"), None)
        mm(SA2, [(B("d8k"), B("oh2"))], start=False)
        mm(LG2, [(B("d8k"), B("oh2"))], start=False)
        cc, dd = ("aa2", 0, 1), ("aa2", 1, 2)
        vred(C("c2r"), ("p0", 256, 385), A.min, True)
        sa(S("jk"), LG2, F.Relu, scale=-1.0, acc=C("d2r"))
        vs(cc, C("r2"), C("kmax2"), A.is_equal, C("c2r"), A.mult)
        vs(dd, C("r2"), C("kmax2"), A.is_equal, C("d2r"), A.mult)
        mm(A2, [(ob, cc, dl), (ob, cc, t3), (nob, cc, c_)] + [(nob, dd, o) for o in (d_, dl, t3, t2)], start=False)
        vs(H("g4"), pw, t3, A.is_gt, C("mba"), A.mult)
        vs(H("g5"), pw, t2, A.is_gt, dl, A.mult)
        vs(H("g6"), pw, d_, A.is_gt, dl, A.mult)
        mm(PL, [(n16, H("g4")), (n16, H("g5")), (i16, H("g6"))], start=False)
        vs(full("pl"), PL, C("pb"), A.add, float(W0), A.add)
        if t < RO - 1:
            shared((wn, W0), XA, "pl", 0, 128, PAR["rv"])
            lists(t + 1)
            vs(C("h0", 2), C("pm0", 2), dl, A.mult, C("k0"), A.add)
            vs(H("h0"), pos, C("a"), A.is_gt, C("h0"), A.mult)
            vs(H("h1"), pos, C("b"), A.is_gt, C("h1"), A.mult)
            vs(H("hr"), pos, C("aI"), A.max, C("bI"), A.min)
            vs(H("h4"), pos, c_, A.is_gt, C("mba"), A.mult)
            vs(H("h5"), pos, d_, A.is_gt, C("mba"), A.mult)
            mm(POS, [(i16, pos), (H("m2i"), H("hr")), (i16, H("f0")), (n16, H("f1m")), (i16, H("h0")), (i16, H("h1")), (n16, H("h4")), (i16, H("h5"))])
            vs(PH, POS, C("pb"), A.add, -1023.5, A.add)
            cv("pos", pos, POS, bias=C("pb"))
            sa(("msg", t * 20 + 4, t * 20 + 20), full("noff", 16), F.Identity, bias=nib)
            for t2 in range(t + 1, RO):
                def e(g, T, x, t=t, t2=t2):
                    i = _LK.index((t2, t)) * 20
                    x["send"](x["user"][t2], ("land", i, i + 20), ("msg", t * 20, t * 20 + 20), "m%d_%d" % (t2, t), "lmsg")
                msgops[(t2, t)] = add("g", 1.5, e, [("msg", t * 20, t * 20 + 20)], [], done=lambda x: ("lmsg", 0), after=step if t2 == t + 1 else [msgops[(t2 - 1, t)]])
        else:
            for k in range(4):
                c = (512 * k, 512 * k + 512)
                gather("vs"[k % 2], ("yo",) + c, (wn, 0, NX), ("pl", 32 * k, 32 * k + 32), C("noff"))
                add("sd" if k % 2 else "d", 0.1, lambda g, T, x, k=k, c=c: (g.scalar if k % 2 else g.sync).dma_start(T.y[:, c[0]:c[1]], _ap(T, ("yo",) + c)), [("yo",) + c], [],
                    done=(lambda x, k=k: ("st%d" % k, 16)), lat=2.0)
    return ops


_QS = {"v": "sv", "s": "ss", "t": "st", "g": "sg"}
_CACHE = {}


def costs(ops, model):
    cyc, gc, fix = model[:3]
    out = []
    for o in ops:
        f, c, n = o["cost"]
        if o["q"] in "vs" and n:
            f += (0.05 if o["q"] == "v" else 0.065) + n * gc * cyc
        elif o["q"] == "v":
            f += fix + c * cyc if fix else max(64, c) * cyc
        elif o["q"] == "s":
            f += fix + 0.015 + c * cyc if fix else (60 + max(64, c)) * cyc
        else:
            f += c * cyc
        out.append(f + 0.02)
    return out


def timing(ops, order, cost, wake, own):
    fin, why, free, last = [0.0] * len(ops), [-1] * len(ops), {}, {}
    for i in order:
        q, after, data, banks = ops[i]["t"]
        st, w = 0.0, -1
        if q in free:
            w = free[q]
            st = fin[w]
        for j in after:
            if fin[j] > st:
                st, w = fin[j], j
        for j, lat, same in data:
            s = fin[j] + lat + (own if same else wake)
            if s > st:
                st, w = s, j
        for b in banks:
            j = last.get(b)
            if j is not None:
                if j[0] != q:
                    j[1], j[0] = j[2], q
                if j[1] >= 0 and fin[j[1]] + wake > st:
                    st, w = fin[j[1]] + wake, j[1]
                j[2] = i
            else:
                last[b] = [q, -1, i]
        fin[i], why[i] = st + cost[i], w
        if q != "x":
            free[q] = i
    return fin, why


def first_order(ops, succ, cost, wake, own):
    n = len(ops)
    way = [0.0] * n
    for i in range(n - 1, -1, -1):
        way[i] = cost[i] + ops[i]["lat"] + max([0.0] + [way[j] + (own if ops[j]["qq"] == ops[i]["qq"] else wake) for j in succ[i]])
    left, est, ready = [len(o["deps"]) for o in ops], [0.0] * n, {}
    for i in range(n):
        if not left[i]:
            ready.setdefault(ops[i]["qq"], []).append(i)
    free, last, order = {}, {}, []
    while len(order) < n:
        best = None
        for q, l in ready.items():
            if l:
                ss = [max([est[i], free.get(q, 0.0) if q != "x" else 0.0] + [t + wake for b in ops[i]["banks"] for q2, t in last.get(b, {}).items() if q2 != q]) for i in l]
                if best is None or min(ss) < best[0]:
                    best = (min(ss), q, l, ss)
        m, q, l, ss = best
        k = max((k for k in range(len(l)) if ss[k] <= m + 0.1), key=lambda k: way[l[k]])
        i = l.pop(k)
        order.append(i)
        free[q] = f = ss[k] + cost[i]
        for b in ops[i]["banks"]:
            last.setdefault(b, {})[q] = f
        for j in succ[i]:
            est[j] = max(est[j], f + (ops[i]["lat"] + (own if ops[j]["qq"] == q else wake) if i in ops[j]["data"] else 0.0))
            left[j] -= 1
            if not left[j]:
                ready.setdefault(ops[j]["qq"], []).append(j)
    return order


def moved(ops, order, pairs):
    for i, j in pairs:
        a, b = order.index(j), order.index(i)
        if a >= b:
            continue
        need, up, stay = set(ops[i]["deps"]), [i], []
        for k in order[b - 1:a:-1]:
            if k in need:
                need.update(ops[k]["deps"])
                up.append(k)
            else:
                stay.append(k)
        if j in need:
            continue
        order = order[:a] + up[::-1] + [j] + stay[::-1] + order[b + 1:]
    return order


def graph():
    ops = build()
    hist = {}
    for i, o in enumerate(ops):
        deps = set()
        q = o["qq"] = "s" if o["q"] == "sd" else o["q"]
        rw = [(0, r) for r in o["reads"]] + [(1, r) for r in o["writes"]]
        for kind, r in rw:
            for (j, k2, a, b, q2) in hist.get(r[0], ()):
                if _ps(r) and q2 == q == "t" and o["acc"] and ops[j]["open"]:
                    continue
                if "row" in o and "row" in ops[j] and kind and o["sec"] == ops[j]["sec"]:
                    continue
                if (kind or k2) and a < r[2] and r[1] < b:
                    deps.add(j)
        for kind, r in rw:
            hl = hist.setdefault(r[0], [])
            if kind and not o.get("acc"):
                hl[:] = [e for e in hl if not (r[1] <= e[2] and e[3] <= r[2])]
            hl.append((i, kind, r[1], r[2], q))
        o["data"] = deps
        o["deps"] = sorted(deps | set(o["after"]))
        o["banks"] = sorted({r[0] for kind, r in rw if _ps(r)})
        o["t"] = (q, o["after"], [(j, ops[j]["lat"], ops[j]["qq"] == q) for j in sorted(deps)], o["banks"])
    return ops


def plan():
    if "o" in _CACHE:
        return _CACHE["o"]
    ops = graph()
    when = {a: int(b) for a, b in (x.rsplit(":", 1) for x in WHEN.split())}
    succ, left = [[] for _ in ops], [len(o["deps"]) for o in ops]
    for i, o in enumerate(ops):
        o["due"] = int(ST[3 * i:3 * i + 3], 36) if len(ST) == 3 * len(ops) else when.get(o["name"], 0) + PERIOD * max(o["sec"], 0)
        for j in o["deps"]:
            succ[j].append(i)
    order, ready = [], [i for i in range(len(ops)) if not left[i]]
    while ready:
        i = min(ready, key=lambda k: (ops[k]["due"], k))
        ready.remove(i)
        order.append(i)
        for j in succ[i]:
            left[j] -= 1
            if not left[j]:
                ready.append(j)
    last = {}
    for i in order:
        o = ops[i]
        for b in o["banks"]:
            o["data"] |= {j for q2, j in last.setdefault(b, {}).items() if q2 != o["qq"]}
            last[b][o["qq"]] = i
    cnt = {}
    for i in order:
        o = ops[i]
        if o["done"] is None:
            s = o["inc"] = _QS[o["q"]]
            v = cnt[s] = cnt.get(s, 0) + 1
            o["done"] = (lambda x, s=s, v=v: (s, v))
    _CACHE["o"] = (ops, order, cnt, None)
    return _CACHE["o"]


def links(rank, N, near, neng, send):
    def direct(r):
        return near(r + RO, r)

    def count(r):
        return neng(r, r - 1) * (1 if near(r, r - 1) else 2)
    dn, far = (rank - 1) % N, (rank - RO) % N
    x = {"send": send, "user": {t: (rank - 1 - t) % N for t in range(RO)}}
    x["dn"], x["far"], x["cross"] = dn, far if direct(far) else None, not near(rank, dn)
    x["fwd"] = [None if k == RO - 2 and direct(dn) else dn for k in range(RO - 1)]
    x["lf"] = [0 if d is None else count(rank) for d in x["fwd"]]
    x["ta"] = [4 * neng(rank + 1, rank)] + [count(rank + 1)] * (RO - 1)
    if direct(rank):
        x["ta"][RO - 1] = neng(rank + RO, rank)
    x["mn"] = {(t, s): neng(rank + 1 + t, rank) for (t, s) in _LK}
    return x


def rank_program(g, core, T, topo):
    rank = T.rank_of(core)
    N = len(T.cores)

    def neng(a, b):
        return len(topo.engines(T.cores[a % N], T.cores[b % N]))

    def near(a, b):
        return topo.chip(T.cores[a % N]) == topo.chip(T.cores[b % N])

    def aide(r):
        c, d = T.cores[r], T.cores[(r - 1) % N]
        l = [h for h in topo.cores_of(c) if T.rank_of(h) is None and topo.die(h) != topo.die(c) and topo.may_write(h, d)]
        return l[0] if l and topo.chip(c) != topo.chip(d) else None

    def spare(r):
        return [e for e in topo.engines(T.cores[r], aide(r)) if e not in topo.engines(T.cores[r], T.cores[(r - 1) % N])]
    if rank is None:
        for r in range(N):
            if aide(r) == core:
                d = T.cores[(r - 1) % N]
                rid, pid, _ = topo.addr(d)
                fwd = links(r, N, near, neng, None)["fwd"]
                pieces = [(0, TP[1])] + [(k + 1, (HC, TW)) for k in range(RO - 1) if fwd[k] is not None]
                for k, c in pieces:
                    a = _ap(T, ("tb%d" % k, W0 + c[0], W0 + c[1]))
                    g.wait_ge(T.sem["ta%d" % k], len(spare(r)))
                    g.remote_dma(a, a, T.sem["ta%d" % k], T.sem.lown, pid, rid, topo.mask(core, d))
                g.wait_ge(T.sem.lown, len(pieces) * len(topo.engines(core, d)))
        return
    ops, order, cnt, _ = plan()
    tot = {}

    def send(d, out, src, rsem, lsem, aided=False):
        dst = T.cores[d]
        es = topo.engines(core, dst)
        if aided and aide(rank) is not None:
            dst, es = aide(rank), spare(rank)
        rid, pid, _ = topo.addr(dst)
        g.remote_dma(_ap(T, out), _ap(T, src), T.sem[rsem], T.sem[lsem], pid, rid, sum(1 << e for e in es))
        tot[lsem] = tot.get(lsem, 0) + len(es)
    x = links(rank, N, near, neng, send)
    eng = {"v": g.vector, "s": g.scalar, "sd": g.scalar, "t": g.tensor, "g": g, "d": g.sync}
    know, opk = {}, {}
    for i in order:
        o = ops[i]
        q = o["qq"]
        kn = dict(know.get(q, {})) if q != "x" else {}
        if q == "x":
            s, v = o["done"](x)
            tot[s] = v
        else:
            need = {}
            for j in sorted(o["data"]):
                s, v = ops[j]["done"](x)
                if v > kn.get(s, 0) and v > need.get(s, (0, 0))[0]:
                    need[s] = (v, j)
            for s in list(need):
                if any(s2 != s and opk[need[s2][1]].get(s, 0) >= need[s][0] for s2 in need):
                    need.pop(s)
            for s, (v, j) in need.items():
                eng[o["q"]].wait_ge(T.sem[s], v)
                for s2, v2 in list(opk[j].items()) + [(s, v)]:
                    kn[s2] = max(kn.get(s2, 0), v2)
            know[q] = kn
            ins = o["emit"](g, T, x)
            if o["q"] in ("d", "sd"):
                s = o["done"](x)[0]
                ins.then_inc(T.sem[s], 16)
                tot[s] = 16
            elif "inc" in o:
                ins.then_inc(T.sem[o["inc"]], 1)
        pre = dict(kn)
        if "inc" in o:
            s, v = o["done"](x)
            pre[s] = max(pre.get(s, 0), v)
        opk[i] = pre
    for s, v in list(cnt.items()) + list(tot.items()):
        if v > 0:
            g.wait_ge(T.sem[s], v)
